import numpy as np, ml_dtypes
CORES = [3,11,19,27,35,43,51,59]
N = 8
BF = ml_dtypes.bfloat16
P, U, S, RO, TH, PH = 4096, 128, 512, 3, 102, 85
def places(rng):
    c = rng.integers(0, 256, (N, 8, 3, 16)); c[:, :, 1] >>= 3
    k = rng.integers(0, 3, (N, 8, P)); a = rng.choice(np.array([4, 16, 48, 128, 255]), (N, 8, 1, P))
    m = np.take_along_axis(c, k[..., None], 2).transpose(0, 1, 3, 2)
    return np.clip(m + np.floor((2 * rng.random((N, 8, 16, P)) - 1) * a).astype(np.int64), 0, 255)
def near(rng, X, n):
    k = rng.integers(0, P, (N, 8, 1, n)); a = rng.choice(np.array([0, 8, 40, 160]), (N, 8, 1, n))
    return np.clip(np.take_along_axis(X, k, 3) + np.floor((2 * rng.random((N, 8, 16, n)) - 1) * a).astype(np.int64), 0, 255)
def parts(rng):
    X = places(rng); nb = rng.integers(0, P, (N, 8, 16, P)); v = rng.integers(0, P, (N, 8, U))
    A = np.where(rng.random((N, 8, 16, U)) < 0.6, v[:, :, None, :], rng.integers(0, P, (N, 8, 16, U)))
    return X, nb, v, A, near(rng, X, U), rng.integers(0, U, (N, 8, S)), near(rng, X, S), rng.integers(0, 4096, (N, 8, 16))
def pack(X, nb, v, A, y, j, z, w):
    fl = lambda a: np.ascontiguousarray(a.reshape(N, 128, -1)).astype(np.float32).astype(BF)
    wh = lambda a, p: np.ascontiguousarray(a.reshape(N, p, -1)).astype(np.int32)
    return {"x": fl(X), "nb": wh(nb, 128), "v0": wh(v, 8), "a0": wh(A, 128), "y0": fl(y), "j0": wh(j, 8), "z0": fl(z), "w": wh(w, 128)}
def setup_inputs(rng):
    return pack(*parts(rng))
def setup_inputs_spread(rng):
    def skew(hi, e, *shape): return (hi * rng.random(shape) ** e).astype(np.int64)
    def size(n): return np.minimum(np.exp2(8 * rng.random((N, 8, 1, n))) * rng.random((N, 8, 16, n)) * 1.5, 255).astype(np.int64)
    return pack(size(P), skew(P, 3, N, 8, 16, P), skew(P, 4, N, 8, U), skew(P, 2, N, 8, 16, U), size(U), skew(U, 3, N, 8, S), size(S), np.exp2(12 * rng.random((N, 8, 16))).astype(np.int64) - 1)
def setup_inputs_ends(rng):
    def edge(hi, *shape): return np.where(rng.random(shape) < 0.7, hi * rng.integers(0, 2, shape), rng.integers(0, hi + 1, shape))
    def bits(n):
        q = rng.integers(0, 4, (N, 8, 1, n)); m = rng.integers(0, 2, (N, 8, 16, n))
        return 255 * np.where(q == 0, 0, np.where(q == 1, 1, m))
    big = np.array([P - 1, P - 2, 1, 2, 3]); X = bits(P); X[:, :, :, 0] = 0; X[:, :, :, big] = 255
    nb = edge(P - 1, N, 8, 16, P); nb[:, 1::2, :, P - 1] = rng.choice(big, (N, 4, 16))
    v, A, y, j, z = edge(P - 1, N, 8, U), edge(P - 1, N, 8, 16, U), bits(U), edge(U - 1, N, 8, S), bits(S)
    for u in (0, 1, 6, U - 1):
        v[:, 1::2, u] = P - 1; y[:, 1::2, :, u] = 0; A[:, 1::2, 15, u] = 0; A[:, 1::2, 14, u] = P - 1
    w = 4095 * rng.integers(0, 2, (N, 8, 16)); w[:, 1] = 4095; w[:, 7] = 4095; w[:, 2] = 0
    for s in (0, S - 1): z[:, 7, :, s] = 255
    for s in (1, S - 2): z[:, 7, :, s] = 0; z[:, 7, 5, s] = 1; j[:, 7, s] = U - 1
    return pack(X, nb, v, A, y, j, z, w)
def level(s):
    return (s >> 4) + (np.arange(16) < (s & 15))
def setup_inputs_corners(rng):
    X, nb, v, A, y, j, z, w = parts(rng); kind = rng.permutation(8); a = np.arange(P); st = P // U; us = rng.permutation(U)
    ut = np.array([4075, 4087, 4089, 0, 0, 4095]); at = np.array([4093, 4089, 4087, 7, 100, 301]) & (P - 1)
    h = (((at * ut) >> 5) + at) & (P - 1); hw = (h + np.array([1, 1, 1, 128 * 7, 128 * 100, -128 * 301])) & (P - 1)
    zt = np.full((16, 6), 250); zt[0] = np.where(ut > 0, 251, 250); zt[14] = np.where(ut > 0, (ut - 3072) >> 4, 0); zt[15] = ut & 15
    for r in range(N):
        for g in range(8):
            f = kind[g]; Xg, n = X[r, g], nb[r, g]
            if f in (0, 4, 5):
                c = rng.integers(0, 256, (16, 1)); Xg[:] = c; y[r, g] = c; n[:] = (a ^ 1) if f == 5 else ((a + 1) & (P - 1))
                v[r, g] = st * rng.permutation(U) + st - 1; A[r, g] = v[r, g]; w[r, g] = rng.choice(np.array([0, 4095, 1, 2048]), 16) if f != 4 else 4095
            if f == 1: n[:] = a; A[r, g] = v[r, g]; w[r, g] = 0
            if f == 2:
                o = rng.permutation(P)
                for l in range(16):
                    for d in range(3): Xg[:, o[3 * l + d]] = level(TH * (l + 1) + d - 1); Xg[:, o[48 + 3 * l + d]] = level(PH * (l + 1) + d - 1)
                Xg[:, o[96]] = 0; Xg[:, o[97]] = level(8 * PH)
                v[r, g] = o[128:128 + U]; odd = np.arange(U) & 1; n[:, v[r, g]] = np.where(odd == 1, o[97], o[96])[None, :]
                y[r, g] = np.where(odd == 1, Xg[:, o[97]][:, None], 0)
                d = np.where(rng.random((16, U)) < 0.6 * odd, 2, rng.integers(0, 3, (16, U))); A[r, g] = o[3 * np.arange(16)[:, None] + d + 48 * odd]
                z[r, g] = 0
            if f == 3:
                q = rng.integers(0, 4, (16, P)); n[:] = np.where(q == 0, 0, np.where(q == 1, P - 1, np.where(q == 2, a, n)))
                q = rng.integers(0, 3, U); v[r, g] = np.where(q == 0, 0, np.where(q == 1, P - 1, v[r, g]))
                q = rng.integers(0, 3, (16, U)); A[r, g] = np.where(q == 0, 0, np.where(q == 1, P - 1, v[r, g])); j[r, g] = (U - 1) * rng.integers(0, 2, S)
            if f == 6: w[r, g] = 4095 * rng.integers(0, 2, 16)
            if f == 7:
                sp = np.concatenate([at, h, hw]); o = rng.permutation(np.setdiff1d(a, sp)); isp = np.zeros(P, bool); isp[sp] = True; isp[o[:8]] = True
                n[:] = np.where(isp[n], rng.choice(o[8:], (16, P)), n)
                v[r, g] = np.where(isp[v[r, g]], rng.choice(o[8:], U), v[r, g]); A[r, g] = np.where(isp[A[r, g]], rng.choice(o[8:], (16, U)), A[r, g])
                c = rng.integers(24, 57, (16, 1)); Xg[:, at] = c; Xg[:, h] = c; Xg[:, hw] = zt; Xg[:, o[:1]] = c; Xg[:, o[1:2]] = c + 60
                n[:, o[0]] = o[0]; v[r, g, us[:6]] = o[0]; y[r, g][:, us[:6]] = c; A[r, g][:15, us[:6]] = at; A[r, g][15, us[:6]] = o[1]
                Xg[:, o[4:8]] = np.stack([level(s) for s in (2052, 2051, 4080, 4079)], axis=1)
                n[:, o[2:4]] = o[[4, 6]]; n[15, o[2:4]] = o[[5, 7]]; v[r, g, us[6:8]] = o[2:4]; y[r, g][:, us[6:8]] = 0
                w[r, g] = 3072; w[r, g, 14] = 16; w[r, g, 15] = 1
                ss = rng.permutation(S)[:48].reshape(6, 8); z[r, g][:, ss] = zt[:, :, None]; j[r, g][ss] = us[:6][:, None]
    return pack(X, nb, v, A, y, j, z, w)
def setup_inputs_crowd(rng):
    X, nb, v, A, y, j, z, w = parts(rng); h = U // 2
    for q in range(N):
        home = (q - 1) % N; miss = int(rng.integers(0, 8))
        for g in range(8):
            Xg, n, m = X[q, g], nb[q, g], g & 3; pl = rng.permutation(P)
            if m == 2: i = int(np.argmin(pl)); pl[i] = pl[0]; pl[0] = 0
            o, e, b = pl[0], pl[1], pl[2]
            ev = pl[16:16 + h].copy() if m == 2 else np.full(h, e)
            if m & 1: ev[rng.integers(0, h)] = pl[3]
            od = np.full(h, o)
            if (g + q) & 1: od[rng.integers(0, h)] = pl[4]
            v[q, g, 0::2] = ev; v[q, g, 1::2] = od; n[:, ev] = ev[None, :]
            if m != 3: n[:, o] = b; n[:, pl[4]] = pl[5]
            Xg[:, b] = 10; Xg[:, o] = 250; Xg[:, pl[6]] = 240; Xg[:, e] = 200
            if m == 2: Xg[:, b] = 250; Xg[:, pl[8]] = 10; n[:, b] = pl[8]
            A[q, g, :, 0::2] = ev; A[q, g, :, 1::2] = (o, o, o, pl[6])[m]
            if m == 1: A[q, g, :, 1 + 2 * int(rng.integers(0, h))] = pl[6]
            t = 2 * rng.integers(0, h, S)
            if m == 0: t[:] = t[0]
            if m == 1: t[:] = t[0]; t[rng.integers(0, S)] = (t[0] + 2) % U
            if (q & 1) and g == miss:
                us = 2 * int(rng.integers(0, h)); Xg[:, pl[7]] = Xg[:, v[q, g, us]]; A[q, g, :, us] = pl[7]
                t = np.where(t == us, (us + 2) % U, t); t[rng.integers(0, S)] = us
            j[home, g] = t
    return pack(X, nb, v, A, y, j, z, w)
def setup_inputs_ties(rng):
    X, nb, v, A, y, j, z, w = parts(rng); c = 17 * rng.integers(0, 16, (N, 8, 16, 12)); c[:, 1::2, :, :6] = (c[:, 1::2, :, :6] >> 2) - ((c[:, 1::2, :, :6] >> 2) % 17)
    def some(n): return np.take_along_axis(c, rng.integers(0, 12, (N, 8, 1, n)), 3)
    X, y, z = some(P), some(U), some(S); nb[:, ::2, 8:] = nb[:, ::2, :8]; nb[:, 3, 1::2] = nb[:, 3, 0::2]
    v[:, 2] = rng.integers(0, 40, (N, U)); v[:, 5] = P - 1 - rng.integers(0, 40, (N, U)); A[:, 2, ::2] = v[:, 2, None, :]
    return pack(X, nb, v, A, y, j, z, w)
def check_inputs(d):
    bad = []
    for k, hi in (("x", 255), ("nb", P - 1), ("v0", P - 1), ("a0", P - 1), ("y0", 255), ("j0", U - 1), ("z0", 255), ("w", 4095)):
        a = np.asarray(d[k]).astype(np.float64)
        if not (np.min(a) >= 0 and np.max(a) <= hi): bad.append("range of " + k)
        elif not np.all(a == np.floor(a)): bad.append("whole numbers of " + k)
    return bad
def pick(X, k):
    return np.take_along_axis(X, k[:, :, None, :], 3)
def far(X, K, y):
    return np.stack([np.sum(np.abs(pick(X, K[:, :, l]) - y), axis=2) for l in range(16)], axis=2)
def reference(x, nb, v0, a0, y0, j0, z0, w):
    def vec(a): return a.astype(np.float32).astype(np.int64).reshape(N, 8, 16, -1)
    X, y, z = vec(x), vec(y0), vec(z0); nbr, A, W = (a.astype(np.int64).reshape(N, 8, 16, -1) for a in (nb, a0, w))
    v, j = v0.astype(np.int64), j0.astype(np.int64); lv = np.arange(1, 17)[None, None, :, None]
    tr = np.tile(np.arange(P), (N, 8, 1)); finds = np.zeros(N, np.int64)
    for t in range(1, RO + 1):
        n = pick(nbr, v); k = np.argmin(far(X, n, y), axis=2)
        v2 = np.take_along_axis(n, k[:, :, None, :], 2)[:, :, 0]; xn = pick(X, v2)
        new = far(X, A, xn) > TH * lv + 16 * (finds & 15)[:, None, None, None]
        top = 15 - np.argmax(new[:, :, ::-1], axis=2); some = np.any(new, axis=2)
        old = np.take_along_axis(A, top[:, :, None, :], 2)[:, :, 0]; xw = (xn + y) >> 1
        for r in range(N):
            for g in range(8):
                o = old[r, g][some[r, g]]; tr[r, g, o] = o
                q, i = np.unique(v[r, g], return_index=True); tr[r, g, q] = v2[r, g, i]
                q, i = np.unique(v2[r, g], return_index=True); X[r, g][:, q] = xw[r, g][:, i]
        A = np.where(new, v2[:, :, None, :], A); y = np.abs(y - xn); v = v2
        zz, jj = np.roll(z, t, axis=0), np.roll(j, t, axis=0)
        u = np.sum(W * zz, axis=2) & 4095; B = pick(A, jj)
        h = (((B * u[:, :, None, :]) >> 5) + B) & (P - 1)
        hit = far(X, h, zz) <= PH * lv
        l = np.where(np.any(hit, axis=2), np.argmax(hit, axis=2), 15)
        p = np.take_along_axis(B, l[:, :, None, :], 2)[:, :, 0]
        for c in range(3): p = np.take_along_axis(tr, p, 2)
        xp = pick(X, p); found = p == np.take_along_axis(v, jj, 2)
        zz = np.where(found[:, :, None, :], (zz + xp) >> 1, np.abs(zz - xp)); jj = np.where(found, u & (U - 1), jj)
        finds = np.sum(found, axis=(1, 2)); z, j = np.roll(zz, -t, axis=0), np.roll(jj, -t, axis=0)
    return {"yv": v.astype(np.float32), "ya": A.reshape(N, 128, U).astype(np.float32), "yy": y.reshape(N, 128, U).astype(np.float32).astype(BF),
            "yj": j.astype(np.float32), "yz": z.reshape(N, 128, S).astype(np.float32).astype(BF), "yt": tr.astype(np.float32)}

@@ -1,0 +1,668 @@
+from concourse.mybir import AluOpType as ALU, AxisListType, ActivationFunctionType as AF
+
+RO = 3
+S18, MAGIC = 262144.0, 12582912.0
+DUM = 4608
+SUBS = [[1, 5, 9, 13], [2, 6, 10, 14], [3, 11], [7, 15], [4, 12], [8]]
+CSET = {1: (1, 5), 2: (1, 5), 3: (1, 2, 5, 6, 9)}
+BSET = {1: (), 2: (), 3: ()}
+BIAS = {}
+T3 = (1, 2, 3)
+TWOB = (1,)
+SEED, NOISE, UB = 0, 0.0, 0.0
+UDVE = {1: (1, 3, 5, 7), 2: (), 3: ()}
+ND = 4
+
+F32, BF, I32, U16 = "float32", "bfloat16", "int32", "uint16"
+SCRATCH = {}
+def _sb(name, cols, dt):
+    SCRATCH[name] = ("sbuf", [128] + (list(cols) if isinstance(cols, (list, tuple)) else [cols]), dt)
+for _n, _c, _d in [
+    ("X", 8832, BF), ("NB", 4096, I32), ("TR", 4736, F32), ("TR3", 4736, F32),
+    ("ci", 512, I32), ("cf", 512, F32), ("c15i", 512, I32), ("c15", 512, F32), ("tmi", 512, I32), ("c4", 128, F32), ("km", 128, F32),
+    ("pci", 8, I32), ("pf", 32, F32), ("wi", 4, I32), ("wf", 8, F32),
+    ("idb", 128, BF), ("nidb", 128, BF), ("hidb", 128, BF), ("nhidb", 128, BF), ("t85", 128, BF), ("idf", 128, F32),
+    ("Wb", 144, BF), ("Wf", 144, F32), ("B8", 8, BF), ("BO", 128, F32), ("Ex", 128, F32), ("diag", 384, F32), ("hold", 384, F32),
+    ("rst", 128, F32), ("kc", 128, BF), ("ncn", 128, BF), ("thc", 512, BF), ("UT", 128, BF), ("ut1", 128, F32), ("Pm", [2, 128], F32),
+    ("MU", [8, 128], BF), ("SJ", [4, 128], BF), ("scn", 512, F32), ("prm", 32, U16), ("bcl", 8, U16), ("uf", 128, F32),
+    ("uwf", 8, F32), ("Dz", 8, F32), ("Dz2", 8, F32), ("Drep", 128, F32), ("q25", 512, BF), ("ones", 128, BF), ("Ec", 2048, BF), ("Eio", 2048, BF),
+    ("vi", 128, I32), ("vf", 128, F32), ("ai", 128, I32), ("ji", 32, I32), ("jf", 32, F32), ("jt", 32, F32),
+    ("rep", [6, 128], F32), ("wsc", [6, 128], F32), ("wtm", 384, F32), ("vw", 48, U16), ("vd", 48, U16), ("vd2", 48, U16),
+    ("key", 128, F32), ("dab", [8, 128], F32), ("low", 8, F32), ("fst", 8, F32), ("dm", 8, F32), ("dm2", 8, F32),
+    ("A1", [4, 128], F32), ("Aoff", 512, U16), ("Y", [4, 128], BF), ("noff", 128, U16), ("nf", 128, F32),
+    ("G1", 2048, BF), ("ab1", 2048, BF), ("G2", 2048, BF), ("ab2", 2048, BF), ("nyT", 128, BF), ("nxT", 128, BF),
+    ("m1", 128, F32), ("e1", 128, F32), ("s2", 128, F32), ("v8", 8, I32), ("v8b", 8, I32), ("vb", 128, F32), ("xn", 128, BF), ("xw", 128, BF),
+    ("dv", 128, F32), ("Am", 128, F32), ("mb", 128, BF), ("tA", 128, F32), ("oh", 128, F32), ("A2", 256, F32), ("K2", 256, F32),
+    ("g1", 384, F32), ("go", 48, U16), ("g3", 384, F32), ("GP", 2048, F32), ("fl", 128, F32), ("Ks", 128, F32), ("xv", 128, BF),
+    ("land", [4, 17, 2, 16], BF), ("snd", [4, 17, 2, 16], BF), ("ui", 512, I32), ("u", 512, I32), ("jw", 32, U16), ("js", 32, U16),
+    ("pr", 512, I32), ("pt", 512, I32), ("t2", 512, F32), ("hT", 512, F32), ("hoff", 480, U16), ("xvj", 512, BF),
+    ("kg", 512, F32), ("KT", 512, F32), ("SC", 512, F32), ("dsl", [ND, 512], BF), ("gsl", [2, 512], BF),
+    ("ki", 32, I32), ("pi", 32, I32), ("pw", 32, U16), ("ff", 32, BF), ("um", 32, I32), ("um2", 32, I32), ("dj", 32, F32), ("tj", 32, F32),
+    ("dz", 512, BF), ("z", 512, BF), ("Fi", 4, I32), ("thr", 4, F32), ("jo", 32, F32),
+]:
+    _sb(_n, _c, _d)
+for _n in "tmi c15i ui Eio vf ut1 km um um2 jf tA dz kg SC vi".split():
+    SCRATCH.pop(_n, None)
+SCRATCH.pop("wtmx", None)
+for _i, _s in enumerate(SUBS):
+    _sb("ab%d_" % _i, [32, len(_s), 16], BF)
+for _n in ("pC0", "pC1", "pD1", "pD2", "pM0"):
+    SCRATCH[_n] = ("psum", [128, 512], F32)
+SCRATCH["pE"] = ("psum", [128, 512], F32)
+SCRATCH["pU"] = ("psum", [128, 512], F32)
+SCRATCH["pM1"] = ("psum", [128, 512], F32)
+for _n in ("Dz2", "dm2", "vd2", "z", "jt", "v8b", "K2"):
+    SCRATCH.pop(_n)
+for _n, _c, _d in (("X", 4736, BF), ("MU", [2, 144], BF), ("bcl", 32, U16), ("land", [4, 544], BF), ("snd", [4, 544], BF), ("uw", 96, F32), ("pr", 512, F32), ("nWb", 144, BF),
+                   ("wt2", [2, 128], F32), ("key", [2, 128], F32), ("dab", [2, 576], F32), ("low", [2, 576], F32), ("rs2", 576, F32), ("enl", 2, U16),
+                   ("fst", [2, 16], F32), ("dm", [2, 8], F32), ("Dz", 16, F32), ("uwf", 16, F32), ("XU", 4736, BF),
+                   ("diag", 512, F32), ("hold", 512, F32), ("GP", 1024, F32), ("scn", 96, F32), ("nxT", [3, 128], BF), ("xw", [3, 128], BF)):
+    _sb(_n, _c, _d)
+NDMA = 24
+SPLITJ = True
+SEMAPHORES = ["cV", "cA", "cP", "cG"] + ["d%d" % i for i in range(NDMA)] + ["ls%d" % i for i in range(8)] + ["rs%d" % i for i in range(8)]
+
+OV = 30.0
+CY, PC, GC = 1.04, 0.5, 1.56
+
+
+def build(g, core, T, topo):
+    ops = []
+    V, A, P = g.vector, g.scalar, g.tensor
+    rank = T.rank_of(core)
+    N = len(T.cores)
+    def add(q, fn, r, w, c, kind="c"): ops.append((q, fn, r.split(), w.split(), c, kind))
+    def vc(n): return OV + max(64, n) * CY
+    def gcst(n): return 60 + n * GC * CY
+    def cp(o, i, r, w, n, G=False): add("V", lambda: V.tensor_copy(o, i), r, w, gcst(n) if G else vc(n))
+    def sct(o, i, r, w, n): add("V", lambda: V.tensor_copy(o, i), r, w, 60 + 3.8 * n * CY)
+    def tt(o, a, b, op, r, w, n, G=False): add("V", lambda: V.tensor_tensor(o, a, b, op), r, w, gcst(n) if G else vc(n))
+    def ts(o, a, s1, op0, r, w, n, s2=None, op1=None):
+        if op1 is None: add("V", lambda: V.tensor_scalar(o, a, s1, None, op0), r, w, vc(n))
+        else: add("V", lambda: V.tensor_scalar(o, a, s1, s2, op0, op1), r, w, vc(n))
+    def scan(o, a, b, op0, op1, r, w, n): add("V", lambda: V.tensor_tensor_scan(o, a, b, 0.0, op0, op1), r, w, vc(n))
+    def red(o, a, op, r, w, n): add("V", lambda: V.tensor_reduce(o, a, AxisListType.X, op), r, w, vc(n))
+    def tr(o, a, r, w, n): add("V", lambda: V.transpose(o, a), r, w, vc(n))
+    def ms(o, c, w, n): add("V", lambda: V.memset(o, c), "", w, vc(n))
+    def act(o, i, f, r, w, n, G=False, **k): add("A", lambda: A.activation(o, i, f, **k), r, w, gcst(n) if G else vc(n))
+    def mm(o, l, rh, st, sp, r, w, n, f=1): add("P", lambda: P.matmul(o, l, rh, st, sp), r, w, max(64, n) * f * PC)
+    def dma(o, i, r, w, kb, q="S"): add(q, lambda: (g.sync if q == "S" else g.scalar).dma_start(o, i), r, w, kb, "d")
+    def iota(o, pat, cm, w, n, small=False):
+        if small: add("G", lambda: g.iota(o, pat, 0, cm, allow_small_or_imprecise_dtypes=True), "", w, 130 + 2 * n * CY)
+        else: add("G", lambda: g.iota(o, pat, 0, cm), "", w, 130 + 2 * n * CY)
+    def send(k, hop, part="zj"):
+        dst = T.cores[(rank + hop) % N]
+        rid, pid, _ = topo.addr(dst)
+        m = topo.mask(core, dst)
+        cnt = len(topo.engines(core, dst))
+        a, b = {"zj": (0, 544), "z": (0, 512), "j": (512, 544)}[part]
+        n = k + 4 * (part == "j")
+        add("G", lambda: g.remote_dma(T.land[:, k, a:b], T.snd[:, k, a:b], T.sem["rs%d" % n], T.sem["ls%d" % n], pid, rid, m),
+            " ".join("snd:%s%d" % (x, k) for x in part), " ".join("land:%s%d" % (x, k) for x in part), cnt, "r%d" % n)
+    eq, mul, ad, sub, AND, SHR = ALU.is_equal, ALU.mult, ALU.add, ALU.subtract, ALU.bitwise_and, ALU.logical_shift_right
+    X2 = T.X[:]
+    X1 = T.X[:, 0:4096]
+
+    dma(T.pt[0:8, 256:384], T.v0[:], "", "pt:2", 4)
+    dma(T.ai[:], T.a0[:], "", "ai", 64)
+    dma(T.XU[:, 0:4096], T.x[:], "", "XU:b", 1024)
+    dma(T.NB[:], T.nb[:], "", "NB", 2048)
+    dma(T.Y[:, 0], T.y0[:], "", "Y:0", 32, "A")
+    dma(T.ji[:, 0:16], T.j0[0::2, :], "", "ji:0", 8, "A")
+    dma(T.ji[:, 16:32], T.j0[1::2, :], "", "ji:1", 8, "A")
+    dma(T.wi[:, 0:1], T.w[:], "", "wi:0", 4, "A")
+    dma(T.snd[:, 0, 0:512], T.z0[:], "", "snd:z0", 128)
+    dma(X1, T.x[:], "", "X:b", 1024)
+    ms(T.XU[:, 4096:4736], 0.0, "XU:q", 320)
+
+    iota(T.pci[:, 0:1], [[0, 1]], 1, "pci:0", 1)
+    iota(T.ci[:], [[1, 512]], 0, "ci", 512)
+    iota(T.G2[:], [[1, 128], [0, 16]], 0, "G2", 2048, True)
+    ts(T.pci[:, 1:2], T.pci[:, 0:1], 15, AND, "pci:0", "pci:1", 1)
+    ts(T.pci[:, 2:3], T.pci[:, 0:1], 4, SHR, "pci:0", "pci:2", 1)
+    ts(T.pci[:, 3:4], T.pci[:, 0:1], 4, SHR, "pci:0", "pci:3", 1, 1, AND)
+    ts(T.pci[:, 4:5], T.pci[:, 0:1], 5, SHR, "pci:0", "pci:4", 1)
+    cp(T.pf[:, 0:5], T.pci[:, 0:5], "pci", "pf:0", 5)
+    def col(i): return T.pf[:, i:i + 1]
+    cP, cR, cG, cB, cA = (col(i) for i in range(5))
+    def pcol(i, src, m, a, r="pf:0"): ts(col(i), src, m, mul, r, "pf:%d" % i, 1, a, ad)
+    pcol(5, cG, 16.0, 15.0)
+    pcol(6, cB, 128.0, 0.0)
+    pcol(7, cB, -128.0, 0.0)
+    pcol(8, cR, 102 * S18, 102 * S18)
+    pcol(9, cR, -8192.0, 15 * 8192.0 + 2048)
+    pcol(12, cB, -1.0, 1.0)
+    pcol(13, cA, 16.0, cR)
+    pcol(16, cA, 32.0, cR); pcol(17, col(16), 1.0, 16.0, "pf:16")
+    pcol(18, cR, 1.0, 4096.0)
+    pcol(19, cR, 16.0, 0.0)
+    cBm = (col(12), cB)
+    cp(T.cf[:], T.ci[:], "ci", "cf", 512)
+    ts(T.u[:], T.ci[:], 15, AND, "ci", "u", 512)
+    cp(T.c15[:], T.u[:], "u", "c15", 512)
+    ts(T.pt[:, 0:128], T.ci[:, 0:128], 4, SHR, "ci", "pt:0", 128)
+    cp(T.c4[:], T.pt[:, 0:128], "pt:0", "c4", 128)
+    c128 = T.cf[:, 0:128]
+    ts(T.Ex[:], T.c4[:], cP, eq, "c4 pf:0", "Ex", 128)
+    ts(T.diag[:], T.c15[:], cR, eq, "c15 pf:0", "diag", 512)
+    ts(T.hold[:], T.c15[:], 1.0, ALU.min, "c15", "hold", 512)
+    for nm, s in (("idb", 1.0), ("nidb", -1.0), ("hidb", .5), ("nhidb", -.5), ("t85", -85 * S18), ("idf", 1.0)):
+        ts(T[nm][:], c128, cP, eq, "cf pf:0", nm, 128, s, mul)
+    ts(T.Wb[:], T.cf[:, 0:144], col(5), eq, "cf pf:5", "Wb", 144, S18, mul)
+    ts(T.nWb[:], T.cf[:, 0:144], col(5), eq, "cf pf:5", "nWb", 144, -S18, mul)
+    ts(T.Wf[:], T.cf[:, 0:144], col(5), eq, "cf pf:5", "Wf", 144, 0.0625, mul)
+    ts(T.B8[:], T.cf[:, 0:8], cG, eq, "cf pf:0", "B8", 8, 1048576.0, mul)
+    ts(T.BO[:], T.c4[:], cG, eq, "c4 pf:0", "BO", 128)
+    ts(T.rst[:], T.c15[:, 0:128], 0.0, eq, "c15", "rst", 128, 2.0 ** 40, mul)
+    ts(T.kc[:], T.c15[:, 0:128], 65536.0, mul, "c15", "kc", 128)
+    ts(T.ncn[:], T.c15[:, 0:128], -4096.0, mul, "c15", "ncn", 128, 61440.0, ad)
+    act(T.thc[:], T.c15[:], AF.Identity, "c15", "thc", 512, scale=-1.0, bias=16.0)
+    ts(T.oh[:], c128, cP, ALU.is_lt, "cf pf:0", "oh", 128, -1.0, mul)
+    tt(T.oh[:], T.oh[:], T.BO[:], mul, "oh BO", "oh", 256)
+    tt(T.UT[:], T.oh[:], T.idf[:], ad, "oh idf", "UT", 256)
+    ts(T.pt[:, 128:256], T.ci[:, 0:128], 5, SHR, "ci", "pt:1", 128)
+    ts(T.Ks[:], T.pt[:, 128:256], 16.0, mul, "pt:1", "Ks", 128, 15.0, ad)
+    tt(T.Ks[:], T.Ks[:], T.c15[:, 0:128], sub, "Ks c15", "Ks", 256)
+    for b in range(2):
+        ts(T.Pm[:, b], T.Ks[:], col(13), eq, "Ks pf:13 pf:12 pf:0", "Pm:%d" % b, 128, cBm[b], mul)
+        for q in range(2):
+            ts(T.SJ[:, 2 * b + q], c128, col(16 + q), eq, "cf pf:16 pf:17 pf:12 pf:0", "SJ:%d" % (2 * b + q), 128, cBm[b], mul)
+    ts(T.wi[:, 1:2], T.wi[:, 0:1], 4032, AND, "wi:0", "wi:1", 1)
+    ts(T.wi[:, 2:3], T.wi[:, 0:1], 63, AND, "wi:0", "wi:2", 1)
+    cp(T.wf[:, 0:2], T.wi[:, 1:3], "wi:1 wi:2", "wf", 2)
+    for h in range(2):
+        ts(T.MU[:, h], T.cf[:, 0:144], col(5), eq, "cf pf:5 wf", "MU:%d" % h, 144, T.wf[:, h:h + 1], mul)
+    ts(T.scn[:, 0:32], T.cf[:, 0:32], 16.0, mul, "cf pf:18", "scn:0", 32, col(18), ad)
+    ts(T.jo[:, 0:32:2], T.cf[:, 0:16], col(19), ad, "cf pf:19", "jo", 16)
+    ts(T.jo[:, 1:32:2], T.cf[:, 256:272], col(19), ad, "cf pf:19", "jo", 16)
+    cp(T.prm[:], T.jo[:], "jo", "prm", 32)
+    cp(T.bcl[:], T.ci[:, 0:32], "ci", "bcl", 32)
+    act(T.uf[:], c128, AF.Identity, "cf", "uf", 128, scale=1.0 / 256)
+    ms(T.rs2[:], 0.0, "rs2", 576)
+    ms(T.rs2[:, 0:1], 1024.0, "rs2", 1)
+    for c in range(1, 8): ms(T.rs2[:, 8 * c * (c + 1):8 * c * (c + 1) + 1], 1024.0 * 1024, "rs2:%d" % c, 1)
+    pcol(10, cR, 8.0, 24.0)
+    ts(col(11), col(10), cR, mul, "pf:10 pf:0", "pf:11", 1, 15.0, ad)
+    ts(T.enl[:, 0:1], col(11), 575.0, ALU.min, "pf:11", "enl", 1)
+    ts(T.Dz[:], T.cf[:, 0:16], 16.0, mul, "cf pf:0", "Dz", 16, cR, ad)
+    ts(T.uwf[:], T.Dz[:], 1.0 / 256, mul, "Dz", "uwf", 8)
+    ts(T.Dz[:], T.Dz[:], float(DUM), ad, "Dz", "Dz", 8)
+    ts(T.Drep[:], c128, float(DUM), ad, "cf", "Drep", 128)
+    ms(T.q25[:], 0.25, "q25", 256)
+    ms(T.ones[:], 1.0, "ones", 64)
+    ms(T.X[:, 4096:4736], 0.0, "X:q", 320)
+    ts(T.Ec[:], T.G2[:], cP, eq, "G2 pf:0", "Ec", 1024)
+    for nm in ("TR", "TR3")[:1 + bool(T3)]:
+        for k in range(10):
+            n = min(512, 4736 - 512 * k)
+            act(T[nm][:, 512 * k:512 * k + n], T.cf[:, 0:n], AF.Identity, "cf", "%s:%d" % (nm, k), n, bias=512.0 * k)
+
+    def finish(ps, pn, i, two):
+        e = int(i > RO)
+        tt(T.wt2[:, e], ps, T.diag[:, 0:128], mul, pn + " diag", "wt2:%d" % e, 128)
+        cp(T.rep[:, i], ps, pn, "rep:%d" % i, 128)
+        tt(T.key[:, e], ps, T.uf[:], ad, pn + " uf", "key:%d" % e, 128)
+        scan(T.wsc[:, i], T.hold[:, 0:128], T.wt2[:, e], mul, ad, "hold wt2:%d" % e, "wsc:%d" % i, 128)
+        wv = T.wsc[:, i, 15::16]
+        if not e: cp(T.vw[:, 8 * i:8 * i + 8], wv, "wsc:%d" % i, "vw:%d" % i, 8)
+        for c in range(8):
+            n, a = 16 * c + 16, 8 * c * (c + 1)
+            act(T.dab[:, e, a:a + n], T.key[:, e, 0:n], AF.Abs, "key:%d wsc:%d" % (e, i), "dab:%d_%d" % (e, c), n, scale=-1.0, bias=T.wsc[:, i, 16 * c + 15:16 * c + 16])
+        scan(T.low[:, e], T.rs2[:], T.dab[:, e], ad, ALU.min, "rs2 " + " ".join("dab:%d_%d" % (e, c) for c in range(8)), "low:%d" % e, 576)
+        tt(T.fst[:, e], T.low[:, e].indirect(T.enl[:, 0:1]), T.uwf[:], eq, "low:%d enl uwf" % e, "fst:%d" % e, 16, True)
+        dm, dn = T.dm[:, e], "dm:%d" % e
+        tt(dm, wv, T.Dz[:, 0:8], sub, "wsc:%d Dz" % i, dn, 16)
+        tt(dm, dm, T.fst[:, e, 0:8], mul, dn + " fst:%d" % e, dn, 16)
+        tt(dm, dm, T.Dz[:, 0:8], ad, dn + " Dz", dn, 16)
+        cp(T.vd[:, 8 * i:8 * i + 8], dm, dn, "vd:%d" % i, 8)
+
+    cp(T.fl[0:8, :], T.pt[0:8, 256:384], "pt:2", "fl", 128)
+    mm(T.pM0[:, 0:128], T.Ex[0:8, :], T.fl[0:8, :], True, True, "Ex fl", "pM0", 128, 4)
+    finish(T.pM0[:, 0:128], "pM0", 0, False)
+    cp(T.A1[:, 0], T.ai[:], "ai", "A1:0", 128)
+    cp(T.Aoff[:, 0:128], T.ai[:], "ai", "Aoff:0", 128)
+    cp(T.dj[:], T.ji[:], "ji", "dj", 32)
+    tr(T.tj[:], T.dj[:], "dj", "tj", 32)
+    ts(T.snd[:, 0, 512:544], T.tj[:], col(6), ad, "tj pf:6", "snd:j0", 32)
+    send(0, 1)
+    XU = T.XU[:, 0:4096]
+
+    def far(t, base, off, on, Gn, an, neg, negT):
+        win, wn = (XU, "XU ") if on == "noff" or t == 1 else (X1, "X:b ")
+        for c in range(4):
+            w = win.indirect(off[:, 32 * c:32 * c + 32]) if on == "noff" else win.indirect(T.Aoff[:, off + 32 * c:off + 32 * c + 32])
+            o = T[Gn][:, 512 * c:512 * c + 512]
+            if base + c in UDVE[t]: cp(o, w, wn + on, "%s:%d" % (Gn, c), 512, True)
+            else: act(o, w, AF.Copy, wn + on, "%s:%d" % (Gn, c), 512, True)
+        for c in range(4):
+            pn = "pC%d" % (c & 1 if t in TWOB else base // 4)
+            mm(T[pn][:], T.idb[:], T[Gn][:, 512 * c:512 * c + 512], True, False, "idb %s:%d" % (Gn, c), pn, 512)
+            mm(T[pn][:], neg, T.Ec[:, 512 * c:512 * c + 512], False, True, "Ec " + negT, pn, 512)
+            act(T[an][:, 512 * c:512 * c + 512], T[pn][:], AF.Abs, pn, "%s:%d" % (an, c), 512)
+
+    def users_a(t):
+        o = t - 1
+        yo = T.Y[:, o]
+        mm(T.pD1[:, 256:384], yo, T.nidb[:], True, True, "Y:%d nidb" % o, "pD1", 128)
+        act(T.nyT[:], T.pD1[:, 256:384], AF.Copy, "pD1", "nyT", 128)
+        cp(T.noff[:], T.NB[:].indirect(T.vw[:, 8 * o:8 * o + 8]), "NB vw:%d" % o, "noff", 128, True)
+        cp(T.nf[:], T.noff[:], "noff", "nf", 128)
+        far(t, 0, T.noff, "noff", "G1", "ab1", T.nyT[:], "nyT")
+        mm(T.pD1[:, 128:256], T.nf[:], T.idf[:], True, False, "nf idf", "pD1", 128, 4)
+        mm(T.pD1[:, 128:256], T.idb[:], T.ncn[:], False, True, "idb ncn", "pD1", 128)
+        mm(T.pD1[:, 0:128], T.idb[:], T.kc[:], True, False, "idb kc", "pD1", 128)
+        for k in range(16):
+            mm(T.pD1[:, k:128:16], T.ab1[:, k::16], T.B8[:], False, k == 15, "ab1 B8", "pD1", 64)
+        scan(T.m1[:], T.rst[:], T.pD1[:, 0:128], ad, ALU.min, "rst pD1", "m1", 128)
+        tt(T.e1[:], T.pD1[:, 0:128], T.m1[:], sub, "pD1 m1", "e1", 128)
+        scan(T.s2[:], T.e1[:], T.pD1[:, 128:256], ALU.min, ALU.max, "e1 pD1", "s2", 128)
+        cp(T.v8[:], T.s2[:, 15::16], "s2", "v8", 8)
+        ts(T.v8[:], T.v8[:], 4095, AND, "v8", "v8", 8)
+        cp(T.vb[:], T.v8[:].indirect(T.bcl[:, 0:8]), "v8 bcl", "vb", 128, True)
+        mm(T.pD1[:, 0:128], T.vb[:], T.idf[:], True, True, "vb idf", "pD1", 128, 4)
+        finish(T.pD1[:, 0:128], "pD1", t, True)
+        act(T.xn[:], XU.indirect(T.vw[:, 8 * t:8 * t + 8]), AF.Copy, "XU vw:%d" % t, "xn", 128, True)
+        mm(T.pD1[:, 128:256], T.xn[:], T.nidb[:], True, True, "xn nidb", "pD1", 128)
+        mm(T.pD1[:, 256:384], T.idb[:], T.xn[:], True, False, "xn idb", "pD1", 128)
+        mm(T.pD1[:, 256:384], T.nidb[:], yo, False, True, "Y:%d nidb" % o, "pD1", 128)
+        mm(T.pD1[:, 384:512], T.hidb[:], T.xn[:], True, False, "xn hidb", "pD1", 128)
+        mm(T.pD1[:, 384:512], T.hidb[:], yo, False, False, "Y:%d hidb" % o, "pD1", 128)
+        mm(T.pD1[:, 384:512], T.nidb[:], T.q25[:, 0:128], False, True, "q25 nidb", "pD1", 128)
+        act(T.nxT[:, o], T.pD1[:, 128:256], AF.Copy, "pD1", "nxT:%d" % o, 128)
+        act(T.Y[:, t], T.pD1[:, 256:384], AF.Abs, "pD1", "Y:%d" % t, 128)
+        ts(T.xw[:, o], T.pD1[:, 384:512], MAGIC, ad, "pD1", "xw:%d" % o, 128, -MAGIC, ad)
+
+    def step_xu(t): sct(T.XU[:].indirect(T.vd[:, 8 * t:8 * t + 8]), T.xw[:, t - 1], "xw:%d vd:%d" % (t - 1, t), "XU", 128)
+
+    def users_far(t):
+        o = t - 1
+        far(t, 4, 128 * o, "Aoff:%d" % o, "G2", "ab2", T.nxT[:, o], "nxT:%d" % o)
+        for l in range(16):
+            mm(T.pD2[:, 0:128], T.Wb[:, 15 - l:143 - l], T.ab2[:, l::16], l == 0, l == 15, "Wb ab2", "pD2", 128)
+        tt(T.dv[:], T.rep[:, t], T.A1[:, o], sub, "rep:%d A1:%d" % (t, o), "dv", 256)
+        if t > 1: tt(T.Am[:], T.A1[:, o], T.Drep[:], sub, "A1:%d Drep" % o, "Am", 256)
+
+    def double(dst, src, sn, **k):
+        for b in range(2):
+            mm(T.pM0[:, 128 * b:128 * b + 128], T.Pm[:, b], src, True, True, "Pm:%d %s" % (b, sn), "pM0", 128, 4)
+        act(T[dst][:], T.pM0[:, 0:256], AF.Identity, "pM0 pf:9", dst, 256, **k)
+
+    def users_b(t):
+        o = t - 1
+        ts(T.mb[:], T.pD2[:, 0:128], col(8) if t == 1 else T.thr[:, 0:1], ALU.is_gt, "pD2 pf:8 thr", "mb", 128)
+        tt(T.fl[:], T.mb[:], T.dv[:], mul, "mb dv", "fl", 256)
+        tt(T.A1[:, t], T.fl[:], T.A1[:, o], ad, "fl A1:%d" % o, "A1:%d" % t, 256)
+        double("A2", T.A1[:, t], "A1:%d" % t, bias=-2048.0)
+        if t < RO: cp(T.Aoff[:, 128 * t:128 * t + 128], T.A1[:, t], "A1:%d" % t, "Aoff:%d" % t, 128)
+        sct(X2.indirect(T.vd[:, 8 * t:8 * t + 8]), T.xw[:, o], "xw:%d vd:%d" % (o, t), "X:b X:q", 128)
+        act(T.xv[:], X1.indirect(T.vw[:, 8 * t:8 * t + 8]), AF.Copy, "X:b vw:%d" % t, "xv", 128, True)
+        if t > 1:
+            i = 2 + t
+            mm(T.pD2[:, 256:384], T.UT[:], T.mb[:], True, True, "UT mb", "pD2", 128)
+            ts(T.oh[:], T.pD2[:, 256:384], 1.0, eq, "pD2", "oh", 128)
+            tt(T.oh[:], T.oh[:], T.Am[:], mul, "oh Am", "oh", 256)
+            mm(T.pD2[:, 384:512], T.idf[:], T.Drep[:], True, False, "idf Drep", "pD2", 128, 4)
+            mm(T.pD2[:, 384:512], T.BO[:], T.oh[:], False, True, "BO oh", "pD2", 128, 4)
+            finish(T.pD2[:, 384:512], "pD2", i, False)
+            sct(T.TR[:].indirect(T.vd[:, 8 * i:8 * i + 8]), T.rep[:, i], "rep:%d vd:%d" % (i, i), "TR", 128)
+        sct(T.TR[:].indirect(T.vd[:, 8 * o:8 * o + 8]), T.rep[:, t], "rep:%d vd:%d" % (t, o), "TR", 128)
+        if t in T3:
+            n = 128 * t
+            on = " ".join("vw:%d" % i for i in range(o))
+            if t == 1: off, on = T.vw[:, 8:16], "vw:1"
+            else:
+                off = T.vw[:, 0:8 * o]
+                cp(T.go[:, 8 * o:8 * t], T.wsc[:, t, 15::16], "wsc:%d" % t, "go:0", 8)
+            for h in range(1 if t == 1 else 0, 2):
+                m = n - 128 * (h == 0)
+                tt(T.wtm[:, 0:m], T.TR[:].indirect(off), T.diag[:, 0:m], mul, "TR diag " + on, "wtm", m, True)
+                scan(T.g1[:, 0:m], T.hold[:, 0:m], T.wtm[:, 0:m], mul, ad, "hold wtm", "g1", m)
+                off, on = T.go[:, 24 * h:24 * h + 8 * t], "go:%d" % h
+                cp(T.go[:, 24 * h:24 * h + m // 16], T.g1[:, 15:m:16], "g1", on, 8 * t)
+            act(T.g3[:, 0:n], T.TR[:].indirect(off), AF.Copy, "TR " + on, "g3", n, True)
+            for i in range(t):
+                sct(T.TR3[:].indirect(T.vd[:, 8 * i:8 * i + 8]), T.g3[:, 128 * i:128 * i + 128], "g3 vd:%d" % i, "TR3", 128)
+        if t == RO:
+            dma(T.yt[:], T.TR[0:128:16, 0:4096], "TR", "", 128)
+            dma(T.ya[:], T.A1[:, t], "A1:%d" % t, "", 64)
+            dma(T.yy[:], T.Y[:, t], "Y:%d" % t, "", 32)
+            dma(T.yv[:], T.rep[0:128:16, t], "rep:%d" % t, "", 4)
+
+    def keys(t):
+        act(T.GP[:, 0:512], T.t2[:], AF.Identity, "t2 pf:9", "GP:0", 512, bias=col(9))
+        tr(T.KT[:], T.GP[:, 0:512], "GP:0", "KT", 512)
+        act(T.GP[:, 512:1024], T.rep[:, t].indirect(T.js[:]), AF.Copy, "rep:%d js" % t, "GP:1", 512, True)
+        for s0 in range(16):
+            mm(T.pM0[:, 256:288], T.Wf[:, 15 - s0:143 - s0], T.GP[:, 512 + s0:1024:16], s0 == 0, s0 == 15, "Wf GP:1", "pM0", 64, 4)
+
+    def seek_head(t):
+        k = t - 1
+        L, J = "land:z%d" % k, "land:j%d" % k
+        z, j = T.land[:, k, 0:512], T.land[:, k, 512:544]
+        for b in range(2):
+            for q in range(2):
+                mm(T.pM1[:, b:32:2], T.SJ[:, 2 * b + q], T.land[:, k, 512 + q:544:2], q == 0, q == 1, "SJ:%d %s" % (2 * b + q, J), "pM1", 16)
+        cp(T.jw[:], T.pM1[:, 0:32], "pM1", "jw", 32)
+        ts(T.js[:], j, col(7), ad, J + " pf:7", "js", 32)
+        act(T.t2[:], T.A2[:].indirect(T.jw[:]), AF.Copy, "A2 jw", "t2", 512, True)
+        tr(T.hT[:], T.t2[:], "t2", "hT", 512)
+        for s0 in range(16):
+            for h in range(2):
+                mm(T.pU[:, 0:32], T.MU[:, h, 15 - s0:143 - s0], T.land[:, k, s0:512:16], s0 + h == 0, s0 + h == 16, "MU:%d %s" % (h, L), "pU", 32)
+        cp(T.ki[:], T.pU[:, 0:32], "pU", "ki", 32)
+        ts(T.pi[:], T.ki[:], 4095, AND, "ki", "pi", 32)
+        ts(T.uw[:, 0:32], T.pi[:], 32.0, ad, "pi", "uw:0", 32)
+        ts(T.ki[:], T.ki[:], 63, AND, "ki", "ki", 32)
+        ts(T.uw[:, 64:96], T.ki[:], 32.0, ad, "ki", "uw:2", 32, 2048.0, mul)
+        tt(T.pr[:], T.uw[:, 0:32].indirect(T.bcl[:]), T.hT[:], mul, "uw:0 bcl hT", "pr", 512, True)
+        tt(T.pt[:], T.uw[:, 64:96].indirect(T.bcl[:]), T.pr[:], ad, "uw:2 bcl pr", "pt", 512, True)
+        ts(T.u[:], T.pt[:], 5, ALU.arith_shift_right, "pt", "u", 512, 4095, AND)
+        cp(T.hoff[:], T.u[:].indirect(T.prm[:, 2:32]), "u prm", "hoff", 480, True)
+        ts(T.ki[:], T.pi[:], 127, AND, "pi", "ki", 32)
+        ts(T.tj[:], T.ki[:], col(6), ad, "ki pf:6", "tj", 32)
+        tt(T.dj[:], T.tj[:], j, sub, "tj " + J, "dj", 64)
+        act(T.xvj[:], T.xv[:].indirect(T.js[:]), AF.Copy, "xv js", "xvj", 512, True)
+        mm(T.pM1[:], T.hidb[:], z, True, False, "hidb " + L, "pM1", 512)
+        mm(T.pM1[:], T.nhidb[:], T.xvj[:], False, False, "nhidb xvj", "pM1", 512)
+        mm(T.pM1[:], T.idb[:], T.q25[:], False, True, "idb q25", "pM1", 512)
+
+    def seek_rest(t):
+        k = t - 1
+        L, J = "land:z%d" % k, "land:j%d" % k
+        z, j = T.land[:, k, 0:512], T.land[:, k, 512:544]
+        XH = X1
+        mm(T.pE[:], T.t85[:], T.thc[:], True, False, "t85 thc", "pE", 512)
+        ts(T.X[:, 4096:4608], T.pM1[:], MAGIC, ad, "pM1", "X:q", 512, -MAGIC, ad)
+        keys(t)
+        nd, ng = 0, 0
+        left = [0]
+        def acc(o, l, rh, r, n):
+            left[0] += 1
+            def f():
+                left[0] -= 1
+                return P.matmul(o, l, rh, False, left[0] == 0)
+            add("P", f, r, "pE:acc", max(64, n) * PC)
+        for si, S in enumerate(SUBS):
+            an = "ab%d_" % si
+            for i, l in enumerate(S):
+                w = XH.indirect(T.hoff[:, 32 * l - 32:32 * l])
+                o = T[an][:, :, i, :]
+                if l in CSET[t]:
+                    s = ng & 1; ng += 1
+                    pn = ("pU", "pM1")[s]
+                    act(T.gsl[:, s], w, AF.Copy, "X:b hoff", "gsl:%d" % s, 512, True)
+                    mm(T[pn][:], T.idb[:], T.gsl[:, s], True, False, "idb gsl:%d" % s, pn, 512)
+                    mm(T[pn][:], T.nidb[:], z, False, True, "nidb " + L, pn, 512)
+                    act(o, T[pn][:], AF.Abs, pn, "%s:%d" % (an, i), 512)
+                else:
+                    s = nd % ND; nd += 1
+                    tt(T.dsl[:, s], w, z, sub, "X:b hoff " + L, "dsl:%d" % s, 512, True)
+                    if l in BSET[t]:
+                        ts(o, T.dsl[:, s], 0.0, ALU.max, "dsl:%d" % s, "%s:%d" % (an, i), 256, 2.0, mul)
+                        for s0 in range(16):
+                            acc(T.pE[:, l::16], T.nWb[:, 15 - s0:143 - s0], T.dsl[:, s, s0::16], "nWb dsl:%d" % s, 32)
+                    else: act(o, T.dsl[:, s], AF.Abs, "dsl:%d" % s, "%s:%d" % (an, i), 512)
+            for s0 in range(16):
+                acc(T.pE[:, S[0]::16 // len(S)], T.Wb[:, 15 - s0:143 - s0], T[an][:, :, :, s0], "Wb " + an, 32 * len(S))
+        scan(T.hT[:], T.pE[:], T.KT[:], ALU.min, ALU.max, "pE KT", "hT", 512)
+        cp(T.ki[:], T.hT[:, 15::16], "hT", "ki", 32)
+        ts(T.pi[:], T.ki[:], 8191, AND, "ki", "pi", 32)
+        cp(T.pw[:], T.pi[:], "pi", "pw", 32)
+        tn = "TR3" if t in T3 else "TR"
+        for h in range(2 if t in T3 else 0, 3):
+            tt(T.t2[:], T[tn][:].indirect(T.pw[:]), T.diag[:], mul, tn + " diag pw", "t2", 512, True)
+            scan(T.hT[:], T.hold[:], T.t2[:], mul, ad, "hold t2", "hT", 512)
+            if h < 2: cp(T.pw[:], T.hT[:, 15::16], "hT", "pw", 32)
+        tt(T.ff[:], T.pM0[:, 256:288], T.hT[:, 15::16], eq, "pM0 hT", "ff", 32)
+        tt(T.scn[:, 32:64], T.ff[:], T.scn[:, 0:32], mul, "ff scn:0", "scn:1", 64)
+        tt(T.scn[:, 64:96], T.scn[:, 32:64], T.hT[:, 15::16], ALU.max, "scn:1 hT", "scn:2", 64)
+        cp(T.pw[:], T.scn[:, 64:96], "scn:2", "pw", 32)
+        tt(T.xvj[:], X2.indirect(T.pw[:]), z, sub, "X:b X:q pw " + L, "xvj", 512, True)
+        act(T.snd[:, t, 0:512], T.xvj[:], AF.Abs, "xvj", "snd:z%d" % t, 512)
+        tt(T.tj[:], T.ff[:], T.dj[:], mul, "ff dj", "tj", 64)
+        if t < RO:
+            tt(T.snd[:, t, 512:544], T.tj[:], j, ad, "tj " + J, "snd:j%d" % t, 64)
+            if SPLITJ: send(t, 1, "j"); send(t, 1, "z")
+            else: send(t, 1)
+            mm(T.pM0[:, 0:32], T.ones[:], T.ff[:], True, True, "ones ff", "pM0", 32)
+            red(T.thr[:, 1:2], T.pM0[:, 0:32], ad, "pM0", "thr:1", 32)
+            cp(T.Fi[:, 0:1], T.thr[:, 1:2], "thr:1", "Fi:0", 1)
+            ts(T.Fi[:, 1:2], T.Fi[:, 0:1], 15, AND, "Fi:0", "Fi:1", 1)
+            ts(T.thr[:, 0:1], T.Fi[:, 1:2], 16 * S18, mul, "Fi:1 pf:8", "thr:0", 1, col(8), ad)
+        else:
+            tt(T.dj[:], T.tj[:], j, ad, "tj " + J, "dj", 64)
+            ts(T.ff[:], T.dj[:], col(7), ad, "dj pf:7", "ff", 32)
+            tr(T.snd[:, t, 512:544], T.ff[:], "ff", "snd:j%d" % t, 32)
+            send(t, -RO)
+
+    part = CACHE.setdefault("part", {})
+    def run(f, t, name):
+        n0 = len(ops)
+        f(t)
+        for i in range(n0, len(ops)): part[i] = name + str(t)
+    run(users_a, 1, "a")
+    run(users_far, 1, "f")
+    for t in range(1, RO):
+        step_xu(t)
+        run(users_a, t + 1, "a")
+    for t in range(1, RO + 1):
+        run(users_b, t, "b")
+        run(seek_head, t, "h")
+        if t < RO: run(users_far, t + 1, "f")
+        run(seek_rest, t, "r")
+    dma(T.yz[:], T.land[:, RO, 0:512], "land:z%d" % RO, "", 128)
+    cp(T.jo[:], T.land[:, RO, 512:544], "land:j%d" % RO, "jo", 32)
+    dma(T.yj[0::2, :], T.jo[:, 0:16], "jo", "", 8, "A")
+    dma(T.yj[1::2, :], T.jo[:, 16:32], "jo", "", 8, "A")
+    return ops
+
+
+def depend(ops):
+    acc = {}
+    deps = []
+    for i, (q, fn, r, w, c, kind) in enumerate(ops):
+        d = {}
+        for lst, wr in ((r, False), (w, True)):
+            for a in lst:
+                b, _, k = a.partition(":")
+                ps = SCRATCH[b][0] == "psum"
+                for (j, k2, wr2) in acc.get(b, ()):
+                    q2, kind2 = ops[j][0], ops[j][5]
+                    same = q2 == q and kind == "c" and kind2 == "c"
+                    if ps:
+                        if k == "acc" and k2 == "acc": continue
+                        if same: d.setdefault(j, False)
+                        else: d[j] = True
+                    elif (k == k2 or not k or not k2) and (wr or wr2):
+                        d[j] = True
+        for lst, wr in ((r, False), (w, True)):
+            for a in lst:
+                b, _, k = a.partition(":")
+                old = acc.get(b, [])
+                if k == "acc": pass
+                elif SCRATCH[b][0] == "psum": old = []
+                elif wr: old = [e for e in old if k and e[1] != k]
+                acc[b] = old + [(i, k, wr)]
+        d.pop(i, None)
+        deps.append(d)
+    return deps
+
+
+HOP, SELF = 150.0, 60.0
+
+
+def plan(ops, deps):
+    n = len(ops)
+    def dur(i):
+        q, c, kind = ops[i][0], ops[i][4], ops[i][5]
+        if kind == "c": return c, c
+        if kind == "d": return 60.0, 2000.0 + c * 5.0
+        return 500.0, (5000.0 if int(kind[1:]) < 4 else 3000.0)
+    succ = [[] for _ in range(n)]
+    for i in range(n):
+        for j in deps[i]: succ[j].append(i)
+    pr = [0.0] * n
+    for i in range(n - 1, -1, -1):
+        pr[i] = dur(i)[1] + max([pr[s] + (HOP if deps[s][i] else 0.0) for s in succ[i]] + [0.0])
+    x = SEED * 7919 + 1
+    for i in range(n):
+        x = (x * 1103515245 + 12345) % 2147483648
+        pr[i] += NOISE * x / 2147483648.0 - (UB if i in CACHE["ua"] else 0.0)
+    left = [len(d) for d in deps]
+    ready = [i for i in range(n) if not left[i]]
+    free = {}
+    done, start = [0.0] * n, [0.0] * n
+    at = [0.0] * n
+    order = []
+    dmafree = 0.0
+    while ready:
+        est = {i: max(free.get(ops[i][0], 0.0), at[i]) for i in ready}
+        i0 = min(ready, key=lambda i: (est[i], -pr[i], i))
+        q = ops[i0][0]
+        if q == "S": i1 = min(i for i in ready if ops[i][0] == q and est[i] <= est[i0])
+        else:
+            i1 = max((i for i in ready if ops[i][0] == q and est[i] <= est[i0] + 30.0), key=lambda i: (pr[i], -i))
+            better = [i for i in ready if ops[i][0] == q and pr[i] > pr[i1] + 1500.0 and est[i] < est[i1] + 0.6 * dur(i1)[0]]
+            if better: i1 = max(better, key=lambda i: pr[i])
+        hold, lat = dur(i1)
+        start[i1] = est[i1]
+        free[q] = est[i1] + hold
+        if ops[i1][5] == "d":
+            dmafree = max(dmafree, est[i1] + 2000.0) + lat - 2000.0
+            done[i1] = dmafree
+        else: done[i1] = est[i1] + lat
+        order.append(i1)
+        ready.remove(i1)
+        for s in succ[i1]:
+            w = deps[s][i1]
+            at[s] = max(at[s], done[i1] + (SELF if ops[s][0] == q else HOP) if w else start[i1])
+            left[s] -= 1
+            if not left[s]: ready.append(s)
+    return order, start, done
+
+
+def plan2(ops, deps):
+    n = len(ops)
+    hold, lat = [0.0] * n, [0.0] * n
+    cum, last = 0.0, {}
+    edges = [dict() for _ in range(n)]
+    for i, (q, fn, r, w, c, kind) in enumerate(ops):
+        if kind == "c": hold[i] = lat[i] = c
+        elif kind == "d":
+            hold[i] = 60.0
+            if r: lat[i] = 2000.0 + c * DK
+            else:
+                cum += c * DK
+                lat[i] = 2000.0 + cum
+                if q in last: edges[i][last[q]] = 60.0
+                last[q] = i
+        else: hold[i], lat[i] = 500.0, (RZ if int(kind[1:]) < 4 else RJ)
+        for j, wt in deps[i].items():
+            edges[i][j] = lat[j] + (SELF if ops[j][0] == q else HOP) if wt else hold[j]
+    succ = [dict() for _ in range(n)]
+    for i in range(n):
+        for j, e in edges[i].items(): succ[j][i] = e
+
+    def place(seq, back):
+        busy = {}
+        st = [0.0] * n
+        for i in seq:
+            if back: t = max([st[s] + e for s, e in succ[i].items()] + [lat[i]]) - hold[i]
+            else: t = max([st[j] + e for j, e in edges[i].items()] + [0.0])
+            b = busy.setdefault(ops[i][0], [])
+            lo, hi = 0, len(b)
+            while lo < hi:
+                m = (lo + hi) // 2
+                if b[m][1] <= t: lo = m + 1
+                else: hi = m
+            while lo < len(b) and b[lo][0] < t + hold[i]:
+                t = max(t, b[lo][1]); lo += 1
+            b.insert(lo, (t, t + hold[i]))
+            st[i] = t + hold[i] if back else t
+        return st
+
+    def topo_order(key, back):
+        pre, post = (succ, edges) if back else (edges, succ)
+        left = [len(pre[i]) for i in range(n)]
+        ready = [i for i in range(n) if not left[i]]
+        out = []
+        while ready:
+            i = min(ready, key=key.get)
+            ready.remove(i); out.append(i)
+            for s in post[i]:
+                left[s] -= 1
+                if not left[s]: ready.append(s)
+        return out
+
+    pr = [0.0] * n
+    for i in range(n - 1, -1, -1): pr[i] = max([pr[s] + e for s, e in succ[i].items()] + [lat[i]])
+    x = SEED * 7919 + 1
+    key = {i: (-pr[i], i) for i in range(n)}
+    best = None
+    for it in range(PASSES):
+        st = place(topo_order(key, False), False)
+        span = max(st[i] + lat[i] for i in range(n))
+        if best is None or span < best[0]: best = (span, st)
+        bk = place(topo_order({i: (-st[i] - hold[i], -i) for i in range(n)}, True), True)
+        key = {}
+        for i in range(n):
+            x = (x * 1103515245 + 12345) % 2147483648
+            key[i] = (-bk[i] + NOISE * x / 2147483648.0 + BIAS.get(CACHE["part"].get(i), 0.0), i)
+    st = best[1]
+    return topo_order({i: (st[i], i) for i in range(n)}, False), st, [st[i] + lat[i] for i in range(n)]
+
+
+DK, RZ, RJ, PASSES = 5.0, 5000.0, 3000.0, 3
+CFG = {'c': {1: (2, 3, 6, 11, 12, 13), 2: (1, 2, 3, 5, 6, 9, 10, 14), 3: (2, 3, 5, 6, 9, 11, 12, 13, 14, 15)}, 'b': {1: (2, 3, 4, 7, 8, 10, 11, 12, 13, 14, 15), 2: (4, 7, 8, 10, 11, 13, 14, 15), 3: (1, 4, 7, 8, 10, 11, 12, 14, 15)}, 'bias': {'r1': 2500, 'h3': -8000, 'f3': 8000, 'r2': 3000, 'r3': 3000, 'h1': -5000, 'a2': -3000, 'b1': -10000, 'f2': 1000, 'a3': -500, 'b3': 2000, 'h2': 3000, 'b2': 2500}, 'ud': {1: (1, 3, 5, 7), 2: (1,), 3: (2,)}, 'seed': 60, 'nz': 200}
+CFG = {'c': {1: (1, 2, 3, 5, 9, 11, 15), 2: (1, 2, 3, 5, 6, 7, 12, 13), 3: (2, 3, 5, 6, 7, 10, 13, 15)}, 'b': {1: (1, 3, 4, 5, 7, 8, 10, 12, 13, 14), 2: (1, 2, 3, 4, 6, 7, 9, 10, 11, 12, 14, 15), 3: (1, 3, 5, 6, 10, 11, 13, 14)}, 'bias': {'r1': 3500, 'h3': 500, 'f3': 6500, 'r2': 3000, 'r3': 1500, 'h1': 0, 'a2': -2000, 'b1': -16000, 'f2': 2000, 'a3': -500, 'b3': 2000, 'h2': 0, 'b2': 2000}, 'ud': {1: (1, 3, 5, 7), 2: (1,), 3: (2,)}, 'seed': 33, 'nz': 200}
+CSET, BSET, BIAS, UDVE, SEED, NOISE = CFG['c'], CFG['b'], CFG['bias'], CFG['ud'], CFG['seed'], CFG['nz']
+CACHE = {}
+
+
+def rank_program(g, core, T, topo):
+    if T.rank_of(core) is None:
+        return
+    ops = build(g, core, T, topo)
+    if "o" not in CACHE:
+        deps = depend(ops)
+        CACHE["o"] = (deps,) + plan2(ops, deps)
+        CACHE["ops"] = ops
+    deps, order = CACHE["o"][0], CACHE["o"][1]
+    Q = {"V": g.vector, "A": g.scalar, "P": g.tensor, "G": g, "S": g.sync}
+    token = {}
+    known = {q: {} for q in Q}
+    clock = {}
+    count = {}
+    nd = 0
+    ends = []
+    for i in order:
+        q, fn, r, w, c, kind = ops[i]
+        kn = known[q]
+        need = {}
+        for j, wt in deps[i].items():
+            if wt:
+                s, v = token[j]
+                if ops[j][5][0] == "r" and not any(a.startswith("land") for a in r): s = "ls" + s[2:]
+                if kn.get(s, 0) < v and need.get(s, (0, 0))[0] < v: need[s] = (v, j)
+        for s, (v, j) in sorted(need.items(), key=lambda e: -order.index(e[1][1])):
+            if kn.get(s, 0) < v:
+                Q[q].wait_ge(T.sem[s], v)
+                kn[s] = v
+                if s[0] != "r":
+                    for s2, v2 in clock[j].items():
+                        if kn.get(s2, 0) < v2: kn[s2] = v2
+        ins = fn()
+        if kind == "c":
+            s = "c" + q
+            count[s] = count.get(s, 0) + 1
+            ins.then_inc(T.sem[s], 1)
+            token[i] = (s, count[s])
+        elif kind == "d":
+            s = "d%d" % nd; nd += 1
+            ins.then_inc(T.sem[s], 16)
+            token[i] = (s, 16); ends.append(token[i])
+        else:
+            token[i] = ("rs" + kind[1:], c); ends.append(token[i]); ends.append(("ls" + kind[1:], c))
+        clock[i] = dict(kn)
+    for s, v in list(count.items()) + ends:
+        if known["G"].get(s, 0) < v: g.wait_ge(T.sem[s], v)

@@ -1,69 +1,53 @@
 from concourse.mybir import AluOpType as ALU, AxisListType, ActivationFunctionType as AF
 
 RO = 3
-S18, MAGIC = 262144.0, 12582912.0
-DUM = 4608
-SUBS = [[1, 5, 9, 13], [2, 6, 10, 14], [3, 11], [7, 15], [4, 12], [8]]
-CSET = {1: (1, 5), 2: (1, 5), 3: (1, 2, 5, 6, 9)}
-BSET = {1: (), 2: (), 3: ()}
-BIAS = {}
-T3 = (1, 2, 3)
-TWOB = (1,)
-SEED, NOISE, UB = 0, 0.0, 0.0
-UDVE = {1: (1, 3, 5, 7), 2: (), 3: ()}
-ND = 4
+BIG, MAGIC = 2.0 ** 25, 12582912.0
+DUM, FND, XW = 4096, 4224, 4736
+TW = 4224
+PAIRS = [(1, 9), (2, 10), (3, 11), (4, 12), (5, 13), (6, 14), (7, 15), (8,)]
+WAYS = {1: 'AVVMAVAA', 2: 'VAVAAVMA', 3: 'AVAAVMAA'}
+CUT = (0, 8, 15)
+UDVE = {1: (1, 3, 7), 2: (1, 2, 4, 6), 3: (2, 3)}
+BIAS = {'a1': 1000, 'b1': 1000, 'r3': 1000}
+OPT = {"seed": 30, "noise": 400.0, "passes": 6, "mw": 1, "mq": 1, "fix": 1, "f": 0.9}
 
-F32, BF, I32, U16 = "float32", "bfloat16", "int32", "uint16"
+F32, BF, F16, I32, U16 = "float32", "bfloat16", "float16", "int32", "uint16"
 SCRATCH = {}
-def _sb(name, cols, dt):
-    SCRATCH[name] = ("sbuf", [128] + (list(cols) if isinstance(cols, (list, tuple)) else [cols]), dt)
 for _n, _c, _d in [
-    ("X", 8832, BF), ("NB", 4096, I32), ("TR", 4736, F32), ("TR3", 4736, F32),
-    ("ci", 512, I32), ("cf", 512, F32), ("c15i", 512, I32), ("c15", 512, F32), ("tmi", 512, I32), ("c4", 128, F32), ("km", 128, F32),
+    ("X", XW, BF), ("NB", 4096, I32), ("TR", TW, F32), ("TR3", TW, F32),
+    ("cf", 512, F32), ("c15", 512, F32), ("c4", 128, F32), ("Ks", 128, F32), ("io", [2, 32], F32),
     ("pci", 8, I32), ("pf", 32, F32), ("wi", 4, I32), ("wf", 8, F32),
-    ("idb", 128, BF), ("nidb", 128, BF), ("hidb", 128, BF), ("nhidb", 128, BF), ("t85", 128, BF), ("idf", 128, F32),
-    ("Wb", 144, BF), ("Wf", 144, F32), ("B8", 8, BF), ("BO", 128, F32), ("Ex", 128, F32), ("diag", 384, F32), ("hold", 384, F32),
-    ("rst", 128, F32), ("kc", 128, BF), ("ncn", 128, BF), ("thc", 512, BF), ("UT", 128, BF), ("ut1", 128, F32), ("Pm", [2, 128], F32),
-    ("MU", [8, 128], BF), ("SJ", [4, 128], BF), ("scn", 512, F32), ("prm", 32, U16), ("bcl", 8, U16), ("uf", 128, F32),
-    ("uwf", 8, F32), ("Dz", 8, F32), ("Dz2", 8, F32), ("Drep", 128, F32), ("q25", 512, BF), ("ones", 128, BF), ("Ec", 2048, BF), ("Eio", 2048, BF),
-    ("vi", 128, I32), ("vf", 128, F32), ("ai", 128, I32), ("ji", 32, I32), ("jf", 32, F32), ("jt", 32, F32),
-    ("rep", [6, 128], F32), ("wsc", [6, 128], F32), ("wtm", 384, F32), ("vw", 48, U16), ("vd", 48, U16), ("vd2", 48, U16),
-    ("key", 128, F32), ("dab", [8, 128], F32), ("low", 8, F32), ("fst", 8, F32), ("dm", 8, F32), ("dm2", 8, F32),
-    ("A1", [4, 128], F32), ("Aoff", 512, U16), ("Y", [4, 128], BF), ("noff", 128, U16), ("nf", 128, F32),
+    ("idb", 128, BF), ("nidb", 128, BF), ("hidb", 128, BF), ("nhidb", 128, BF), ("t85", 128, BF), ("n26", 128, BF), ("zb", 128, BF),
+    ("idf", 128, F32), ("i8k", 128, BF), ("dg8", 128, BF),
+    ("Wb", 144, BF), ("nWb", 144, BF), ("B8", 8, BF), ("BO", 128, BF), ("nBO", 128, BF), ("Ex", 128, BF), ("diag", 512, F32), ("hold", 512, F32),
+    ("rst", 128, F32), ("kc", 128, BF), ("ncn", 128, BF), ("thc", 512, BF), ("UT", 128, BF), ("Pm", [2, 128], BF), ("Pv", [2, 128], F32),
+    ("MU", 144, F16), ("SJ", [4, 128], BF), ("cjb", 32, BF), ("scn", 96, F32), ("prm", 32, U16), ("rl", 32, U16), ("bcl", 8, U16),
+    ("offc", 512, F32), ("uf", 128, BF), ("uwf", 16, F32), ("Dz", 16, F32), ("q25", 512, BF), ("ones", 128, BF),
+    ("Ec", 2048, BF), ("rs2", 576, F32), ("enl", 2, U16),
+    ("vi", 128, I32), ("ai", 128, I32), ("ji", 32, I32),
+    ("rep", [6, 128], F32), ("wsc", [6, 128], F32), ("wtm", 384, F32), ("vw", 48, U16), ("vd", 48, U16),
+    ("dab", [2, 576], F32), ("low", [2, 576], F32), ("fst", [2, 16], F32), ("dm", [2, 8], F32),
+    ("A1", [4, 128], F16), ("Aoff", 512, U16), ("Y", [4, 128], BF), ("noff", 128, U16), ("nf", 128, F16),
     ("G1", 2048, BF), ("ab1", 2048, BF), ("G2", 2048, BF), ("ab2", 2048, BF), ("nyT", 128, BF), ("nxT", 128, BF),
-    ("m1", 128, F32), ("e1", 128, F32), ("s2", 128, F32), ("v8", 8, I32), ("v8b", 8, I32), ("vb", 128, F32), ("xn", 128, BF), ("xw", 128, BF),
-    ("dv", 128, F32), ("Am", 128, F32), ("mb", 128, BF), ("tA", 128, F32), ("oh", 128, F32), ("A2", 256, F32), ("K2", 256, F32),
-    ("g1", 384, F32), ("go", 48, U16), ("g3", 384, F32), ("GP", 2048, F32), ("fl", 128, F32), ("Ks", 128, F32), ("xv", 128, BF),
-    ("land", [4, 17, 2, 16], BF), ("snd", [4, 17, 2, 16], BF), ("ui", 512, I32), ("u", 512, I32), ("jw", 32, U16), ("js", 32, U16),
-    ("pr", 512, I32), ("pt", 512, I32), ("t2", 512, F32), ("hT", 512, F32), ("hoff", 480, U16), ("xvj", 512, BF),
-    ("kg", 512, F32), ("KT", 512, F32), ("SC", 512, F32), ("dsl", [ND, 512], BF), ("gsl", [2, 512], BF),
-    ("ki", 32, I32), ("pi", 32, I32), ("pw", 32, U16), ("ff", 32, BF), ("um", 32, I32), ("um2", 32, I32), ("dj", 32, F32), ("tj", 32, F32),
-    ("dz", 512, BF), ("z", 512, BF), ("Fi", 4, I32), ("thr", 4, F32), ("jo", 32, F32),
+    ("m1", 128, F32), ("e1", 128, F32), ("s2", 128, F32), ("v8", 8, I32), ("vb", 128, F16), ("xn", 128, BF), ("xw", 128, BF),
+    ("mb", 128, BF), ("oh", 128, F16), ("K2", 256, F32), ("fl", 128, F32),
+    ("g1", 384, F32), ("go", 48, U16), ("g3", 384, F32), ("xv", 128, BF),
+    ("land", [4, 544], BF), ("snd", [4, 544], BF), ("jw", 32, U16), ("js", 32, U16),
+    ("t2", 512, F32), ("KT", 512, F32), ("hT", 512, F32), ("pr", 512, F32), ("pt", 512, I32), ("hi", 512, I32), ("hoff", 480, U16),
+    ("xvj", 512, BF), ("gsl", [2, 512], BF), ("uw", 64, F32),
+    ("ki", 32, I32), ("pi", 32, I32), ("um", 32, I32), ("vj", 32, I32), ("pw", 32, U16), ("ff", 32, BF), ("dj", 32, F32), ("tj", 32, F32),
+    ("jb", 32, BF), ("Fi", 4, I32), ("thr", 4, F32), ("jo", 32, F32),
 ]:
-    _sb(_n, _c, _d)
-for _n in "tmi c15i ui Eio vf ut1 km um um2 jf tA dz kg SC vi".split():
-    SCRATCH.pop(_n, None)
-SCRATCH.pop("wtmx", None)
-for _i, _s in enumerate(SUBS):
-    _sb("ab%d_" % _i, [32, len(_s), 16], BF)
-for _n in ("pC0", "pC1", "pD1", "pD2", "pM0"):
+    SCRATCH[_n] = ("sbuf", [128] + (list(_c) if isinstance(_c, list) else [_c]), _d)
+for _n in ("lv", "df"):
+    SCRATCH[_n] = ("sbuf", [128, len(PAIRS), 512, 2], BF)
+for _n in ("pC0", "pC1", "pD1", "pD2", "pM0", "pE", "pU", "pM1"):
     SCRATCH[_n] = ("psum", [128, 512], F32)
-SCRATCH["pE"] = ("psum", [128, 512], F32)
-SCRATCH["pU"] = ("psum", [128, 512], F32)
-SCRATCH["pM1"] = ("psum", [128, 512], F32)
-for _n in ("Dz2", "dm2", "vd2", "z", "jt", "v8b", "K2"):
-    SCRATCH.pop(_n)
-for _n, _c, _d in (("X", 4736, BF), ("MU", [2, 144], BF), ("bcl", 32, U16), ("land", [4, 544], BF), ("snd", [4, 544], BF), ("uw", 96, F32), ("pr", 512, F32), ("nWb", 144, BF),
-                   ("wt2", [2, 128], F32), ("key", [2, 128], F32), ("dab", [2, 576], F32), ("low", [2, 576], F32), ("rs2", 576, F32), ("enl", 2, U16),
-                   ("fst", [2, 16], F32), ("dm", [2, 8], F32), ("Dz", 16, F32), ("uwf", 16, F32), ("XU", 4736, BF),
-                   ("diag", 512, F32), ("hold", 512, F32), ("GP", 1024, F32), ("scn", 96, F32), ("nxT", [3, 128], BF), ("xw", [3, 128], BF)):
-    _sb(_n, _c, _d)
-NDMA = 24
-SPLITJ = True
+NDMA = 20
 SEMAPHORES = ["cV", "cA", "cP", "cG"] + ["d%d" % i for i in range(NDMA)] + ["ls%d" % i for i in range(8)] + ["rs%d" % i for i in range(8)]
 
 OV = 30.0
-CY, PC, GC = 1.04, 0.5, 1.56
+CY, PC, GC, SC = 1.04, 0.5, 1.56, 3.8
 
 
 def build(g, core, T, topo):
@@ -75,7 +59,7 @@ def build(g, core, T, topo):
     def vc(n): return OV + max(64, n) * CY
     def gcst(n): return 60 + n * GC * CY
     def cp(o, i, r, w, n, G=False): add("V", lambda: V.tensor_copy(o, i), r, w, gcst(n) if G else vc(n))
-    def sct(o, i, r, w, n): add("V", lambda: V.tensor_copy(o, i), r, w, 60 + 3.8 * n * CY)
+    def sct(o, i, r, w, n): add("V", lambda: V.tensor_copy(o, i), r, w, 60 + SC * n * CY)
     def tt(o, a, b, op, r, w, n, G=False): add("V", lambda: V.tensor_tensor(o, a, b, op), r, w, gcst(n) if G else vc(n))
     def ts(o, a, s1, op0, r, w, n, s2=None, op1=None):
         if op1 is None: add("V", lambda: V.tensor_scalar(o, a, s1, None, op0), r, w, vc(n))
@@ -87,9 +71,8 @@ def build(g, core, T, topo):
     def act(o, i, f, r, w, n, G=False, **k): add("A", lambda: A.activation(o, i, f, **k), r, w, gcst(n) if G else vc(n))
     def mm(o, l, rh, st, sp, r, w, n, f=1): add("P", lambda: P.matmul(o, l, rh, st, sp), r, w, max(64, n) * f * PC)
     def dma(o, i, r, w, kb, q="S"): add(q, lambda: (g.sync if q == "S" else g.scalar).dma_start(o, i), r, w, kb, "d")
-    def iota(o, pat, cm, w, n, small=False):
-        if small: add("G", lambda: g.iota(o, pat, 0, cm, allow_small_or_imprecise_dtypes=True), "", w, 130 + 2 * n * CY)
-        else: add("G", lambda: g.iota(o, pat, 0, cm), "", w, 130 + 2 * n * CY)
+    def iota(o, pat, base, cm, w, n):
+        add("G", lambda: g.iota(o, pat, base, cm, allow_small_or_imprecise_dtypes=True), "", w, 130 + 2 * n * CY)
     def send(k, hop, part="zj"):
         dst = T.cores[(rank + hop) % N]
         rid, pid, _ = topo.addr(dst)
@@ -100,24 +83,28 @@ def build(g, core, T, topo):
         add("G", lambda: g.remote_dma(T.land[:, k, a:b], T.snd[:, k, a:b], T.sem["rs%d" % n], T.sem["ls%d" % n], pid, rid, m),
             " ".join("snd:%s%d" % (x, k) for x in part), " ".join("land:%s%d" % (x, k) for x in part), cnt, "r%d" % n)
     eq, mul, ad, sub, AND, SHR = ALU.is_equal, ALU.mult, ALU.add, ALU.subtract, ALU.bitwise_and, ALU.logical_shift_right
-    X2 = T.X[:]
-    X1 = T.X[:, 0:4096]
+    X1, XD, X2 = T.X[:, 0:DUM], T.X[:, 0:FND], T.X[:]
 
-    dma(T.pt[0:8, 256:384], T.v0[:], "", "pt:2", 4)
+    dma(T.vi[0:8, :], T.v0[:], "", "vi", 4)
     dma(T.ai[:], T.a0[:], "", "ai", 64)
-    dma(T.XU[:, 0:4096], T.x[:], "", "XU:b", 1024)
-    dma(T.NB[:], T.nb[:], "", "NB", 2048)
     dma(T.Y[:, 0], T.y0[:], "", "Y:0", 32, "A")
     dma(T.ji[:, 0:16], T.j0[0::2, :], "", "ji:0", 8, "A")
     dma(T.ji[:, 16:32], T.j0[1::2, :], "", "ji:1", 8, "A")
     dma(T.wi[:, 0:1], T.w[:], "", "wi:0", 4, "A")
-    dma(T.snd[:, 0, 0:512], T.z0[:], "", "snd:z0", 128)
     dma(X1, T.x[:], "", "X:b", 1024)
-    ms(T.XU[:, 4096:4736], 0.0, "XU:q", 320)
+    dma(T.NB[:], T.nb[:], "", "NB", 2048)
+    dma(T.snd[:, 0, 0:512], T.z0[:], "", "snd:z0", 128)
 
-    iota(T.pci[:, 0:1], [[0, 1]], 1, "pci:0", 1)
-    iota(T.ci[:], [[1, 512]], 0, "ci", 512)
-    iota(T.G2[:], [[1, 128], [0, 16]], 0, "G2", 2048, True)
+    add("G", lambda: g.iota(T.pci[:, 0:1], [[0, 1]], 0, 1), "", "pci:0", 132)
+    iota(T.cf[:], [[1, 512]], 0, 0, "cf", 512)
+    iota(T.c4[:], [[1, 8], [0, 16]], 0, 0, "c4", 128)
+    iota(T.c15[:], [[0, 32], [1, 16]], 0, 0, "c15", 512)
+    iota(T.G1[:], [[1, 128], [0, 16]], 0, 0, "G1", 2048)
+    iota(T.Ks[:], [[16, 4], [0, 2], [-1, 16]], 15, 0, "Ks", 128)
+    iota(T["io"][:, 0], [[1, 8], [8, 2], [256, 2]], 1, 0, "io:0", 32)
+    iota(T["io"][:, 1], [[0, 16], [16, 2]], 0, 0, "io:1", 32)
+    iota(T.offc[:], [[-4096, 8], [-32768, 2], [0, 32]], 2048 - 4096, 0, "offc", 512)
+    iota(T.TR3[:], [[1, TW]], 0, 0, "TR3", TW)
     ts(T.pci[:, 1:2], T.pci[:, 0:1], 15, AND, "pci:0", "pci:1", 1)
     ts(T.pci[:, 2:3], T.pci[:, 0:1], 4, SHR, "pci:0", "pci:2", 1)
     ts(T.pci[:, 3:4], T.pci[:, 0:1], 4, SHR, "pci:0", "pci:3", 1, 1, AND)
@@ -127,115 +114,114 @@ def build(g, core, T, topo):
     cP, cR, cG, cB, cA = (col(i) for i in range(5))
     def pcol(i, src, m, a, r="pf:0"): ts(col(i), src, m, mul, r, "pf:%d" % i, 1, a, ad)
     pcol(5, cG, 16.0, 15.0)
-    pcol(6, cB, 128.0, 0.0)
-    pcol(7, cB, -128.0, 0.0)
-    pcol(8, cR, 102 * S18, 102 * S18)
-    pcol(9, cR, -8192.0, 15 * 8192.0 + 2048)
+    pcol(6, cB, 256.0, 0.0)
+    pcol(7, cB, -256.0, 256.0)
+    pcol(8, cR, 102 * BIG, 102 * BIG)
+    pcol(9, cR, -4096.0, 2048.0)
     pcol(12, cB, -1.0, 1.0)
     pcol(13, cA, 16.0, cR)
+    pcol(14, cA, 16.0, 15.0)
     pcol(16, cA, 32.0, cR); pcol(17, col(16), 1.0, 16.0, "pf:16")
-    pcol(18, cR, 1.0, 4096.0)
+    pcol(18, cR, 1.0, float(FND))
     pcol(19, cR, 16.0, 0.0)
     cBm = (col(12), cB)
-    cp(T.cf[:], T.ci[:], "ci", "cf", 512)
-    ts(T.u[:], T.ci[:], 15, AND, "ci", "u", 512)
-    cp(T.c15[:], T.u[:], "u", "c15", 512)
-    ts(T.pt[:, 0:128], T.ci[:, 0:128], 4, SHR, "ci", "pt:0", 128)
-    cp(T.c4[:], T.pt[:, 0:128], "pt:0", "c4", 128)
     c128 = T.cf[:, 0:128]
     ts(T.Ex[:], T.c4[:], cP, eq, "c4 pf:0", "Ex", 128)
     ts(T.diag[:], T.c15[:], cR, eq, "c15 pf:0", "diag", 512)
-    ts(T.hold[:], T.c15[:], 1.0, ALU.min, "c15", "hold", 512)
-    for nm, s in (("idb", 1.0), ("nidb", -1.0), ("hidb", .5), ("nhidb", -.5), ("t85", -85 * S18), ("idf", 1.0)):
-        ts(T[nm][:], c128, cP, eq, "cf pf:0", nm, 128, s, mul)
-    ts(T.Wb[:], T.cf[:, 0:144], col(5), eq, "cf pf:5", "Wb", 144, S18, mul)
-    ts(T.nWb[:], T.cf[:, 0:144], col(5), eq, "cf pf:5", "nWb", 144, -S18, mul)
-    ts(T.Wf[:], T.cf[:, 0:144], col(5), eq, "cf pf:5", "Wf", 144, 0.0625, mul)
+    act(T.hold[:], T.c15[:], AF.Sign, "c15", "hold", 512)
+    act(T.dg8[:], T.diag[:, 0:128], AF.Copy, "diag", "dg8", 128, scale=8192.0)
+    ts(T.idf[:], c128, cP, eq, "cf pf:0", "idf", 128)
+    for nm, s in (("idb", 1.0), ("nidb", -1.0), ("hidb", .5), ("nhidb", -.5), ("t85", -85 * BIG), ("n26", -2 * BIG), ("zb", 0.0), ("i8k", 8192.0)):
+        act(T[nm][:], T.idf[:], AF.Copy, "idf", nm, 128, scale=s)
+    ts(T.Wb[:], T.cf[:, 0:144], col(5), eq, "cf pf:5", "Wb", 144, BIG, mul)
+    act(T.nWb[:], T.Wb[:], AF.Copy, "Wb", "nWb", 144, scale=-1.0)
     ts(T.B8[:], T.cf[:, 0:8], cG, eq, "cf pf:0", "B8", 8, 1048576.0, mul)
     ts(T.BO[:], T.c4[:], cG, eq, "c4 pf:0", "BO", 128)
     ts(T.rst[:], T.c15[:, 0:128], 0.0, eq, "c15", "rst", 128, 2.0 ** 40, mul)
-    ts(T.kc[:], T.c15[:, 0:128], 65536.0, mul, "c15", "kc", 128)
-    ts(T.ncn[:], T.c15[:, 0:128], -4096.0, mul, "c15", "ncn", 128, 61440.0, ad)
+    act(T.kc[:], T.c15[:, 0:128], AF.Copy, "c15", "kc", 128, scale=65536.0)
+    act(T.ncn[:], T.c15[:, 0:128], AF.Identity, "c15", "ncn", 128, scale=-4096.0, bias=63488.0)
     act(T.thc[:], T.c15[:], AF.Identity, "c15", "thc", 512, scale=-1.0, bias=16.0)
-    ts(T.oh[:], c128, cP, ALU.is_lt, "cf pf:0", "oh", 128, -1.0, mul)
-    tt(T.oh[:], T.oh[:], T.BO[:], mul, "oh BO", "oh", 256)
-    tt(T.UT[:], T.oh[:], T.idf[:], ad, "oh idf", "UT", 256)
-    ts(T.pt[:, 128:256], T.ci[:, 0:128], 5, SHR, "ci", "pt:1", 128)
-    ts(T.Ks[:], T.pt[:, 128:256], 16.0, mul, "pt:1", "Ks", 128, 15.0, ad)
-    tt(T.Ks[:], T.Ks[:], T.c15[:, 0:128], sub, "Ks c15", "Ks", 256)
+    ts(T.mb[:], c128, cP, ALU.is_lt, "cf pf:0", "mb", 128, -1.0, mul)
+    tt(T.mb[:], T.mb[:], T.BO[:], mul, "mb BO", "mb", 256)
+    tt(T.UT[:], T.mb[:], T.idf[:], ad, "mb idf", "UT", 256)
+    act(T.nBO[:], T.BO[:], AF.Copy, "BO", "nBO", 128, scale=-2048.0)
     for b in range(2):
         ts(T.Pm[:, b], T.Ks[:], col(13), eq, "Ks pf:13 pf:12 pf:0", "Pm:%d" % b, 128, cBm[b], mul)
+        ts(T.Pv[:, b], T.Ks[:], col(14), eq, "Ks pf:14 pf:6 pf:7", "Pv:%d" % b, 128, col(7 - b), mul)
         for q in range(2):
             ts(T.SJ[:, 2 * b + q], c128, col(16 + q), eq, "cf pf:16 pf:17 pf:12 pf:0", "SJ:%d" % (2 * b + q), 128, cBm[b], mul)
-    ts(T.wi[:, 1:2], T.wi[:, 0:1], 4032, AND, "wi:0", "wi:1", 1)
-    ts(T.wi[:, 2:3], T.wi[:, 0:1], 63, AND, "wi:0", "wi:2", 1)
-    cp(T.wf[:, 0:2], T.wi[:, 1:3], "wi:1 wi:2", "wf", 2)
-    for h in range(2):
-        ts(T.MU[:, h], T.cf[:, 0:144], col(5), eq, "cf pf:5 wf", "MU:%d" % h, 144, T.wf[:, h:h + 1], mul)
+    ts(T.wf[:, 0:1], T.wi[:, 0:1], 2048.0, ALU.is_ge, "wi:0", "wf:0", 1, -4096.0, mul)
+    tt(T.wf[:, 1:2], T.wf[:, 0:1], T.wi[:, 0:1], ad, "wf:0 wi:0", "wf:1", 1)
+    ts(T.MU[:], T.cf[:, 0:144], col(5), eq, "cf pf:5 wf:1", "MU", 144, T.wf[:, 1:2], mul)
     ts(T.scn[:, 0:32], T.cf[:, 0:32], 16.0, mul, "cf pf:18", "scn:0", 32, col(18), ad)
-    ts(T.jo[:, 0:32:2], T.cf[:, 0:16], col(19), ad, "cf pf:19", "jo", 16)
-    ts(T.jo[:, 1:32:2], T.cf[:, 256:272], col(19), ad, "cf pf:19", "jo", 16)
-    cp(T.prm[:], T.jo[:], "jo", "prm", 32)
-    cp(T.bcl[:], T.ci[:, 0:32], "ci", "bcl", 32)
+    ts(T.prm[:], T["io"][:, 0], col(19), ad, "io:0 pf:19", "prm", 32)
+    ts(T.rl[:], T["io"][:, 1], cR, ad, "io:1 pf:0", "rl", 32)
+    act(T.cjb[:], T["io"][:, 1], AF.Copy, "io:1", "cjb", 32, scale=8.0)
+    cp(T.bcl[:], T.cf[:, 0:8], "cf", "bcl", 8)
     act(T.uf[:], c128, AF.Identity, "cf", "uf", 128, scale=1.0 / 256)
     ms(T.rs2[:], 0.0, "rs2", 576)
-    ms(T.rs2[:, 0:1], 1024.0, "rs2", 1)
-    for c in range(1, 8): ms(T.rs2[:, 8 * c * (c + 1):8 * c * (c + 1) + 1], 1024.0 * 1024, "rs2:%d" % c, 1)
+    for c in range(8): ms(T.rs2[:, 8 * c * (c + 1):8 * c * (c + 1) + 1], 1048576.0, "rs2", 1)
     pcol(10, cR, 8.0, 24.0)
     ts(col(11), col(10), cR, mul, "pf:10 pf:0", "pf:11", 1, 15.0, ad)
     ts(T.enl[:, 0:1], col(11), 575.0, ALU.min, "pf:11", "enl", 1)
     ts(T.Dz[:], T.cf[:, 0:16], 16.0, mul, "cf pf:0", "Dz", 16, cR, ad)
     ts(T.uwf[:], T.Dz[:], 1.0 / 256, mul, "Dz", "uwf", 8)
-    ts(T.Dz[:], T.Dz[:], float(DUM), ad, "Dz", "Dz", 8)
-    ts(T.Drep[:], c128, float(DUM), ad, "cf", "Drep", 128)
+    ts(T.Dz[:, 8:16], T.Dz[:, 0:8], DUM + 4096.0, ad, "Dz", "Dz", 8)
+    ts(T.Dz[:, 0:8], T.Dz[:, 0:8], DUM + 6144.0, ad, "Dz", "Dz", 8)
     ms(T.q25[:], 0.25, "q25", 256)
     ms(T.ones[:], 1.0, "ones", 64)
-    ms(T.X[:, 4096:4736], 0.0, "X:q", 320)
-    ts(T.Ec[:], T.G2[:], cP, eq, "G2 pf:0", "Ec", 1024)
-    for nm in ("TR", "TR3")[:1 + bool(T3)]:
-        for k in range(10):
-            n = min(512, 4736 - 512 * k)
-            act(T[nm][:, 512 * k:512 * k + n], T.cf[:, 0:n], AF.Identity, "cf", "%s:%d" % (nm, k), n, bias=512.0 * k)
+    ms(T.X[:, DUM:XW], 0.0, "X:d X:q", 320)
+    ts(T.Ec[:], T.G1[:], cP, eq, "G1 pf:0", "Ec", 1024)
+    for k in range(9):
+        n = min(512, TW - 512 * k)
+        act(T.TR[:, 512 * k:512 * k + n], T.cf[:, 0:n], AF.Identity, "cf", "TR:%d" % k, n, bias=512.0 * k)
 
-    def finish(ps, pn, i, two):
+    def whole(o, i, tmp, r, w, tn, n, scalar):
+        if scalar:
+            act(tmp, i, AF.Identity, r, tn, n, bias=MAGIC)
+            act(o, tmp, AF.Identity, tn, w, n, bias=-MAGIC)
+        else: ts(o, i, MAGIC, ad, r, w, n, -MAGIC, ad)
+
+    def finish(terms, pn, i):
         e = int(i > RO)
-        tt(T.wt2[:, e], ps, T.diag[:, 0:128], mul, pn + " diag", "wt2:%d" % e, 128)
-        cp(T.rep[:, i], ps, pn, "rep:%d" % i, 128)
-        tt(T.key[:, e], ps, T.uf[:], ad, pn + " uf", "key:%d" % e, 128)
-        scan(T.wsc[:, i], T.hold[:, 0:128], T.wt2[:, e], mul, ad, "hold wt2:%d" % e, "wsc:%d" % i, 128)
+        off = 2048.0 * (1 + e)
+        p0, p1, p2 = (T[pn][:, a:a + 128] for a in (0, 128, 256))
+        for n, (l, rh, r) in enumerate(terms): mm(p1, l, rh, n == 0, False, r, pn, 128)
+        mm(p1, T.idb[:], T.dg8[:], False, True, "idb dg8", pn, 128)
+        for n, (l, rh, r) in enumerate(terms): mm(p0, l, rh, n == 0, n == len(terms) - 1, r, pn, 128)
+        for n, (l, rh, r) in enumerate(terms): mm(p2, l, rh, n == 0, False, r, pn, 128)
+        mm(p2, T.idb[:], T.uf[:], False, False, "idb uf", pn, 128)
+        mm(p2, T.i8k[:], T.ones[:], False, True, "i8k ones", pn, 128)
+        scan(T.wsc[:, i], T.hold[:, 0:128], p1, mul, ALU.max, "hold " + pn, "wsc:%d" % i, 128)
+        act(T.rep[:, i], p0, AF.Identity, pn, "rep:%d" % i, 128, bias=off)
         wv = T.wsc[:, i, 15::16]
-        if not e: cp(T.vw[:, 8 * i:8 * i + 8], wv, "wsc:%d" % i, "vw:%d" % i, 8)
+        if not e: ts(T.vw[:, 8 * i:8 * i + 8], wv, off - 8192.0, ad, "wsc:%d" % i, "vw:%d" % i, 8)
         for c in range(8):
             n, a = 16 * c + 16, 8 * c * (c + 1)
-            act(T.dab[:, e, a:a + n], T.key[:, e, 0:n], AF.Abs, "key:%d wsc:%d" % (e, i), "dab:%d_%d" % (e, c), n, scale=-1.0, bias=T.wsc[:, i, 16 * c + 15:16 * c + 16])
+            act(T.dab[:, e, a:a + n], T[pn][:, 256:256 + n], AF.Abs, pn + " wsc:%d" % i, "dab:%d_%d" % (e, c), n, scale=-1.0, bias=T.wsc[:, i, 16 * c + 15:16 * c + 16])
         scan(T.low[:, e], T.rs2[:], T.dab[:, e], ad, ALU.min, "rs2 " + " ".join("dab:%d_%d" % (e, c) for c in range(8)), "low:%d" % e, 576)
-        tt(T.fst[:, e], T.low[:, e].indirect(T.enl[:, 0:1]), T.uwf[:], eq, "low:%d enl uwf" % e, "fst:%d" % e, 16, True)
+        tt(T.fst[:, e], T.low[:, e].indirect(T.enl[:, 0:1]), T.uwf[:], ALU.not_equal, "low:%d enl uwf" % e, "fst:%d" % e, 16, True)
         dm, dn = T.dm[:, e], "dm:%d" % e
-        tt(dm, wv, T.Dz[:, 0:8], sub, "wsc:%d Dz" % i, dn, 16)
-        tt(dm, dm, T.fst[:, e, 0:8], mul, dn + " fst:%d" % e, dn, 16)
-        tt(dm, dm, T.Dz[:, 0:8], ad, dn + " Dz", dn, 16)
-        cp(T.vd[:, 8 * i:8 * i + 8], dm, dn, "vd:%d" % i, 8)
+        tt(dm, T.fst[:, e, 0:8], T.Dz[:, 8 * e:8 * e + 8], mul, "Dz fst:%d" % e, dn, 16)
+        tt(dm, dm, wv, ALU.max, dn + " wsc:%d" % i, dn, 16)
+        ts(T.vd[:, 8 * i:8 * i + 8], dm, off - 8192.0, ad, dn, "vd:%d" % i, 8)
 
-    cp(T.fl[0:8, :], T.pt[0:8, 256:384], "pt:2", "fl", 128)
-    mm(T.pM0[:, 0:128], T.Ex[0:8, :], T.fl[0:8, :], True, True, "Ex fl", "pM0", 128, 4)
-    finish(T.pM0[:, 0:128], "pM0", 0, False)
-    cp(T.A1[:, 0], T.ai[:], "ai", "A1:0", 128)
+    ts(T.oh[0:8, :], T.vi[0:8, :], -2048.0, ad, "vi", "oh", 128)
+    finish([(T.Ex[0:8, :], T.oh[0:8, :], "Ex oh")], "pD1", 0)
+    ts(T.A1[:, 0], T.ai[:], -2048.0, ad, "ai", "A1:0", 128)
     cp(T.Aoff[:, 0:128], T.ai[:], "ai", "Aoff:0", 128)
-    cp(T.dj[:], T.ji[:], "ji", "dj", 32)
-    tr(T.tj[:], T.dj[:], "dj", "tj", 32)
-    ts(T.snd[:, 0, 512:544], T.tj[:], col(6), ad, "tj pf:6", "snd:j0", 32)
+    cp(T.jb[:], T.ji[:], "ji", "jb", 32)
+    tr(T.snd[:, 0, 512:544], T.jb[:], "jb", "snd:j0", 32)
     send(0, 1)
-    XU = T.XU[:, 0:4096]
 
     def far(t, base, off, on, Gn, an, neg, negT):
-        win, wn = (XU, "XU ") if on == "noff" or t == 1 else (X1, "X:b ")
         for c in range(4):
-            w = win.indirect(off[:, 32 * c:32 * c + 32]) if on == "noff" else win.indirect(T.Aoff[:, off + 32 * c:off + 32 * c + 32])
+            w = X1.indirect(off[:, 32 * c:32 * c + 32]) if on == "noff" else X1.indirect(T.Aoff[:, off + 32 * c:off + 32 * c + 32])
             o = T[Gn][:, 512 * c:512 * c + 512]
-            if base + c in UDVE[t]: cp(o, w, wn + on, "%s:%d" % (Gn, c), 512, True)
-            else: act(o, w, AF.Copy, wn + on, "%s:%d" % (Gn, c), 512, True)
+            if base + c in UDVE[t]: cp(o, w, "X:b " + on, "%s:%d" % (Gn, c), 512, True)
+            else: act(o, w, AF.Copy, "X:b " + on, "%s:%d" % (Gn, c), 512, True)
         for c in range(4):
-            pn = "pC%d" % (c & 1 if t in TWOB else base // 4)
+            pn = "pC%d" % (c & 1 if t == 1 else base // 4)
             mm(T[pn][:], T.idb[:], T[Gn][:, 512 * c:512 * c + 512], True, False, "idb %s:%d" % (Gn, c), pn, 512)
             mm(T[pn][:], neg, T.Ec[:, 512 * c:512 * c + 512], False, True, "Ec " + negT, pn, 512)
             act(T[an][:, 512 * c:512 * c + 512], T[pn][:], AF.Abs, pn, "%s:%d" % (an, c), 512)
@@ -246,9 +232,9 @@ def build(g, core, T, topo):
         mm(T.pD1[:, 256:384], yo, T.nidb[:], True, True, "Y:%d nidb" % o, "pD1", 128)
         act(T.nyT[:], T.pD1[:, 256:384], AF.Copy, "pD1", "nyT", 128)
         cp(T.noff[:], T.NB[:].indirect(T.vw[:, 8 * o:8 * o + 8]), "NB vw:%d" % o, "noff", 128, True)
-        cp(T.nf[:], T.noff[:], "noff", "nf", 128)
+        ts(T.nf[:], T.noff[:], -2048.0, ad, "noff", "nf", 64)
         far(t, 0, T.noff, "noff", "G1", "ab1", T.nyT[:], "nyT")
-        mm(T.pD1[:, 128:256], T.nf[:], T.idf[:], True, False, "nf idf", "pD1", 128, 4)
+        mm(T.pD1[:, 128:256], T.nf[:], T.idb[:], True, False, "nf idb", "pD1", 128)
         mm(T.pD1[:, 128:256], T.idb[:], T.ncn[:], False, True, "idb ncn", "pD1", 128)
         mm(T.pD1[:, 0:128], T.idb[:], T.kc[:], True, False, "idb kc", "pD1", 128)
         for k in range(16):
@@ -258,181 +244,171 @@ def build(g, core, T, topo):
         scan(T.s2[:], T.e1[:], T.pD1[:, 128:256], ALU.min, ALU.max, "e1 pD1", "s2", 128)
         cp(T.v8[:], T.s2[:, 15::16], "s2", "v8", 8)
         ts(T.v8[:], T.v8[:], 4095, AND, "v8", "v8", 8)
-        cp(T.vb[:], T.v8[:].indirect(T.bcl[:, 0:8]), "v8 bcl", "vb", 128, True)
-        mm(T.pD1[:, 0:128], T.vb[:], T.idf[:], True, True, "vb idf", "pD1", 128, 4)
-        finish(T.pD1[:, 0:128], "pD1", t, True)
-        act(T.xn[:], XU.indirect(T.vw[:, 8 * t:8 * t + 8]), AF.Copy, "XU vw:%d" % t, "xn", 128, True)
-        mm(T.pD1[:, 128:256], T.xn[:], T.nidb[:], True, True, "xn nidb", "pD1", 128)
-        mm(T.pD1[:, 256:384], T.idb[:], T.xn[:], True, False, "xn idb", "pD1", 128)
-        mm(T.pD1[:, 256:384], T.nidb[:], yo, False, True, "Y:%d nidb" % o, "pD1", 128)
-        mm(T.pD1[:, 384:512], T.hidb[:], T.xn[:], True, False, "xn hidb", "pD1", 128)
-        mm(T.pD1[:, 384:512], T.hidb[:], yo, False, False, "Y:%d hidb" % o, "pD1", 128)
-        mm(T.pD1[:, 384:512], T.nidb[:], T.q25[:, 0:128], False, True, "q25 nidb", "pD1", 128)
-        act(T.nxT[:, o], T.pD1[:, 128:256], AF.Copy, "pD1", "nxT:%d" % o, 128)
-        act(T.Y[:, t], T.pD1[:, 256:384], AF.Abs, "pD1", "Y:%d" % t, 128)
-        ts(T.xw[:, o], T.pD1[:, 384:512], MAGIC, ad, "pD1", "xw:%d" % o, 128, -MAGIC, ad)
-
-    def step_xu(t): sct(T.XU[:].indirect(T.vd[:, 8 * t:8 * t + 8]), T.xw[:, t - 1], "xw:%d vd:%d" % (t - 1, t), "XU", 128)
+        add("V", lambda: V.tensor_scalar(T.vb[:], T.v8[:].indirect(T.bcl[:]), -2048.0, None, ad), "v8 bcl", "vb", gcst(128))
+        finish([(T.vb[:], T.idb[:], "vb idb")], "pD1", t)
+        act(T.xn[:], X1.indirect(T.vw[:, 8 * t:8 * t + 8]), AF.Copy, "X:b vw:%d" % t, "xn", 128, True)
+        pn = "pC0"
+        mm(T[pn][:, 128:256], T.xn[:], T.nidb[:], True, True, "xn nidb", pn, 128)
+        mm(T[pn][:, 256:384], T.idb[:], T.xn[:], True, False, "xn idb", pn, 128)
+        mm(T[pn][:, 256:384], T.nidb[:], yo, False, True, "Y:%d nidb" % o, pn, 128)
+        mm(T[pn][:, 384:512], T.hidb[:], T.xn[:], True, False, "xn hidb", pn, 128)
+        mm(T[pn][:, 384:512], T.hidb[:], yo, False, False, "Y:%d hidb" % o, pn, 128)
+        mm(T[pn][:, 384:512], T.nidb[:], T.q25[:, 0:128], False, True, "q25 nidb", pn, 128)
+        act(T.nxT[:], T[pn][:, 128:256], AF.Copy, pn, "nxT", 128)
+        act(T.Y[:, t], T[pn][:, 256:384], AF.Abs, pn, "Y:%d" % t, 128)
+        whole(T.xw[:], T[pn][:, 384:512], T.e1[:], pn, "xw", "e1", 128, OPT["mw"])
 
     def users_far(t):
         o = t - 1
-        far(t, 4, 128 * o, "Aoff:%d" % o, "G2", "ab2", T.nxT[:, o], "nxT:%d" % o)
+        Ao, an, rn = T.A1[:, o], " A1:%d" % o, " rep:%d" % t
+        far(t, 4, 128 * o, "Aoff:%d" % o, "G2", "ab2", T.nxT[:], "nxT")
+        mm(T.pD2[:, 128:256], T.vb[:], T.idb[:], True, False, "idb vb", "pD2", 128)
+        mm(T.pD2[:, 128:256], T.nidb[:], Ao, False, True, "nidb" + an, "pD2", 128)
+        mm(T.pD2[:, 384:512], T.idb[:], Ao, True, True, "idb" + an, "pD2", 128)
         for l in range(16):
             mm(T.pD2[:, 0:128], T.Wb[:, 15 - l:143 - l], T.ab2[:, l::16], l == 0, l == 15, "Wb ab2", "pD2", 128)
-        tt(T.dv[:], T.rep[:, t], T.A1[:, o], sub, "rep:%d A1:%d" % (t, o), "dv", 256)
-        if t > 1: tt(T.Am[:], T.A1[:, o], T.Drep[:], sub, "A1:%d Drep" % o, "Am", 256)
-
-    def double(dst, src, sn, **k):
+        mm(T.pM0[:, 0:256], T.zb[:], T.thc[:, 0:256], True, False, "zb thc", "pM0", 256)
         for b in range(2):
-            mm(T.pM0[:, 128 * b:128 * b + 128], T.Pm[:, b], src, True, True, "Pm:%d %s" % (b, sn), "pM0", 128, 4)
-        act(T[dst][:], T.pM0[:, 0:256], AF.Identity, "pM0 pf:9", dst, 256, **k)
+            mm(T.pM0[:, 128 * b:128 * b + 128], T.Pv[:, b], T.rep[:, t], False, False, "Pv:%d" % b + rn, "pM0", 128, 4)
 
     def users_b(t):
         o = t - 1
         ts(T.mb[:], T.pD2[:, 0:128], col(8) if t == 1 else T.thr[:, 0:1], ALU.is_gt, "pD2 pf:8 thr", "mb", 128)
-        tt(T.fl[:], T.mb[:], T.dv[:], mul, "mb dv", "fl", 256)
-        tt(T.A1[:, t], T.fl[:], T.A1[:, o], ad, "fl A1:%d" % o, "A1:%d" % t, 256)
-        double("A2", T.A1[:, t], "A1:%d" % t, bias=-2048.0)
-        if t < RO: cp(T.Aoff[:, 128 * t:128 * t + 128], T.A1[:, t], "A1:%d" % t, "Aoff:%d" % t, 128)
-        sct(X2.indirect(T.vd[:, 8 * t:8 * t + 8]), T.xw[:, o], "xw:%d vd:%d" % (o, t), "X:b X:q", 128)
+        tt(T.fl[:], T.mb[:], T.pD2[:, 128:256], mul, "mb pD2", "fl", 128)
+        tt(T.A1[:, t], T.fl[:], T.pD2[:, 384:512], ad, "fl pD2", "A1:%d" % t, 128)
+        for b in range(2):
+            mm(T.pM0[:, 128 * b:128 * b + 128], T.Pm[:, b], T.A1[:, t], False, b == 1, "Pm:%d A1:%d" % (b, t), "pM0", 128)
+        act(T.K2[:], T.pM0[:, 0:256], AF.Identity, "pM0 pf:9", "K2", 256, bias=col(9))
+        if t < RO: ts(T.Aoff[:, 128 * t:128 * t + 128], T.A1[:, t], 2048.0, ad, "A1:%d" % t, "Aoff:%d" % t, 64)
+        else: ts(T.fl[:], T.A1[:, t], 2048.0, ad, "A1:%d" % t, "fl", 128)
+        sct(XD.indirect(T.vd[:, 8 * t:8 * t + 8]), T.xw[:], "xw vd:%d" % t, "X:b X:d", 128)
         act(T.xv[:], X1.indirect(T.vw[:, 8 * t:8 * t + 8]), AF.Copy, "X:b vw:%d" % t, "xv", 128, True)
         if t > 1:
             i = 2 + t
             mm(T.pD2[:, 256:384], T.UT[:], T.mb[:], True, True, "UT mb", "pD2", 128)
-            ts(T.oh[:], T.pD2[:, 256:384], 1.0, eq, "pD2", "oh", 128)
-            tt(T.oh[:], T.oh[:], T.Am[:], mul, "oh Am", "oh", 256)
-            mm(T.pD2[:, 384:512], T.idf[:], T.Drep[:], True, False, "idf Drep", "pD2", 128, 4)
-            mm(T.pD2[:, 384:512], T.BO[:], T.oh[:], False, True, "BO oh", "pD2", 128, 4)
-            finish(T.pD2[:, 384:512], "pD2", i, False)
+            ts(T.mb[:], T.pD2[:, 256:384], 1.0, eq, "pD2", "mb", 128)
+            tt(T.oh[:], T.mb[:], T.pD2[:, 384:512], mul, "mb pD2", "oh", 128)
+            finish([(T.nBO[:], T.mb[:], "nBO mb"), (T.BO[:], T.oh[:], "BO oh")], "pD2", i)
             sct(T.TR[:].indirect(T.vd[:, 8 * i:8 * i + 8]), T.rep[:, i], "rep:%d vd:%d" % (i, i), "TR", 128)
         sct(T.TR[:].indirect(T.vd[:, 8 * o:8 * o + 8]), T.rep[:, t], "rep:%d vd:%d" % (t, o), "TR", 128)
-        if t in T3:
-            n = 128 * t
-            on = " ".join("vw:%d" % i for i in range(o))
-            if t == 1: off, on = T.vw[:, 8:16], "vw:1"
-            else:
-                off = T.vw[:, 0:8 * o]
-                cp(T.go[:, 8 * o:8 * t], T.wsc[:, t, 15::16], "wsc:%d" % t, "go:0", 8)
-            for h in range(1 if t == 1 else 0, 2):
-                m = n - 128 * (h == 0)
-                tt(T.wtm[:, 0:m], T.TR[:].indirect(off), T.diag[:, 0:m], mul, "TR diag " + on, "wtm", m, True)
-                scan(T.g1[:, 0:m], T.hold[:, 0:m], T.wtm[:, 0:m], mul, ad, "hold wtm", "g1", m)
-                off, on = T.go[:, 24 * h:24 * h + 8 * t], "go:%d" % h
-                cp(T.go[:, 24 * h:24 * h + m // 16], T.g1[:, 15:m:16], "g1", on, 8 * t)
-            act(T.g3[:, 0:n], T.TR[:].indirect(off), AF.Copy, "TR " + on, "g3", n, True)
-            for i in range(t):
-                sct(T.TR3[:].indirect(T.vd[:, 8 * i:8 * i + 8]), T.g3[:, 128 * i:128 * i + 128], "g3 vd:%d" % i, "TR3", 128)
+        n = 128 * t
+        on = " ".join("vw:%d" % i for i in range(o))
+        if t == 1: off, on = T.vw[:, 8:16], "vw:1"
+        else:
+            off = T.vw[:, 0:8 * o]
+            cp(T.go[:, 8 * o:8 * t], T.vw[:, 8 * t:8 * t + 8], "vw:%d" % t, "go:0", 8)
+        for h in range(1 if t == 1 else 0, 2):
+            m = n - 128 * (h == 0)
+            tt(T.wtm[:, 0:m], T.TR[:].indirect(off), T.diag[:, 0:m], mul, "TR diag " + on, "wtm", m, True)
+            scan(T.g1[:, 0:m], T.hold[:, 0:m], T.wtm[:, 0:m], mul, ad, "hold wtm", "g1", m)
+            off, on = T.go[:, 24 * h:24 * h + 8 * t], "go:%d" % h
+            cp(T.go[:, 24 * h:24 * h + m // 16], T.g1[:, 15:m:16], "g1", on, 8 * t)
+        act(T.g3[:, 0:n], T.TR[:].indirect(off), AF.Copy, "TR " + on, "g3", n, True)
+        for i in range(t):
+            sct(T.TR3[:].indirect(T.vd[:, 8 * i:8 * i + 8]), T.g3[:, 128 * i:128 * i + 128], "g3 vd:%d" % i, "TR3", 128)
         if t == RO:
             dma(T.yt[:], T.TR[0:128:16, 0:4096], "TR", "", 128)
-            dma(T.ya[:], T.A1[:, t], "A1:%d" % t, "", 64)
+            dma(T.ya[:], T.fl[:], "fl", "", 64)
             dma(T.yy[:], T.Y[:, t], "Y:%d" % t, "", 32)
             dma(T.yv[:], T.rep[0:128:16, t], "rep:%d" % t, "", 4)
-
-    def keys(t):
-        act(T.GP[:, 0:512], T.t2[:], AF.Identity, "t2 pf:9", "GP:0", 512, bias=col(9))
-        tr(T.KT[:], T.GP[:, 0:512], "GP:0", "KT", 512)
-        act(T.GP[:, 512:1024], T.rep[:, t].indirect(T.js[:]), AF.Copy, "rep:%d js" % t, "GP:1", 512, True)
-        for s0 in range(16):
-            mm(T.pM0[:, 256:288], T.Wf[:, 15 - s0:143 - s0], T.GP[:, 512 + s0:1024:16], s0 == 0, s0 == 15, "Wf GP:1", "pM0", 64, 4)
 
     def seek_head(t):
         k = t - 1
         L, J = "land:z%d" % k, "land:j%d" % k
         z, j = T.land[:, k, 0:512], T.land[:, k, 512:544]
+        mm(T.pM1[:, 0:32], T.idb[:], T.cjb[:], True, False, "idb cjb", "pM1", 32)
         for b in range(2):
             for q in range(2):
-                mm(T.pM1[:, b:32:2], T.SJ[:, 2 * b + q], T.land[:, k, 512 + q:544:2], q == 0, q == 1, "SJ:%d %s" % (2 * b + q, J), "pM1", 16)
+                mm(T.pM1[:, b:32:2], T.SJ[:, 2 * b + q], T.land[:, k, 512 + q:544:2], False, b + q == 2, "SJ:%d %s" % (2 * b + q, J), "pM1", 16)
         cp(T.jw[:], T.pM1[:, 0:32], "pM1", "jw", 32)
-        ts(T.js[:], j, col(7), ad, J + " pf:7", "js", 32)
-        act(T.t2[:], T.A2[:].indirect(T.jw[:]), AF.Copy, "A2 jw", "t2", 512, True)
-        tr(T.hT[:], T.t2[:], "t2", "hT", 512)
+        cp(T.js[:], j, J, "js", 32)
+        act(T.t2[:], T.K2[:].indirect(T.jw[:]), AF.Copy, "K2 jw", "t2", 512, True)
+        tr(T.KT[:], T.t2[:], "t2", "KT", 512)
         for s0 in range(16):
-            for h in range(2):
-                mm(T.pU[:, 0:32], T.MU[:, h, 15 - s0:143 - s0], T.land[:, k, s0:512:16], s0 + h == 0, s0 + h == 16, "MU:%d %s" % (h, L), "pU", 32)
+            mm(T.pU[:, 0:32], T.MU[:, 15 - s0:143 - s0], T.land[:, k, s0:512:16], s0 == 0, s0 == 15, "MU " + L, "pU", 32)
         cp(T.ki[:], T.pU[:, 0:32], "pU", "ki", 32)
         ts(T.pi[:], T.ki[:], 4095, AND, "ki", "pi", 32)
         ts(T.uw[:, 0:32], T.pi[:], 32.0, ad, "pi", "uw:0", 32)
-        ts(T.ki[:], T.ki[:], 63, AND, "ki", "ki", 32)
-        ts(T.uw[:, 64:96], T.ki[:], 32.0, ad, "ki", "uw:2", 32, 2048.0, mul)
-        tt(T.pr[:], T.uw[:, 0:32].indirect(T.bcl[:]), T.hT[:], mul, "uw:0 bcl hT", "pr", 512, True)
-        tt(T.pt[:], T.uw[:, 64:96].indirect(T.bcl[:]), T.pr[:], ad, "uw:2 bcl pr", "pt", 512, True)
-        ts(T.u[:], T.pt[:], 5, ALU.arith_shift_right, "pt", "u", 512, 4095, AND)
-        cp(T.hoff[:], T.u[:].indirect(T.prm[:, 2:32]), "u prm", "hoff", 480, True)
-        ts(T.ki[:], T.pi[:], 127, AND, "pi", "ki", 32)
-        ts(T.tj[:], T.ki[:], col(6), ad, "ki pf:6", "tj", 32)
-        tt(T.dj[:], T.tj[:], j, sub, "tj " + J, "dj", 64)
+        ts(T.um[:], T.ki[:], 127, AND, "ki", "um", 32)
+        ts(T.uw[:, 32:64], T.um[:], 32.0, ad, "um", "uw:1", 32, 2048.0, mul)
+        for c in range(len(CUT) - 1):
+            a, b = CUT[c], CUT[c + 1]
+            s, n, m = slice(32 * a, 32 * b), 32 * (b - a), ":%d" % c
+            tt(T.hT[:, s], T.KT[:].indirect(T.prm[:, 2 * a:2 * b]), T.offc[:, s], sub, "KT prm offc", "hT" + m, n, True)
+            tt(T.pr[:, s], T.uw[:, 0:32].indirect(T.rl[:, 2 * a:2 * b]), T.hT[:, s], mul, "uw:0 rl hT" + m, "pr" + m, n, True)
+            tt(T.pt[:, s], T.uw[:, 32:64].indirect(T.rl[:, 2 * a:2 * b]), T.pr[:, s], ad, "uw:1 rl pr" + m, "pt" + m, n, True)
+            ts(T.hi[:, s], T.pt[:, s], 5, ALU.arith_shift_right, "pt" + m, "hi" + m, n, 4095, AND)
+            cp(T.hoff[:, s], T.hi[:, s], "hi" + m, "hoff" + m, n)
+        tt(T.dj[:], T.um[:], j, sub, "um " + J, "dj", 64)
+        cp(T.vj[:], T.KT[:, 0::16], "KT", "vj", 32)
+        ts(T.vj[:], T.vj[:], 12, SHR, "vj", "vj", 32)
         act(T.xvj[:], T.xv[:].indirect(T.js[:]), AF.Copy, "xv js", "xvj", 512, True)
         mm(T.pM1[:], T.hidb[:], z, True, False, "hidb " + L, "pM1", 512)
         mm(T.pM1[:], T.nhidb[:], T.xvj[:], False, False, "nhidb xvj", "pM1", 512)
         mm(T.pM1[:], T.idb[:], T.q25[:], False, True, "idb q25", "pM1", 512)
+        whole(T.X[:, FND:XW], T.pM1[:], T.t2[:], "pM1", "X:q", "t2", 512, OPT["mq"])
 
     def seek_rest(t):
         k = t - 1
         L, J = "land:z%d" % k, "land:j%d" % k
         z, j = T.land[:, k, 0:512], T.land[:, k, 512:544]
-        XH = X1
         mm(T.pE[:], T.t85[:], T.thc[:], True, False, "t85 thc", "pE", 512)
-        ts(T.X[:, 4096:4608], T.pM1[:], MAGIC, ad, "pM1", "X:q", 512, -MAGIC, ad)
-        keys(t)
-        nd, ng = 0, 0
+        mm(T.pE[:], T.n26[:], T.q25[:], False, False, "n26 q25", "pE", 512)
+        ng, n = 0, 0
         left = [0]
         def acc(o, l, rh, r, n):
             left[0] += 1
             def f():
                 left[0] -= 1
                 return P.matmul(o, l, rh, False, left[0] == 0)
-            add("P", f, r, "pE:acc", max(64, n) * PC)
-        for si, S in enumerate(SUBS):
-            an = "ab%d_" % si
-            for i, l in enumerate(S):
-                w = XH.indirect(T.hoff[:, 32 * l - 32:32 * l])
-                o = T[an][:, :, i, :]
-                if l in CSET[t]:
+            add("P", f, r, "pE" if OPT["fix"] else "pE:acc", max(64, n) * PC)
+        for si, S in enumerate(PAIRS):
+            way, m = WAYS[t][si], len(S)
+            an, dn = (" ".join("%s:%d_%d" % (b, si, i) for i in range(m)) for b in ("lv", "df"))
+            e = T.pE[:, S[0]::16 // m]
+            for i in range(m):
+                w = X1.indirect(T.hoff[:, 32 * n:32 * n + 32])
+                hn = "X:b hoff:%d " % max(c for c in range(len(CUT)) if CUT[c] <= n)
+                n += 1
+                o, d, on, di = T.lv[:, si, :, i], T.df[:, si, :, i], "lv:%d_%d" % (si, i), "df:%d_%d" % (si, i)
+                if way == "A":
                     s = ng & 1; ng += 1
                     pn = ("pU", "pM1")[s]
-                    act(T.gsl[:, s], w, AF.Copy, "X:b hoff", "gsl:%d" % s, 512, True)
+                    act(T.gsl[:, s], w, AF.Copy, hn, "gsl:%d" % s, 512, True)
                     mm(T[pn][:], T.idb[:], T.gsl[:, s], True, False, "idb gsl:%d" % s, pn, 512)
                     mm(T[pn][:], T.nidb[:], z, False, True, "nidb " + L, pn, 512)
-                    act(o, T[pn][:], AF.Abs, pn, "%s:%d" % (an, i), 512)
+                    act(o, T[pn][:], AF.Abs, pn, on, 512)
                 else:
-                    s = nd % ND; nd += 1
-                    tt(T.dsl[:, s], w, z, sub, "X:b hoff " + L, "dsl:%d" % s, 512, True)
-                    if l in BSET[t]:
-                        ts(o, T.dsl[:, s], 0.0, ALU.max, "dsl:%d" % s, "%s:%d" % (an, i), 256, 2.0, mul)
-                        for s0 in range(16):
-                            acc(T.pE[:, l::16], T.nWb[:, 15 - s0:143 - s0], T.dsl[:, s, s0::16], "nWb dsl:%d" % s, 32)
-                    else: act(o, T.dsl[:, s], AF.Abs, "dsl:%d" % s, "%s:%d" % (an, i), 512)
-            for s0 in range(16):
-                acc(T.pE[:, S[0]::16 // len(S)], T.Wb[:, 15 - s0:143 - s0], T[an][:, :, :, s0], "Wb " + an, 32 * len(S))
+                    tt(d, w, z, sub, hn + L, di, 512, True)
+                    if way == "M": act(o, d, AF.Abs, di, on, 512)
+            if way == "V":
+                ts(T.lv[:, si, :, 0:m], T.df[:, si, :, 0:m], 0.0, ALU.max, dn, an, 256 * m, 2.0, mul)
+                for s0 in range(16): acc(e, T.nWb[:, 15 - s0:143 - s0], T.df[:, si, s0::16, 0:m], "nWb " + dn, 32 * m)
+            for s0 in range(16): acc(e, T.Wb[:, 15 - s0:143 - s0], T.lv[:, si, s0::16, 0:m], "Wb " + an, 32 * m)
         scan(T.hT[:], T.pE[:], T.KT[:], ALU.min, ALU.max, "pE KT", "hT", 512)
         cp(T.ki[:], T.hT[:, 15::16], "hT", "ki", 32)
-        ts(T.pi[:], T.ki[:], 8191, AND, "ki", "pi", 32)
+        ts(T.pi[:], T.ki[:], 4095, AND, "ki", "pi", 32)
         cp(T.pw[:], T.pi[:], "pi", "pw", 32)
-        tn = "TR3" if t in T3 else "TR"
-        for h in range(2 if t in T3 else 0, 3):
-            tt(T.t2[:], T[tn][:].indirect(T.pw[:]), T.diag[:], mul, tn + " diag pw", "t2", 512, True)
-            scan(T.hT[:], T.hold[:], T.t2[:], mul, ad, "hold t2", "hT", 512)
-            if h < 2: cp(T.pw[:], T.hT[:, 15::16], "hT", "pw", 32)
-        tt(T.ff[:], T.pM0[:, 256:288], T.hT[:, 15::16], eq, "pM0 hT", "ff", 32)
+        tt(T.t2[:], T.TR3[:].indirect(T.pw[:]), T.diag[:], mul, "TR3 diag pw", "t2", 512, True)
+        scan(T.hT[:], T.hold[:], T.t2[:], mul, ad, "hold t2", "hT", 512)
+        tt(T.ff[:], T.vj[:], T.hT[:, 15::16], eq, "vj hT", "ff", 64)
         tt(T.scn[:, 32:64], T.ff[:], T.scn[:, 0:32], mul, "ff scn:0", "scn:1", 64)
         tt(T.scn[:, 64:96], T.scn[:, 32:64], T.hT[:, 15::16], ALU.max, "scn:1 hT", "scn:2", 64)
         cp(T.pw[:], T.scn[:, 64:96], "scn:2", "pw", 32)
-        tt(T.xvj[:], X2.indirect(T.pw[:]), z, sub, "X:b X:q pw " + L, "xvj", 512, True)
+        tt(T.xvj[:], X2.indirect(T.pw[:]), z, sub, "X:b X:d X:q pw " + L, "xvj", 512, True)
         act(T.snd[:, t, 0:512], T.xvj[:], AF.Abs, "xvj", "snd:z%d" % t, 512)
         tt(T.tj[:], T.ff[:], T.dj[:], mul, "ff dj", "tj", 64)
         if t < RO:
             tt(T.snd[:, t, 512:544], T.tj[:], j, ad, "tj " + J, "snd:j%d" % t, 64)
-            if SPLITJ: send(t, 1, "j"); send(t, 1, "z")
-            else: send(t, 1)
-            mm(T.pM0[:, 0:32], T.ones[:], T.ff[:], True, True, "ones ff", "pM0", 32)
-            red(T.thr[:, 1:2], T.pM0[:, 0:32], ad, "pM0", "thr:1", 32)
+            send(t, 1, "j"); send(t, 1, "z")
+            mm(T.pU[:, 0:32], T.ones[:], T.ff[:], True, True, "ones ff", "pU", 32)
+            red(T.thr[:, 1:2], T.pU[:, 0:32], ad, "pU", "thr:1", 32)
             cp(T.Fi[:, 0:1], T.thr[:, 1:2], "thr:1", "Fi:0", 1)
             ts(T.Fi[:, 1:2], T.Fi[:, 0:1], 15, AND, "Fi:0", "Fi:1", 1)
-            ts(T.thr[:, 0:1], T.Fi[:, 1:2], 16 * S18, mul, "Fi:1 pf:8", "thr:0", 1, col(8), ad)
+            ts(T.thr[:, 0:1], T.Fi[:, 1:2], 16 * BIG, mul, "Fi:1 pf:8", "thr:0", 1, col(8), ad)
         else:
-            tt(T.dj[:], T.tj[:], j, ad, "tj " + J, "dj", 64)
-            ts(T.ff[:], T.dj[:], col(7), ad, "dj pf:7", "ff", 32)
-            tr(T.snd[:, t, 512:544], T.ff[:], "ff", "snd:j%d" % t, 32)
+            tt(T.jb[:], T.tj[:], j, ad, "tj " + J, "jb", 64)
+            tr(T.snd[:, t, 512:544], T.jb[:], "jb", "snd:j%d" % t, 32)
             send(t, -RO)
 
     part = CACHE.setdefault("part", {})
@@ -442,13 +418,12 @@ def build(g, core, T, topo):
         for i in range(n0, len(ops)): part[i] = name + str(t)
     run(users_a, 1, "a")
     run(users_far, 1, "f")
-    for t in range(1, RO):
-        step_xu(t)
-        run(users_a, t + 1, "a")
     for t in range(1, RO + 1):
         run(users_b, t, "b")
         run(seek_head, t, "h")
-        if t < RO: run(users_far, t + 1, "f")
+        if t < RO:
+            run(users_a, t + 1, "a")
+            run(users_far, t + 1, "f")
         run(seek_rest, t, "r")
     dma(T.yz[:], T.land[:, RO, 0:512], "land:z%d" % RO, "", 128)
     cp(T.jo[:], T.land[:, RO, 512:544], "land:j%d" % RO, "jo", 32)
@@ -488,66 +463,16 @@ def depend(ops):
     return deps
 
 
-HOP, SELF = 150.0, 60.0
+HOP, SELF, DK, RZ, RJ = 280.0, 140.0, 3.0, 3500.0, 2500.0
 
 
 def plan(ops, deps):
-    n = len(ops)
-    def dur(i):
-        q, c, kind = ops[i][0], ops[i][4], ops[i][5]
-        if kind == "c": return c, c
-        if kind == "d": return 60.0, 2000.0 + c * 5.0
-        return 500.0, (5000.0 if int(kind[1:]) < 4 else 3000.0)
-    succ = [[] for _ in range(n)]
-    for i in range(n):
-        for j in deps[i]: succ[j].append(i)
-    pr = [0.0] * n
-    for i in range(n - 1, -1, -1):
-        pr[i] = dur(i)[1] + max([pr[s] + (HOP if deps[s][i] else 0.0) for s in succ[i]] + [0.0])
-    x = SEED * 7919 + 1
-    for i in range(n):
-        x = (x * 1103515245 + 12345) % 2147483648
-        pr[i] += NOISE * x / 2147483648.0 - (UB if i in CACHE["ua"] else 0.0)
-    left = [len(d) for d in deps]
-    ready = [i for i in range(n) if not left[i]]
-    free = {}
-    done, start = [0.0] * n, [0.0] * n
-    at = [0.0] * n
-    order = []
-    dmafree = 0.0
-    while ready:
-        est = {i: max(free.get(ops[i][0], 0.0), at[i]) for i in ready}
-        i0 = min(ready, key=lambda i: (est[i], -pr[i], i))
-        q = ops[i0][0]
-        if q == "S": i1 = min(i for i in ready if ops[i][0] == q and est[i] <= est[i0])
-        else:
-            i1 = max((i for i in ready if ops[i][0] == q and est[i] <= est[i0] + 30.0), key=lambda i: (pr[i], -i))
-            better = [i for i in ready if ops[i][0] == q and pr[i] > pr[i1] + 1500.0 and est[i] < est[i1] + 0.6 * dur(i1)[0]]
-            if better: i1 = max(better, key=lambda i: pr[i])
-        hold, lat = dur(i1)
-        start[i1] = est[i1]
-        free[q] = est[i1] + hold
-        if ops[i1][5] == "d":
-            dmafree = max(dmafree, est[i1] + 2000.0) + lat - 2000.0
-            done[i1] = dmafree
-        else: done[i1] = est[i1] + lat
-        order.append(i1)
-        ready.remove(i1)
-        for s in succ[i1]:
-            w = deps[s][i1]
-            at[s] = max(at[s], done[i1] + (SELF if ops[s][0] == q else HOP) if w else start[i1])
-            left[s] -= 1
-            if not left[s]: ready.append(s)
-    return order, start, done
-
-
-def plan2(ops, deps):
     n = len(ops)
     hold, lat = [0.0] * n, [0.0] * n
     cum, last = 0.0, {}
     edges = [dict() for _ in range(n)]
     for i, (q, fn, r, w, c, kind) in enumerate(ops):
-        if kind == "c": hold[i] = lat[i] = c
+        if kind == "c": hold[i] = lat[i] = c * OPT["f"]
         elif kind == "d":
             hold[i] = 60.0
             if r: lat[i] = 2000.0 + c * DK
@@ -596,10 +521,9 @@ def plan2(ops, deps):
 
     pr = [0.0] * n
     for i in range(n - 1, -1, -1): pr[i] = max([pr[s] + e for s, e in succ[i].items()] + [lat[i]])
-    x = SEED * 7919 + 1
     key = {i: (-pr[i], i) for i in range(n)}
-    best = None
-    for it in range(PASSES):
+    best, x = None, OPT["seed"]
+    for it in range(OPT["passes"]):
         st = place(topo_order(key, False), False)
         span = max(st[i] + lat[i] for i in range(n))
         if best is None or span < best[0]: best = (span, st)
@@ -607,15 +531,11 @@ def plan2(ops, deps):
         key = {}
         for i in range(n):
             x = (x * 1103515245 + 12345) % 2147483648
-            key[i] = (-bk[i] + NOISE * x / 2147483648.0 + BIAS.get(CACHE["part"].get(i), 0.0), i)
+            key[i] = (-bk[i] + BIAS.get(CACHE["part"].get(i), 0.0) + OPT["noise"] * x / 2147483648.0, i)
     st = best[1]
     return topo_order({i: (st[i], i) for i in range(n)}, False), st, [st[i] + lat[i] for i in range(n)]
 
 
-DK, RZ, RJ, PASSES = 5.0, 5000.0, 3000.0, 3
-CFG = {'c': {1: (2, 3, 6, 11, 12, 13), 2: (1, 2, 3, 5, 6, 9, 10, 14), 3: (2, 3, 5, 6, 9, 11, 12, 13, 14, 15)}, 'b': {1: (2, 3, 4, 7, 8, 10, 11, 12, 13, 14, 15), 2: (4, 7, 8, 10, 11, 13, 14, 15), 3: (1, 4, 7, 8, 10, 11, 12, 14, 15)}, 'bias': {'r1': 2500, 'h3': -8000, 'f3': 8000, 'r2': 3000, 'r3': 3000, 'h1': -5000, 'a2': -3000, 'b1': -10000, 'f2': 1000, 'a3': -500, 'b3': 2000, 'h2': 3000, 'b2': 2500}, 'ud': {1: (1, 3, 5, 7), 2: (1,), 3: (2,)}, 'seed': 60, 'nz': 200}
-CFG = {'c': {1: (1, 2, 3, 5, 9, 11, 15), 2: (1, 2, 3, 5, 6, 7, 12, 13), 3: (2, 3, 5, 6, 7, 10, 13, 15)}, 'b': {1: (1, 3, 4, 5, 7, 8, 10, 12, 13, 14), 2: (1, 2, 3, 4, 6, 7, 9, 10, 11, 12, 14, 15), 3: (1, 3, 5, 6, 10, 11, 13, 14)}, 'bias': {'r1': 3500, 'h3': 500, 'f3': 6500, 'r2': 3000, 'r3': 1500, 'h1': 0, 'a2': -2000, 'b1': -16000, 'f2': 2000, 'a3': -500, 'b3': 2000, 'h2': 0, 'b2': 2000}, 'ud': {1: (1, 3, 5, 7), 2: (1,), 3: (2,)}, 'seed': 33, 'nz': 200}
-CSET, BSET, BIAS, UDVE, SEED, NOISE = CFG['c'], CFG['b'], CFG['bias'], CFG['ud'], CFG['seed'], CFG['nz']
 CACHE = {}
 
 
@@ -625,9 +545,9 @@ def rank_program(g, core, T, topo):
     ops = build(g, core, T, topo)
     if "o" not in CACHE:
         deps = depend(ops)
-        CACHE["o"] = (deps,) + plan2(ops, deps)
-        CACHE["ops"] = ops
+        CACHE["o"] = (deps,) + plan(ops, deps)
     deps, order = CACHE["o"][0], CACHE["o"][1]
+    at = {i: n for n, i in enumerate(order)}
     Q = {"V": g.vector, "A": g.scalar, "P": g.tensor, "G": g, "S": g.sync}
     token = {}
     known = {q: {} for q in Q}
@@ -644,7 +564,7 @@ def rank_program(g, core, T, topo):
                 s, v = token[j]
                 if ops[j][5][0] == "r" and not any(a.startswith("land") for a in r): s = "ls" + s[2:]
                 if kn.get(s, 0) < v and need.get(s, (0, 0))[0] < v: need[s] = (v, j)
-        for s, (v, j) in sorted(need.items(), key=lambda e: -order.index(e[1][1])):
+        for s, (v, j) in sorted(need.items(), key=lambda e: -at[e[1][1]]):
             if kn.get(s, 0) < v:
                 Q[q].wait_ge(T.sem[s], v)
                 kn[s] = v

@@ -5,11 +5,12 @@ BIG, MAGIC = 2.0 ** 25, 12582912.0
 DUM, FND, XW = 4096, 4224, 4736
 TW = 4224
 PAIRS = [(1, 9), (2, 10), (3, 11), (4, 12), (5, 13), (6, 14), (7, 15), (8,)]
-WAYS = {1: 'AVVMAVAA', 2: 'VAVAAVMA', 3: 'AVAAVMAA'}
+WAYS = {1: 'AVVAMVAA', 2: 'AVVAMVAM', 3: 'VAVAAVAA'}
 CUT = (0, 8, 15)
-UDVE = {1: (1, 3, 7), 2: (1, 2, 4, 6), 3: (2, 3)}
-BIAS = {'a1': 1000, 'b1': 1000, 'r3': 1000}
-OPT = {"seed": 30, "noise": 400.0, "passes": 6, "mw": 1, "mq": 1, "fix": 1, "f": 0.9}
+UDVE = {1: (1, 3, 4), 2: (2, 4, 5), 3: (3,)}
+ADVE = {1: (1, 3, 5), 2: (1,), 3: ()}
+BIAS = {'b3': -1000, 'r3': 1000, 'a1': -4000, 'b1': -1000, 'f2': 1000, 'h2': 1000, 'h1': -6000}
+OPT = {"seed": 1, "noise": 400.0, "passes": 6, "mw": 1, "mq": 1, "fix": 1, "f": 0.9, "nx": 3, "cut": 8, "bc": 0, "hs": 3, "steps": 7000, "us": 2}
 
 F32, BF, F16, I32, U16 = "float32", "bfloat16", "float16", "int32", "uint16"
 SCRATCH = {}
@@ -18,25 +19,25 @@ for _n, _c, _d in [
     ("cf", 512, F32), ("c15", 512, F32), ("c4", 128, F32), ("Ks", 128, F32), ("io", [2, 32], F32),
     ("pci", 8, I32), ("pf", 32, F32), ("wi", 4, I32), ("wf", 8, F32),
     ("idb", 128, BF), ("nidb", 128, BF), ("hidb", 128, BF), ("nhidb", 128, BF), ("t85", 128, BF), ("n26", 128, BF), ("zb", 128, BF),
-    ("idf", 128, F32), ("i8k", 128, BF), ("dg8", 128, BF),
-    ("Wb", 144, BF), ("nWb", 144, BF), ("B8", 8, BF), ("BO", 128, BF), ("nBO", 128, BF), ("Ex", 128, BF), ("diag", 512, F32), ("hold", 512, F32),
+    ("idf", 128, F32), ("i8k", 128, BF), ("i83", 128, BF), ("sndu", [4, 96], F16 if OPT["bc"] else F32), ("landu", [4, 96], F16 if OPT["bc"] else F32), ("dg8", 128, BF),
+    ("Wb", 144, BF), ("nWb", 144, BF), ("B8", 16, BF), ("BB", 128, BF), ("BO", 128, BF), ("nBO", 128, BF), ("Ex", 128, BF), ("diag", 512, BF), ("hold", 512, BF),
     ("rst", 128, F32), ("kc", 128, BF), ("ncn", 128, BF), ("thc", 512, BF), ("UT", 128, BF), ("Pm", [2, 128], BF), ("Pv", [2, 128], F32),
-    ("MU", 144, F16), ("SJ", [4, 128], BF), ("cjb", 32, BF), ("scn", 96, F32), ("prm", 32, U16), ("rl", 32, U16), ("bcl", 8, U16),
+    ("MU", 144, F16), ("SJ", [4, 128], BF), ("cjb", 32, BF), ("scn", 128, F32), ("prm", 32, U16), ("rl", 32, U16), ("bcl", 8, U16),
     ("offc", 512, F32), ("uf", 128, BF), ("uwf", 16, F32), ("Dz", 16, F32), ("q25", 512, BF), ("ones", 128, BF),
-    ("Ec", 2048, BF), ("rs2", 576, F32), ("enl", 2, U16),
+    ("Ec", 2048, BF), ("rs2", 576, BF), ("enl", 2, U16),
     ("vi", 128, I32), ("ai", 128, I32), ("ji", 32, I32),
-    ("rep", [6, 128], F32), ("wsc", [6, 128], F32), ("wtm", 384, F32), ("vw", 48, U16), ("vd", 48, U16),
-    ("dab", [2, 576], F32), ("low", [2, 576], F32), ("fst", [2, 16], F32), ("dm", [2, 8], F32),
+    ("rep", [6, 128], F32), ("wsc", [6, 128], F32), ("wtm", 512, F16), ("vw", 48, U16), ("vd", 48, U16),
+    ("dab", [2, 576], BF), ("low", [2, 576], BF), ("fst", [2, 16], F32), ("dm", [2, 8], F32),
     ("A1", [4, 128], F16), ("Aoff", 512, U16), ("Y", [4, 128], BF), ("noff", 128, U16), ("nf", 128, F16),
     ("G1", 2048, BF), ("ab1", 2048, BF), ("G2", 2048, BF), ("ab2", 2048, BF), ("nyT", 128, BF), ("nxT", 128, BF),
     ("m1", 128, F32), ("e1", 128, F32), ("s2", 128, F32), ("v8", 8, I32), ("vb", 128, F16), ("xn", 128, BF), ("xw", 128, BF),
     ("mb", 128, BF), ("oh", 128, F16), ("K2", 256, F32), ("fl", 128, F32),
-    ("g1", 384, F32), ("go", 48, U16), ("g3", 384, F32), ("xv", 128, BF),
+    ("g1", 512, F16), ("go", 48, U16), ("g3", 384, F32), ("xv", 128, BF),
     ("land", [4, 544], BF), ("snd", [4, 544], BF), ("jw", 32, U16), ("js", 32, U16),
     ("t2", 512, F32), ("KT", 512, F32), ("hT", 512, F32), ("pr", 512, F32), ("pt", 512, I32), ("hi", 512, I32), ("hoff", 480, U16),
-    ("xvj", 512, BF), ("gsl", [2, 512], BF), ("uw", 64, F32),
-    ("ki", 32, I32), ("pi", 32, I32), ("um", 32, I32), ("vj", 32, I32), ("pw", 32, U16), ("ff", 32, BF), ("dj", 32, F32), ("tj", 32, F32),
-    ("jb", 32, BF), ("Fi", 4, I32), ("thr", 4, F32), ("jo", 32, F32),
+    ("xvj", 512, BF), ("gsl", [2, 512], BF),
+    ("ki", 32, I32), ("pi", 32, I32), ("um", 32, I32), ("vc", 32, I32), ("pw", 32, U16), ("ff", 32, BF), ("dj", 32, F32), ("tj", 32, F32),
+    ("jb", 32, BF),
 ]:
     SCRATCH[_n] = ("sbuf", [128] + (list(_c) if isinstance(_c, list) else [_c]), _d)
 for _n in ("lv", "df"):
@@ -44,7 +45,7 @@ for _n in ("lv", "df"):
 for _n in ("pC0", "pC1", "pD1", "pD2", "pM0", "pE", "pU", "pM1"):
     SCRATCH[_n] = ("psum", [128, 512], F32)
 NDMA = 20
-SEMAPHORES = ["cV", "cA", "cP", "cG"] + ["d%d" % i for i in range(NDMA)] + ["ls%d" % i for i in range(8)] + ["rs%d" % i for i in range(8)]
+SEMAPHORES = ["cV", "cA", "cP", "cG"] + ["d%d" % i for i in range(NDMA)] + ["ls%d" % i for i in range(12)] + ["rs%d" % i for i in range(12)]
 
 OV = 30.0
 CY, PC, GC, SC = 1.04, 0.5, 1.56, 3.8
@@ -52,14 +53,18 @@ CY, PC, GC, SC = 1.04, 0.5, 1.56, 3.8
 
 def build(g, core, T, topo):
     ops = []
+    CUT = (0, OPT["cut"], 15) if OPT["cut"] else (0, 15)
     V, A, P = g.vector, g.scalar, g.tensor
     rank = T.rank_of(core)
     N = len(T.cores)
     def add(q, fn, r, w, c, kind="c"): ops.append((q, fn, r.split(), w.split(), c, kind))
     def vc(n): return OV + max(64, n) * CY
-    def gcst(n): return 60 + n * GC * CY
+    index = CACHE["index"] = {}
+    def gcst(n, by="g"):
+        index[len(ops)] = by
+        return 60 + n * (GC if by == "g" else SC) * CY
     def cp(o, i, r, w, n, G=False): add("V", lambda: V.tensor_copy(o, i), r, w, gcst(n) if G else vc(n))
-    def sct(o, i, r, w, n): add("V", lambda: V.tensor_copy(o, i), r, w, 60 + SC * n * CY)
+    def sct(o, i, r, w, n): add("V", lambda: V.tensor_copy(o, i), r, w, gcst(n, "s"))
     def tt(o, a, b, op, r, w, n, G=False): add("V", lambda: V.tensor_tensor(o, a, b, op), r, w, gcst(n) if G else vc(n))
     def ts(o, a, s1, op0, r, w, n, s2=None, op1=None):
         if op1 is None: add("V", lambda: V.tensor_scalar(o, a, s1, None, op0), r, w, vc(n))
@@ -76,12 +81,17 @@ def build(g, core, T, topo):
     def send(k, hop, part="zj"):
         dst = T.cores[(rank + hop) % N]
         rid, pid, _ = topo.addr(dst)
-        m = topo.mask(core, dst)
-        cnt = len(topo.engines(core, dst))
-        a, b = {"zj": (0, 544), "z": (0, 512), "j": (512, 544)}[part]
-        n = k + 4 * (part == "j")
-        add("G", lambda: g.remote_dma(T.land[:, k, a:b], T.snd[:, k, a:b], T.sem["rs%d" % n], T.sem["ls%d" % n], pid, rid, m),
-            " ".join("snd:%s%d" % (x, k) for x in part), " ".join("land:%s%d" % (x, k) for x in part), cnt, "r%d" % n)
+        en = topo.engines(core, dst)
+        if OPT["us"] > 1 and 0 < k < RO: en = en[part != "z"::2]
+        m = sum(1 << e for e in en)
+        if part == "u": o, i, n = T.landu[:, k], T.sndu[:, k], 8 + k
+        elif part == "w": o, i, n = T.landu[:, RO, 0:1], T.sndu[:, RO, 0:1], 8 + RO
+        else:
+            a, b = {"zj": (0, 544), "z": (0, 512), "j": (512, 544)}[part]
+            o, i, n = T.land[:, k, a:b], T.snd[:, k, a:b], k + 4 * (part == "j")
+        x = "u" if part in "uw" else ""
+        add("G", lambda: g.remote_dma(o, i, T.sem["rs%d" % n], T.sem["ls%d" % n], pid, rid, m),
+            " ".join("snd%s:%s%d" % (x, y, k) for y in part.replace("u", "abc")), " ".join("land%s:%s%d" % (x, y, k) for y in part), len(en), "r%d" % n)
     eq, mul, ad, sub, AND, SHR = ALU.is_equal, ALU.mult, ALU.add, ALU.subtract, ALU.bitwise_and, ALU.logical_shift_right
     X1, XD, X2 = T.X[:, 0:DUM], T.X[:, 0:FND], T.X[:]
 
@@ -90,7 +100,7 @@ def build(g, core, T, topo):
     dma(T.Y[:, 0], T.y0[:], "", "Y:0", 32, "A")
     dma(T.ji[:, 0:16], T.j0[0::2, :], "", "ji:0", 8, "A")
     dma(T.ji[:, 16:32], T.j0[1::2, :], "", "ji:1", 8, "A")
-    dma(T.wi[:, 0:1], T.w[:], "", "wi:0", 4, "A")
+    dma(T.wi[:, 0:1], T.w[:], "", "wi:0", 4)
     dma(X1, T.x[:], "", "X:b", 1024)
     dma(T.NB[:], T.nb[:], "", "NB", 2048)
     dma(T.snd[:, 0, 0:512], T.z0[:], "", "snd:z0", 128)
@@ -104,6 +114,8 @@ def build(g, core, T, topo):
     iota(T["io"][:, 0], [[1, 8], [8, 2], [256, 2]], 1, 0, "io:0", 32)
     iota(T["io"][:, 1], [[0, 16], [16, 2]], 0, 0, "io:1", 32)
     iota(T.offc[:], [[-4096, 8], [-32768, 2], [0, 32]], 2048 - 4096, 0, "offc", 512)
+    ms(T.rs2[:], 0.0, "rs2", 288)
+    for c in range(8): iota(T.rs2[:, 8 * c * (c + 1):8 * c * (c + 1) + 1], [[0, 1]], 1048576, 0, "rs2:%d" % c, 1)
     iota(T.TR3[:], [[1, TW]], 0, 0, "TR3", TW)
     ts(T.pci[:, 1:2], T.pci[:, 0:1], 15, AND, "pci:0", "pci:1", 1)
     ts(T.pci[:, 2:3], T.pci[:, 0:1], 4, SHR, "pci:0", "pci:2", 1)
@@ -112,7 +124,9 @@ def build(g, core, T, topo):
     cp(T.pf[:, 0:5], T.pci[:, 0:5], "pci", "pf:0", 5)
     def col(i): return T.pf[:, i:i + 1]
     cP, cR, cG, cB, cA = (col(i) for i in range(5))
-    def pcol(i, src, m, a, r="pf:0"): ts(col(i), src, m, mul, r, "pf:%d" % i, 1, a, ad)
+    def pcol(i, src, m, a, r="pf:0"):
+        if i in (5, 10): ts(col(i), src, m, mul, r, "pf:%d" % i, 1, a, ad)
+        else: act(col(i), src, AF.Identity, r, "pf:%d" % i, 1, scale=m, bias=a)
     pcol(5, cG, 16.0, 15.0)
     pcol(6, cB, 256.0, 0.0)
     pcol(7, cB, -256.0, 256.0)
@@ -122,21 +136,24 @@ def build(g, core, T, topo):
     pcol(13, cA, 16.0, cR)
     pcol(14, cA, 16.0, 15.0)
     pcol(16, cA, 32.0, cR); pcol(17, col(16), 1.0, 16.0, "pf:16")
-    pcol(18, cR, 1.0, float(FND))
+    pcol(18, cR, 1.0, FND - 2048.0)
     pcol(19, cR, 16.0, 0.0)
     cBm = (col(12), cB)
     c128 = T.cf[:, 0:128]
     ts(T.Ex[:], T.c4[:], cP, eq, "c4 pf:0", "Ex", 128)
-    ts(T.diag[:], T.c15[:], cR, eq, "c15 pf:0", "diag", 512)
-    act(T.hold[:], T.c15[:], AF.Sign, "c15", "hold", 512)
-    act(T.dg8[:], T.diag[:, 0:128], AF.Copy, "diag", "dg8", 128, scale=8192.0)
+    ts(T.t2[:], T.c15[:], cR, eq, "c15 pf:0", "t2", 512)
+    act(T.diag[:], T.t2[:], AF.Identity, "t2", "diag", 512, scale=-6144.0, bias=8192.0)
+    act(T.dg8[:], T.t2[:, 0:128], AF.Copy, "t2", "dg8", 128, scale=8192.0)
+    ts(T.hold[:], T.c15[:], 0.0, eq, "c15", "hold", 512, -1048576.0, mul)
     ts(T.idf[:], c128, cP, eq, "cf pf:0", "idf", 128)
-    for nm, s in (("idb", 1.0), ("nidb", -1.0), ("hidb", .5), ("nhidb", -.5), ("t85", -85 * BIG), ("n26", -2 * BIG), ("zb", 0.0), ("i8k", 8192.0)):
+    for nm, s in (("idb", 1.0), ("nidb", -1.0), ("hidb", .5), ("nhidb", -.5), ("t85", -85 * BIG), ("n26", -2 * BIG), ("zb", 0.0), ("i8k", 8192.0), ("i83", 8320.0)):
         act(T[nm][:], T.idf[:], AF.Copy, "idf", nm, 128, scale=s)
     ts(T.Wb[:], T.cf[:, 0:144], col(5), eq, "cf pf:5", "Wb", 144, BIG, mul)
     act(T.nWb[:], T.Wb[:], AF.Copy, "Wb", "nWb", 144, scale=-1.0)
-    ts(T.B8[:], T.cf[:, 0:8], cG, eq, "cf pf:0", "B8", 8, 1048576.0, mul)
+    ts(T.B8[:, 0:8], T.cf[:, 0:8], cG, eq, "cf pf:0", "B8:0", 8, 1048576.0, mul)
+    ts(T.B8[:, 8:16], T.cf[:, 0:8], cG, eq, "cf pf:0", "B8:1", 8, -1048576.0, mul)
     ts(T.BO[:], T.c4[:], cG, eq, "c4 pf:0", "BO", 128)
+    act(T.BB[:], T.BO[:], AF.Copy, "BO", "BB", 128, scale=BIG)
     ts(T.rst[:], T.c15[:, 0:128], 0.0, eq, "c15", "rst", 128, 2.0 ** 40, mul)
     act(T.kc[:], T.c15[:, 0:128], AF.Copy, "c15", "kc", 128, scale=65536.0)
     act(T.ncn[:], T.c15[:, 0:128], AF.Identity, "c15", "ncn", 128, scale=-4096.0, bias=63488.0)
@@ -152,15 +169,17 @@ def build(g, core, T, topo):
             ts(T.SJ[:, 2 * b + q], c128, col(16 + q), eq, "cf pf:16 pf:17 pf:12 pf:0", "SJ:%d" % (2 * b + q), 128, cBm[b], mul)
     ts(T.wf[:, 0:1], T.wi[:, 0:1], 2048.0, ALU.is_ge, "wi:0", "wf:0", 1, -4096.0, mul)
     tt(T.wf[:, 1:2], T.wf[:, 0:1], T.wi[:, 0:1], ad, "wf:0 wi:0", "wf:1", 1)
+    if OPT["us"]:
+        cp(T.sndu[:, RO, 0:1], T.wf[:, 1:2], "wf:1", "sndu:w%d" % RO, 1)
+        send(RO, -1, "w")
+        cp(T.wf[:, 1:2], T.landu[:, RO, 0:1], "landu:w%d" % RO, "wf:1", 1)
     ts(T.MU[:], T.cf[:, 0:144], col(5), eq, "cf pf:5 wf:1", "MU", 144, T.wf[:, 1:2], mul)
-    ts(T.scn[:, 0:32], T.cf[:, 0:32], 16.0, mul, "cf pf:18", "scn:0", 32, col(18), ad)
+    ts(T.scn[:, 96:128], T.cf[:, 0:32], 16.0, mul, "cf pf:18", "scn:3", 32, col(18), ad)
     ts(T.prm[:], T["io"][:, 0], col(19), ad, "io:0 pf:19", "prm", 32)
     ts(T.rl[:], T["io"][:, 1], cR, ad, "io:1 pf:0", "rl", 32)
     act(T.cjb[:], T["io"][:, 1], AF.Copy, "io:1", "cjb", 32, scale=8.0)
     cp(T.bcl[:], T.cf[:, 0:8], "cf", "bcl", 8)
     act(T.uf[:], c128, AF.Identity, "cf", "uf", 128, scale=1.0 / 256)
-    ms(T.rs2[:], 0.0, "rs2", 576)
-    for c in range(8): ms(T.rs2[:, 8 * c * (c + 1):8 * c * (c + 1) + 1], 1048576.0, "rs2", 1)
     pcol(10, cR, 8.0, 24.0)
     ts(col(11), col(10), cR, mul, "pf:10 pf:0", "pf:11", 1, 15.0, ad)
     ts(T.enl[:, 0:1], col(11), 575.0, ALU.min, "pf:11", "enl", 1)
@@ -192,14 +211,14 @@ def build(g, core, T, topo):
         for n, (l, rh, r) in enumerate(terms): mm(p2, l, rh, n == 0, False, r, pn, 128)
         mm(p2, T.idb[:], T.uf[:], False, False, "idb uf", pn, 128)
         mm(p2, T.i8k[:], T.ones[:], False, True, "i8k ones", pn, 128)
-        scan(T.wsc[:, i], T.hold[:, 0:128], p1, mul, ALU.max, "hold " + pn, "wsc:%d" % i, 128)
+        scan(T.wsc[:, i], T.hold[:, 0:128], p1, ad, ALU.max, "hold " + pn, "wsc:%d" % i, 128)
         act(T.rep[:, i], p0, AF.Identity, pn, "rep:%d" % i, 128, bias=off)
         wv = T.wsc[:, i, 15::16]
         if not e: ts(T.vw[:, 8 * i:8 * i + 8], wv, off - 8192.0, ad, "wsc:%d" % i, "vw:%d" % i, 8)
         for c in range(8):
             n, a = 16 * c + 16, 8 * c * (c + 1)
             act(T.dab[:, e, a:a + n], T[pn][:, 256:256 + n], AF.Abs, pn + " wsc:%d" % i, "dab:%d_%d" % (e, c), n, scale=-1.0, bias=T.wsc[:, i, 16 * c + 15:16 * c + 16])
-        scan(T.low[:, e], T.rs2[:], T.dab[:, e], ad, ALU.min, "rs2 " + " ".join("dab:%d_%d" % (e, c) for c in range(8)), "low:%d" % e, 576)
+        scan(T.low[:, e], T.rs2[:], T.dab[:, e], ad, ALU.min, "rs2 " + " ".join("dab:%d_%d" % (e, c) for c in range(8)), "low:%d" % e, 288)
         tt(T.fst[:, e], T.low[:, e].indirect(T.enl[:, 0:1]), T.uwf[:], ALU.not_equal, "low:%d enl uwf" % e, "fst:%d" % e, 16, True)
         dm, dn = T.dm[:, e], "dm:%d" % e
         tt(dm, T.fst[:, e, 0:8], T.Dz[:, 8 * e:8 * e + 8], mul, "Dz fst:%d" % e, dn, 16)
@@ -221,10 +240,14 @@ def build(g, core, T, topo):
             if base + c in UDVE[t]: cp(o, w, "X:b " + on, "%s:%d" % (Gn, c), 512, True)
             else: act(o, w, AF.Copy, "X:b " + on, "%s:%d" % (Gn, c), 512, True)
         for c in range(4):
-            pn = "pC%d" % (c & 1 if t == 1 else base // 4)
+            pn = ("pC0", "pC1", "pE", "pM1")[c] if t == 1 else "pC%d" % (1 - c % 2)
             mm(T[pn][:], T.idb[:], T[Gn][:, 512 * c:512 * c + 512], True, False, "idb %s:%d" % (Gn, c), pn, 512)
-            mm(T[pn][:], neg, T.Ec[:, 512 * c:512 * c + 512], False, True, "Ec " + negT, pn, 512)
-            act(T[an][:, 512 * c:512 * c + 512], T[pn][:], AF.Abs, pn, "%s:%d" % (an, c), 512)
+            if neg is None:
+                for l in range(16): mm(T[pn][:, l::16], T.nidb[:], T.xn[:, 32 * c:32 * c + 32], False, l == 15, "nidb xn", pn, 32)
+            else: mm(T[pn][:], neg, T.Ec[:, 512 * c:512 * c + 512], False, True, "Ec " + negT, pn, 512)
+            o = T[an][:, 512 * c:512 * c + 512]
+            if base + c in ADVE[t]: ts(o, T[pn][:], 0.0, ALU.max, pn, "%s:%d" % (an, c), 512, 2.0, mul)
+            else: act(o, T[pn][:], AF.Abs, pn, "%s:%d" % (an, c), 512)
 
     def users_a(t):
         o = t - 1
@@ -237,8 +260,11 @@ def build(g, core, T, topo):
         mm(T.pD1[:, 128:256], T.nf[:], T.idb[:], True, False, "nf idb", "pD1", 128)
         mm(T.pD1[:, 128:256], T.idb[:], T.ncn[:], False, True, "idb ncn", "pD1", 128)
         mm(T.pD1[:, 0:128], T.idb[:], T.kc[:], True, False, "idb kc", "pD1", 128)
+        for c in range(4):
+            for k in range(16 * (c in ADVE[t])):
+                mm(T.pD1[32 * c:32 * c + 32, k:128:16], T.G1[:, 512 * c + k:512 * c + 512:16], T.B8[:, 8:16], False, False, "B8 G1:%d" % c, "pD1", 64, 0.5)
         for k in range(16):
-            mm(T.pD1[:, k:128:16], T.ab1[:, k::16], T.B8[:], False, k == 15, "ab1 B8", "pD1", 64)
+            mm(T.pD1[:, k:128:16], T.ab1[:, k::16], T.B8[:, 0:8], False, k == 15, "ab1 B8", "pD1", 64)
         scan(T.m1[:], T.rst[:], T.pD1[:, 0:128], ad, ALU.min, "rst pD1", "m1", 128)
         tt(T.e1[:], T.pD1[:, 0:128], T.m1[:], sub, "pD1 m1", "e1", 128)
         scan(T.s2[:], T.e1[:], T.pD1[:, 128:256], ALU.min, ALU.max, "e1 pD1", "s2", 128)
@@ -247,33 +273,43 @@ def build(g, core, T, topo):
         add("V", lambda: V.tensor_scalar(T.vb[:], T.v8[:].indirect(T.bcl[:]), -2048.0, None, ad), "v8 bcl", "vb", gcst(128))
         finish([(T.vb[:], T.idb[:], "vb idb")], "pD1", t)
         act(T.xn[:], X1.indirect(T.vw[:, 8 * t:8 * t + 8]), AF.Copy, "X:b vw:%d" % t, "xn", 128, True)
-        pn = "pC0"
-        mm(T[pn][:, 128:256], T.xn[:], T.nidb[:], True, True, "xn nidb", pn, 128)
+        pn = "pC0" if t > 1 else "pU"
+        if t > OPT["nx"]: mm(T[pn][:, 128:256], T.xn[:], T.nidb[:], True, True, "xn nidb", pn, 128)
         mm(T[pn][:, 256:384], T.idb[:], T.xn[:], True, False, "xn idb", pn, 128)
         mm(T[pn][:, 256:384], T.nidb[:], yo, False, True, "Y:%d nidb" % o, pn, 128)
         mm(T[pn][:, 384:512], T.hidb[:], T.xn[:], True, False, "xn hidb", pn, 128)
         mm(T[pn][:, 384:512], T.hidb[:], yo, False, False, "Y:%d hidb" % o, pn, 128)
         mm(T[pn][:, 384:512], T.nidb[:], T.q25[:, 0:128], False, True, "q25 nidb", pn, 128)
-        act(T.nxT[:], T[pn][:, 128:256], AF.Copy, pn, "nxT", 128)
+        if t > OPT["nx"]: act(T.nxT[:], T[pn][:, 128:256], AF.Copy, pn, "nxT", 128)
         act(T.Y[:, t], T[pn][:, 256:384], AF.Abs, pn, "Y:%d" % t, 128)
         whole(T.xw[:], T[pn][:, 384:512], T.e1[:], pn, "xw", "e1", 128, OPT["mw"])
 
     def users_far(t):
         o = t - 1
         Ao, an, rn = T.A1[:, o], " A1:%d" % o, " rep:%d" % t
-        far(t, 4, 128 * o, "Aoff:%d" % o, "G2", "ab2", T.nxT[:], "nxT")
+        far(t, 4, 128 * o, "Aoff:%d" % o, "G2", "ab2", T.nxT[:] if t > OPT["nx"] else None, "nxT")
         mm(T.pD2[:, 128:256], T.vb[:], T.idb[:], True, False, "idb vb", "pD2", 128)
         mm(T.pD2[:, 128:256], T.nidb[:], Ao, False, True, "nidb" + an, "pD2", 128)
         mm(T.pD2[:, 384:512], T.idb[:], Ao, True, True, "idb" + an, "pD2", 128)
-        for l in range(16):
-            mm(T.pD2[:, 0:128], T.Wb[:, 15 - l:143 - l], T.ab2[:, l::16], l == 0, l == 15, "Wb ab2", "pD2", 128)
+        some = [c for c in range(4) if c + 4 in ADVE[t]]
+        hs = 2 if t <= OPT["hs"] else 1
+        if some or hs > 1: mm(T.pD2[:, 0:128], T.zb[:], T.ones[:], True, False, "zb ones", "pD2", 128)
+        for c in some:
+            for l in range(16):
+                mm(T.pD2[:, 32 * c:32 * c + 32], T.nWb[:, 15 - l:143 - l], T.G2[:, 512 * c + l:512 * c + 512:16], False, False, "nWb G2:%d" % c, "pD2", 32)
+            mm(T.pD2[:, 32 * c:32 * c + 32], T.BB[:], T.xn[:, 32 * c:32 * c + 32], False, False, "BB xn", "pD2", 32)
+        for h in range(hs):
+            n = 128 // hs
+            for l in range(16):
+                mm(T.pD2[:, n * h:n * h + n], T.Wb[:, 15 - l:143 - l], T.ab2[:, 16 * n * h + l:16 * n * (h + 1):16], l == 0 and not some and hs == 1,
+                   l == 15 and h == hs - 1, "Wb " + ("ab2" if hs == 1 else "ab2:%d ab2:%d" % (2 * h, 2 * h + 1)), "pD2", n)
         mm(T.pM0[:, 0:256], T.zb[:], T.thc[:, 0:256], True, False, "zb thc", "pM0", 256)
         for b in range(2):
             mm(T.pM0[:, 128 * b:128 * b + 128], T.Pv[:, b], T.rep[:, t], False, False, "Pv:%d" % b + rn, "pM0", 128, 4)
 
     def users_b(t):
         o = t - 1
-        ts(T.mb[:], T.pD2[:, 0:128], col(8) if t == 1 else T.thr[:, 0:1], ALU.is_gt, "pD2 pf:8 thr", "mb", 128)
+        ts(T.mb[:], T.pD2[:, 0:128], col(8 if t == 1 else 20), ALU.is_gt, "pD2 pf:8 pf:20", "mb", 128)
         tt(T.fl[:], T.mb[:], T.pD2[:, 128:256], mul, "mb pD2", "fl", 128)
         tt(T.A1[:, t], T.fl[:], T.pD2[:, 384:512], ad, "fl pD2", "A1:%d" % t, 128)
         for b in range(2):
@@ -299,10 +335,10 @@ def build(g, core, T, topo):
             cp(T.go[:, 8 * o:8 * t], T.vw[:, 8 * t:8 * t + 8], "vw:%d" % t, "go:0", 8)
         for h in range(1 if t == 1 else 0, 2):
             m = n - 128 * (h == 0)
-            tt(T.wtm[:, 0:m], T.TR[:].indirect(off), T.diag[:, 0:m], mul, "TR diag " + on, "wtm", m, True)
-            scan(T.g1[:, 0:m], T.hold[:, 0:m], T.wtm[:, 0:m], mul, ad, "hold wtm", "g1", m)
+            tt(T.wtm[:, 0:m], T.TR[:].indirect(off), T.diag[:, 0:m], sub, "TR diag " + on, "wtm", m, True)
+            scan(T.g1[:, 0:m], T.hold[:, 0:m], T.wtm[:, 0:m], ad, ALU.max, "hold wtm", "g1", m // 2)
             off, on = T.go[:, 24 * h:24 * h + 8 * t], "go:%d" % h
-            cp(T.go[:, 24 * h:24 * h + m // 16], T.g1[:, 15:m:16], "g1", on, 8 * t)
+            ts(T.go[:, 24 * h:24 * h + m // 16], T.g1[:, 15:m:16], 2048.0, ad, "g1", on, 8 * t)
         act(T.g3[:, 0:n], T.TR[:].indirect(off), AF.Copy, "TR " + on, "g3", n, True)
         for i in range(t):
             sct(T.TR3[:].indirect(T.vd[:, 8 * i:8 * i + 8]), T.g3[:, 128 * i:128 * i + 128], "g3 vd:%d" % i, "TR3", 128)
@@ -311,6 +347,17 @@ def build(g, core, T, topo):
             dma(T.ya[:], T.fl[:], "fl", "", 64)
             dma(T.yy[:], T.Y[:, t], "Y:%d" % t, "", 32)
             dma(T.yv[:], T.rep[0:128:16, t], "rep:%d" % t, "", 4)
+
+    def make_u(k, b):
+        for s0 in range(16):
+            mm(T.pU[:, 0:32], T.MU[:, 15 - s0:143 - s0], T[b][:, k, s0:512:16], s0 == 0, s0 == 15, "MU %s:z%d" % (b, k), "pU", 32)
+        cp(T.ki[:], T.pU[:, 0:32], "pU", "ki", 32)
+        ts(T.pi[:], T.ki[:], 4095, AND, "ki", "pi", 32)
+        ts(T.sndu[:, k, 0:32], T.pi[:], -2048.0 if OPT["bc"] else 32.0, ad, "pi", "sndu:a%d" % k, 32)
+        ts(T.um[:], T.ki[:], 127, AND, "ki", "um", 32)
+        ts(T.sndu[:, k, 32:64], T.um[:], 32.0, ad, "um", "sndu:b%d" % k, 32, 0.25 if OPT["bc"] else 2048.0, mul)
+        tt(T.sndu[:, k, 64:96], T.um[:], T[b][:, k, 512:544], sub, "um %s:j%d" % (b, k), "sndu:c%d" % k, 64)
+        if OPT["us"]: send(k, 1, "u")
 
     def seek_head(t):
         k = t - 1
@@ -324,24 +371,34 @@ def build(g, core, T, topo):
         cp(T.js[:], j, J, "js", 32)
         act(T.t2[:], T.K2[:].indirect(T.jw[:]), AF.Copy, "K2 jw", "t2", 512, True)
         tr(T.KT[:], T.t2[:], "t2", "KT", 512)
-        for s0 in range(16):
-            mm(T.pU[:, 0:32], T.MU[:, 15 - s0:143 - s0], T.land[:, k, s0:512:16], s0 == 0, s0 == 15, "MU " + L, "pU", 32)
-        cp(T.ki[:], T.pU[:, 0:32], "pU", "ki", 32)
-        ts(T.pi[:], T.ki[:], 4095, AND, "ki", "pi", 32)
-        ts(T.uw[:, 0:32], T.pi[:], 32.0, ad, "pi", "uw:0", 32)
-        ts(T.um[:], T.ki[:], 127, AND, "ki", "um", 32)
-        ts(T.uw[:, 32:64], T.um[:], 32.0, ad, "um", "uw:1", 32, 2048.0, mul)
+        if not OPT["us"]: make_u(k, "land")
+        ub = "landu" if OPT["us"] else "sndu"
+        u0, u1 = (T[ub][:, k, a:a + 32] for a in (0, 32))
+        n0, n1 = ("landu:u%d" % k,) * 2 if OPT["us"] else ("sndu:a%d" % k, "sndu:b%d" % k)
+        if OPT["bc"]:
+            mm(T.pE[:, 0:480], T.i83[:], T.q25[:, 0:480], True, False, "i83 q25", "pE", 480)
+            for n in range(15): mm(T.pE[:, 32 * n:32 * n + 32], T.idb[:], u0, False, n == 14, "idb " + n0, "pE", 32)
+            for n in range(15): mm(T.pU[:, 32 * n:32 * n + 32], T.i8k[:], u1, True, True, "i8k " + n1, "pU", 32)
         for c in range(len(CUT) - 1):
             a, b = CUT[c], CUT[c + 1]
             s, n, m = slice(32 * a, 32 * b), 32 * (b - a), ":%d" % c
             tt(T.hT[:, s], T.KT[:].indirect(T.prm[:, 2 * a:2 * b]), T.offc[:, s], sub, "KT prm offc", "hT" + m, n, True)
-            tt(T.pr[:, s], T.uw[:, 0:32].indirect(T.rl[:, 2 * a:2 * b]), T.hT[:, s], mul, "uw:0 rl hT" + m, "pr" + m, n, True)
-            tt(T.pt[:, s], T.uw[:, 32:64].indirect(T.rl[:, 2 * a:2 * b]), T.pr[:, s], ad, "uw:1 rl pr" + m, "pt" + m, n, True)
+            if OPT["bc"]:
+                tt(T.pr[:, s], T.hT[:, s], T.pE[:, s], mul, "pE hT" + m, "pr" + m, n)
+                tt(T.pt[:, s], T.pr[:, s], T.pU[:, s], ad, "pU pr" + m, "pt" + m, n)
+            else:
+                tt(T.pr[:, s], u0.indirect(T.rl[:, 2 * a:2 * b]), T.hT[:, s], mul, n0 + " rl hT" + m, "pr" + m, n, True)
+                tt(T.pt[:, s], u1.indirect(T.rl[:, 2 * a:2 * b]), T.pr[:, s], ad, n1 + " rl pr" + m, "pt" + m, n, True)
             ts(T.hi[:, s], T.pt[:, s], 5, ALU.arith_shift_right, "pt" + m, "hi" + m, n, 4095, AND)
             cp(T.hoff[:, s], T.hi[:, s], "hi" + m, "hoff" + m, n)
-        tt(T.dj[:], T.um[:], j, sub, "um " + J, "dj", 64)
-        cp(T.vj[:], T.KT[:, 0::16], "KT", "vj", 32)
-        ts(T.vj[:], T.vj[:], 12, SHR, "vj", "vj", 32)
+        ts(T.vc[:], T.KT[:, 0::16], -2.0 ** 23, ad, "KT", "vc", 32)
+        ts(T.vc[:], T.vc[:], 12, ALU.arith_shift_right, "vc", "vc", 32)
+        tt(T.scn[:, 0:32], T.scn[:, 96:128], T.vc[:], sub, "scn:3 vc", "scn:0", 64)
+        if OPT["mq"] == 2:
+            tt(T.xvj[:], T.xv[:].indirect(T.js[:]), z, sub, "xv js " + L, "xvj", 512, True)
+            ts(T.wtm[:], T.xvj[:], -0.5, mul, "xvj", "wtm", 256, 1536.25, ad)
+            ts(T.X[:, FND:XW], T.wtm[:], -1536.0, ad, "wtm", "X:q", 256)
+            return
         act(T.xvj[:], T.xv[:].indirect(T.js[:]), AF.Copy, "xv js", "xvj", 512, True)
         mm(T.pM1[:], T.hidb[:], z, True, False, "hidb " + L, "pM1", 512)
         mm(T.pM1[:], T.nhidb[:], T.xvj[:], False, False, "nhidb xvj", "pM1", 512)
@@ -354,7 +411,7 @@ def build(g, core, T, topo):
         z, j = T.land[:, k, 0:512], T.land[:, k, 512:544]
         mm(T.pE[:], T.t85[:], T.thc[:], True, False, "t85 thc", "pE", 512)
         mm(T.pE[:], T.n26[:], T.q25[:], False, False, "n26 q25", "pE", 512)
-        ng, n = 0, 0
+        ng, n, nq = 0, 0, 0
         left = [0]
         def acc(o, l, rh, r, n):
             left[0] += 1
@@ -389,23 +446,25 @@ def build(g, core, T, topo):
         cp(T.ki[:], T.hT[:, 15::16], "hT", "ki", 32)
         ts(T.pi[:], T.ki[:], 4095, AND, "ki", "pi", 32)
         cp(T.pw[:], T.pi[:], "pi", "pw", 32)
-        tt(T.t2[:], T.TR3[:].indirect(T.pw[:]), T.diag[:], mul, "TR3 diag pw", "t2", 512, True)
-        scan(T.hT[:], T.hold[:], T.t2[:], mul, ad, "hold t2", "hT", 512)
-        tt(T.ff[:], T.vj[:], T.hT[:, 15::16], eq, "vj hT", "ff", 64)
+        tt(T.wtm[:], T.TR3[:].indirect(T.pw[:]), T.diag[:], sub, "TR3 diag pw", "wtm", 512, True)
+        scan(T.g1[:], T.hold[:], T.wtm[:], ad, ALU.max, "hold wtm", "g1", 256)
+        tt(T.ff[:], T.vc[:], T.g1[:, 15::16], eq, "vc g1", "ff", 64)
         tt(T.scn[:, 32:64], T.ff[:], T.scn[:, 0:32], mul, "ff scn:0", "scn:1", 64)
-        tt(T.scn[:, 64:96], T.scn[:, 32:64], T.hT[:, 15::16], ALU.max, "scn:1 hT", "scn:2", 64)
-        cp(T.pw[:], T.scn[:, 64:96], "scn:2", "pw", 32)
+        tt(T.scn[:, 64:96], T.scn[:, 32:64], T.g1[:, 15::16], ad, "scn:1 g1", "scn:2", 64)
+        ts(T.pw[:], T.scn[:, 64:96], 2048.0, ad, "scn:2", "pw", 32)
         tt(T.xvj[:], X2.indirect(T.pw[:]), z, sub, "X:b X:d X:q pw " + L, "xvj", 512, True)
         act(T.snd[:, t, 0:512], T.xvj[:], AF.Abs, "xvj", "snd:z%d" % t, 512)
-        tt(T.tj[:], T.ff[:], T.dj[:], mul, "ff dj", "tj", 64)
+        if OPT["us"]: tt(T.tj[:], T.ff[:], T.landu[:, k, 64:96], mul, "ff landu:u%d" % k, "tj", 64)
+        else: tt(T.tj[:], T.ff[:], T.sndu[:, k, 64:96], mul, "ff sndu:c%d" % k, "tj", 64)
         if t < RO:
             tt(T.snd[:, t, 512:544], T.tj[:], j, ad, "tj " + J, "snd:j%d" % t, 64)
             send(t, 1, "j"); send(t, 1, "z")
             mm(T.pU[:, 0:32], T.ones[:], T.ff[:], True, True, "ones ff", "pU", 32)
-            red(T.thr[:, 1:2], T.pU[:, 0:32], ad, "pU", "thr:1", 32)
-            cp(T.Fi[:, 0:1], T.thr[:, 1:2], "thr:1", "Fi:0", 1)
-            ts(T.Fi[:, 1:2], T.Fi[:, 0:1], 15, AND, "Fi:0", "Fi:1", 1)
-            ts(T.thr[:, 0:1], T.Fi[:, 1:2], 16 * BIG, mul, "Fi:1 pf:8", "thr:0", 1, col(8), ad)
+            red(col(21), T.pU[:, 0:32], ad, "pU", "pf:21", 32)
+            cp(T.pci[:, 5:6], col(21), "pf:21", "pci:5", 1)
+            ts(T.pci[:, 6:7], T.pci[:, 5:6], 15, AND, "pci:5", "pci:6", 1)
+            ts(col(20), T.pci[:, 6:7], 16 * BIG, mul, "pci:6 pf:8", "pf:20", 1, col(8), ad)
+            if OPT["us"]: make_u(t, "snd")
         else:
             tt(T.jb[:], T.tj[:], j, ad, "tj " + J, "jb", 64)
             tr(T.snd[:, t, 512:544], T.jb[:], "jb", "snd:j%d" % t, 32)
@@ -418,6 +477,7 @@ def build(g, core, T, topo):
         for i in range(n0, len(ops)): part[i] = name + str(t)
     run(users_a, 1, "a")
     run(users_far, 1, "f")
+    if OPT["us"]: make_u(0, "snd")
     for t in range(1, RO + 1):
         run(users_b, t, "b")
         run(seek_head, t, "h")
@@ -426,9 +486,9 @@ def build(g, core, T, topo):
             run(users_far, t + 1, "f")
         run(seek_rest, t, "r")
     dma(T.yz[:], T.land[:, RO, 0:512], "land:z%d" % RO, "", 128)
-    cp(T.jo[:], T.land[:, RO, 512:544], "land:j%d" % RO, "jo", 32)
-    dma(T.yj[0::2, :], T.jo[:, 0:16], "jo", "", 8, "A")
-    dma(T.yj[1::2, :], T.jo[:, 16:32], "jo", "", 8, "A")
+    cp(T.dj[:], T.land[:, RO, 512:544], "land:j%d" % RO, "dj", 32)
+    dma(T.yj[0::2, :], T.dj[:, 0:16], "dj", "", 8, "A")
+    dma(T.yj[1::2, :], T.dj[:, 16:32], "dj", "", 8, "A")
     return ops
 
 
@@ -472,10 +532,14 @@ def plan(ops, deps):
     cum, last = 0.0, {}
     edges = [dict() for _ in range(n)]
     for i, (q, fn, r, w, c, kind) in enumerate(ops):
-        if kind == "c": hold[i] = lat[i] = c * OPT["f"]
+        if kind == "c":
+            hold[i] = lat[i] = c * OPT["f"]
+            if q == "G":
+                if q in last: edges[i][last[q]] = hold[last[q]]
+                last[q] = i
         elif kind == "d":
-            hold[i] = 60.0
-            if r: lat[i] = 2000.0 + c * DK
+            hold[i] = 1000.0 if q == "G" else 60.0
+            if r: lat[i] = 2000.0 + c * DK + 500.0 * (q == "G")
             else:
                 cum += c * DK
                 lat[i] = 2000.0 + cum
@@ -536,6 +600,82 @@ def plan(ops, deps):
     return topo_order({i: (st[i], i) for i in range(n)}, False), st, [st[i] + lat[i] for i in range(n)]
 
 
+CASES = [(1.3, 3.0, .87, 3.0, 3500, 2500, 280, 140), (1.56, 3.8, 1.0, 4.0, 4500, 3000, 200, 100),
+         (1.8, 5.0, 1.15, 3.5, 4000, 3000, 300, 150), (1.2, 2.5, .8, 2.5, 3000, 2500, 300, 140)]
+
+
+def polish(ops, deps, order, steps):
+    n = len(ops)
+    qs = [o[0] for o in ops]
+    succ = [set() for _ in range(n)]
+    for i in range(n):
+        for j in deps[i]: succ[j].add(i)
+    cases = []
+    for gc, sc, f, dk, rz, rj, hop, slf in CASES:
+        dur, hold = [0.0] * n, [0.0] * n
+        for i, (q, fn, r, w, c, kind) in enumerate(ops):
+            if kind == "c":
+                by = CACHE["index"].get(i)
+                if by: c = 60 + (c - 60) * (gc / GC if by == "g" else sc / SC)
+                dur[i] = hold[i] = c * f
+            elif kind == "d": hold[i], dur[i] = 1000.0 if q == "G" else 60.0, -c * dk
+            else: hold[i], dur[i] = 500.0, rz if int(kind[1:]) < 4 else rj
+        cases.append((dur, hold, [[(j, slf if qs[j] == qs[i] else hop) for j, wt in deps[i].items() if wt] for i in range(n)]))
+
+    def replay(case, seq):
+        dur, hold, pre = case
+        done, why, byq = [0.0] * n, [-1] * n, [False] * n
+        free, last, dma = {}, {}, 0.0
+        for i in seq:
+            q = qs[i]
+            t, w, b = free.get(q, 0.0), last.get(q, -1), True
+            for j, e in pre[i]:
+                if e + done[j] > t: t, w, b = e + done[j], j, False
+            why[i], byq[i], free[q], last[q] = w, b, t + hold[i], i
+            if dur[i] < 0: done[i] = dma = max(dma, t + 1970.0 + hold[i] / 2) - dur[i]
+            else: done[i] = t + dur[i]
+        i = done.index(max(done))
+        span, pairs = done[i], []
+        while i >= 0:
+            if byq[i] and why[i] >= 0 and qs[i] in "VAP" and why[i] not in deps[i]: pairs.append((i, why[i]))
+            i = why[i]
+        return span, pairs
+
+    base = [replay(c, order)[0] for c in cases]
+    def worth(seq):
+        r = [replay(c, seq) for c in cases]
+        return sum(x[0] / b for x, b in zip(r, base)), [p for x in r for p in x[1]]
+    best, pairs = worth(order)
+    x = [OPT["seed"]]
+    def draw(m):
+        x[0] = (x[0] * 1103515245 + 12345) % 2147483648
+        return (x[0] >> 8) % m
+    for _ in range(steps):
+        i, j = pairs[draw(len(pairs))]
+        a, b, k = order.index(j), order.index(i), (0, 0, 1, 2, 4)[draw(5)]
+        if draw(2):
+            while k and a > 0:
+                a -= 1
+                k -= qs[order[a]] == qs[i]
+            mv = [i]
+            for y in reversed(order[a:b]):
+                if not succ[y].isdisjoint(mv): mv.append(y)
+            if j in mv: continue
+            seq = order[:a] + mv[::-1] + [y for y in order[a:b] if y not in mv] + order[b + 1:]
+        else:
+            while k and b < n - 1:
+                b += 1
+                k -= qs[order[b]] == qs[i]
+            mv = [j]
+            for y in order[a + 1:b + 1]:
+                if any(z in deps[y] for z in mv): mv.append(y)
+            if i in mv: continue
+            seq = order[:a] + [y for y in order[a + 1:b + 1] if y not in mv] + mv + order[b + 1:]
+        s, p = worth(seq)
+        if s <= best + 0.0001: best, order, pairs = s, seq, p
+    return order
+
+
 CACHE = {}
 
 
@@ -545,8 +685,8 @@ def rank_program(g, core, T, topo):
     ops = build(g, core, T, topo)
     if "o" not in CACHE:
         deps = depend(ops)
-        CACHE["o"] = (deps,) + plan(ops, deps)
-    deps, order = CACHE["o"][0], CACHE["o"][1]
+        CACHE["o"] = (deps, polish(ops, deps, plan(ops, deps)[0], OPT["steps"]))
+    deps, order = CACHE["o"]
     at = {i: n for n, i in enumerate(order)}
     Q = {"V": g.vector, "A": g.scalar, "P": g.tensor, "G": g, "S": g.sync}
     token = {}

@@ -5,12 +5,12 @@ BIG, MAGIC = 2.0 ** 25, 12582912.0
 DUM, FND, XW = 4096, 4224, 4736
 TW = 4224
 PAIRS = [(1, 9), (2, 10), (3, 11), (4, 12), (5, 13), (6, 14), (7, 15), (8,)]
-WAYS = {1: 'AVVAMVAA', 2: 'AVVAMVAM', 3: 'VAVAAVAA'}
+WAYS = {1: 'AVVAMVAA', 2: 'VAMAMVAV', 3: 'AVAAVVAA'}
 CUT = (0, 8, 15)
-UDVE = {1: (1, 3, 4), 2: (2, 4, 5), 3: (3,)}
-ADVE = {1: (1, 3, 5), 2: (1,), 3: ()}
-BIAS = {'b3': -1000, 'r3': 1000, 'a1': -4000, 'b1': -1000, 'f2': 1000, 'h2': 1000, 'h1': -6000}
-OPT = {"seed": 1, "noise": 400.0, "passes": 6, "mw": 1, "mq": 1, "fix": 1, "f": 0.9, "nx": 3, "cut": 8, "bc": 0, "hs": 3, "steps": 7000, "us": 2}
+UDVE = {1: (1, 3, 4, 5, 6), 2: (2, 4, 5), 3: (3,)}
+ADVE = {1: (1, 3, 5), 2: (1,), 3: (7,)}
+BIAS = {'b3': -2000, 'r3': 1000, 'a1': -3000, 'f2': 1000, 'h1': -5000, 'b2': -1000, 'a2': -3000}
+OPT = {"seed": 1, "noise": 200.0, "passes": 6, "mw": 1, "mq": 1, "fix": 1, "f": 0.9, "nx": 3, "cut": 8, "bc": 0, "hs": 3, "steps": 16000, "us": 2, "slack": 0.0001, "xu": 0, "q1": 1, "q2": 1, "q3": 1}
 
 F32, BF, F16, I32, U16 = "float32", "bfloat16", "float16", "int32", "uint16"
 SCRATCH = {}
@@ -18,7 +18,7 @@ for _n, _c, _d in [
     ("X", XW, BF), ("NB", 4096, I32), ("TR", TW, F32), ("TR3", TW, F32),
     ("cf", 512, F32), ("c15", 512, F32), ("c4", 128, F32), ("Ks", 128, F32), ("io", [2, 32], F32),
     ("pci", 8, I32), ("pf", 32, F32), ("wi", 4, I32), ("wf", 8, F32),
-    ("idb", 128, BF), ("nidb", 128, BF), ("hidb", 128, BF), ("nhidb", 128, BF), ("t85", 128, BF), ("n26", 128, BF), ("zb", 128, BF),
+    ("idb", 128, BF), ("nidb", 128, BF), ("hidb", 128, BF), ("nhidb", 128, BF), ("t85", 128, BF), ("zb", 128, BF),
     ("idf", 128, F32), ("i8k", 128, BF), ("i83", 128, BF), ("sndu", [4, 96], F16 if OPT["bc"] else F32), ("landu", [4, 96], F16 if OPT["bc"] else F32), ("dg8", 128, BF),
     ("Wb", 144, BF), ("nWb", 144, BF), ("B8", 16, BF), ("BB", 128, BF), ("BO", 128, BF), ("nBO", 128, BF), ("Ex", 128, BF), ("diag", 512, BF), ("hold", 512, BF),
     ("rst", 128, F32), ("kc", 128, BF), ("ncn", 128, BF), ("thc", 512, BF), ("UT", 128, BF), ("Pm", [2, 128], BF), ("Pv", [2, 128], F32),
@@ -30,22 +30,23 @@ for _n, _c, _d in [
     ("dab", [2, 576], BF), ("low", [2, 576], BF), ("fst", [2, 16], F32), ("dm", [2, 8], F32),
     ("A1", [4, 128], F16), ("Aoff", 512, U16), ("Y", [4, 128], BF), ("noff", 128, U16), ("nf", 128, F16),
     ("G1", 2048, BF), ("ab1", 2048, BF), ("G2", 2048, BF), ("ab2", 2048, BF), ("nyT", 128, BF), ("nxT", 128, BF),
-    ("m1", 128, F32), ("e1", 128, F32), ("s2", 128, F32), ("v8", 8, I32), ("vb", 128, F16), ("xn", 128, BF), ("xw", 128, BF),
+    ("m1", 128, F32), ("e1", 128, F32), ("s2", 128, F32), ("v8", 8, I32), ("vb", 128, F16), ("xn", 128, BF), ("xw", [RO, 128], BF), ("XU", FND, BF),
     ("mb", 128, BF), ("oh", 128, F16), ("K2", 256, F32), ("fl", 128, F32),
     ("g1", 512, F16), ("go", 48, U16), ("g3", 384, F32), ("xv", 128, BF),
     ("land", [4, 544], BF), ("snd", [4, 544], BF), ("jw", 32, U16), ("js", 32, U16),
     ("t2", 512, F32), ("KT", 512, F32), ("hT", 512, F32), ("pr", 512, F32), ("pt", 512, I32), ("hi", 512, I32), ("hoff", 480, U16),
-    ("xvj", 512, BF), ("gsl", [2, 512], BF),
-    ("ki", 32, I32), ("pi", 32, I32), ("um", 32, I32), ("vc", 32, I32), ("pw", 32, U16), ("ff", 32, BF), ("dj", 32, F32), ("tj", 32, F32),
+    ("xvj", 512, BF), ("gsl", [4, 512], BF),
+    ("ki", 32, I32), ("pi", 32, I32), ("um", 32, I32), ("vc", 32, I32), ("pw", 32, U16), ("ff", 34, BF), ("o16", 128, BF), ("dj", 32, F32), ("tj", 32, F32),
     ("jb", 32, BF),
 ]:
     SCRATCH[_n] = ("sbuf", [128] + (list(_c) if isinstance(_c, list) else [_c]), _d)
+if not OPT["xu"]: SCRATCH.pop("XU")
 for _n in ("lv", "df"):
     SCRATCH[_n] = ("sbuf", [128, len(PAIRS), 512, 2], BF)
 for _n in ("pC0", "pC1", "pD1", "pD2", "pM0", "pE", "pU", "pM1"):
     SCRATCH[_n] = ("psum", [128, 512], F32)
 NDMA = 20
-SEMAPHORES = ["cV", "cA", "cP", "cG"] + ["d%d" % i for i in range(NDMA)] + ["ls%d" % i for i in range(12)] + ["rs%d" % i for i in range(12)]
+SEMAPHORES = ["cV", "cA", "cP", "cG"] + ["d%d" % i for i in range(NDMA)] + ["ls%d" % i for i in range(14)] + ["rs%d" % i for i in range(14)]
 
 OV = 30.0
 CY, PC, GC, SC = 1.04, 0.5, 1.56, 3.8
@@ -87,8 +88,8 @@ def build(g, core, T, topo):
         if part == "u": o, i, n = T.landu[:, k], T.sndu[:, k], 8 + k
         elif part == "w": o, i, n = T.landu[:, RO, 0:1], T.sndu[:, RO, 0:1], 8 + RO
         else:
-            a, b = {"zj": (0, 544), "z": (0, 512), "j": (512, 544)}[part]
-            o, i, n = T.land[:, k, a:b], T.snd[:, k, a:b], k + 4 * (part == "j")
+            a, b = {"zj": (0, 544), "z": (0, 512 if k < RO else 256), "j": (512, 544), "yj": (256, 544)}[part]
+            o, i, n = T.land[:, k, a:b], T.snd[:, k, a:b], 12 + (part == "z") if k == RO else k + 4 * (part == "j")
         x = "u" if part in "uw" else ""
         add("G", lambda: g.remote_dma(o, i, T.sem["rs%d" % n], T.sem["ls%d" % n], pid, rid, m),
             " ".join("snd%s:%s%d" % (x, y, k) for y in part.replace("u", "abc")), " ".join("land%s:%s%d" % (x, y, k) for y in part), len(en), "r%d" % n)
@@ -116,7 +117,7 @@ def build(g, core, T, topo):
     iota(T.offc[:], [[-4096, 8], [-32768, 2], [0, 32]], 2048 - 4096, 0, "offc", 512)
     ms(T.rs2[:], 0.0, "rs2", 288)
     for c in range(8): iota(T.rs2[:, 8 * c * (c + 1):8 * c * (c + 1) + 1], [[0, 1]], 1048576, 0, "rs2:%d" % c, 1)
-    iota(T.TR3[:], [[1, TW]], 0, 0, "TR3", TW)
+    for k in range(6): iota(T.TR3[:, 704 * k:704 * k + 704], [[1, 704]], 704 * k, 0, "TR3:%d" % k, 704)
     ts(T.pci[:, 1:2], T.pci[:, 0:1], 15, AND, "pci:0", "pci:1", 1)
     ts(T.pci[:, 2:3], T.pci[:, 0:1], 4, SHR, "pci:0", "pci:2", 1)
     ts(T.pci[:, 3:4], T.pci[:, 0:1], 4, SHR, "pci:0", "pci:3", 1, 1, AND)
@@ -131,6 +132,9 @@ def build(g, core, T, topo):
     pcol(6, cB, 256.0, 0.0)
     pcol(7, cB, -256.0, 256.0)
     pcol(8, cR, 102 * BIG, 102 * BIG)
+    pcol(26, cR, 102 * BIG, 222 * BIG)
+    ms(T.o16[:], 1.0 / 16, "o16", 64)
+    ms(T.ff[:, 32:34], -15.0 / 256, "ff:c", 2)
     pcol(9, cR, -4096.0, 2048.0)
     pcol(12, cB, -1.0, 1.0)
     pcol(13, cA, 16.0, cR)
@@ -138,6 +142,7 @@ def build(g, core, T, topo):
     pcol(16, cA, 32.0, cR); pcol(17, col(16), 1.0, 16.0, "pf:16")
     pcol(18, cR, 1.0, FND - 2048.0)
     pcol(19, cR, 16.0, 0.0)
+    ms(T.ones[:], 1.0, "ones", 64)
     cBm = (col(12), cB)
     c128 = T.cf[:, 0:128]
     ts(T.Ex[:], T.c4[:], cP, eq, "c4 pf:0", "Ex", 128)
@@ -146,7 +151,7 @@ def build(g, core, T, topo):
     act(T.dg8[:], T.t2[:, 0:128], AF.Copy, "t2", "dg8", 128, scale=8192.0)
     ts(T.hold[:], T.c15[:], 0.0, eq, "c15", "hold", 512, -1048576.0, mul)
     ts(T.idf[:], c128, cP, eq, "cf pf:0", "idf", 128)
-    for nm, s in (("idb", 1.0), ("nidb", -1.0), ("hidb", .5), ("nhidb", -.5), ("t85", -85 * BIG), ("n26", -2 * BIG), ("zb", 0.0), ("i8k", 8192.0), ("i83", 8320.0)):
+    for nm, s in (("idb", 1.0), ("nidb", -1.0), ("hidb", .5), ("nhidb", -.5), ("zb", 0.0), ("i8k", 8192.0), ("i83", 8320.0)):
         act(T[nm][:], T.idf[:], AF.Copy, "idf", nm, 128, scale=s)
     ts(T.Wb[:], T.cf[:, 0:144], col(5), eq, "cf pf:5", "Wb", 144, BIG, mul)
     act(T.nWb[:], T.Wb[:], AF.Copy, "Wb", "nWb", 144, scale=-1.0)
@@ -157,7 +162,9 @@ def build(g, core, T, topo):
     ts(T.rst[:], T.c15[:, 0:128], 0.0, eq, "c15", "rst", 128, 2.0 ** 40, mul)
     act(T.kc[:], T.c15[:, 0:128], AF.Copy, "c15", "kc", 128, scale=65536.0)
     act(T.ncn[:], T.c15[:, 0:128], AF.Identity, "c15", "ncn", 128, scale=-4096.0, bias=63488.0)
-    act(T.thc[:], T.c15[:], AF.Identity, "c15", "thc", 512, scale=-1.0, bias=16.0)
+    pcol(22, cP, 1.0, -1.0); pcol(23, cP, -15.0, 16.0); pcol(24, cP, 84.5 * BIG, -85 * BIG)
+    act(T.thc[:], T.c15[:], AF.Identity, "c15 pf:22 pf:23", "thc", 512, scale=col(22), bias=col(23))
+    act(T.t85[:], T.ones[:], AF.Copy, "ones pf:24", "t85", 128, scale=col(24))
     ts(T.mb[:], c128, cP, ALU.is_lt, "cf pf:0", "mb", 128, -1.0, mul)
     tt(T.mb[:], T.mb[:], T.BO[:], mul, "mb BO", "mb", 256)
     tt(T.UT[:], T.mb[:], T.idf[:], ad, "mb idf", "UT", 256)
@@ -188,7 +195,6 @@ def build(g, core, T, topo):
     ts(T.Dz[:, 8:16], T.Dz[:, 0:8], DUM + 4096.0, ad, "Dz", "Dz", 8)
     ts(T.Dz[:, 0:8], T.Dz[:, 0:8], DUM + 6144.0, ad, "Dz", "Dz", 8)
     ms(T.q25[:], 0.25, "q25", 256)
-    ms(T.ones[:], 1.0, "ones", 64)
     ms(T.X[:, DUM:XW], 0.0, "X:d X:q", 320)
     ts(T.Ec[:], T.G1[:], cP, eq, "G1 pf:0", "Ec", 1024)
     for k in range(9):
@@ -233,18 +239,27 @@ def build(g, core, T, topo):
     tr(T.snd[:, 0, 512:544], T.jb[:], "jb", "snd:j0", 32)
     send(0, 1)
 
+    def ahead(t): return (T.XU[:, 0:DUM], "XU ") if t == RO and OPT["xu"] else (X1, "X:b ")
+
+    def copy_x(t):
+        dma(T.XU[:], XD, "X:b X:d", "XU", 1056)
+    def step_x(t): sct(T.XU[:].indirect(T.vd[:, 8 * t:8 * t + 8]), T.xw[:, t - 1], "xw:%d vd:%d" % (t - 1, t), "XU", 128)
+
     def far(t, base, off, on, Gn, an, neg, negT):
         for c in range(4):
-            w = X1.indirect(off[:, 32 * c:32 * c + 32]) if on == "noff" else X1.indirect(T.Aoff[:, off + 32 * c:off + 32 * c + 32])
+            win, wn = ahead(t) if on == "noff" else (X1, "X:b ")
+            w = win.indirect(off[:, 32 * c:32 * c + 32]) if on == "noff" else X1.indirect(T.Aoff[:, off + 32 * c:off + 32 * c + 32])
             o = T[Gn][:, 512 * c:512 * c + 512]
-            if base + c in UDVE[t]: cp(o, w, "X:b " + on, "%s:%d" % (Gn, c), 512, True)
-            else: act(o, w, AF.Copy, "X:b " + on, "%s:%d" % (Gn, c), 512, True)
+            if base + c in UDVE[t]: cp(o, w, wn + on, "%s:%d" % (Gn, c), 512, True)
+            else: act(o, w, AF.Copy, wn + on, "%s:%d" % (Gn, c), 512, True)
         for c in range(4):
             pn = ("pC0", "pC1", "pE", "pM1")[c] if t == 1 else "pC%d" % (1 - c % 2)
-            mm(T[pn][:], T.idb[:], T[Gn][:, 512 * c:512 * c + 512], True, False, "idb %s:%d" % (Gn, c), pn, 512)
+            first = base == 0
+            if first: mm(T[pn][:], neg, T.Ec[:, 512 * c:512 * c + 512], True, False, "Ec " + negT, pn, 512)
+            mm(T[pn][:], T.idb[:], T[Gn][:, 512 * c:512 * c + 512], not first, first, "idb %s:%d" % (Gn, c), pn, 512)
             if neg is None:
                 for l in range(16): mm(T[pn][:, l::16], T.nidb[:], T.xn[:, 32 * c:32 * c + 32], False, l == 15, "nidb xn", pn, 32)
-            else: mm(T[pn][:], neg, T.Ec[:, 512 * c:512 * c + 512], False, True, "Ec " + negT, pn, 512)
+            elif not first: mm(T[pn][:], neg, T.Ec[:, 512 * c:512 * c + 512], False, True, "Ec " + negT, pn, 512)
             o = T[an][:, 512 * c:512 * c + 512]
             if base + c in ADVE[t]: ts(o, T[pn][:], 0.0, ALU.max, pn, "%s:%d" % (an, c), 512, 2.0, mul)
             else: act(o, T[pn][:], AF.Abs, pn, "%s:%d" % (an, c), 512)
@@ -263,8 +278,13 @@ def build(g, core, T, topo):
         for c in range(4):
             for k in range(16 * (c in ADVE[t])):
                 mm(T.pD1[32 * c:32 * c + 32, k:128:16], T.G1[:, 512 * c + k:512 * c + 512:16], T.B8[:, 8:16], False, False, "B8 G1:%d" % c, "pD1", 64, 0.5)
-        for k in range(16):
-            mm(T.pD1[:, k:128:16], T.ab1[:, k::16], T.B8[:, 0:8], False, k == 15, "ab1 B8", "pD1", 64)
+        if t > 1:
+            for k in range(16): mm(T.pD1[:, k:128:16], T.ab1[:, k::16], T.B8[:, 0:8], False, k == 15, "ab1 B8", "pD1", 64)
+        else:
+            for c in range(4):
+                for k in range(16):
+                    mm(T.pD1[32 * c:32 * c + 32, k:128:16], T.ab1[:, 512 * c + k:512 * c + 512:16], T.B8[:, 0:8], False, False, "B8 ab1:%d" % c, "pD1", 64, 0.5)
+            mm(T.pD1[:, 0:128], T.zb[:], T.ones[:], False, True, "zb ones", "pD1", 128)
         scan(T.m1[:], T.rst[:], T.pD1[:, 0:128], ad, ALU.min, "rst pD1", "m1", 128)
         tt(T.e1[:], T.pD1[:, 0:128], T.m1[:], sub, "pD1 m1", "e1", 128)
         scan(T.s2[:], T.e1[:], T.pD1[:, 128:256], ALU.min, ALU.max, "e1 pD1", "s2", 128)
@@ -272,7 +292,7 @@ def build(g, core, T, topo):
         ts(T.v8[:], T.v8[:], 4095, AND, "v8", "v8", 8)
         add("V", lambda: V.tensor_scalar(T.vb[:], T.v8[:].indirect(T.bcl[:]), -2048.0, None, ad), "v8 bcl", "vb", gcst(128))
         finish([(T.vb[:], T.idb[:], "vb idb")], "pD1", t)
-        act(T.xn[:], X1.indirect(T.vw[:, 8 * t:8 * t + 8]), AF.Copy, "X:b vw:%d" % t, "xn", 128, True)
+        act(T.xn[:], ahead(t)[0].indirect(T.vw[:, 8 * t:8 * t + 8]), AF.Copy, ahead(t)[1] + "vw:%d" % t, "xn", 128, True)
         pn = "pC0" if t > 1 else "pU"
         if t > OPT["nx"]: mm(T[pn][:, 128:256], T.xn[:], T.nidb[:], True, True, "xn nidb", pn, 128)
         mm(T[pn][:, 256:384], T.idb[:], T.xn[:], True, False, "xn idb", pn, 128)
@@ -282,7 +302,7 @@ def build(g, core, T, topo):
         mm(T[pn][:, 384:512], T.nidb[:], T.q25[:, 0:128], False, True, "q25 nidb", pn, 128)
         if t > OPT["nx"]: act(T.nxT[:], T[pn][:, 128:256], AF.Copy, pn, "nxT", 128)
         act(T.Y[:, t], T[pn][:, 256:384], AF.Abs, pn, "Y:%d" % t, 128)
-        whole(T.xw[:], T[pn][:, 384:512], T.e1[:], pn, "xw", "e1", 128, OPT["mw"])
+        whole(T.xw[:, o], T[pn][:, 384:512], T.e1[:], pn, "xw:%d" % o, "e1", 128, OPT["mw"])
 
     def users_far(t):
         o = t - 1
@@ -309,7 +329,8 @@ def build(g, core, T, topo):
 
     def users_b(t):
         o = t - 1
-        ts(T.mb[:], T.pD2[:, 0:128], col(8 if t == 1 else 20), ALU.is_gt, "pD2 pf:8 pf:20", "mb", 128)
+        if t == 1: ts(T.mb[:], T.pD2[:, 0:128], col(8), ALU.is_gt, "pD2 pf:8", "mb", 128)
+        else: ts(T.mb[:], T.pD2[:, 0:128], col(26), sub, "pD2 pf:26 pf:20", "mb", 128, col(20), ALU.is_gt)
         tt(T.fl[:], T.mb[:], T.pD2[:, 128:256], mul, "mb pD2", "fl", 128)
         tt(T.A1[:, t], T.fl[:], T.pD2[:, 384:512], ad, "fl pD2", "A1:%d" % t, 128)
         for b in range(2):
@@ -317,7 +338,8 @@ def build(g, core, T, topo):
         act(T.K2[:], T.pM0[:, 0:256], AF.Identity, "pM0 pf:9", "K2", 256, bias=col(9))
         if t < RO: ts(T.Aoff[:, 128 * t:128 * t + 128], T.A1[:, t], 2048.0, ad, "A1:%d" % t, "Aoff:%d" % t, 64)
         else: ts(T.fl[:], T.A1[:, t], 2048.0, ad, "A1:%d" % t, "fl", 128)
-        sct(XD.indirect(T.vd[:, 8 * t:8 * t + 8]), T.xw[:], "xw vd:%d" % t, "X:b X:d", 128)
+        sct(XD.indirect(T.vd[:, 8 * t:8 * t + 8]), T.xw[:, o], "xw:%d vd:%d" % (o, t), "X:b X:d", 128)
+        if t == RO - 2 and OPT["xu"]: copy_x(t)
         act(T.xv[:], X1.indirect(T.vw[:, 8 * t:8 * t + 8]), AF.Copy, "X:b vw:%d" % t, "xv", 128, True)
         if t > 1:
             i = 2 + t
@@ -400,17 +422,16 @@ def build(g, core, T, topo):
             ts(T.X[:, FND:XW], T.wtm[:], -1536.0, ad, "wtm", "X:q", 256)
             return
         act(T.xvj[:], T.xv[:].indirect(T.js[:]), AF.Copy, "xv js", "xvj", 512, True)
-        mm(T.pM1[:], T.hidb[:], z, True, False, "hidb " + L, "pM1", 512)
-        mm(T.pM1[:], T.nhidb[:], T.xvj[:], False, False, "nhidb xvj", "pM1", 512)
-        mm(T.pM1[:], T.idb[:], T.q25[:], False, True, "idb q25", "pM1", 512)
-        whole(T.X[:, FND:XW], T.pM1[:], T.t2[:], "pM1", "X:q", "t2", 512, OPT["mq"])
+        mm(T.pM0[:], T.idb[:], T.q25[:], True, False, "idb q25", "pM0", 512)
+        mm(T.pM0[:], T.nhidb[:], T.xvj[:], False, False, "nhidb xvj", "pM0", 512)
+        mm(T.pM0[:], T.hidb[:], z, False, True, "hidb " + L, "pM0", 512)
+        whole(T.X[:, FND:XW], T.pM0[:], T.t2[:], "pM0", "X:q", "t2", 512, OPT["q%d" % t])
 
     def seek_rest(t):
         k = t - 1
         L, J = "land:z%d" % k, "land:j%d" % k
         z, j = T.land[:, k, 0:512], T.land[:, k, 512:544]
-        mm(T.pE[:], T.t85[:], T.thc[:], True, False, "t85 thc", "pE", 512)
-        mm(T.pE[:], T.n26[:], T.q25[:], False, False, "n26 q25", "pE", 512)
+        mm(T.pE[:], T.t85[0:2, :], T.thc[0:2, :], True, False, "t85 thc", "pE", 512)
         ng, n, nq = 0, 0, 0
         left = [0]
         def acc(o, l, rh, r, n):
@@ -429,11 +450,11 @@ def build(g, core, T, topo):
                 n += 1
                 o, d, on, di = T.lv[:, si, :, i], T.df[:, si, :, i], "lv:%d_%d" % (si, i), "df:%d_%d" % (si, i)
                 if way == "A":
-                    s = ng & 1; ng += 1
-                    pn = ("pU", "pM1")[s]
+                    s, pn = ng % 4, ("pM1", "pU")[ng & 1]
+                    ng += 1
                     act(T.gsl[:, s], w, AF.Copy, hn, "gsl:%d" % s, 512, True)
-                    mm(T[pn][:], T.idb[:], T.gsl[:, s], True, False, "idb gsl:%d" % s, pn, 512)
-                    mm(T[pn][:], T.nidb[:], z, False, True, "nidb " + L, pn, 512)
+                    mm(T[pn][:], T.nidb[:], z, True, False, "nidb " + L, pn, 512)
+                    mm(T[pn][:], T.idb[:], T.gsl[:, s], False, True, "idb gsl:%d" % s, pn, 512)
                     act(o, T[pn][:], AF.Abs, pn, on, 512)
                 else:
                     tt(d, w, z, sub, hn + L, di, 512, True)
@@ -448,27 +469,28 @@ def build(g, core, T, topo):
         cp(T.pw[:], T.pi[:], "pi", "pw", 32)
         tt(T.wtm[:], T.TR3[:].indirect(T.pw[:]), T.diag[:], sub, "TR3 diag pw", "wtm", 512, True)
         scan(T.g1[:], T.hold[:], T.wtm[:], ad, ALU.max, "hold wtm", "g1", 256)
-        tt(T.ff[:], T.vc[:], T.g1[:, 15::16], eq, "vc g1", "ff", 64)
-        tt(T.scn[:, 32:64], T.ff[:], T.scn[:, 0:32], mul, "ff scn:0", "scn:1", 64)
+        ff = T.ff[:, 0:32]
+        tt(ff, T.vc[:], T.g1[:, 15::16], eq, "vc g1", "ff:f", 64)
+        tt(T.scn[:, 32:64], ff, T.scn[:, 0:32], mul, "ff:f scn:0", "scn:1", 64)
         tt(T.scn[:, 64:96], T.scn[:, 32:64], T.g1[:, 15::16], ad, "scn:1 g1", "scn:2", 64)
         ts(T.pw[:], T.scn[:, 64:96], 2048.0, ad, "scn:2", "pw", 32)
-        tt(T.xvj[:], X2.indirect(T.pw[:]), z, sub, "X:b X:d X:q pw " + L, "xvj", 512, True)
-        act(T.snd[:, t, 0:512], T.xvj[:], AF.Abs, "xvj", "snd:z%d" % t, 512)
-        if OPT["us"]: tt(T.tj[:], T.ff[:], T.landu[:, k, 64:96], mul, "ff landu:u%d" % k, "tj", 64)
-        else: tt(T.tj[:], T.ff[:], T.sndu[:, k, 64:96], mul, "ff sndu:c%d" % k, "tj", 64)
+        for a, b, x in ((0, 512, "z"),) if t < RO else ((256, 512, "y"), (0, 256, "z")):
+            tt(T.xvj[:, a:b], X2.indirect(T.pw[:, a // 16:b // 16]), T.land[:, k, a:b], sub, "X:b X:d X:q pw " + L, "xvj:" + x, b - a, True)
+            act(T.snd[:, t, a:b], T.xvj[:, a:b], AF.Abs, "xvj:" + x, "snd:%s%d" % (x, t), b - a)
+        if OPT["us"]: tt(T.tj[:], ff, T.landu[:, k, 64:96], mul, "ff:f landu:u%d" % k, "tj", 64)
+        else: tt(T.tj[:], ff, T.sndu[:, k, 64:96], mul, "ff:f sndu:c%d" % k, "tj", 64)
         if t < RO:
             tt(T.snd[:, t, 512:544], T.tj[:], j, ad, "tj " + J, "snd:j%d" % t, 64)
             send(t, 1, "j"); send(t, 1, "z")
-            mm(T.pU[:, 0:32], T.ones[:], T.ff[:], True, True, "ones ff", "pU", 32)
-            red(col(21), T.pU[:, 0:32], ad, "pU", "pf:21", 32)
-            cp(T.pci[:, 5:6], col(21), "pf:21", "pci:5", 1)
-            ts(T.pci[:, 6:7], T.pci[:, 5:6], 15, AND, "pci:5", "pci:6", 1)
-            ts(col(20), T.pci[:, 6:7], 16 * BIG, mul, "pci:6 pf:8", "pf:20", 1, col(8), ad)
+            mm(T.pU[:, 0:33], T.o16[:], T.ff[:, 0:33], True, True, "o16 ff", "pU", 33)
+            red(col(21), T.pU[:, 0:33], ad, "pU", "pf:21", 33)
+            ts(col(25), col(21), MAGIC, ad, "pf:21", "pf:25", 1, -MAGIC, ad)
+            ts(col(20), col(25), col(21), sub, "pf:25 pf:21", "pf:20", 1, -256 * BIG, mul)
             if OPT["us"]: make_u(t, "snd")
         else:
             tt(T.jb[:], T.tj[:], j, ad, "tj " + J, "jb", 64)
             tr(T.snd[:, t, 512:544], T.jb[:], "jb", "snd:j%d" % t, 32)
-            send(t, -RO)
+            send(t, -RO, "yj"); send(t, -RO, "z")
 
     part = CACHE.setdefault("part", {})
     def run(f, t, name):
@@ -482,10 +504,14 @@ def build(g, core, T, topo):
         run(users_b, t, "b")
         run(seek_head, t, "h")
         if t < RO:
-            run(users_a, t + 1, "a")
+            if t + 1 < RO or not OPT["xu"]: run(users_a, t + 1, "a")
             run(users_far, t + 1, "f")
+        if t == RO - 2 and OPT["xu"]:
+            run(step_x, t + 1, "a")
+            run(users_a, t + 2, "a")
         run(seek_rest, t, "r")
-    dma(T.yz[:], T.land[:, RO, 0:512], "land:z%d" % RO, "", 128)
+    dma(T.yz[:, 256:512], T.land[:, RO, 256:512], "land:y%d" % RO, "", 64)
+    dma(T.yz[:, 0:256], T.land[:, RO, 0:256], "land:z%d" % RO, "", 64)
     cp(T.dj[:], T.land[:, RO, 512:544], "land:j%d" % RO, "dj", 32)
     dma(T.yj[0::2, :], T.dj[:, 0:16], "dj", "", 8, "A")
     dma(T.yj[1::2, :], T.dj[:, 16:32], "dj", "", 8, "A")
@@ -523,7 +549,7 @@ def depend(ops):
     return deps
 
 
-HOP, SELF, DK, RZ, RJ = 280.0, 140.0, 3.0, 3500.0, 2500.0
+HOP, SELF, DK, RZ, RJ = 270.0, 130.0, 2.5, 4800.0, 2400.0
 
 
 def plan(ops, deps):
@@ -545,7 +571,7 @@ def plan(ops, deps):
                 lat[i] = 2000.0 + cum
                 if q in last: edges[i][last[q]] = 60.0
                 last[q] = i
-        else: hold[i], lat[i] = 500.0, (RZ if int(kind[1:]) < 4 else RJ)
+        else: hold[i], lat[i] = 500.0, RZ if int(kind[1:]) < 4 else RJ if int(kind[1:]) < 12 else (RZ + RJ) / 2
         for j, wt in deps[i].items():
             edges[i][j] = lat[j] + (SELF if ops[j][0] == q else HOP) if wt else hold[j]
     succ = [dict() for _ in range(n)]
@@ -600,8 +626,8 @@ def plan(ops, deps):
     return topo_order({i: (st[i], i) for i in range(n)}, False), st, [st[i] + lat[i] for i in range(n)]
 
 
-CASES = [(1.3, 3.0, .87, 3.0, 3500, 2500, 280, 140), (1.56, 3.8, 1.0, 4.0, 4500, 3000, 200, 100),
-         (1.8, 5.0, 1.15, 3.5, 4000, 3000, 300, 150), (1.2, 2.5, .8, 2.5, 3000, 2500, 300, 140)]
+CASES = [(1.35, 3.0, .84, 2.5, 4500, 2200, 270, 130, 500), (1.56, 3.8, 1.0, 4.0, 5500, 3000, 200, 100, 700),
+         (1.9, 5.0, 1.12, 3.0, 4500, 2500, 300, 150, 500), (1.2, 2.5, .82, 2.5, 5000, 2800, 290, 140, 800)]
 
 
 def polish(ops, deps, order, steps):
@@ -611,7 +637,7 @@ def polish(ops, deps, order, steps):
     for i in range(n):
         for j in deps[i]: succ[j].add(i)
     cases = []
-    for gc, sc, f, dk, rz, rj, hop, slf in CASES:
+    for gc, sc, f, dk, rz, rj, hop, slf, issue in CASES:
         dur, hold = [0.0] * n, [0.0] * n
         for i, (q, fn, r, w, c, kind) in enumerate(ops):
             if kind == "c":
@@ -619,33 +645,43 @@ def polish(ops, deps, order, steps):
                 if by: c = 60 + (c - 60) * (gc / GC if by == "g" else sc / SC)
                 dur[i] = hold[i] = c * f
             elif kind == "d": hold[i], dur[i] = 1000.0 if q == "G" else 60.0, -c * dk
-            else: hold[i], dur[i] = 500.0, rz if int(kind[1:]) < 4 else rj
+            else: hold[i], dur[i] = issue, rz if int(kind[1:]) < 4 else rj if int(kind[1:]) < 12 else (rz + rj) / 2
         cases.append((dur, hold, [[(j, slf if qs[j] == qs[i] else hop) for j, wt in deps[i].items() if wt] for i in range(n)]))
 
-    def replay(case, seq):
+    def replay(case, seq, a, old):
         dur, hold, pre = case
-        done, why, byq = [0.0] * n, [-1] * n, [False] * n
+        done, why, byq = (list(x) for x in old)
         free, last, dma = {}, {}, 0.0
-        for i in seq:
+        for i in seq[:a]:
+            last[qs[i]] = i
+            if dur[i] < 0: dma = done[i]
+        for q, i in last.items(): free[q] = byq[i] + hold[i]
+        for i in seq[a:]:
             q = qs[i]
-            t, w, b = free.get(q, 0.0), last.get(q, -1), True
+            t, w = free.get(q, 0.0), -2 - last.get(q, -1)
             for j, e in pre[i]:
-                if e + done[j] > t: t, w, b = e + done[j], j, False
-            why[i], byq[i], free[q], last[q] = w, b, t + hold[i], i
-            if dur[i] < 0: done[i] = dma = max(dma, t + 1970.0 + hold[i] / 2) - dur[i]
+                e += done[j]
+                if e > t: t, w = e, j
+            why[i], byq[i], free[q], last[q] = w, t, t + hold[i], i
+            if dur[i] < 0: done[i] = dma = max(dma, t + 2000.0) - dur[i]
             else: done[i] = t + dur[i]
-        i = done.index(max(done))
-        span, pairs = done[i], []
-        while i >= 0:
-            if byq[i] and why[i] >= 0 and qs[i] in "VAP" and why[i] not in deps[i]: pairs.append((i, why[i]))
-            i = why[i]
-        return span, pairs
+        return done, why, byq
 
-    base = [replay(c, order)[0] for c in cases]
-    def worth(seq):
-        r = [replay(c, seq) for c in cases]
-        return sum(x[0] / b for x, b in zip(r, base)), [p for x in r for p in x[1]]
-    best, pairs = worth(order)
+    def bound(r):
+        pairs = []
+        for done, why, byq in r:
+            i = done.index(max(done))
+            while i >= 0:
+                j = why[i]
+                if j < -1:
+                    j = -2 - j
+                    if qs[i] != "S" and j not in deps[i]: pairs.append((i, j))
+                i = j
+        return pairs
+
+    now = [replay(c, order, 0, ([0.0] * n,) * 3) for c in cases]
+    base = [max(r[0]) for r in now]
+    best, pairs = float(len(cases)), bound(now)
     x = [OPT["seed"]]
     def draw(m):
         x[0] = (x[0] * 1103515245 + 12345) % 2147483648
@@ -671,8 +707,9 @@ def polish(ops, deps, order, steps):
                 if any(z in deps[y] for z in mv): mv.append(y)
             if i in mv: continue
             seq = order[:a] + [y for y in order[a + 1:b + 1] if y not in mv] + mv + order[b + 1:]
-        s, p = worth(seq)
-        if s <= best + 0.0001: best, order, pairs = s, seq, p
+        r = [replay(c, seq, a, old) for c, old in zip(cases, now)]
+        s = sum(max(x[0]) / y for x, y in zip(r, base))
+        if s <= best + OPT["slack"]: best, order, now, pairs = s, seq, r, bound(r)
     return order
 
 

@@ -4,49 +4,48 @@ RO = 3
 BIG, MAGIC = 2.0 ** 25, 12582912.0
 DUM, FND, XW = 4096, 4224, 4736
 TW = 4224
-PAIRS = [(1, 9), (2, 10), (3, 11), (4, 12), (5, 13), (6, 14), (7, 15), (8,)]
-WAYS = {1: 'AVVAMVAA', 2: 'VAMAMVAV', 3: 'AVAAVVAA'}
-CUT = (0, 8, 15)
-UDVE = {1: (1, 3, 4, 5, 6), 2: (2, 4, 5), 3: (3,)}
-ADVE = {1: (1, 3, 5), 2: (1,), 3: (7,)}
-BIAS = {'b3': -2000, 'r3': 1000, 'a1': -3000, 'f2': 1000, 'h1': -5000, 'b2': -1000, 'a2': -3000}
-OPT = {"seed": 1, "noise": 200.0, "passes": 6, "mw": 1, "mq": 1, "fix": 1, "f": 0.9, "nx": 3, "cut": 8, "bc": 0, "hs": 3, "steps": 16000, "us": 2, "slack": 0.0001, "xu": 0, "q1": 1, "q2": 1, "q3": 1}
+WAYS = {1: 'VAVAVAVA', 2: 'VAVAVAVA', 3: 'VAVAAVAV'}
+AWAY = {1: 'AVAV', 2: 'AAAA', 3: 'AAAA'}
+FWAY = {1: 'AAAA', 2: 'AAAA', 3: 'AAAA'}
+SP = {1: 0, 2: 0, 3: 1}
+HP = {1: 0, 2: 0, 3: 0, 4: 1}
+BIAS = {}
+OPT = {"seed": 2, "noise": 400.0, "passes": 12, "cut": 0, "steps": 100000, "slack": 0.004, "xu": 0,
+       "nbf": 1, "pc": 1, "vb": 300, "hq": 1, "tq": 2, "mix": 7, "far": 80, "pw": 1, "up": 0, "al": 1, "xa": "", "wide": 160, "sweeps": 20}
 
 F32, BF, F16, I32, U16 = "float32", "bfloat16", "float16", "int32", "uint16"
+CB = "idb nidb hidb nhidb t85 i8k i83 i4k i2k i18 i254 m1x m7x m12x dg8 BO nBO Ex UT ones o16 uf tq lv2 kc n20 Pm0 Pm1 Pv0 Pv1 SJ0 SJ1 SJ2 SJ3".split()
 SCRATCH = {}
 for _n, _c, _d in [
-    ("X", XW, BF), ("NB", 4096, I32), ("TR", TW, F32), ("TR3", TW, F32),
-    ("cf", 512, F32), ("c15", 512, F32), ("c4", 128, F32), ("Ks", 128, F32), ("io", [2, 32], F32),
+    ("X", XW, BF), ("NB", 4096, I32), ("TR", TW, F32), ("TR3", TW, F32), ("cb", [len(CB), 128], BF),
+    ("cf", 512, F32), ("c15", 512, F32), ("c4", 128, F32), ("Ks", 128, F32), ("io", [2, 48], F32), ("q4", 144, F32),
     ("pci", 8, I32), ("pf", 32, F32), ("wi", 4, I32), ("wf", 8, F32),
-    ("idb", 128, BF), ("nidb", 128, BF), ("hidb", 128, BF), ("nhidb", 128, BF), ("t85", 128, BF), ("zb", 128, BF),
-    ("idf", 128, F32), ("i8k", 128, BF), ("i83", 128, BF), ("sndu", [4, 96], F16 if OPT["bc"] else F32), ("landu", [4, 96], F16 if OPT["bc"] else F32), ("dg8", 128, BF),
-    ("Wb", 144, BF), ("nWb", 144, BF), ("B8", 16, BF), ("BB", 128, BF), ("BO", 128, BF), ("nBO", 128, BF), ("Ex", 128, BF), ("diag", 512, BF), ("hold", 512, BF),
-    ("rst", 128, F32), ("kc", 128, BF), ("ncn", 128, BF), ("thc", 512, BF), ("UT", 128, BF), ("Pm", [2, 128], BF), ("Pv", [2, 128], F32),
-    ("MU", 144, F16), ("SJ", [4, 128], BF), ("cjb", 32, BF), ("scn", 128, F32), ("prm", 32, U16), ("rl", 32, U16), ("bcl", 8, U16),
-    ("offc", 512, F32), ("uf", 128, BF), ("uwf", 16, F32), ("Dz", 16, F32), ("q25", 512, BF), ("ones", 128, BF),
-    ("Ec", 2048, BF), ("rs2", 576, BF), ("enl", 2, U16),
+    ("idf", 128, F32), ("sndu", [4, 32], F16), ("landu", [4, 32], F16),
+    ("W", [3, 144], BF), ("B8", 16, BF), ("diag", 512, BF), ("hold", 512, BF),
+    ("rst", 128, F32), ("bcl", 8, U16), ("thc", 512, BF),
+    ("MU", [2, 144], F16), ("cjb", 32, BF), ("scn", 128, F32), ("prm", 48, U16), ("pr2", 8, U16),
+    ("offc", 768, F32), ("uwf", 16, F32), ("Dz", 16, F32), ("q25", 512, BF), ("nq", 512, BF), ("rs2", 576, BF), ("enl", 2, U16),
     ("vi", 128, I32), ("ai", 128, I32), ("ji", 32, I32),
-    ("rep", [6, 128], F32), ("wsc", [6, 128], F32), ("wtm", 512, F16), ("vw", 48, U16), ("vd", 48, U16),
+    ("rep", [6, 128], F32), ("wsc", [6, 128], F32), ("wtm", 512, F16), ("vw", 56, U16), ("vd", 48, U16),
     ("dab", [2, 576], BF), ("low", [2, 576], BF), ("fst", [2, 16], F32), ("dm", [2, 8], F32),
-    ("A1", [4, 128], F16), ("Aoff", 512, U16), ("Y", [4, 128], BF), ("noff", 128, U16), ("nf", 128, F16),
-    ("G1", 2048, BF), ("ab1", 2048, BF), ("G2", 2048, BF), ("ab2", 2048, BF), ("nyT", 128, BF), ("nxT", 128, BF),
-    ("m1", 128, F32), ("e1", 128, F32), ("s2", 128, F32), ("v8", 8, I32), ("vb", 128, F16), ("xn", 128, BF), ("xw", [RO, 128], BF), ("XU", FND, BF),
-    ("mb", 128, BF), ("oh", 128, F16), ("K2", 256, F32), ("fl", 128, F32),
-    ("g1", 512, F16), ("go", 48, U16), ("g3", 384, F32), ("xv", 128, BF),
-    ("land", [4, 544], BF), ("snd", [4, 544], BF), ("jw", 32, U16), ("js", 32, U16),
-    ("t2", 512, F32), ("KT", 512, F32), ("hT", 512, F32), ("pr", 512, F32), ("pt", 512, I32), ("hi", 512, I32), ("hoff", 480, U16),
-    ("xvj", 512, BF), ("gsl", [4, 512], BF),
-    ("ki", 32, I32), ("pi", 32, I32), ("um", 32, I32), ("vc", 32, I32), ("pw", 32, U16), ("ff", 34, BF), ("o16", 128, BF), ("dj", 32, F32), ("tj", 32, F32),
-    ("jb", 32, BF),
+    ("A1", [4, 128], F16), ("lst", [2 * RO, 128], U16), ("ltr", [2, 128], F32), ("Y", [4, 512], BF), ("nf", [1, 128], F16),
+    ("G1", [4, 512], BF), ("ab1", [4, 512], BF), ("G2", [4, 512], BF), ("ab2", [4, 512], BF),
+    ("m1", [2, 128], F32), ("e1", 128, F32), ("hit", 130, BF), ("sel", [RO, 128], F16), ("xn", [RO, 512], BF), ("xw", [RO, 128], BF), ("XU", FND, BF),
+    ("mb", 128, BF), ("top", 128, BF), ("oh", 128, F16), ("K2", 256, F32), ("fl", 128, F32),
+    ("g1", 512, F16), ("go", 24, U16), ("g3", 384, F32),
+    ("land", [4, 576], BF), ("snd", [4, 576], BF), ("landj", 32, F32), ("sndj", 32, F32), ("jw", 32, U16), ("js", 32, U16),
+    ("t2", 512, F32), ("KT", 512, F32), ("hT", 512, F32), ("pr", 512, F32), ("pt", 512, I32), ("hi", 512, I32), ("hoff", 512, U16),
+    ("sk", 512, F32), ("xvj", 512, BF), ("xf", 512, BF), ("gsl", [4, 512], BF), ("lv", [10, 256, 4], BF), ("df", [10, 256, 4], BF), ("dp", [6, 512, 2], BF),
+    ("ki", 32, I32), ("pi", 32, I32), ("ku", 32, I32), ("pu", 32, I32), ("um", 32, I32), ("vc", 32, I32), ("pw", 32, U16), ("ff", 48, BF),
+    ("jf", 32, F32), ("tj", 32, F32), ("jb", 32, BF),
 ]:
     SCRATCH[_n] = ("sbuf", [128] + (list(_c) if isinstance(_c, list) else [_c]), _d)
 if not OPT["xu"]: SCRATCH.pop("XU")
-for _n in ("lv", "df"):
-    SCRATCH[_n] = ("sbuf", [128, len(PAIRS), 512, 2], BF)
-for _n in ("pC0", "pC1", "pD1", "pD2", "pM0", "pE", "pU", "pM1"):
-    SCRATCH[_n] = ("psum", [128, 512], F32)
-NDMA = 20
-SEMAPHORES = ["cV", "cA", "cP", "cG"] + ["d%d" % i for i in range(NDMA)] + ["ls%d" % i for i in range(14)] + ["rs%d" % i for i in range(14)]
+BANKS, ROWS16 = ("pC0", "pC1", "pD1", "pD2", "pM0", "pE", "pU", "pM1"), ("pC0", "pC1", "pU", "pM1")
+for _n in BANKS:
+    SCRATCH[_n] = ("psum", [128, 32, 16] if _n in ROWS16 else [128, 512], F32)
+NDMA, NREM = 20, 28
+SEMAPHORES = ["cV", "cA", "cP", "cG"] + ["d%d" % i for i in range(NDMA)] + ["ls%d" % i for i in range(NREM)] + ["rs%d" % i for i in range(NREM)]
 
 OV = 30.0
 CY, PC, GC, SC = 1.04, 0.5, 1.56, 3.8
@@ -54,70 +53,100 @@ CY, PC, GC, SC = 1.04, 0.5, 1.56, 3.8
 
 def build(g, core, T, topo):
     ops = []
-    CUT = (0, OPT["cut"], 15) if OPT["cut"] else (0, 15)
     V, A, P = g.vector, g.scalar, g.tensor
     rank = T.rank_of(core)
     N = len(T.cores)
-    def add(q, fn, r, w, c, kind="c"): ops.append((q, fn, r.split(), w.split(), c, kind))
+    C = {n: T.cb[:, i] for i, n in enumerate(CB)}
+    def rows(n, k): return T.cb[0:k, CB.index(n)]
+    fixed = set(CB) | {"W", "B8", "MU", "thc", "q25", "nq", "cjb"}
+    index, alt, part, size, label = {}, {}, {}, {}, [None]
+    CACHE.update(index=index, alt=alt, part=part, size=size)
+    def add(q, fn, r, w, c, kind="c"):
+        if label[0]: part[len(ops)] = label[0]
+        ops.append((q, fn, r.split(), w.split(), c, kind))
     def vc(n): return OV + max(64, n) * CY
-    index = CACHE["index"] = {}
     def gcst(n, by="g"):
         index[len(ops)] = by
-        return 60 + n * (GC if by == "g" else SC) * CY
-    def cp(o, i, r, w, n, G=False): add("V", lambda: V.tensor_copy(o, i), r, w, gcst(n) if G else vc(n))
+        return 60 + n * (SC if by == "s" else GC) * CY
+    def cp(o, i, r, w, n): add("V", lambda: V.tensor_copy(o, i), r, w, vc(n))
     def sct(o, i, r, w, n): add("V", lambda: V.tensor_copy(o, i), r, w, gcst(n, "s"))
-    def tt(o, a, b, op, r, w, n, G=False): add("V", lambda: V.tensor_tensor(o, a, b, op), r, w, gcst(n) if G else vc(n))
-    def ts(o, a, s1, op0, r, w, n, s2=None, op1=None):
-        if op1 is None: add("V", lambda: V.tensor_scalar(o, a, s1, None, op0), r, w, vc(n))
+    def tt(o, a, b, op, r, w, n, G=False): add("V", lambda: V.tensor_tensor(o, a, b, op), r, w, gcst(n, "t") if G else vc(n))
+    def ts(o, a, s1, op0, r, w, n, s2=None, op1=None, G=False):
+        if op1 is None: add("V", lambda: V.tensor_scalar(o, a, s1, None, op0), r, w, gcst(n) if G else vc(n))
         else: add("V", lambda: V.tensor_scalar(o, a, s1, s2, op0, op1), r, w, vc(n))
     def scan(o, a, b, op0, op1, r, w, n): add("V", lambda: V.tensor_tensor_scan(o, a, b, 0.0, op0, op1), r, w, vc(n))
     def red(o, a, op, r, w, n): add("V", lambda: V.tensor_reduce(o, a, AxisListType.X, op), r, w, vc(n))
     def tr(o, a, r, w, n): add("V", lambda: V.transpose(o, a), r, w, vc(n))
-    def ms(o, c, w, n): add("V", lambda: V.memset(o, c), "", w, vc(n))
-    def act(o, i, f, r, w, n, G=False, **k): add("A", lambda: A.activation(o, i, f, **k), r, w, gcst(n) if G else vc(n))
-    def mm(o, l, rh, st, sp, r, w, n, f=1): add("P", lambda: P.matmul(o, l, rh, st, sp), r, w, max(64, n) * f * PC)
+    def act(o, i, f, r, w, n, G=False, half=False, scale=1.0, bias=0.0):
+        c = vc(n // (1 + half))
+        if f is AF.Relu: alt[len(ops)] = (lambda: V.tensor_scalar(o, i, 0.0, scale, ALU.max, ALU.mult), c)
+        elif f is AF.Copy and scale == 1.0: alt[len(ops)] = (lambda: V.tensor_copy(o, i), c)
+        elif f is not AF.Abs: alt[len(ops)] = (lambda: V.tensor_scalar(o, i, scale, bias, ALU.mult, ALU.add), c)
+        add("A", lambda: A.activation(o, i, f, bias=bias, scale=scale), r, w, gcst(n) if G else vc(n))
+    def ms(o, c, w, n):
+        alt[len(ops)] = (lambda: V.memset(o, c), vc(n // 2))
+        add("A", lambda: A.activation(o, T.cf[:, 0:n], AF.Identity, bias=c, scale=0.0), "cf", w, vc(n))
+    def mm(o, l, rh, st, sp, r, w, n):
+        f, c = (lambda: P.matmul(o, l, rh, st, sp)), max(64, n) * PC
+        if ops[-1][0] == "P" and ops[-1][3] == [w] and set(r.split()) - fixed <= set(ops[-1][2]):
+            _, f0, r0, w0, c0, _ = ops.pop()
+            def both():
+                f0()
+                return f()
+            ops.append(("P", both, r0 + [x for x in r.split() if x not in r0], w0, c0 + c, "c"))
+        else: add("P", f, r, w, c)
     def dma(o, i, r, w, kb, q="S"): add(q, lambda: (g.sync if q == "S" else g.scalar).dma_start(o, i), r, w, kb, "d")
     def iota(o, pat, base, cm, w, n):
         add("G", lambda: g.iota(o, pat, base, cm, allow_small_or_imprecise_dtypes=True), "", w, 130 + 2 * n * CY)
-    def send(k, hop, part="zj"):
+    def ps(b, a, e): return T[b][:, a // 16:e // 16] if b in ROWS16 else T[b][:, a:e]
+    def shift(k, s): return T.W[:, k, 15 - s:143 - s]
+    def nm(x, a, b): return " ".join("%s_%d" % (x, h) for h in range(a, b))
+    def send(k, hop, what, a=0, b=2):
         dst = T.cores[(rank + hop) % N]
         rid, pid, _ = topo.addr(dst)
         en = topo.engines(core, dst)
-        if OPT["us"] > 1 and 0 < k < RO: en = en[part != "z"::2]
-        m = sum(1 << e for e in en)
-        if part == "u": o, i, n = T.landu[:, k], T.sndu[:, k], 8 + k
-        elif part == "w": o, i, n = T.landu[:, RO, 0:1], T.sndu[:, RO, 0:1], 8 + RO
-        else:
-            a, b = {"zj": (0, 544), "z": (0, 512 if k < RO else 256), "j": (512, 544), "yj": (256, 544)}[part]
-            o, i, n = T.land[:, k, a:b], T.snd[:, k, a:b], 12 + (part == "z") if k == RO else k + 4 * (part == "j")
-        x = "u" if part in "uw" else ""
+        if 0 < k < RO: en = en[what != "z"::2]
+        m, n = sum(1 << e for e in en), len(size)
+        x, lo, hi = {"z": ("", 256 * a, 256 * b), "j": ("", 512 + 16 * a, 512 + 16 * b), "zj": ("", 0, 544), "u": ("u", 16 * a, 16 * b),
+                     "c": ("", 544 + 16 * a, 544 + 16 * b), "w": ("u", 0, 1), "f": ("j", 0, 32)}[what]
+        o, i = (T[y + x][:] if x == "j" else T[y + x][:, k, lo:hi] for y in ("land", "snd"))
+        size[len(ops)] = (hi - lo) / 128.0 / len(en)
         add("G", lambda: g.remote_dma(o, i, T.sem["rs%d" % n], T.sem["ls%d" % n], pid, rid, m),
-            " ".join("snd%s:%s%d" % (x, y, k) for y in part.replace("u", "abc")), " ".join("land%s:%s%d" % (x, y, k) for y in part), len(en), "r%d" % n)
+            *(" ".join(nm("%s%s:%s%d" % (y, x, z, k), a, b) for z in what) for y in ("snd", "land")), len(en), "r%d" % n)
     eq, mul, ad, sub, AND, SHR = ALU.is_equal, ALU.mult, ALU.add, ALU.subtract, ALU.bitwise_and, ALU.logical_shift_right
     X1, XD, X2 = T.X[:, 0:DUM], T.X[:, 0:FND], T.X[:]
 
     dma(T.vi[0:8, :], T.v0[:], "", "vi", 4)
-    dma(T.ai[:], T.a0[:], "", "ai", 64)
-    dma(T.Y[:, 0], T.y0[:], "", "Y:0", 32, "A")
+    if not OPT["al"]: dma(T.ai[:], T.a0[:], "", "ai", 64)
+    dma(T.Y[:, 0, 0:128], T.y0[:], "", "Y:0", 32, "A")
     dma(T.ji[:, 0:16], T.j0[0::2, :], "", "ji:0", 8, "A")
     dma(T.ji[:, 16:32], T.j0[1::2, :], "", "ji:1", 8, "A")
     dma(T.wi[:, 0:1], T.w[:], "", "wi:0", 4)
-    dma(X1, T.x[:], "", "X:b", 1024)
-    dma(T.NB[:], T.nb[:], "", "NB", 2048)
-    dma(T.snd[:, 0, 0:512], T.z0[:], "", "snd:z0", 128)
+    big = [(X1, T.x[:], "", "X:b", 1024), (T.NB[:], T.nb[:], "", "NB", 2048)]
+    for a in big[::-1] if OPT["nbf"] else big: dma(*a)
+    if OPT["al"]: dma(T.ai[:], T.a0[:], "", "ai", 64)
+    dma(T.snd[:, 0, 0:512], T.z0[:], "", nm("snd:z0", 0, 2), 128)
 
     add("G", lambda: g.iota(T.pci[:, 0:1], [[0, 1]], 0, 1), "", "pci:0", 132)
     iota(T.cf[:], [[1, 512]], 0, 0, "cf", 512)
     iota(T.c4[:], [[1, 8], [0, 16]], 0, 0, "c4", 128)
     iota(T.c15[:], [[0, 32], [1, 16]], 0, 0, "c15", 512)
-    iota(T.G1[:], [[1, 128], [0, 16]], 0, 0, "G1", 2048)
+    iota(T.e1[:], [[1, 16], [16, 2], [32, 4]], 0, 0, "e1", 128)
     iota(T.Ks[:], [[16, 4], [0, 2], [-1, 16]], 15, 0, "Ks", 128)
-    iota(T["io"][:, 0], [[1, 8], [8, 2], [256, 2]], 1, 0, "io:0", 32)
-    iota(T["io"][:, 1], [[0, 16], [16, 2]], 0, 0, "io:1", 32)
-    iota(T.offc[:], [[-4096, 8], [-32768, 2], [0, 32]], 2048 - 4096, 0, "offc", 512)
-    ms(T.rs2[:], 0.0, "rs2", 288)
-    for c in range(8): iota(T.rs2[:, 8 * c * (c + 1):8 * c * (c + 1) + 1], [[0, 1]], 1048576, 0, "rs2:%d" % c, 1)
-    for k in range(6): iota(T.TR3[:, 704 * k:704 * k + 704], [[1, 704]], 704 * k, 0, "TR3:%d" % k, 704)
+    iota(T.q4[:], [[1, 36], [0, 4]], 0, 0, "q4", 144)
+    iota(T["io"][:, 0, 0:32], [[1, 8], [8, 2], [256, 2]], 1, 0, "io:0", 32)
+    iota(T["io"][:, 0, 32:48], [[1, 4], [4, 4]], 1, 0, "io:0", 16)
+    iota(T["io"][:, 1, 0:32], [[0, 16], [16, 2]], 0, 0, "io:1", 32)
+    iota(T.pr[:], [[1, 8], [8, 2], [0, 32]], 1, 0, "pr", 512)
+    iota(T.sk[:, 0:256], [[1, 4], [4, 4], [0, 16]], 1, 0, "sk", 256)
+    for b in ("TR", "TR3"):
+        for k in range(6): iota(T[b][:, 704 * k:704 * k + 704], [[1, 704]], 704 * k, 0, "%s:%d" % (b, k), 704)
+    act(T.offc[:, 0:512], T.pr[:], AF.Identity, "pr", "offc:0", 512, scale=-1.0, bias=0.5)
+    act(T.offc[:, 512:768], T.sk[:, 0:256], AF.Identity, "sk", "offc:1", 256, scale=-1.0, bias=0.5)
+    ms(T.rs2[:, 0:288], 0.0, "rs2", 288); ms(T.rs2[:, 288:576], 0.0, "rs2", 288)
+    for c in range(8): ms(T.rs2[:, 8 * c * (c + 1):8 * c * (c + 1) + 1], 1048576.0, "rs2:%d" % c, 1)
+    for b in ("lv", "df"):
+        for k in (8, 9): ms(T[b][:, k, :, 0], 0.0, "%s:%d_0" % (b, k), 256)
     ts(T.pci[:, 1:2], T.pci[:, 0:1], 15, AND, "pci:0", "pci:1", 1)
     ts(T.pci[:, 2:3], T.pci[:, 0:1], 4, SHR, "pci:0", "pci:2", 1)
     ts(T.pci[:, 3:4], T.pci[:, 0:1], 4, SHR, "pci:0", "pci:3", 1, 1, AND)
@@ -125,105 +154,109 @@ def build(g, core, T, topo):
     cp(T.pf[:, 0:5], T.pci[:, 0:5], "pci", "pf:0", 5)
     def col(i): return T.pf[:, i:i + 1]
     cP, cR, cG, cB, cA = (col(i) for i in range(5))
-    def pcol(i, src, m, a, r="pf:0"):
-        if i in (5, 10): ts(col(i), src, m, mul, r, "pf:%d" % i, 1, a, ad)
-        else: act(col(i), src, AF.Identity, r, "pf:%d" % i, 1, scale=m, bias=a)
+    def pcol(i, src, m, a, r="pf:0"): act(col(i), src, AF.Identity, r, "pf:%d" % i, 1, scale=m, bias=a)
     pcol(5, cG, 16.0, 15.0)
-    pcol(6, cB, 256.0, 0.0)
-    pcol(7, cB, -256.0, 256.0)
-    pcol(8, cR, 102 * BIG, 102 * BIG)
-    pcol(26, cR, 102 * BIG, 222 * BIG)
-    ms(T.o16[:], 1.0 / 16, "o16", 64)
-    ms(T.ff[:, 32:34], -15.0 / 256, "ff:c", 2)
-    pcol(9, cR, -4096.0, 2048.0)
+    pcol(6, cB, 4096.0, 0.0)
+    pcol(7, cB, -4096.0, 4096.0)
+    ms(C["o16"], 2.0 ** 29, "o16", 128)
+    ms(T.ff[:, 32:48], 0.0, "ff:c", 16)
+    ms(T.ff[:, 32:33], -15.0 / 256, "ff:c", 1)
+    ts(col(8), cR, 0.0, eq, "pf:0", "pf:8", 1, 2048.0, mul)
+    pcol(26, cR, -1.0, 0.5)
+    pcol(9, col(26), 1.0, col(8), "pf:8 pf:26")
     pcol(12, cB, -1.0, 1.0)
     pcol(13, cA, 16.0, cR)
     pcol(14, cA, 16.0, 15.0)
+    pcol(15, cG, 4.0, 3.0)
     pcol(16, cA, 32.0, cR); pcol(17, col(16), 1.0, 16.0, "pf:16")
     pcol(18, cR, 1.0, FND - 2048.0)
     pcol(19, cR, 16.0, 0.0)
-    ms(T.ones[:], 1.0, "ones", 64)
+    ms(C["ones"], 1.0, "ones", 128)
     cBm = (col(12), cB)
     c128 = T.cf[:, 0:128]
-    ts(T.Ex[:], T.c4[:], cP, eq, "c4 pf:0", "Ex", 128)
+    ts(C["Ex"], T.c4[:], cP, eq, "c4 pf:0", "Ex", 128)
     ts(T.t2[:], T.c15[:], cR, eq, "c15 pf:0", "t2", 512)
     act(T.diag[:], T.t2[:], AF.Identity, "t2", "diag", 512, scale=-6144.0, bias=8192.0)
-    act(T.dg8[:], T.t2[:, 0:128], AF.Copy, "t2", "dg8", 128, scale=8192.0)
+    act(C["dg8"], T.t2[:, 0:128], AF.Copy, "t2", "dg8", 128, scale=8192.0)
     ts(T.hold[:], T.c15[:], 0.0, eq, "c15", "hold", 512, -1048576.0, mul)
     ts(T.idf[:], c128, cP, eq, "cf pf:0", "idf", 128)
-    for nm, s in (("idb", 1.0), ("nidb", -1.0), ("hidb", .5), ("nhidb", -.5), ("zb", 0.0), ("i8k", 8192.0), ("i83", 8320.0)):
-        act(T[nm][:], T.idf[:], AF.Copy, "idf", nm, 128, scale=s)
-    ts(T.Wb[:], T.cf[:, 0:144], col(5), eq, "cf pf:5", "Wb", 144, BIG, mul)
-    act(T.nWb[:], T.Wb[:], AF.Copy, "Wb", "nWb", 144, scale=-1.0)
-    ts(T.B8[:, 0:8], T.cf[:, 0:8], cG, eq, "cf pf:0", "B8:0", 8, 1048576.0, mul)
-    ts(T.B8[:, 8:16], T.cf[:, 0:8], cG, eq, "cf pf:0", "B8:1", 8, -1048576.0, mul)
-    ts(T.BO[:], T.c4[:], cG, eq, "c4 pf:0", "BO", 128)
-    act(T.BB[:], T.BO[:], AF.Copy, "BO", "BB", 128, scale=BIG)
-    ts(T.rst[:], T.c15[:, 0:128], 0.0, eq, "c15", "rst", 128, 2.0 ** 40, mul)
-    act(T.kc[:], T.c15[:, 0:128], AF.Copy, "c15", "kc", 128, scale=65536.0)
-    act(T.ncn[:], T.c15[:, 0:128], AF.Identity, "c15", "ncn", 128, scale=-4096.0, bias=63488.0)
+    for n, s in (("idb", 1.0), ("nidb", -1.0), ("hidb", .5), ("nhidb", -.5), ("i8k", 8192.0), ("i83", 8320.0 * 4096), ("i4k", 4096.0), ("i2k", 2048.0), ("i18", 2.0 ** 18),
+                 ("i254", 254.0), ("m1x", 4 * MAGIC), ("m7x", 512 * MAGIC), ("m12x", 16384 * MAGIC)):
+        act(C[n], T.idf[:], AF.Copy, "idf", n, 128, scale=s)
+    ts(T.W[:, 0], T.cf[:, 0:144], col(5), eq, "cf pf:5", "W:0", 144, BIG, mul)
+    act(T.W[:, 1], T.W[:, 0], AF.Copy, "W:0", "W:1", 144, half=True, scale=-1.0)
+    ts(T.W[:, 2], T.q4[:], col(15), eq, "q4 pf:15", "W:2", 144, BIG, mul)
+    for i, s in enumerate((16.0, -16.0)): ts(T.B8[:, 8 * i:8 * i + 8], T.cf[:, 0:8], cG, eq, "cf pf:0", "B8:%d" % i, 8, s, mul)
+    ts(C["BO"], T.c4[:], cG, eq, "c4 pf:0", "BO", 128)
+    act(T.rst[:], T.hold[:, 0:128], AF.Copy, "hold", "rst", 128, scale=-16.0)
+    act(C["kc"], T.c15[:, 0:128], AF.Copy, "c15", "kc", 128)
+    ms(C["n20"], -2.0 ** -20, "n20", 128)
+    ms(T.hit[:, 0:2], 1.0, "hit:1", 2)
+    ts(T.bcl[:], T.cf[:, 0:128:16], 15.0, ad, "cf", "bcl", 8)
     pcol(22, cP, 1.0, -1.0); pcol(23, cP, -15.0, 16.0); pcol(24, cP, 84.5 * BIG, -85 * BIG)
+    pcol(27, cP, -1.0, 1.0); pcol(28, cP, -18 * BIG, -102 * BIG)
     act(T.thc[:], T.c15[:], AF.Identity, "c15 pf:22 pf:23", "thc", 512, scale=col(22), bias=col(23))
-    act(T.t85[:], T.ones[:], AF.Copy, "ones pf:24", "t85", 128, scale=col(24))
+    act(C["t85"], C["ones"], AF.Identity, "ones pf:24", "t85", 128, scale=col(24))
+    act(C["lv2"], T.c15[:, 0:128], AF.Identity, "c15 pf:27", "lv2", 128, scale=col(27), bias=1.0)
+    act(C["tq"], C["ones"], AF.Identity, "ones pf:28", "tq", 128, scale=col(28))
     ts(T.mb[:], c128, cP, ALU.is_lt, "cf pf:0", "mb", 128, -1.0, mul)
-    tt(T.mb[:], T.mb[:], T.BO[:], mul, "mb BO", "mb", 256)
-    tt(T.UT[:], T.mb[:], T.idf[:], ad, "mb idf", "UT", 256)
-    act(T.nBO[:], T.BO[:], AF.Copy, "BO", "nBO", 128, scale=-2048.0)
+    tt(T.mb[:], T.mb[:], C["BO"], mul, "mb BO", "mb", 256)
+    tt(C["UT"], T.mb[:], T.idf[:], ad, "mb idf", "UT", 256)
+    act(C["nBO"], C["BO"], AF.Copy, "BO", "nBO", 128, half=True, scale=-2048.0)
     for b in range(2):
-        ts(T.Pm[:, b], T.Ks[:], col(13), eq, "Ks pf:13 pf:12 pf:0", "Pm:%d" % b, 128, cBm[b], mul)
-        ts(T.Pv[:, b], T.Ks[:], col(14), eq, "Ks pf:14 pf:6 pf:7", "Pv:%d" % b, 128, col(7 - b), mul)
+        ts(C["Pm%d" % b], T.Ks[:], col(13), eq, "Ks pf:13 pf:12 pf:0", "Pm%d" % b, 128, cBm[b], mul)
+        ts(C["Pv%d" % b], T.Ks[:], col(14), eq, "Ks pf:14 pf:6 pf:7", "Pv%d" % b, 128, col(7 - b), mul)
         for q in range(2):
-            ts(T.SJ[:, 2 * b + q], c128, col(16 + q), eq, "cf pf:16 pf:17 pf:12 pf:0", "SJ:%d" % (2 * b + q), 128, cBm[b], mul)
+            ts(C["SJ%d" % (2 * b + q)], c128, col(16 + q), eq, "cf pf:16 pf:17 pf:12 pf:0", "SJ%d" % (2 * b + q), 128, cBm[b], mul)
     ts(T.wf[:, 0:1], T.wi[:, 0:1], 2048.0, ALU.is_ge, "wi:0", "wf:0", 1, -4096.0, mul)
-    tt(T.wf[:, 1:2], T.wf[:, 0:1], T.wi[:, 0:1], ad, "wf:0 wi:0", "wf:1", 1)
-    if OPT["us"]:
-        cp(T.sndu[:, RO, 0:1], T.wf[:, 1:2], "wf:1", "sndu:w%d" % RO, 1)
-        send(RO, -1, "w")
-        cp(T.wf[:, 1:2], T.landu[:, RO, 0:1], "landu:w%d" % RO, "wf:1", 1)
-    ts(T.MU[:], T.cf[:, 0:144], col(5), eq, "cf pf:5 wf:1", "MU", 144, T.wf[:, 1:2], mul)
-    ts(T.scn[:, 96:128], T.cf[:, 0:32], 16.0, mul, "cf pf:18", "scn:3", 32, col(18), ad)
-    ts(T.prm[:], T["io"][:, 0], col(19), ad, "io:0 pf:19", "prm", 32)
-    ts(T.rl[:], T["io"][:, 1], cR, ad, "io:1 pf:0", "rl", 32)
-    act(T.cjb[:], T["io"][:, 1], AF.Copy, "io:1", "cjb", 32, scale=8.0)
-    cp(T.bcl[:], T.cf[:, 0:8], "cf", "bcl", 8)
-    act(T.uf[:], c128, AF.Identity, "cf", "uf", 128, scale=1.0 / 256)
+    tt(T.sndu[:, RO, 0:1], T.wf[:, 0:1], T.wi[:, 0:1], ad, "wf:0 wi:0", "sndu:w%d_0" % RO, 1)
+    send(RO, -1, "w", 0, 1)
+    cp(T.wf[:, 1:2], T.landu[:, RO, 0:1], "landu:w%d_0" % RO, "wf:1", 1)
+    ts(T.MU[:, 0], T.cf[:, 0:144], col(5), eq, "cf pf:5 wf:1", "MU:0", 144, T.wf[:, 1:2], mul)
+    ts(T.MU[:, 1], T.MU[:, 0], -1.0, mul, "MU:0", "MU:1", 72)
+    act(T.scn[:, 96:128], T.cf[:, 0:32], AF.Identity, "cf pf:18", "scn:3", 32, scale=16.0, bias=col(18))
+    ts(T.prm[:], T["io"][:, 0], col(19), ad, "io:0 pf:19", "prm", 48)
+    tt(T.wtm[:, 0:128], T.e1[:], T.diag[:, 0:128], sub, "e1 diag", "wtm", 256)
+    scan(T.g1[:, 0:128], T.hold[:, 0:128], T.wtm[:, 0:128], ad, ALU.max, "hold wtm", "g1", 64)
+    ts(T.pr2[:], T.g1[:, 15:128:16], 2048.0, ad, "g1", "pr2", 8)
+    act(T.cjb[:], T["io"][:, 1, 0:32], AF.Copy, "io:1", "cjb", 32, scale=8.0)
+    act(C["uf"], c128, AF.Identity, "cf", "uf", 128, scale=1.0 / 256)
     pcol(10, cR, 8.0, 24.0)
-    ts(col(11), col(10), cR, mul, "pf:10 pf:0", "pf:11", 1, 15.0, ad)
+    act(col(11), col(10), AF.Identity, "pf:10 pf:0", "pf:11", 1, scale=cR, bias=15.0)
     ts(T.enl[:, 0:1], col(11), 575.0, ALU.min, "pf:11", "enl", 1)
-    ts(T.Dz[:], T.cf[:, 0:16], 16.0, mul, "cf pf:0", "Dz", 16, cR, ad)
-    ts(T.uwf[:], T.Dz[:], 1.0 / 256, mul, "Dz", "uwf", 8)
-    ts(T.Dz[:, 8:16], T.Dz[:, 0:8], DUM + 4096.0, ad, "Dz", "Dz", 8)
-    ts(T.Dz[:, 0:8], T.Dz[:, 0:8], DUM + 6144.0, ad, "Dz", "Dz", 8)
-    ms(T.q25[:], 0.25, "q25", 256)
-    ms(T.X[:, DUM:XW], 0.0, "X:d X:q", 320)
-    ts(T.Ec[:], T.G1[:], cP, eq, "G1 pf:0", "Ec", 1024)
-    for k in range(9):
-        n = min(512, TW - 512 * k)
-        act(T.TR[:, 512 * k:512 * k + n], T.cf[:, 0:n], AF.Identity, "cf", "TR:%d" % k, n, bias=512.0 * k)
+    act(T.Dz[:], T.cf[:, 0:16], AF.Identity, "cf pf:0", "Dz", 16, scale=16.0, bias=cR)
+    act(T.uwf[:], T.Dz[:], AF.Identity, "Dz", "uwf", 16, scale=1.0 / 256)
+    act(T.Dz[:, 8:16], T.Dz[:, 0:8], AF.Identity, "Dz", "Dz", 8, bias=DUM + 4096.0)
+    act(T.Dz[:, 0:8], T.Dz[:, 0:8], AF.Identity, "Dz", "Dz", 8, bias=DUM + 6144.0)
+    ms(T.q25[:], 0.25, "q25", 512); ms(T.nq[:], -0.25, "nq", 512)
+    ms(T.X[:, DUM:FND], 0.0, "X:d", 128)
+    ms(T.X[:, FND:XW], 0.0, nm("X:q", 0, 2), 512)
+    idb, nidb = C["idb"], C["nidb"]
 
-    def whole(o, i, tmp, r, w, tn, n, scalar):
-        if scalar:
-            act(tmp, i, AF.Identity, r, tn, n, bias=MAGIC)
-            act(o, tmp, AF.Identity, tn, w, n, bias=-MAGIC)
-        else: ts(o, i, MAGIC, ad, r, w, n, -MAGIC, ad)
+    def whole(p, pn, n, x, stop):
+        mm(p, C[x], T.q25[:, 0:n], False, False, x + " q25", pn, n)
+        mm(p, C[x], T.nq[:, 0:n], False, stop, x + " nq", pn, n)
 
-    def finish(terms, pn, i):
+    VW = (0, 8, 24, 48)
+    def vw(t): return T.vw[:, VW[t]:VW[t] + 8]
+
+    def finish(terms, pn, pw, i):
         e = int(i > RO)
         off = 2048.0 * (1 + e)
-        p0, p1, p2 = (T[pn][:, a:a + 128] for a in (0, 128, 256))
-        for n, (l, rh, r) in enumerate(terms): mm(p1, l, rh, n == 0, False, r, pn, 128)
-        mm(p1, T.idb[:], T.dg8[:], False, True, "idb dg8", pn, 128)
+        p0, p1, p2 = ps(pn, 0, 128), ps(pw, 128, 256), ps(pn, 256, 384)
+        mm(p1, idb, C["dg8"], True, False, "idb dg8", pw, 128)
+        for n, (l, rh, r) in enumerate(terms): mm(p1, l, rh, False, n == len(terms) - 1, r, pw, 128)
         for n, (l, rh, r) in enumerate(terms): mm(p0, l, rh, n == 0, n == len(terms) - 1, r, pn, 128)
         for n, (l, rh, r) in enumerate(terms): mm(p2, l, rh, n == 0, False, r, pn, 128)
-        mm(p2, T.idb[:], T.uf[:], False, False, "idb uf", pn, 128)
-        mm(p2, T.i8k[:], T.ones[:], False, True, "i8k ones", pn, 128)
-        scan(T.wsc[:, i], T.hold[:, 0:128], p1, ad, ALU.max, "hold " + pn, "wsc:%d" % i, 128)
-        act(T.rep[:, i], p0, AF.Identity, pn, "rep:%d" % i, 128, bias=off)
+        mm(p2, idb, C["uf"], False, False, "idb uf", pn, 128)
+        mm(p2, C["i8k"], C["ones"], False, True, "i8k ones", pn, 128)
+        scan(T.wsc[:, i], T.hold[:, 0:128], p1, ad, ALU.max, "hold " + pw, "wsc:%d" % i, 128)
         wv = T.wsc[:, i, 15::16]
-        if not e: ts(T.vw[:, 8 * i:8 * i + 8], wv, off - 8192.0, ad, "wsc:%d" % i, "vw:%d" % i, 8)
+        if not e: ts(vw(i), wv, off - 8192.0, ad, "wsc:%d" % i, "vw:%d" % i, 8)
         for c in range(8):
             n, a = 16 * c + 16, 8 * c * (c + 1)
-            act(T.dab[:, e, a:a + n], T[pn][:, 256:256 + n], AF.Abs, pn + " wsc:%d" % i, "dab:%d_%d" % (e, c), n, scale=-1.0, bias=T.wsc[:, i, 16 * c + 15:16 * c + 16])
+            act(T.dab[:, e, a:a + n], ps(pn, 256, 256 + n), AF.Abs, pn + " wsc:%d" % i, "dab:%d_%d" % (e, c), n, scale=-1.0, bias=T.wsc[:, i, 16 * c + 15:16 * c + 16])
+        act(T.rep[:, i], p0, AF.Identity, pn, "rep:%d" % i, 128, bias=off)
         scan(T.low[:, e], T.rs2[:], T.dab[:, e], ad, ALU.min, "rs2 " + " ".join("dab:%d_%d" % (e, c) for c in range(8)), "low:%d" % e, 288)
         tt(T.fst[:, e], T.low[:, e].indirect(T.enl[:, 0:1]), T.uwf[:], ALU.not_equal, "low:%d enl uwf" % e, "fst:%d" % e, 16, True)
         dm, dn = T.dm[:, e], "dm:%d" % e
@@ -231,13 +264,25 @@ def build(g, core, T, topo):
         tt(dm, dm, wv, ALU.max, dn + " wsc:%d" % i, dn, 16)
         ts(T.vd[:, 8 * i:8 * i + 8], dm, off - 8192.0, ad, dn, "vd:%d" % i, 8)
 
+    def turn(buf, k, e, t, pn):
+        for b in range(2):
+            for q in range(2):
+                mm(T[pn][:, b:8:2, :], C["SJ%d" % (2 * b + q)], T[buf][:, k, 64 * q:64 * q + 64], q == 0, q == 1, "%s:%d SJ%d" % (buf, k, 2 * b + q), pn, 64)
+        tr(T.ltr[:, e], ps(pn, 0, 128), pn, "ltr:%d" % e, 128)
+        n = 2 * (t - 1) + e
+        ts(T.lst[:, n], T.ltr[:, e].indirect(T.pr2[:]), 2048.0, ad, "ltr:%d pr2" % e, "lst:%d" % n, 128, G=True)
+
+    def four(buf, k):
+        name = "%s:%d" % (buf, k)
+        act(T[buf][:, k, 128:256], T[buf][:, k, 0:128], AF.Copy, name, name + "x", 128, half=True)
+        act(T[buf][:, k, 256:512], T[buf][:, k, 0:256], AF.Copy, name + " " + name + "x", name + "x", 256, half=True)
+
     ts(T.oh[0:8, :], T.vi[0:8, :], -2048.0, ad, "vi", "oh", 128)
-    finish([(T.Ex[0:8, :], T.oh[0:8, :], "Ex oh")], "pD1", 0)
+    finish([(rows("Ex", 8), T.oh[0:8, :], "Ex oh")], "pD1", "pD2", 0)
     ts(T.A1[:, 0], T.ai[:], -2048.0, ad, "ai", "A1:0", 128)
-    cp(T.Aoff[:, 0:128], T.ai[:], "ai", "Aoff:0", 128)
     cp(T.jb[:], T.ji[:], "ji", "jb", 32)
-    tr(T.snd[:, 0, 512:544], T.jb[:], "jb", "snd:j0", 32)
-    send(0, 1)
+    tr(T.snd[:, 0, 512:544], T.jb[:], "jb", nm("snd:j0", 0, 2), 32)
+    send(0, 1, "zj")
 
     def ahead(t): return (T.XU[:, 0:DUM], "XU ") if t == RO and OPT["xu"] else (X1, "X:b ")
 
@@ -245,276 +290,327 @@ def build(g, core, T, topo):
         dma(T.XU[:], XD, "X:b X:d", "XU", 1056)
     def step_x(t): sct(T.XU[:].indirect(T.vd[:, 8 * t:8 * t + 8]), T.xw[:, t - 1], "xw:%d vd:%d" % (t - 1, t), "XU", 128)
 
-    def far(t, base, off, on, Gn, an, neg, negT):
-        for c in range(4):
-            win, wn = ahead(t) if on == "noff" else (X1, "X:b ")
-            w = win.indirect(off[:, 32 * c:32 * c + 32]) if on == "noff" else X1.indirect(T.Aoff[:, off + 32 * c:off + 32 * c + 32])
-            o = T[Gn][:, 512 * c:512 * c + 512]
-            if base + c in UDVE[t]: cp(o, w, wn + on, "%s:%d" % (Gn, c), 512, True)
-            else: act(o, w, AF.Copy, wn + on, "%s:%d" % (Gn, c), 512, True)
-        for c in range(4):
-            pn = ("pC0", "pC1", "pE", "pM1")[c] if t == 1 else "pC%d" % (1 - c % 2)
-            first = base == 0
-            if first: mm(T[pn][:], neg, T.Ec[:, 512 * c:512 * c + 512], True, False, "Ec " + negT, pn, 512)
-            mm(T[pn][:], T.idb[:], T[Gn][:, 512 * c:512 * c + 512], not first, first, "idb %s:%d" % (Gn, c), pn, 512)
-            if neg is None:
-                for l in range(16): mm(T[pn][:, l::16], T.nidb[:], T.xn[:, 32 * c:32 * c + 32], False, l == 15, "nidb xn", pn, 32)
-            elif not first: mm(T[pn][:], neg, T.Ec[:, 512 * c:512 * c + 512], False, True, "Ec " + negT, pn, 512)
-            o = T[an][:, 512 * c:512 * c + 512]
-            if base + c in ADVE[t]: ts(o, T[pn][:], 0.0, ALU.max, pn, "%s:%d" % (an, c), 512, 2.0, mul)
-            else: act(o, T[pn][:], AF.Abs, pn, "%s:%d" % (an, c), 512)
+    def gathers(t, e, ways, win, wn):
+        Gn, n = ("G1", "G2")[e], 2 * (t - 1) + e
+        for c, way in enumerate(ways):
+            if way in "AC": act(T[Gn][:, c], win.indirect(T.lst[:, n, 32 * c:32 * c + 32]), AF.Copy, wn + "lst:%d" % n, "%s:%d" % (Gn, c), 512, True)
+
+    def sizes(t, e, ways, win, wn, buf, k, banks):
+        ref, ref4, rn, n = T[buf][:, k, 0:128], T[buf][:, k], "%s:%d" % (buf, k), 2 * (t - 1) + e
+        Gn, an = ("G1", "G2")[e], ("ab1", "ab2")[e]
+        early, late = [], []
+        for c, way in enumerate(ways):
+            pn, o, on, a, am = banks[c % len(banks)], T[Gn][:, c], "%s:%d" % (Gn, c), T[an][:, c], "%s:%d" % (an, c)
+            if way in "AC":
+                if e == 0:
+                    for i in range(4): mm(ps(pn, 128 * i, 128 * i + 128), nidb, ref, i == 0, False, "nidb " + rn, pn, 128)
+                    mm(T[pn][:], idb, o, False, True, "idb " + on, pn, 512)
+                else:
+                    mm(T[pn][:], idb, o, True, False, "idb " + on, pn, 512)
+                    for i in range(4): mm(ps(pn, 128 * i, 128 * i + 128), nidb, ref, False, i == 3, "nidb " + rn, pn, 128)
+                if way == "A": act(a, T[pn][:], AF.Abs, pn, am, 512)
+                else: act(a, T[pn][:], AF.Relu, pn, am, 512, scale=2.0)
+            else:
+                tt(o, win.indirect(T.lst[:, n, 32 * c:32 * c + 32]), ref4, sub, wn + "lst:%d %s %sx" % (n, rn, rn), on, 512, True)
+                if way == "V": act(a, o, AF.Relu, on, am, 512, half=True, scale=2.0)
+                else: act(a, o, AF.Abs, on, am, 512)
+            if way in "CV": early += [(4 * c + i, 1, T[Gn][:, c, 128 * i:128 * i + 128], on) for i in range(4)]
+            late += [(4 * c + i, 0, T[an][:, c, 128 * i:128 * i + 128], am) for i in range(4)]
+        return early + late
 
     def users_a(t):
         o = t - 1
-        yo = T.Y[:, o]
-        mm(T.pD1[:, 256:384], yo, T.nidb[:], True, True, "Y:%d nidb" % o, "pD1", 128)
-        act(T.nyT[:], T.pD1[:, 256:384], AF.Copy, "pD1", "nyT", 128)
-        cp(T.noff[:], T.NB[:].indirect(T.vw[:, 8 * o:8 * o + 8]), "NB vw:%d" % o, "noff", 128, True)
-        ts(T.nf[:], T.noff[:], -2048.0, ad, "noff", "nf", 64)
-        far(t, 0, T.noff, "noff", "G1", "ab1", T.nyT[:], "nyT")
-        mm(T.pD1[:, 128:256], T.nf[:], T.idb[:], True, False, "nf idb", "pD1", 128)
-        mm(T.pD1[:, 128:256], T.idb[:], T.ncn[:], False, True, "idb ncn", "pD1", 128)
-        mm(T.pD1[:, 0:128], T.idb[:], T.kc[:], True, False, "idb kc", "pD1", 128)
-        for c in range(4):
-            for k in range(16 * (c in ADVE[t])):
-                mm(T.pD1[32 * c:32 * c + 32, k:128:16], T.G1[:, 512 * c + k:512 * c + 512:16], T.B8[:, 8:16], False, False, "B8 G1:%d" % c, "pD1", 64, 0.5)
-        if t > 1:
-            for k in range(16): mm(T.pD1[:, k:128:16], T.ab1[:, k::16], T.B8[:, 0:8], False, k == 15, "ab1 B8", "pD1", 64)
-        else:
-            for c in range(4):
-                for k in range(16):
-                    mm(T.pD1[32 * c:32 * c + 32, k:128:16], T.ab1[:, 512 * c + k:512 * c + 512:16], T.B8[:, 0:8], False, False, "B8 ab1:%d" % c, "pD1", 64, 0.5)
-            mm(T.pD1[:, 0:128], T.zb[:], T.ones[:], False, True, "zb ones", "pD1", 128)
-        scan(T.m1[:], T.rst[:], T.pD1[:, 0:128], ad, ALU.min, "rst pD1", "m1", 128)
-        tt(T.e1[:], T.pD1[:, 0:128], T.m1[:], sub, "pD1 m1", "e1", 128)
-        scan(T.s2[:], T.e1[:], T.pD1[:, 128:256], ALU.min, ALU.max, "e1 pD1", "s2", 128)
-        cp(T.v8[:], T.s2[:, 15::16], "s2", "v8", 8)
-        ts(T.v8[:], T.v8[:], 4095, AND, "v8", "v8", 8)
-        add("V", lambda: V.tensor_scalar(T.vb[:], T.v8[:].indirect(T.bcl[:]), -2048.0, None, ad), "v8 bcl", "vb", gcst(128))
-        finish([(T.vb[:], T.idb[:], "vb idb")], "pD1", t)
-        act(T.xn[:], ahead(t)[0].indirect(T.vw[:, 8 * t:8 * t + 8]), AF.Copy, ahead(t)[1] + "vw:%d" % t, "xn", 128, True)
+        yo, yn = T.Y[:, o, 0:128], "Y:%d" % o
+        win, wn = ahead(t)
+        if set(AWAY[t]) & set("VM"): four("Y", o)
+        ts(T.nf[:, 0], T.NB[:].indirect(vw(o)), -2048.0, ad, "NB vw:%d" % o, "nf:0", 128, G=True)
+        turn("nf", 0, 0, t, "pC0")
+        gathers(t, 0, AWAY[t], win, wn)
+        terms = sizes(t, 0, AWAY[t], win, wn, "Y", o, ("pC0", "pC1", "pE", "pM1") if t == 1 else ("pC1", "pC0"))
+        mm(ps("pD1", 0, 128), idb, C["kc"], True, False, "idb kc", "pD1", 128)
+        terms = [(k, 0, yo, yn) for k in range(16) if AWAY[t][k // 4] == "C"] + terms
+        for n, (k, s, tile, tn) in enumerate(terms):
+            mm(T.pD1[:, k:128:16], tile, T.B8[:, 8 * s:8 * s + 8], False, n == len(terms) - 1, "B8 " + tn, "pD1", 64)
+        for i in range(2): scan(T.m1[:, i], T.rst[:], ps("pD1", 0, 128), ad, ALU.min, "rst pD1", "m1:%d" % i, 128)
+        tt(T.hit[:, 2:130], T.m1[:, 0].indirect(T.bcl[:]), T.m1[:, 1], eq, "m1 bcl", "hit:0", 128, True)
+        mm(ps("pD1", 384, 512), T.hold[0:1, 0:128], rows("n20", 1), True, False, "hold n20", "pD1", 128)
+        mm(ps("pD1", 384, 512), T.hit[:, 2:130], idb, False, False, "hit idb", "pD1", 128)
+        mm(ps("pD1", 384, 512), T.hit[:, 1:129], nidb, False, True, "hit nidb", "pD1", 128)
+        tt(T.sel[:, o], ps("pD1", 384, 512), T.nf[:, 0], mul, "pD1 nf:0", "sel:%d" % o, 128)
+        finish([(C["BO"], T.sel[:, o], "BO sel:%d" % o)], "pD1", "pM0" if t <= OPT["pw"] else "pD1", t)
+        xn, xm = T.xn[:, o, 0:128], "xn:%d" % o
+        act(xn, win.indirect(vw(t)), AF.Copy, wn + "vw:%d" % t, xm, 128, True)
+        if set(FWAY[t]) & set("VM"): four("xn", o)
+
+    def users_y(t):
+        o = t - 1
+        yo, yn, xn, xm = T.Y[:, o, 0:128], "Y:%d" % o, T.xn[:, o, 0:128], "xn:%d" % o
         pn = "pC0" if t > 1 else "pU"
-        if t > OPT["nx"]: mm(T[pn][:, 128:256], T.xn[:], T.nidb[:], True, True, "xn nidb", pn, 128)
-        mm(T[pn][:, 256:384], T.idb[:], T.xn[:], True, False, "xn idb", pn, 128)
-        mm(T[pn][:, 256:384], T.nidb[:], yo, False, True, "Y:%d nidb" % o, pn, 128)
-        mm(T[pn][:, 384:512], T.hidb[:], T.xn[:], True, False, "xn hidb", pn, 128)
-        mm(T[pn][:, 384:512], T.hidb[:], yo, False, False, "Y:%d hidb" % o, pn, 128)
-        mm(T[pn][:, 384:512], T.nidb[:], T.q25[:, 0:128], False, True, "q25 nidb", pn, 128)
-        if t > OPT["nx"]: act(T.nxT[:], T[pn][:, 128:256], AF.Copy, pn, "nxT", 128)
-        act(T.Y[:, t], T[pn][:, 256:384], AF.Abs, pn, "Y:%d" % t, 128)
-        whole(T.xw[:, o], T[pn][:, 384:512], T.e1[:], pn, "xw:%d" % o, "e1", 128, OPT["mw"])
+        mm(ps(pn, 256, 384), idb, xn, True, False, xm + " idb", pn, 128)
+        mm(ps(pn, 256, 384), nidb, yo, False, True, yn + " nidb", pn, 128)
+        mm(ps(pn, 384, 512), C["hidb"], xn, True, False, xm + " hidb", pn, 128)
+        mm(ps(pn, 384, 512), C["hidb"], yo, False, False, yn + " hidb", pn, 128)
+        mm(ps(pn, 384, 512), nidb, T.q25[:, 0:128], False, False, "q25 nidb", pn, 128)
+        whole(ps(pn, 384, 512), pn, 128, "m1x", True)
+        act(T.xw[:, o], ps(pn, 384, 512), AF.Copy, pn, "xw:%d" % o, 128)
+        act(T.Y[:, t, 0:128], ps(pn, 256, 384), AF.Abs, pn, "Y:%d" % t, 128)
+
+    def users_g(t):
+        turn("A1", t - 1, 1, t, "pC1")
+        gathers(t, 1, FWAY[t], X1, "X:b ")
 
     def users_far(t):
         o = t - 1
-        Ao, an, rn = T.A1[:, o], " A1:%d" % o, " rep:%d" % t
-        far(t, 4, 128 * o, "Aoff:%d" % o, "G2", "ab2", T.nxT[:] if t > OPT["nx"] else None, "nxT")
-        mm(T.pD2[:, 128:256], T.vb[:], T.idb[:], True, False, "idb vb", "pD2", 128)
-        mm(T.pD2[:, 128:256], T.nidb[:], Ao, False, True, "nidb" + an, "pD2", 128)
-        mm(T.pD2[:, 384:512], T.idb[:], Ao, True, True, "idb" + an, "pD2", 128)
-        some = [c for c in range(4) if c + 4 in ADVE[t]]
-        hs = 2 if t <= OPT["hs"] else 1
-        if some or hs > 1: mm(T.pD2[:, 0:128], T.zb[:], T.ones[:], True, False, "zb ones", "pD2", 128)
-        for c in some:
-            for l in range(16):
-                mm(T.pD2[:, 32 * c:32 * c + 32], T.nWb[:, 15 - l:143 - l], T.G2[:, 512 * c + l:512 * c + 512:16], False, False, "nWb G2:%d" % c, "pD2", 32)
-            mm(T.pD2[:, 32 * c:32 * c + 32], T.BB[:], T.xn[:, 32 * c:32 * c + 32], False, False, "BB xn", "pD2", 32)
-        for h in range(hs):
-            n = 128 // hs
-            for l in range(16):
-                mm(T.pD2[:, n * h:n * h + n], T.Wb[:, 15 - l:143 - l], T.ab2[:, 16 * n * h + l:16 * n * (h + 1):16], l == 0 and not some and hs == 1,
-                   l == 15 and h == hs - 1, "Wb " + ("ab2" if hs == 1 else "ab2:%d ab2:%d" % (2 * h, 2 * h + 1)), "pD2", n)
-        mm(T.pM0[:, 0:256], T.zb[:], T.thc[:, 0:256], True, False, "zb thc", "pM0", 256)
-        for b in range(2):
-            mm(T.pM0[:, 128 * b:128 * b + 128], T.Pv[:, b], T.rep[:, t], False, False, "Pv:%d" % b + rn, "pM0", 128, 4)
+        Ao, an, sn = T.A1[:, o], " A1:%d" % o, " sel:%d" % o
+        terms = sizes(t, 1, FWAY[t], X1, "X:b ", "xn", o, ("pC0", "pC1", "pE", "pM1") if t == 1 else ("pC1", "pC0"))
+        mm(ps("pD2", 128, 256), C["BO"], T.sel[:, o], True, False, "BO" + sn, "pD2", 128)
+        mm(ps("pD2", 128, 256), nidb, Ao, False, True, "nidb" + an, "pD2", 128)
+        mm(ps("pD2", 384, 512), idb, Ao, True, True, "idb" + an, "pD2", 128)
+        mm(ps("pD2", 0, 128), rows("lv2", 2), rows("tq", 2), True, False, "lv2 tq", "pD2", 128)
+        for c in range(4):
+            if FWAY[t][c] == "C": mm(ps("pD2", 0, 128), T.W[:, 2, 12 - 4 * c:140 - 4 * c], T.xn[:, o, 0:128], False, False, "W xn:%d" % o, "pD2", 128)
+        for n, (l, s, tile, tn) in enumerate(terms): mm(ps("pD2", 0, 128), shift(s, l), tile, False, n == len(terms) - 1, "W " + tn, "pD2", 128)
 
     def users_b(t):
         o = t - 1
-        if t == 1: ts(T.mb[:], T.pD2[:, 0:128], col(8), ALU.is_gt, "pD2 pf:8", "mb", 128)
-        else: ts(T.mb[:], T.pD2[:, 0:128], col(26), sub, "pD2 pf:26 pf:20", "mb", 128, col(20), ALU.is_gt)
-        tt(T.fl[:], T.mb[:], T.pD2[:, 128:256], mul, "mb pD2", "fl", 128)
-        tt(T.A1[:, t], T.fl[:], T.pD2[:, 384:512], ad, "fl pD2", "A1:%d" % t, 128)
         for b in range(2):
-            mm(T.pM0[:, 128 * b:128 * b + 128], T.Pm[:, b], T.A1[:, t], False, b == 1, "Pm:%d A1:%d" % (b, t), "pM0", 128)
-        act(T.K2[:], T.pM0[:, 0:256], AF.Identity, "pM0 pf:9", "K2", 256, bias=col(9))
-        if t < RO: ts(T.Aoff[:, 128 * t:128 * t + 128], T.A1[:, t], 2048.0, ad, "A1:%d" % t, "Aoff:%d" % t, 64)
-        else: ts(T.fl[:], T.A1[:, t], 2048.0, ad, "A1:%d" % t, "fl", 128)
+            mm(ps("pM0", 128 * b, 128 * b + 128), C["Pv%d" % b], T.sel[:, o], b == 0, False, "Pv%d sel:%d" % (b, o), "pM0", 128)
+        if t == 1: ts(T.mb[:], ps("pD2", 0, 128), -120 * BIG, ALU.is_gt, "pD2", "mb", 128)
+        else: ts(T.mb[:], ps("pD2", 0, 128), col(25), ad, "pD2 pf:25 pf:21", "mb", 128, col(21), ALU.is_gt)
+        tt(T.fl[:], T.mb[:], ps("pD2", 128, 256), mul, "mb pD2", "fl", 128)
+        tt(T.A1[:, t], T.fl[:], ps("pD2", 384, 512), ad, "fl pD2", "A1:%d" % t, 128)
+        for b in range(2):
+            mm(ps("pM0", 128 * b, 128 * b + 128), C["Pm%d" % b], T.A1[:, t], False, b == 1, "Pm%d A1:%d" % (b, t), "pM0", 128)
+        act(T.K2[:], ps("pM0", 0, 256), AF.Identity, "pM0 pf:9", "K2", 256, scale=1.0 / 4096, bias=col(9))
+        if t == RO: ts(T.fl[:], T.A1[:, t], 2048.0, ad, "A1:%d" % t, "fl", 128)
         sct(XD.indirect(T.vd[:, 8 * t:8 * t + 8]), T.xw[:, o], "xw:%d vd:%d" % (o, t), "X:b X:d", 128)
         if t == RO - 2 and OPT["xu"]: copy_x(t)
-        act(T.xv[:], X1.indirect(T.vw[:, 8 * t:8 * t + 8]), AF.Copy, "X:b vw:%d" % t, "xv", 128, True)
         if t > 1:
             i = 2 + t
-            mm(T.pD2[:, 256:384], T.UT[:], T.mb[:], True, True, "UT mb", "pD2", 128)
-            ts(T.mb[:], T.pD2[:, 256:384], 1.0, eq, "pD2", "mb", 128)
-            tt(T.oh[:], T.mb[:], T.pD2[:, 384:512], mul, "mb pD2", "oh", 128)
-            finish([(T.nBO[:], T.mb[:], "nBO mb"), (T.BO[:], T.oh[:], "BO oh")], "pD2", i)
+            mm(ps("pD2", 256, 384), C["UT"], T.mb[:], True, True, "UT mb", "pD2", 128)
+            ts(T.top[:], ps("pD2", 256, 384), 1.0, eq, "pD2", "top", 128)
+            tt(T.oh[:], T.top[:], ps("pD2", 384, 512), mul, "top pD2", "oh", 128)
+            finish([(C["nBO"], T.top[:], "nBO top oh"), (C["BO"], T.oh[:], "BO oh top")], "pD2", "pD2", i)
             sct(T.TR[:].indirect(T.vd[:, 8 * i:8 * i + 8]), T.rep[:, i], "rep:%d vd:%d" % (i, i), "TR", 128)
         sct(T.TR[:].indirect(T.vd[:, 8 * o:8 * o + 8]), T.rep[:, t], "rep:%d vd:%d" % (t, o), "TR", 128)
         n = 128 * t
         on = " ".join("vw:%d" % i for i in range(o))
-        if t == 1: off, on = T.vw[:, 8:16], "vw:1"
-        else:
-            off = T.vw[:, 0:8 * o]
-            cp(T.go[:, 8 * o:8 * t], T.vw[:, 8 * t:8 * t + 8], "vw:%d" % t, "go:0", 8)
+        if t == 1: off, on = vw(1), "vw:1"
+        else: off = T.vw[:, 0:8 * o]
         for h in range(1 if t == 1 else 0, 2):
             m = n - 128 * (h == 0)
             tt(T.wtm[:, 0:m], T.TR[:].indirect(off), T.diag[:, 0:m], sub, "TR diag " + on, "wtm", m, True)
             scan(T.g1[:, 0:m], T.hold[:, 0:m], T.wtm[:, 0:m], ad, ALU.max, "hold wtm", "g1", m // 2)
-            off, on = T.go[:, 24 * h:24 * h + 8 * t], "go:%d" % h
-            ts(T.go[:, 24 * h:24 * h + m // 16], T.g1[:, 15:m:16], 2048.0, ad, "g1", on, 8 * t)
+            b, a, on = (T.go, 0, "go") if h else (T.vw, VW[t] - 8 * o, "vw:g%d" % t)
+            ts(b[:, a:a + m // 16], T.g1[:, 15:m:16], 2048.0, ad, "g1", on, 8 * t)
+            off, on = b[:, a:a + 8 * t], on + (" vw:%d" % t) * (1 - h)
         act(T.g3[:, 0:n], T.TR[:].indirect(off), AF.Copy, "TR " + on, "g3", n, True)
         for i in range(t):
             sct(T.TR3[:].indirect(T.vd[:, 8 * i:8 * i + 8]), T.g3[:, 128 * i:128 * i + 128], "g3 vd:%d" % i, "TR3", 128)
         if t == RO:
             dma(T.yt[:], T.TR[0:128:16, 0:4096], "TR", "", 128)
             dma(T.ya[:], T.fl[:], "fl", "", 64)
-            dma(T.yy[:], T.Y[:, t], "Y:%d" % t, "", 32)
+            dma(T.yy[:], T.Y[:, t, 0:128], "Y:%d" % t, "", 32)
             dma(T.yv[:], T.rep[0:128:16, t], "rep:%d" % t, "", 4)
 
-    def make_u(k, b):
-        for s0 in range(16):
-            mm(T.pU[:, 0:32], T.MU[:, 15 - s0:143 - s0], T[b][:, k, s0:512:16], s0 == 0, s0 == 15, "MU %s:z%d" % (b, k), "pU", 32)
-        cp(T.ki[:], T.pU[:, 0:32], "pU", "ki", 32)
-        ts(T.pi[:], T.ki[:], 4095, AND, "ki", "pi", 32)
-        ts(T.sndu[:, k, 0:32], T.pi[:], -2048.0 if OPT["bc"] else 32.0, ad, "pi", "sndu:a%d" % k, 32)
-        ts(T.um[:], T.ki[:], 127, AND, "ki", "um", 32)
-        ts(T.sndu[:, k, 32:64], T.um[:], 32.0, ad, "um", "sndu:b%d" % k, 32, 0.25 if OPT["bc"] else 2048.0, mul)
-        tt(T.sndu[:, k, 64:96], T.um[:], T[b][:, k, 512:544], sub, "um %s:j%d" % (b, k), "sndu:c%d" % k, 64)
-        if OPT["us"]: send(k, 1, "u")
-
-    def seek_head(t):
-        k = t - 1
-        L, J = "land:z%d" % k, "land:j%d" % k
-        z, j = T.land[:, k, 0:512], T.land[:, k, 512:544]
-        mm(T.pM1[:, 0:32], T.idb[:], T.cjb[:], True, False, "idb cjb", "pM1", 32)
-        for b in range(2):
-            for q in range(2):
-                mm(T.pM1[:, b:32:2], T.SJ[:, 2 * b + q], T.land[:, k, 512 + q:544:2], False, b + q == 2, "SJ:%d %s" % (2 * b + q, J), "pM1", 16)
-        cp(T.jw[:], T.pM1[:, 0:32], "pM1", "jw", 32)
-        cp(T.js[:], j, J, "js", 32)
-        act(T.t2[:], T.K2[:].indirect(T.jw[:]), AF.Copy, "K2 jw", "t2", 512, True)
-        tr(T.KT[:], T.t2[:], "t2", "KT", 512)
-        if not OPT["us"]: make_u(k, "land")
-        ub = "landu" if OPT["us"] else "sndu"
-        u0, u1 = (T[ub][:, k, a:a + 32] for a in (0, 32))
-        n0, n1 = ("landu:u%d" % k,) * 2 if OPT["us"] else ("sndu:a%d" % k, "sndu:b%d" % k)
-        if OPT["bc"]:
-            mm(T.pE[:, 0:480], T.i83[:], T.q25[:, 0:480], True, False, "i83 q25", "pE", 480)
-            for n in range(15): mm(T.pE[:, 32 * n:32 * n + 32], T.idb[:], u0, False, n == 14, "idb " + n0, "pE", 32)
-            for n in range(15): mm(T.pU[:, 32 * n:32 * n + 32], T.i8k[:], u1, True, True, "i8k " + n1, "pU", 32)
-        for c in range(len(CUT) - 1):
-            a, b = CUT[c], CUT[c + 1]
-            s, n, m = slice(32 * a, 32 * b), 32 * (b - a), ":%d" % c
-            tt(T.hT[:, s], T.KT[:].indirect(T.prm[:, 2 * a:2 * b]), T.offc[:, s], sub, "KT prm offc", "hT" + m, n, True)
-            if OPT["bc"]:
-                tt(T.pr[:, s], T.hT[:, s], T.pE[:, s], mul, "pE hT" + m, "pr" + m, n)
-                tt(T.pt[:, s], T.pr[:, s], T.pU[:, s], ad, "pU pr" + m, "pt" + m, n)
-            else:
-                tt(T.pr[:, s], u0.indirect(T.rl[:, 2 * a:2 * b]), T.hT[:, s], mul, n0 + " rl hT" + m, "pr" + m, n, True)
-                tt(T.pt[:, s], u1.indirect(T.rl[:, 2 * a:2 * b]), T.pr[:, s], ad, n1 + " rl pr" + m, "pt" + m, n, True)
-            ts(T.hi[:, s], T.pt[:, s], 5, ALU.arith_shift_right, "pt" + m, "hi" + m, n, 4095, AND)
-            cp(T.hoff[:, s], T.hi[:, s], "hi" + m, "hoff" + m, n)
-        ts(T.vc[:], T.KT[:, 0::16], -2.0 ** 23, ad, "KT", "vc", 32)
-        ts(T.vc[:], T.vc[:], 12, ALU.arith_shift_right, "vc", "vc", 32)
-        tt(T.scn[:, 0:32], T.scn[:, 96:128], T.vc[:], sub, "scn:3 vc", "scn:0", 64)
-        if OPT["mq"] == 2:
-            tt(T.xvj[:], T.xv[:].indirect(T.js[:]), z, sub, "xv js " + L, "xvj", 512, True)
-            ts(T.wtm[:], T.xvj[:], -0.5, mul, "xvj", "wtm", 256, 1536.25, ad)
-            ts(T.X[:, FND:XW], T.wtm[:], -1536.0, ad, "wtm", "X:q", 256)
-            return
-        act(T.xvj[:], T.xv[:].indirect(T.js[:]), AF.Copy, "xv js", "xvj", 512, True)
-        mm(T.pM0[:], T.idb[:], T.q25[:], True, False, "idb q25", "pM0", 512)
-        mm(T.pM0[:], T.nhidb[:], T.xvj[:], False, False, "nhidb xvj", "pM0", 512)
-        mm(T.pM0[:], T.hidb[:], z, False, True, "hidb " + L, "pM0", 512)
-        whole(T.X[:, FND:XW], T.pM0[:], T.t2[:], "pM0", "X:q", "t2", 512, OPT["q%d" % t])
-
-    def seek_rest(t):
-        k = t - 1
-        L, J = "land:z%d" % k, "land:j%d" % k
-        z, j = T.land[:, k, 0:512], T.land[:, k, 512:544]
-        mm(T.pE[:], T.t85[0:2, :], T.thc[0:2, :], True, False, "t85 thc", "pE", 512)
-        ng, n, nq = 0, 0, 0
-        left = [0]
-        def acc(o, l, rh, r, n):
-            left[0] += 1
-            def f():
-                left[0] -= 1
-                return P.matmul(o, l, rh, False, left[0] == 0)
-            add("P", f, r, "pE" if OPT["fix"] else "pE:acc", max(64, n) * PC)
-        for si, S in enumerate(PAIRS):
-            way, m = WAYS[t][si], len(S)
-            an, dn = (" ".join("%s:%d_%d" % (b, si, i) for i in range(m)) for b in ("lv", "df"))
-            e = T.pE[:, S[0]::16 // m]
-            for i in range(m):
-                w = X1.indirect(T.hoff[:, 32 * n:32 * n + 32])
-                hn = "X:b hoff:%d " % max(c for c in range(len(CUT)) if CUT[c] <= n)
-                n += 1
-                o, d, on, di = T.lv[:, si, :, i], T.df[:, si, :, i], "lv:%d_%d" % (si, i), "df:%d_%d" % (si, i)
-                if way == "A":
-                    s, pn = ng % 4, ("pM1", "pU")[ng & 1]
-                    ng += 1
-                    act(T.gsl[:, s], w, AF.Copy, hn, "gsl:%d" % s, 512, True)
-                    mm(T[pn][:], T.nidb[:], z, True, False, "nidb " + L, pn, 512)
-                    mm(T[pn][:], T.idb[:], T.gsl[:, s], False, True, "idb gsl:%d" % s, pn, 512)
-                    act(o, T[pn][:], AF.Abs, pn, on, 512)
-                else:
-                    tt(d, w, z, sub, hn + L, di, 512, True)
-                    if way == "M": act(o, d, AF.Abs, di, on, 512)
-            if way == "V":
-                ts(T.lv[:, si, :, 0:m], T.df[:, si, :, 0:m], 0.0, ALU.max, dn, an, 256 * m, 2.0, mul)
-                for s0 in range(16): acc(e, T.nWb[:, 15 - s0:143 - s0], T.df[:, si, s0::16, 0:m], "nWb " + dn, 32 * m)
-            for s0 in range(16): acc(e, T.Wb[:, 15 - s0:143 - s0], T.lv[:, si, s0::16, 0:m], "Wb " + an, 32 * m)
-        scan(T.hT[:], T.pE[:], T.KT[:], ALU.min, ALU.max, "pE KT", "hT", 512)
-        cp(T.ki[:], T.hT[:, 15::16], "hT", "ki", 32)
-        ts(T.pi[:], T.ki[:], 4095, AND, "ki", "pi", 32)
-        cp(T.pw[:], T.pi[:], "pi", "pw", 32)
-        tt(T.wtm[:], T.TR3[:].indirect(T.pw[:]), T.diag[:], sub, "TR3 diag pw", "wtm", 512, True)
-        scan(T.g1[:], T.hold[:], T.wtm[:], ad, ALU.max, "hold wtm", "g1", 256)
-        ff = T.ff[:, 0:32]
-        tt(ff, T.vc[:], T.g1[:, 15::16], eq, "vc g1", "ff:f", 64)
-        tt(T.scn[:, 32:64], ff, T.scn[:, 0:32], mul, "ff:f scn:0", "scn:1", 64)
-        tt(T.scn[:, 64:96], T.scn[:, 32:64], T.g1[:, 15::16], ad, "scn:1 g1", "scn:2", 64)
-        ts(T.pw[:], T.scn[:, 64:96], 2048.0, ad, "scn:2", "pw", 32)
-        for a, b, x in ((0, 512, "z"),) if t < RO else ((256, 512, "y"), (0, 256, "z")):
-            tt(T.xvj[:, a:b], X2.indirect(T.pw[:, a // 16:b // 16]), T.land[:, k, a:b], sub, "X:b X:d X:q pw " + L, "xvj:" + x, b - a, True)
-            act(T.snd[:, t, a:b], T.xvj[:, a:b], AF.Abs, "xvj:" + x, "snd:%s%d" % (x, t), b - a)
-        if OPT["us"]: tt(T.tj[:], ff, T.landu[:, k, 64:96], mul, "ff:f landu:u%d" % k, "tj", 64)
-        else: tt(T.tj[:], ff, T.sndu[:, k, 64:96], mul, "ff:f sndu:c%d" % k, "tj", 64)
-        if t < RO:
-            tt(T.snd[:, t, 512:544], T.tj[:], j, ad, "tj " + J, "snd:j%d" % t, 64)
-            send(t, 1, "j"); send(t, 1, "z")
-            mm(T.pU[:, 0:33], T.o16[:], T.ff[:, 0:33], True, True, "o16 ff", "pU", 33)
-            red(col(21), T.pU[:, 0:33], ad, "pU", "pf:21", 33)
-            ts(col(25), col(21), MAGIC, ad, "pf:21", "pf:25", 1, -MAGIC, ad)
-            ts(col(20), col(25), col(21), sub, "pf:25 pf:21", "pf:20", 1, -256 * BIG, mul)
-            if OPT["us"]: make_u(t, "snd")
+    def make_u(k, a, b):
+        c, n = slice(16 * a, 16 * b), 16 * (b - a)
+        p, zn, un = ps("pU", 16 * a, 16 * b), nm("snd:z%d" % k, a, b), nm("sndu:u%d" % k, a, b)
+        if OPT["up"]:
+            mm(p, C["i8k"], T.nq[:, 0:n], True, False, "i8k nq", "pU", n)
+            mm(p, C["hidb"], T.cb[:, CB.index("ones"), 0:n], False, False, "hidb ones", "pU", n)
+            for y in range(2):
+                for s0 in range(16): mm(p, T.MU[:, y, 15 - s0:143 - s0], T.snd[:, k, 256 * a + s0:256 * b:16], False, False, "MU " + zn, "pU", n)
+                if y == 0: whole(p, "pU", n, "m12x", False)
+            mm(p, C["i8k"], T.q25[:, 0:n], False, True, "i8k q25", "pU", n)
+            ts(T.sndu[:, k, c], p, -1.0, mul, "pU", un, n)
         else:
-            tt(T.jb[:], T.tj[:], j, ad, "tj " + J, "jb", 64)
-            tr(T.snd[:, t, 512:544], T.jb[:], "jb", "snd:j%d" % t, 32)
-            send(t, -RO, "yj"); send(t, -RO, "z")
+            for s0 in range(16): mm(p, T.MU[:, 0, 15 - s0:143 - s0], T.snd[:, k, 256 * a + s0:256 * b:16], s0 == 0, s0 == 15, "MU " + zn, "pU", n)
+            cp(T.ku[:, c], p, "pU", nm("ku:", a, b), n)
+            ts(T.pu[:, c], T.ku[:, c], 4095, AND, nm("ku:", a, b), nm("pu:", a, b), n)
+            ts(T.sndu[:, k, c], T.pu[:, c], -2048.0, ad, nm("pu:", a, b), un, n)
+        send(k, 1, "u", a, b)
+        mm(p, C["i254"], T.nq[:, 0:n], True, False, "i254 nq", "pU", n)
+        mm(p, idb, T.sndu[:, k, c], False, False, "idb " + un, "pU", n)
+        whole(p, "pU", n, "m7x", False)
+        mm(p, nidb, T.sndu[:, k, c], False, False, "nidb " + un, "pU", n)
+        mm(p, idb, T.snd[:, k, 512 + 16 * a:512 + 16 * b], False, True, "idb " + nm("snd:j%d" % k, a, b), "pU", n)
+        act(T.snd[:, k, 544 + 16 * a:544 + 16 * b], p, AF.Copy, "pU", nm("snd:c%d" % k, a, b), n, scale=-1.0)
+        send(k, 1, "c", a, b)
 
-    part = CACHE.setdefault("part", {})
-    def run(f, t, name):
-        n0 = len(ops)
-        f(t)
-        for i in range(n0, len(ops)): part[i] = name + str(t)
-    run(users_a, 1, "a")
-    run(users_far, 1, "f")
-    if OPT["us"]: make_u(0, "snd")
-    for t in range(1, RO + 1):
-        run(users_b, t, "b")
-        run(seek_head, t, "h")
+    def seek_head(t, a, b):
+        k, c, s, n = t - 1, slice(16 * a, 16 * b), slice(256 * a, 256 * b), 16 * (b - a)
+        def h_(x): return nm(x, a, b)
+        L, J, U = h_("land:z%d" % k), h_("land:j%d" % k), h_("landu:u%d" % k)
+        mm(ps("pM1", 16 * a, 16 * b), idb, T.cjb[:, 0:n], True, False, "idb cjb", "pM1", n)
+        for x in range(2):
+            for q in range(2):
+                mm(T.pM1[:, a:b, x::2], C["SJ%d" % (2 * x + q)], T.land[:, k, 512 + 16 * a + q:512 + 16 * b:2], False, x + q == 2, "SJ%d %s" % (2 * x + q, J), "pM1", 16)
+        cp(T.jw[:, c], ps("pM1", 16 * a, 16 * b), "pM1", h_("jw:"), n)
+        act(T.t2[:, s], T.K2[:].indirect(T.jw[:, c]), AF.Copy, "K2 " + h_("jw:"), h_("t2:"), 16 * n, True)
+        tr(T.KT[:, s], T.t2[:, s], h_("t2:"), h_("KT:"), 16 * n)
+        pu = "pM1" if SP[t] else "pE"
+        for pn, x in ((pu, "i83"), ("pU", "i18")):
+            mm(ps(pn, 256 * a, 256 * b), C[x], T.q25[:, 0:16 * n], True, False, x + " q25", pn, 16 * n)
+        for pn, y in ((pu, "i4k"), ("pU", "i2k")):
+            for i in range(15): mm(T[pn][:, 16 * a + i:16 * b:16] if SP[t] else ps(pn, 32 * i, 32 * i + 32), C[y], T.landu[:, k, c], False, i == 14, y + " " + U, pn, n)
+        for h in range(a, b):
+            lo, hi, m = 256 * h, 256 * h + (240 if SP[t] else 256 - 32 * h), ":%d" % h
+            w = hi - lo
+            if SP[t]: tt(T.hT[:, lo:hi], T.KT[:, lo:lo + 256].indirect(T.prm[:, 32:47]), T.offc[:, 512:752], sub, "KT:_%d prm offc" % h, "hT" + m, w, True)
+            else: tt(T.hT[:, lo:hi], T.KT[:].indirect(T.prm[:, lo // 16:hi // 16]), T.offc[:, lo:hi], sub, "KT prm offc", "hT" + m, w, True)
+            tt(T.pr[:, lo:hi], T.hT[:, lo:hi], ps(pu, lo, hi), mul, pu + " hT" + m, "pr" + m, w)
+            tt(T.pt[:, lo:hi], T.pr[:, lo:hi], ps("pU", lo, hi), ad, "pU pr" + m, "pt" + m, w)
+            ts(T.hi[:, lo:hi], T.pt[:, lo:hi], 5, ALU.arith_shift_right, "pt" + m, "hi" + m, w, 4095, AND)
+            cp(T.hoff[:, lo:hi], T.hi[:, lo:hi], "hi" + m, "hoff" + m, w)
+        ts(T.vc[:, c], T.KT[:, 256 * a:256 * b:16], -2048.5, ad, h_("KT:"), h_("vc:"), n, 2.0 ** -13, ad)
+        tt(T.scn[:, c], T.scn[:, 96 + 16 * a:96 + 16 * b], T.vc[:, c], sub, "scn:3 " + h_("vc:"), h_("scn:0"), 2 * n)
+        ts(T.js[:, c], T.vc[:, c], 2048.0, ad, h_("vc:"), h_("js:"), n)
+        act(T.xvj[:, s], X1.indirect(T.js[:, c]), AF.Copy, "X:b " + h_("js:"), h_("xvj:"), 16 * n, True)
+        mm(T.pM0[:, s], idb, T.q25[:, 0:16 * n], True, False, "idb q25", "pM0", 16 * n)
+        mm(T.pM0[:, s], C["hidb"], T.land[:, k, s], False, False, "hidb " + L, "pM0", 16 * n)
+        mm(T.pM0[:, s], C["nhidb"], T.xvj[:, s], False, False, "nhidb " + h_("xvj:"), "pM0", 16 * n)
+        whole(T.pM0[:, s], "pM0", 16 * n, "m1x", True)
+        act(T.X[:, FND + 256 * a:FND + 256 * b], T.pM0[:, s], AF.Copy, "pM0", h_("X:q"), 16 * n)
+
+    ng = [0]
+    def pair(t, gi):
+        k, way, m = t - 1, WAYS[t][gi], 2 - (gi == 7)
+        z, L = T.land[:, k, 0:512], nm("land:z%d" % k, 0, 2)
+        if gi == 0: mm(T.pE[:], rows("t85", 2), T.thc[0:2, :], True, False, "t85 thc", "pE", 512)
+        e = T.pE[:, gi + 1::16 // m]
+        gd = gi - WAYS[t][:gi].count("A")
+        an, dn = (" ".join("%s:%d_%d" % (b, y, i) for i in range(m)) for b, y in (("lv", gi), ("dp", gd)))
+        for i in range(m):
+            n = 2 * gi + i
+            w, hn = X1.indirect(T.hoff[:, 32 * n:32 * n + 32]), "X:b hoff:%d " % (n // 8)
+            o, on, di = T.lv[:, gi, :, i::2], "lv:%d_%d" % (gi, i), "dp:%d_%d" % (gd, i)
+            if way == "A" or way == "B" and i == 0:
+                s, pn = ng[0] % 4, ("pM1", "pU")[ng[0] & 1]
+                ng[0] += 1
+                act(T.gsl[:, s], w, AF.Copy, hn, "gsl:%d" % s, 512, True)
+                mm(T[pn][:], nidb, z, True, False, "nidb " + L, pn, 512)
+                mm(T[pn][:], idb, T.gsl[:, s], False, True, "idb gsl:%d" % s, pn, 512)
+                act(o, T[pn][:], AF.Abs, pn, on, 512)
+            else:
+                tt(T.dp[:, gd, :, i], w, z, sub, hn + L, di, 512, True)
+                if way != "V": act(o, T.dp[:, gd, :, i], AF.Abs, di, on, 512)
+        if way == "V":
+            act(T.lv[:, gi, :, 0::3 - m], T.dp[:, gd, :, 0:m], AF.Relu, dn, an, 512 * m, half=True, scale=2.0)
+            for s0 in range(16): mm(e, shift(1, s0), T.dp[:, gd, s0::16, 0:m], False, False, "W " + dn, "pE", 32 * m)
+        for s0 in range(16): mm(e, shift(0, s0), T.lv[:, gi, s0 // 2::8, 2 * (s0 % 2):2 * (s0 % 2) + m], False, gi == 7 and s0 == 15, "W " + an, "pE", 32 * m)
+
+    def levels(t, h, q):
+        if not SP[t]: return pair(t, 4 * h + q)
+        k, gi, way, i0 = t - 1, 4 * h + q if q < 3 else 8 + h, WAYS[t][4 * h + q], int(q == 3)
+        z, L = T.land[:, k, 256 * h:256 * h + 256], "land:z%d_%d" % (k, h)
+        if q == 0: mm(T.pE[:, 256 * h:256 * h + 256], rows("t85", 2), T.thc[0:2, 0:256], True, False, "t85 thc", "pE", 256)
+        e = T.pE[:, 256 * h + (q + 1) % 4:256 * h + 256:4]
+        an, dn = (" ".join("%s:%d_%d" % (b, gi, i) for i in range(4)) for b in ("lv", "df"))
+        for i in range(i0, 4, 2):
+            m, n = min(2, 4 - i), 4 * q + i - i0
+            hn = "X:b hoff:%d " % h
+            o, on = T.lv[:, gi, :, i:i + m], " ".join("lv:%d_%d" % (gi, y) for y in range(i, i + m))
+            if way == "A" or way == "B" and i == i0:
+                s, pn = ng[0] % 4, ("pM1", "pU")[ng[0] & 1]
+                ng[0] += 1
+                out = [T[pn][:, :, y::2] for y in range(2)] if m == 2 else [ps(pn, 0, 256)]
+                act(T.gsl[:, s, 0:256 * m], X1.indirect(T.hoff[:, 256 * h + 16 * n:256 * h + 16 * (n + m)]), AF.Copy, hn, "gsl:%d" % s, 256 * m, True)
+                for y in range(m): mm(out[y], nidb, z, y == 0, False, "nidb " + L, pn, 256)
+                for y in range(m): mm(out[y], idb, T.gsl[:, s, 256 * y:256 * y + 256], False, y == m - 1, "idb gsl:%d" % s, pn, 256)
+                act(o, ps(pn, 0, 256 * m), AF.Abs, pn, on, 256 * m)
+            else:
+                for y in range(m):
+                    tt(T.df[:, gi, :, i + y], X1.indirect(T.hoff[:, 256 * h + 16 * (n + y):256 * h + 16 * (n + y + 1)]), z, sub, hn + L, "df:%d_%d" % (gi, i + y), 256, True)
+                if way != "V": act(o, T.df[:, gi, :, i:i + m], AF.Abs, on.replace("lv", "df"), on, 256 * m)
+        if way == "V":
+            act(T.lv[:, gi], T.df[:, gi], AF.Relu, dn, an, 1024, half=True, scale=2.0)
+            for s0 in range(16): mm(e, shift(1, s0), T.df[:, gi, s0::16], False, False, "W " + dn, "pE", 64)
+        for s0 in range(16): mm(e, shift(0, s0), T.lv[:, gi, s0::16], False, q == 3 and s0 == 15, "W " + an, "pE", 64)
+
+    def choose(t, a, b):
+        s = slice(256 * a, 256 * b)
+        scan(T.sk[:, s], T.pE[:, s], T.KT[:, s], ALU.min, ALU.max, "pE " + nm("KT:", a, b), nm("sk:", a, b), 256 * (b - a))
+
+    def seek_end(t, a, b):
+        k, c, s, n = t - 1, slice(16 * a, 16 * b), slice(256 * a, 256 * b), 16 * (b - a)
+        def h_(x): return nm(x, a, b)
+        J, p3 = h_("land:j%d" % k), T.g1[:, 256 * a + 15:256 * b:16]
+        ts(T.ki[:, c], T.sk[:, 256 * a + 15:256 * b:16], 4096.0, mul, h_("sk:"), h_("ki:"), n)
+        ts(T.pi[:, c], T.ki[:, c], 4095, AND, h_("ki:"), h_("pi:"), n)
+        cp(T.pw[:, c], T.pi[:, c], h_("pi:"), h_("pw:"), n)
+        tt(T.wtm[:, s], T.TR3[:].indirect(T.pw[:, c]), T.diag[:, s], sub, "TR3 diag " + h_("pw:"), h_("wtm:"), 16 * n, True)
+        scan(T.g1[:, s], T.hold[:, s], T.wtm[:, s], ad, ALU.max, "hold " + h_("wtm:"), h_("g1:"), 8 * n)
+        ff, s1, s2 = T.ff[:, c], T.scn[:, 32 + 16 * a:32 + 16 * b], T.scn[:, 64 + 16 * a:64 + 16 * b]
+        tt(ff, T.vc[:, c], p3, eq, h_("vc:") + " " + h_("g1:"), h_("ff:f"), 2 * n)
+        tt(s1, ff, T.scn[:, c], mul, h_("ff:f") + " " + h_("scn:0"), h_("scn:1"), 2 * n)
+        tt(s2, s1, p3, ad, h_("scn:1") + " " + h_("g1:"), h_("scn:2"), 2 * n)
+        ts(T.pw[:, c], s2, 2048.0, ad, h_("scn:2"), h_("pw:"), n)
+        xn, L = "X:b X:d %s %s " % (nm("X:q", 0, 2), h_("pw:")), h_("land:z%d" % k)
+        if str(t) in OPT["xa"]:
+            act(T.xf[:, s], X2.indirect(T.pw[:, c]), AF.Copy, xn, h_("xf:"), 16 * n, True)
+            mm(T.pM0[:, s], nidb, T.land[:, k, s], True, False, "nidb " + L, "pM0", 16 * n)
+            mm(T.pM0[:, s], idb, T.xf[:, s], False, True, "idb " + h_("xf:"), "pM0", 16 * n)
+            act(T.snd[:, t, s], T.pM0[:, s], AF.Abs, "pM0", h_("snd:z%d" % t), 16 * n)
+        else:
+            tt(T.xf[:, s], X2.indirect(T.pw[:, c]), T.land[:, k, s], sub, xn + L, h_("xf:"), 16 * n, True)
+            act(T.snd[:, t, s], T.xf[:, s], AF.Abs, h_("xf:"), h_("snd:z%d" % t), 16 * n)
+        tt(T.tj[:, c], ff, T.land[:, k, 544 + 16 * a:544 + 16 * b], mul, h_("ff:f") + " " + h_("land:c%d" % k), h_("tj:"), 2 * n)
+        o, on = (T.snd[:, t, 512 + 16 * a:512 + 16 * b], h_("snd:j%d" % t)) if t < RO else (T.jf[:, c], h_("jf:"))
+        tt(o, T.tj[:, c], T.land[:, k, 512 + 16 * a:512 + 16 * b], ad, h_("tj:") + " " + J, on, 2 * n)
+
+    def leave(t, a, b):
         if t < RO:
-            if t + 1 < RO or not OPT["xu"]: run(users_a, t + 1, "a")
-            run(users_far, t + 1, "f")
+            send(t, 1, "j", a, b); send(t, 1, "z", a, b)
+            make_u(t, a, b)
+            return
+        if b == 2:
+            tr(T.sndj[:], T.jf[:], "jf", nm("sndj:f%d" % t, 0, 2), 32)
+            send(t, -RO, "f")
+            dma(T.yj[0::2, :], T.landj[:, 0:16], "landj", "", 8, "A")
+            dma(T.yj[1::2, :], T.landj[:, 16:32], "landj", "", 8, "A")
+        send(t, -RO, "z", a, b)
+        dma(T.yz[:, 256 * a:256 * b], T.land[:, RO, 256 * a:256 * b], nm("land:z%d" % RO, a, b), "", 64 * (b - a))
+
+    def finds(t):
+        mm(ps("pE", 0, 48), C["o16"], T.ff[:], True, True, "o16 ff", "pE", 48)
+        red(col(21), ps("pE", 0, 48), ad, "pE", "pf:21", 48)
+        ts(col(25), col(21), MAGIC * 2.0 ** 33, ad, "pf:21", "pf:25", 1, -MAGIC * 2.0 ** 33, ad)
+
+    def run(name, f, t, *a):
+        label[0] = name + str(t)
+        f(t, *a)
+    run("f", users_g, 1)
+    run("a", users_a, 1)
+    run("a", users_y, 1)
+    run("f", users_far, 1)
+    run("a", make_u, 0, 0, 2)
+    for t in range(1, RO + 1):
+        run("b", users_b, t)
+        run("h", seek_head, t, 0, 2 - HP[t])
+        if t < RO:
+            if t + 1 < RO or not OPT["xu"]:
+                run("a", users_a, t + 1)
+                run("a", users_y, t + 1)
+            run("f", users_g, t + 1)
+            run("f", users_far, t + 1)
         if t == RO - 2 and OPT["xu"]:
-            run(step_x, t + 1, "a")
-            run(users_a, t + 2, "a")
-        run(seek_rest, t, "r")
-    dma(T.yz[:, 256:512], T.land[:, RO, 256:512], "land:y%d" % RO, "", 64)
-    dma(T.yz[:, 0:256], T.land[:, RO, 0:256], "land:z%d" % RO, "", 64)
-    cp(T.dj[:], T.land[:, RO, 512:544], "land:j%d" % RO, "dj", 32)
-    dma(T.yj[0::2, :], T.dj[:, 0:16], "dj", "", 8, "A")
-    dma(T.yj[1::2, :], T.dj[:, 16:32], "dj", "", 8, "A")
+            run("a", step_x, t + 1)
+            run("a", users_a, t + 2)
+            run("a", users_y, t + 2)
+        for q in range(4):
+            run("r", levels, t, 0, q)
+            if HP[t] and q == OPT["hq"]: run("h", seek_head, t, 1, 2)
+        if SP[t]: run("e", choose, t, 0, 1)
+        for q in range(4):
+            run("r", levels, t, 1, q)
+            if SP[t] and q == OPT["tq"]:
+                run("e", seek_end, t, 0, 1)
+                if HP[t + 1]: run("e", leave, t, 0, 1)
+        run("e", choose, t, SP[t], 2)
+        run("e", seek_end, t, SP[t], 2)
+        if t < RO: run("e", finds, t)
+        run("e", leave, t, SP[t] * HP[t + 1], 2)
     return ops
 
 
@@ -526,22 +622,14 @@ def depend(ops):
         for lst, wr in ((r, False), (w, True)):
             for a in lst:
                 b, _, k = a.partition(":")
-                ps = SCRATCH[b][0] == "psum"
                 for (j, k2, wr2) in acc.get(b, ()):
-                    q2, kind2 = ops[j][0], ops[j][5]
-                    same = q2 == q and kind == "c" and kind2 == "c"
-                    if ps:
-                        if k == "acc" and k2 == "acc": continue
-                        if same: d.setdefault(j, False)
-                        else: d[j] = True
-                    elif (k == k2 or not k or not k2) and (wr or wr2):
-                        d[j] = True
+                    if b in BANKS: d.setdefault(j, False)
+                    elif (k == k2 or not k or not k2) and (wr or wr2): d[j] = True
         for lst, wr in ((r, False), (w, True)):
             for a in lst:
                 b, _, k = a.partition(":")
                 old = acc.get(b, [])
-                if k == "acc": pass
-                elif SCRATCH[b][0] == "psum": old = []
+                if b in BANKS: old = []
                 elif wr: old = [e for e in old if k and e[1] != k]
                 acc[b] = old + [(i, k, wr)]
         d.pop(i, None)
@@ -549,55 +637,100 @@ def depend(ops):
     return deps
 
 
-HOP, SELF, DK, RZ, RJ = 270.0, 130.0, 2.5, 4800.0, 2400.0
+CASES = [(1.35, 3.0, .84, 2.5, 4500, 2200, 270, 130, 500, 0, 1.15), (1.56, 3.8, 1.0, 3.2, 5500, 3000, 220, 100, 700, 0, 1.1),
+         (1.9, 5.0, 1.12, 3.0, 4500, 2500, 300, 150, 500, 0, 1.0), (1.2, 2.5, .82, 2.5, 5000, 2800, 300, 150, 800, 0, 1.25)]
+
+
+def timing(ops, deps, case):
+    gc, sc, f, dk, rz, rj, hop, slf, issue, two, pe = case
+    n = len(ops)
+    dur, alt, hold, eng = [0.0] * n, [0.0] * n, [0.0] * n, [0.0] * n
+    for i, (q, fn, r, w, c, kind) in enumerate(ops):
+        if kind == "c":
+            by = CACHE["index"].get(i)
+            if by: c = 60 + (c - 60) * (gc / GC if by == "g" else sc / SC if by == "s" else max(gc, two) / GC)
+            dur[i] = alt[i] = c * f * (pe if q == "P" else 1.0)
+            if i in CACHE["alt"] and not by: alt[i] = CACHE["alt"][i][1] * f
+        elif kind == "d": hold[i], eng[i] = 60.0, c * dk
+        else: hold[i], dur[i] = issue, rj + (rz - rj) * CACHE["size"][i]
+    return dur, alt, hold, eng, hop, slf, [list(d.items()) for d in deps]
+
+
+def replay(qs, case, seq, a, old):
+    dur, alt, hold, eng, hop, slf, pre = case
+    done, why, byq = (list(x) for x in old)
+    free, last, dma = {}, {}, 0.0
+    for i in seq[:a]:
+        last[qs[i]] = i
+        if eng[i]: dma = done[i]
+    for q, i in last.items(): free[q] = byq[i] + hold[i] if hold[i] else done[i]
+    for i in seq[a:]:
+        q = qs[i]
+        t, w = free.get(q, 0.0), -2 - last.get(q, -1)
+        for j, hard in pre[i]:
+            if qs[j] != q: e = done[j] + hop
+            elif hard: e = done[j] + slf
+            else: continue
+            if e > t: t, w = e, j
+        why[i], byq[i], last[q] = w, t, i
+        if eng[i]:
+            done[i] = dma = max(dma, t + 2000.0) + eng[i]
+            free[q] = t + hold[i]
+        elif hold[i]:
+            done[i] = t + dur[i]
+            free[q] = t + hold[i]
+        else: free[q] = done[i] = t + (alt[i] if q == "V" else dur[i])
+    return done, why, byq
 
 
 def plan(ops, deps):
     n = len(ops)
-    hold, lat = [0.0] * n, [0.0] * n
+    dur, alt, hold, eng, hop, slf, pre = timing(ops, deps, CASES[OPT["pc"]])
+    qs = [o[0] for o in ops]
     cum, last = 0.0, {}
-    edges = [dict() for _ in range(n)]
+    extra = [0.0] * n
+    before = [dict(d) for d in deps]
     for i, (q, fn, r, w, c, kind) in enumerate(ops):
-        if kind == "c":
-            hold[i] = lat[i] = c * OPT["f"]
-            if q == "G":
-                if q in last: edges[i][last[q]] = hold[last[q]]
-                last[q] = i
-        elif kind == "d":
-            hold[i] = 1000.0 if q == "G" else 60.0
-            if r: lat[i] = 2000.0 + c * DK + 500.0 * (q == "G")
-            else:
-                cum += c * DK
-                lat[i] = 2000.0 + cum
-                if q in last: edges[i][last[q]] = 60.0
-                last[q] = i
-        else: hold[i], lat[i] = 500.0, RZ if int(kind[1:]) < 4 else RJ if int(kind[1:]) < 12 else (RZ + RJ) / 2
-        for j, wt in deps[i].items():
-            edges[i][j] = lat[j] + (SELF if ops[j][0] == q else HOP) if wt else hold[j]
-    succ = [dict() for _ in range(n)]
+        if kind == "c" and q == "G" or kind == "d" and not r:
+            if q in last: before[i].setdefault(last[q], None)
+            last[q] = i
+        if kind == "d" and not r:
+            cum += eng[i]
+            extra[i] = 2000.0 + cum
+        elif eng[i]: extra[i] = 2000.0 + eng[i]
+    after = [dict() for _ in range(n)]
     for i in range(n):
-        for j, e in edges[i].items(): succ[j][i] = e
+        for j, e in before[i].items(): after[j][i] = e
+    def held(i, q): return hold[i] or (alt[i] if q == "V" else dur[i])
+    def lat(i, q): return extra[i] + (alt[i] if q == "V" else dur[i])
+    def edge(j, qj, qi, hard): return held(j, qj) if hard is None or (qi == qj and not hard) else lat(j, qj) + (slf if qi == qj else hop)
 
     def place(seq, back):
         busy = {}
         st = [0.0] * n
         for i in seq:
-            if back: t = max([st[s] + e for s, e in succ[i].items()] + [lat[i]]) - hold[i]
-            else: t = max([st[j] + e for j, e in edges[i].items()] + [0.0])
-            b = busy.setdefault(ops[i][0], [])
-            lo, hi = 0, len(b)
-            while lo < hi:
-                m = (lo + hi) // 2
-                if b[m][1] <= t: lo = m + 1
-                else: hi = m
-            while lo < len(b) and b[lo][0] < t + hold[i]:
-                t = max(t, b[lo][1]); lo += 1
-            b.insert(lo, (t, t + hold[i]))
-            st[i] = t + hold[i] if back else t
+            best = None
+            for q in "AV" if i in CACHE["alt"] and not back else qs[i]:
+                h = held(i, q)
+                if back: t = max([st[s] + edge(i, q, qs[s], e) for s, e in after[i].items()] + [lat(i, q)]) - h
+                else: t = max([st[j] + edge(j, qs[j], q, e) for j, e in before[i].items()] + [0.0])
+                b = busy.setdefault(q, [])
+                lo, hi = 0, len(b)
+                while lo < hi:
+                    m = (lo + hi) // 2
+                    if b[m][1] <= t: lo = m + 1
+                    else: hi = m
+                while lo < len(b) and b[lo][0] < t + h:
+                    t = max(t, b[lo][1]); lo += 1
+                x = t + h + OPT["vb"] * (q == "V")
+                if best is None or x < best[0]: best = (x, q, lo, t, h)
+            _, qs[i], lo, t, h = best
+            busy[qs[i]].insert(lo, (t, t + h))
+            st[i] = t + h if back else t
         return st
 
     def topo_order(key, back):
-        pre, post = (succ, edges) if back else (edges, succ)
+        pre, post = (after, before) if back else (before, after)
         left = [len(pre[i]) for i in range(n)]
         ready = [i for i in range(n) if not left[i]]
         out = []
@@ -610,107 +743,165 @@ def plan(ops, deps):
         return out
 
     pr = [0.0] * n
-    for i in range(n - 1, -1, -1): pr[i] = max([pr[s] + e for s, e in succ[i].items()] + [lat[i]])
+    for i in range(n - 1, -1, -1): pr[i] = max([pr[s] + edge(i, qs[i], qs[s], e) for s, e in after[i].items()] + [lat(i, qs[i])])
     key = {i: (-pr[i], i) for i in range(n)}
     best, x = None, OPT["seed"]
+    cases = [timing(ops, deps, c) for c in CASES]
     for it in range(OPT["passes"]):
         st = place(topo_order(key, False), False)
-        span = max(st[i] + lat[i] for i in range(n))
-        if best is None or span < best[0]: best = (span, st)
-        bk = place(topo_order({i: (-st[i] - hold[i], -i) for i in range(n)}, True), True)
+        seq = topo_order({i: (st[i], i) for i in range(n)}, False)
+        span = sum(max(replay(qs, c, seq, 0, ([0.0] * n,) * 3)[0]) for c in cases)
+        if best is None or span < best[0]: best = (span, seq, list(qs))
+        bk = place(topo_order({i: (-st[i] - held(i, qs[i]), -i) for i in range(n)}, True), True)
         key = {}
         for i in range(n):
             x = (x * 1103515245 + 12345) % 2147483648
             key[i] = (-bk[i] + BIAS.get(CACHE["part"].get(i), 0.0) + OPT["noise"] * x / 2147483648.0, i)
-    st = best[1]
-    return topo_order({i: (st[i], i) for i in range(n)}, False), st, [st[i] + lat[i] for i in range(n)]
+    return best[1], best[2]
 
 
-CASES = [(1.35, 3.0, .84, 2.5, 4500, 2200, 270, 130, 500), (1.56, 3.8, 1.0, 4.0, 5500, 3000, 200, 100, 700),
-         (1.9, 5.0, 1.12, 3.0, 4500, 2500, 300, 150, 500), (1.2, 2.5, .82, 2.5, 5000, 2800, 290, 140, 800)]
-
-
-def polish(ops, deps, order, steps):
+def polish(ops, deps, order, qs, steps):
     n = len(ops)
-    qs = [o[0] for o in ops]
-    succ = [set() for _ in range(n)]
+    succ = [dict() for _ in range(n)]
     for i in range(n):
-        for j in deps[i]: succ[j].add(i)
-    cases = []
-    for gc, sc, f, dk, rz, rj, hop, slf, issue in CASES:
-        dur, hold = [0.0] * n, [0.0] * n
-        for i, (q, fn, r, w, c, kind) in enumerate(ops):
-            if kind == "c":
-                by = CACHE["index"].get(i)
-                if by: c = 60 + (c - 60) * (gc / GC if by == "g" else sc / SC)
-                dur[i] = hold[i] = c * f
-            elif kind == "d": hold[i], dur[i] = 1000.0 if q == "G" else 60.0, -c * dk
-            else: hold[i], dur[i] = issue, rz if int(kind[1:]) < 4 else rj if int(kind[1:]) < 12 else (rz + rj) / 2
-        cases.append((dur, hold, [[(j, slf if qs[j] == qs[i] else hop) for j, wt in deps[i].items() if wt] for i in range(n)]))
+        for j, hard in deps[i].items(): succ[j][i] = hard
+    after = [list(d.items()) for d in succ]
+    cases = [timing(ops, deps, c) for c in CASES]
 
-    def replay(case, seq, a, old):
-        dur, hold, pre = case
-        done, why, byq = (list(x) for x in old)
-        free, last, dma = {}, {}, 0.0
-        for i in seq[:a]:
-            last[qs[i]] = i
-            if dur[i] < 0: dma = done[i]
-        for q, i in last.items(): free[q] = byq[i] + hold[i]
-        for i in seq[a:]:
+    def near(rng):
+        d = {}
+        for k in rng:
+            d.setdefault(qs[order[k]], order[k])
+            if cases[0][3][order[k]]: d.setdefault("D", order[k])
+            if len(d) == 6: break
+        return d
+
+    def tails(case, ts, a, b, then):
+        dur, alt, hold, eng, hop, slf, pre = case
+        nxt = dict(then)
+        for i in reversed(order[a:b + 1]):
             q = qs[i]
-            t, w = free.get(q, 0.0), -2 - last.get(q, -1)
-            for j, e in pre[i]:
-                e += done[j]
-                if e > t: t, w = e, j
-            why[i], byq[i], free[q], last[q] = w, t, t + hold[i], i
-            if dur[i] < 0: done[i] = dma = max(dma, t + 2000.0) - dur[i]
-            else: done[i] = t + dur[i]
-        return done, why, byq
+            d = 2000.0 + eng[i] if eng[i] else alt[i] if q == "V" else dur[i]
+            t = 0.0
+            for s, hard in after[i]:
+                if qs[s] != q: e = hop + ts[s]
+                elif hard: e = slf + ts[s]
+                else: continue
+                if e > t: t = e
+            if eng[i]:
+                if "D" in nxt: t = max(t, ts[nxt["D"]] - 2000.0)
+                nxt["D"] = i
+            t += d
+            if q in nxt: t = max(t, (hold[i] or d) + ts[nxt[q]])
+            ts[i], nxt[q] = t, i
 
-    def bound(r):
+    def through(case, old, ts, win, q2, first, then, e):
+        dur, alt, hold, eng, hop, slf, pre = case
+        done, why, byq = list(old[0]), list(old[1]), list(old[2])
+        free = {q: byq[i] + hold[i] if hold[i] and q != "D" else done[i] for q, i in first.items()}
+        last, most, top = dict(first), 0.0, -1
+        for i in win:
+            q = q2[i]
+            t, w = free.get(q, 0.0), -2 - last.get(q, -1)
+            for j, hard in pre[i]:
+                if q2[j] != q: x = done[j] + hop
+                elif hard: x = done[j] + slf
+                else: continue
+                if x > t: t, w = x, j
+            why[i], byq[i], last[q] = w, t, i
+            if eng[i]:
+                free[q] = t + hold[i]
+                free["D"] = t = max(free.get("D", 0.0), t + 2000.0) + eng[i]
+                last["D"] = i
+            elif hold[i]: free[q], t = t + hold[i], t + dur[i]
+            else: free[q] = t = t + (alt[i] if q == "V" else dur[i])
+            done[i] = t
+            if t > most: most, top = t, i
+            for s, hard in after[i]:
+                if pos[s] > e:
+                    x = t + ts[s] + (hop if q2[s] != q else slf if hard else 0.0)
+                    if x > most: most, top = x, i
+        for q, i in then.items():
+            x = free.get(q, 0.0) + ts[i] - 2000.0 * (q == "D")
+            if x > most: most, top = x, last.get(q, -1)
+        return done, why, byq, most, top
+
+    def bound(r, lo):
         pairs = []
-        for done, why, byq in r:
-            i = done.index(max(done))
-            while i >= 0:
+        for done, why, byq, most, i in r:
+            while i >= 0 and pos[i] >= lo:
                 j = why[i]
                 if j < -1:
                     j = -2 - j
-                    if qs[i] != "S" and j not in deps[i]: pairs.append((i, j))
+                    if qs[i] != "S" and pos[j] >= lo: pairs.append((i, j))
                 i = j
         return pairs
 
-    now = [replay(c, order, 0, ([0.0] * n,) * 3) for c in cases]
-    base = [max(r[0]) for r in now]
-    best, pairs = float(len(cases)), bound(now)
     x = [OPT["seed"]]
     def draw(m):
         x[0] = (x[0] * 1103515245 + 12345) % 2147483648
         return (x[0] >> 8) % m
-    for _ in range(steps):
-        i, j = pairs[draw(len(pairs))]
-        a, b, k = order.index(j), order.index(i), (0, 0, 1, 2, 4)[draw(5)]
-        if draw(2):
-            while k and a > 0:
-                a -= 1
-                k -= qs[order[a]] == qs[i]
-            mv = [i]
-            for y in reversed(order[a:b]):
-                if not succ[y].isdisjoint(mv): mv.append(y)
-            if j in mv: continue
-            seq = order[:a] + mv[::-1] + [y for y in order[a:b] if y not in mv] + order[b + 1:]
-        else:
-            while k and b < n - 1:
-                b += 1
-                k -= qs[order[b]] == qs[i]
-            mv = [j]
-            for y in order[a + 1:b + 1]:
-                if any(z in deps[y] for z in mv): mv.append(y)
-            if i in mv: continue
-            seq = order[:a] + [y for y in order[a + 1:b + 1] if y not in mv] + mv + order[b + 1:]
-        r = [replay(c, seq, a, old) for c, old in zip(cases, now)]
-        s = sum(max(x[0]) / y for x, y in zip(r, base))
-        if s <= best + OPT["slack"]: best, order, now, pairs = s, seq, r, bound(r)
-    return order
+    wide, base, best = OPT["wide"], None, None
+    starts = list(range(0, n - wide // 2, wide // 2))
+    rounds = OPT["sweeps"] * len(starts)
+    for turn in range(rounds + 1):
+        pos = {y: k for k, y in enumerate(order)}
+        tl = [[0.0] * n for c in cases]
+        for c, ts in zip(cases, tl): tails(c, ts, 0, n, {})
+        now = [through(c, ([0.0] * n,) * 3, ts, order, qs, {}, {}, n) for c, ts in zip(cases, tl)]
+        base = base or [r[3] for r in now]
+        cur = sum(r[3] / y for r, y in zip(now, base))
+        if best is None or cur < best[0]: best = (cur, order, qs)
+        if turn == rounds: return best[1], best[2]
+        lo = starts[turn % len(starts)]
+        hi = min(n, lo + wide) - 1
+        end = near(range(hi + 1, n))
+        now = [through(c, r, ts, order[lo:hi + 1], qs, near(range(lo - 1, -1, -1)), end, hi) for c, r, ts in zip(cases, now, tl)]
+        pairs = bound(now, lo)
+        for step in range(steps // rounds if pairs else 0):
+            i, j = pairs[draw(len(pairs))]
+            a, b, k, how, q2 = pos[j], pos[i], (0, 0, 1, 2, 4, 8)[draw(6)], draw(OPT["mix"]), qs
+            if how >= 4:
+                y = (i, j)[draw(2)]
+                if y in CACHE["alt"] and how < 6:
+                    q2 = list(qs)
+                    q2[y] = "A" if qs[y] == "V" else "V"
+                elif how == 4: continue
+                a = b = pos[y]
+                if how > 4:
+                    b = max([pos[z] + 1 for z in deps[y]] + [a - OPT["far"], lo])
+                    b += draw(min([pos[z] - 1 for z in succ[y]] + [a + OPT["far"], hi]) - b + 1)
+                if b < a: a, b, win = b, a, [y] + order[b:a]
+                else: win = order[a + 1:b + 1] + [y]
+            elif j in deps[i]: continue
+            elif how & 1:
+                while k and a > lo:
+                    a -= 1
+                    k -= qs[order[a]] == qs[i]
+                mv = [i]
+                for y in reversed(order[a:b]):
+                    if any(z in succ[y] for z in mv): mv.append(y)
+                if j in mv: continue
+                win = mv[::-1] + [y for y in order[a:b] if y not in mv]
+            else:
+                while k and b < hi:
+                    b += 1
+                    k -= qs[order[b]] == qs[i]
+                mv = [j]
+                for y in order[a + 1:b + 1]:
+                    if any(z in deps[y] for z in mv): mv.append(y)
+                if i in mv: continue
+                win = [y for y in order[a + 1:b + 1] if y not in mv] + mv
+            most = cur + OPT["slack"] * (1 - turn / rounds) * draw(1000) / 500
+            first, then = near(range(a - 1, -1, -1)), near(range(b + 1, n))
+            if cur + sum((through(c, r, ts, win, q2, first, then, b)[3] - r[3]) / y for c, r, ts, y in zip(cases, now, tl, base)) > most: continue
+            r = [through(c, r, ts, win + order[b + 1:hi + 1], q2, first, end, hi) for c, r, ts in zip(cases, now, tl)]
+            s = sum(y[3] / z for y, z in zip(r, base))
+            if s <= most:
+                cur, order, qs, now = s, order[:a] + win + order[b + 1:], q2, r
+                for k, y in enumerate(win): pos[y] = a + k
+                for c, ts in zip(cases, tl): tails(c, ts, lo, b, then)
+                pairs = bound(r, lo) or pairs
 
 
 CACHE = {}
@@ -722,8 +913,8 @@ def rank_program(g, core, T, topo):
     ops = build(g, core, T, topo)
     if "o" not in CACHE:
         deps = depend(ops)
-        CACHE["o"] = (deps, polish(ops, deps, plan(ops, deps)[0], OPT["steps"]))
-    deps, order = CACHE["o"]
+        CACHE["o"] = (deps,) + polish(ops, deps, *plan(ops, deps), OPT["steps"])
+    deps, order, qs = CACHE["o"]
     at = {i: n for n, i in enumerate(order)}
     Q = {"V": g.vector, "A": g.scalar, "P": g.tensor, "G": g, "S": g.sync}
     token = {}
@@ -734,10 +925,11 @@ def rank_program(g, core, T, topo):
     ends = []
     for i in order:
         q, fn, r, w, c, kind = ops[i]
+        if qs[i] != q: q, fn = qs[i], CACHE["alt"][i][0]
         kn = known[q]
         need = {}
-        for j, wt in deps[i].items():
-            if wt:
+        for j, hard in deps[i].items():
+            if hard or qs[j] != q:
                 s, v = token[j]
                 if ops[j][5][0] == "r" and not any(a.startswith("land") for a in r): s = "ls" + s[2:]
                 if kn.get(s, 0) < v and need.get(s, (0, 0))[0] < v: need[s] = (v, j)

from concourse.mybir import AluOpType as ALU, AxisListType, ActivationFunctionType as AF

RO = 3
BIG, MAGIC = 2.0 ** 25, 12582912.0
DUM, FND, XW = 4096, 4224, 4736
TW = 4224
WAYS = {1: 'VAVAVAVA', 2: 'VAVAVAVA', 3: 'VAVAAVAV'}
AWAY = {1: 'AVAV', 2: 'AAAA', 3: 'AAAA'}
FWAY = {1: 'AAAA', 2: 'AAAA', 3: 'AAAA'}
SP = {1: 0, 2: 0, 3: 1}
HP = {1: 0, 2: 0, 3: 0, 4: 1}
BIAS = {}
OPT = {"seed": 2, "noise": 400.0, "passes": 12, "cut": 0, "steps": 100000, "slack": 0.004, "xu": 0,
       "nbf": 1, "pc": 1, "vb": 300, "hq": 1, "tq": 2, "mix": 7, "far": 80, "pw": 1, "up": 0, "al": 1, "xa": "", "wide": 160, "sweeps": 20}

F32, BF, F16, I32, U16 = "float32", "bfloat16", "float16", "int32", "uint16"
CB = "idb nidb hidb nhidb t85 i8k i83 i4k i2k i18 i254 m1x m7x m12x dg8 BO nBO Ex UT ones o16 uf tq lv2 kc n20 Pm0 Pm1 Pv0 Pv1 SJ0 SJ1 SJ2 SJ3".split()
SCRATCH = {}
for _n, _c, _d in [
    ("X", XW, BF), ("NB", 4096, I32), ("TR", TW, F32), ("TR3", TW, F32), ("cb", [len(CB), 128], BF),
    ("cf", 512, F32), ("c15", 512, F32), ("c4", 128, F32), ("Ks", 128, F32), ("io", [2, 48], F32), ("q4", 144, F32),
    ("pci", 8, I32), ("pf", 32, F32), ("wi", 4, I32), ("wf", 8, F32),
    ("idf", 128, F32), ("sndu", [4, 32], F16), ("landu", [4, 32], F16),
    ("W", [3, 144], BF), ("B8", 16, BF), ("diag", 512, BF), ("hold", 512, BF),
    ("rst", 128, F32), ("bcl", 8, U16), ("thc", 512, BF),
    ("MU", [2, 144], F16), ("cjb", 32, BF), ("scn", 128, F32), ("prm", 48, U16), ("pr2", 8, U16),
    ("offc", 768, F32), ("uwf", 16, F32), ("Dz", 16, F32), ("q25", 512, BF), ("nq", 512, BF), ("rs2", 576, BF), ("enl", 2, U16),
    ("vi", 128, I32), ("ai", 128, I32), ("ji", 32, I32),
    ("rep", [6, 128], F32), ("wsc", [6, 128], F32), ("wtm", 512, F16), ("vw", 56, U16), ("vd", 48, U16),
    ("dab", [2, 576], BF), ("low", [2, 576], BF), ("fst", [2, 16], F32), ("dm", [2, 8], F32),
    ("A1", [4, 128], F16), ("lst", [2 * RO, 128], U16), ("ltr", [2, 128], F32), ("Y", [4, 512], BF), ("nf", [1, 128], F16),
    ("G1", [4, 512], BF), ("ab1", [4, 512], BF), ("G2", [4, 512], BF), ("ab2", [4, 512], BF),
    ("m1", [2, 128], F32), ("e1", 128, F32), ("hit", 130, BF), ("sel", [RO, 128], F16), ("xn", [RO, 512], BF), ("xw", [RO, 128], BF), ("XU", FND, BF),
    ("mb", 128, BF), ("top", 128, BF), ("oh", 128, F16), ("K2", 256, F32), ("fl", 128, F32),
    ("g1", 512, F16), ("go", 24, U16), ("g3", 384, F32),
    ("land", [4, 576], BF), ("snd", [4, 576], BF), ("landj", 32, F32), ("sndj", 32, F32), ("jw", 32, U16), ("js", 32, U16),
    ("t2", 512, F32), ("KT", 512, F32), ("hT", 512, F32), ("pr", 512, F32), ("pt", 512, I32), ("hi", 512, I32), ("hoff", 512, U16),
    ("sk", 512, F32), ("xvj", 512, BF), ("xf", 512, BF), ("gsl", [4, 512], BF), ("lv", [10, 256, 4], BF), ("df", [10, 256, 4], BF), ("dp", [6, 512, 2], BF),
    ("ki", 32, I32), ("pi", 32, I32), ("ku", 32, I32), ("pu", 32, I32), ("um", 32, I32), ("vc", 32, I32), ("pw", 32, U16), ("ff", 48, BF),
    ("jf", 32, F32), ("tj", 32, F32), ("jb", 32, BF),
]:
    SCRATCH[_n] = ("sbuf", [128] + (list(_c) if isinstance(_c, list) else [_c]), _d)
if not OPT["xu"]: SCRATCH.pop("XU")
BANKS, ROWS16 = ("pC0", "pC1", "pD1", "pD2", "pM0", "pE", "pU", "pM1"), ("pC0", "pC1", "pU", "pM1")
for _n in BANKS:
    SCRATCH[_n] = ("psum", [128, 32, 16] if _n in ROWS16 else [128, 512], F32)
NDMA, NREM = 20, 28
SEMAPHORES = ["cV", "cA", "cP", "cG"] + ["d%d" % i for i in range(NDMA)] + ["ls%d" % i for i in range(NREM)] + ["rs%d" % i for i in range(NREM)]

OV = 30.0
CY, PC, GC, SC = 1.04, 0.5, 1.56, 3.8


def build(g, core, T, topo):
    ops = []
    V, A, P = g.vector, g.scalar, g.tensor
    rank = T.rank_of(core)
    N = len(T.cores)
    C = {n: T.cb[:, i] for i, n in enumerate(CB)}
    def rows(n, k): return T.cb[0:k, CB.index(n)]
    fixed = set(CB) | {"W", "B8", "MU", "thc", "q25", "nq", "cjb"}
    index, alt, part, size, label = {}, {}, {}, {}, [None]
    CACHE.update(index=index, alt=alt, part=part, size=size)
    def add(q, fn, r, w, c, kind="c"):
        if label[0]: part[len(ops)] = label[0]
        ops.append((q, fn, r.split(), w.split(), c, kind))
    def vc(n): return OV + max(64, n) * CY
    def gcst(n, by="g"):
        index[len(ops)] = by
        return 60 + n * (SC if by == "s" else GC) * CY
    def cp(o, i, r, w, n): add("V", lambda: V.tensor_copy(o, i), r, w, vc(n))
    def sct(o, i, r, w, n): add("V", lambda: V.tensor_copy(o, i), r, w, gcst(n, "s"))
    def tt(o, a, b, op, r, w, n, G=False): add("V", lambda: V.tensor_tensor(o, a, b, op), r, w, gcst(n, "t") if G else vc(n))
    def ts(o, a, s1, op0, r, w, n, s2=None, op1=None, G=False):
        if op1 is None: add("V", lambda: V.tensor_scalar(o, a, s1, None, op0), r, w, gcst(n) if G else vc(n))
        else: add("V", lambda: V.tensor_scalar(o, a, s1, s2, op0, op1), r, w, vc(n))
    def scan(o, a, b, op0, op1, r, w, n): add("V", lambda: V.tensor_tensor_scan(o, a, b, 0.0, op0, op1), r, w, vc(n))
    def red(o, a, op, r, w, n): add("V", lambda: V.tensor_reduce(o, a, AxisListType.X, op), r, w, vc(n))
    def tr(o, a, r, w, n): add("V", lambda: V.transpose(o, a), r, w, vc(n))
    def act(o, i, f, r, w, n, G=False, half=False, scale=1.0, bias=0.0):
        c = vc(n // (1 + half))
        if f is AF.Relu: alt[len(ops)] = (lambda: V.tensor_scalar(o, i, 0.0, scale, ALU.max, ALU.mult), c)
        elif f is AF.Copy and scale == 1.0: alt[len(ops)] = (lambda: V.tensor_copy(o, i), c)
        elif f is not AF.Abs: alt[len(ops)] = (lambda: V.tensor_scalar(o, i, scale, bias, ALU.mult, ALU.add), c)
        add("A", lambda: A.activation(o, i, f, bias=bias, scale=scale), r, w, gcst(n) if G else vc(n))
    def ms(o, c, w, n):
        alt[len(ops)] = (lambda: V.memset(o, c), vc(n // 2))
        add("A", lambda: A.activation(o, T.cf[:, 0:n], AF.Identity, bias=c, scale=0.0), "cf", w, vc(n))
    def mm(o, l, rh, st, sp, r, w, n):
        f, c = (lambda: P.matmul(o, l, rh, st, sp)), max(64, n) * PC
        if ops[-1][0] == "P" and ops[-1][3] == [w] and set(r.split()) - fixed <= set(ops[-1][2]):
            _, f0, r0, w0, c0, _ = ops.pop()
            def both():
                f0()
                return f()
            ops.append(("P", both, r0 + [x for x in r.split() if x not in r0], w0, c0 + c, "c"))
        else: add("P", f, r, w, c)
    def dma(o, i, r, w, kb, q="S"): add(q, lambda: (g.sync if q == "S" else g.scalar).dma_start(o, i), r, w, kb, "d")
    def iota(o, pat, base, cm, w, n):
        add("G", lambda: g.iota(o, pat, base, cm, allow_small_or_imprecise_dtypes=True), "", w, 130 + 2 * n * CY)
    def ps(b, a, e): return T[b][:, a // 16:e // 16] if b in ROWS16 else T[b][:, a:e]
    def shift(k, s): return T.W[:, k, 15 - s:143 - s]
    def nm(x, a, b): return " ".join("%s_%d" % (x, h) for h in range(a, b))
    def send(k, hop, what, a=0, b=2):
        dst = T.cores[(rank + hop) % N]
        rid, pid, _ = topo.addr(dst)
        en = topo.engines(core, dst)
        if 0 < k < RO: en = en[what != "z"::2]
        m, n = sum(1 << e for e in en), len(size)
        x, lo, hi = {"z": ("", 256 * a, 256 * b), "j": ("", 512 + 16 * a, 512 + 16 * b), "zj": ("", 0, 544), "u": ("u", 16 * a, 16 * b),
                     "c": ("", 544 + 16 * a, 544 + 16 * b), "w": ("u", 0, 1), "f": ("j", 0, 32)}[what]
        o, i = (T[y + x][:] if x == "j" else T[y + x][:, k, lo:hi] for y in ("land", "snd"))
        size[len(ops)] = (hi - lo) / 128.0 / len(en)
        add("G", lambda: g.remote_dma(o, i, T.sem["rs%d" % n], T.sem["ls%d" % n], pid, rid, m),
            *(" ".join(nm("%s%s:%s%d" % (y, x, z, k), a, b) for z in what) for y in ("snd", "land")), len(en), "r%d" % n)
    eq, mul, ad, sub, AND, SHR = ALU.is_equal, ALU.mult, ALU.add, ALU.subtract, ALU.bitwise_and, ALU.logical_shift_right
    X1, XD, X2 = T.X[:, 0:DUM], T.X[:, 0:FND], T.X[:]

    dma(T.vi[0:8, :], T.v0[:], "", "vi", 4)
    if not OPT["al"]: dma(T.ai[:], T.a0[:], "", "ai", 64)
    dma(T.Y[:, 0, 0:128], T.y0[:], "", "Y:0", 32, "A")
    dma(T.ji[:, 0:16], T.j0[0::2, :], "", "ji:0", 8, "A")
    dma(T.ji[:, 16:32], T.j0[1::2, :], "", "ji:1", 8, "A")
    dma(T.wi[:, 0:1], T.w[:], "", "wi:0", 4)
    big = [(X1, T.x[:], "", "X:b", 1024), (T.NB[:], T.nb[:], "", "NB", 2048)]
    for a in big[::-1] if OPT["nbf"] else big: dma(*a)
    if OPT["al"]: dma(T.ai[:], T.a0[:], "", "ai", 64)
    dma(T.snd[:, 0, 0:512], T.z0[:], "", nm("snd:z0", 0, 2), 128)

    add("G", lambda: g.iota(T.pci[:, 0:1], [[0, 1]], 0, 1), "", "pci:0", 132)
    iota(T.cf[:], [[1, 512]], 0, 0, "cf", 512)
    iota(T.c4[:], [[1, 8], [0, 16]], 0, 0, "c4", 128)
    iota(T.c15[:], [[0, 32], [1, 16]], 0, 0, "c15", 512)
    iota(T.e1[:], [[1, 16], [16, 2], [32, 4]], 0, 0, "e1", 128)
    iota(T.Ks[:], [[16, 4], [0, 2], [-1, 16]], 15, 0, "Ks", 128)
    iota(T.q4[:], [[1, 36], [0, 4]], 0, 0, "q4", 144)
    iota(T["io"][:, 0, 0:32], [[1, 8], [8, 2], [256, 2]], 1, 0, "io:0", 32)
    iota(T["io"][:, 0, 32:48], [[1, 4], [4, 4]], 1, 0, "io:0", 16)
    iota(T["io"][:, 1, 0:32], [[0, 16], [16, 2]], 0, 0, "io:1", 32)
    iota(T.pr[:], [[1, 8], [8, 2], [0, 32]], 1, 0, "pr", 512)
    iota(T.sk[:, 0:256], [[1, 4], [4, 4], [0, 16]], 1, 0, "sk", 256)
    for b in ("TR", "TR3"):
        for k in range(6): iota(T[b][:, 704 * k:704 * k + 704], [[1, 704]], 704 * k, 0, "%s:%d" % (b, k), 704)
    act(T.offc[:, 0:512], T.pr[:], AF.Identity, "pr", "offc:0", 512, scale=-1.0, bias=0.5)
    act(T.offc[:, 512:768], T.sk[:, 0:256], AF.Identity, "sk", "offc:1", 256, scale=-1.0, bias=0.5)
    ms(T.rs2[:, 0:288], 0.0, "rs2", 288); ms(T.rs2[:, 288:576], 0.0, "rs2", 288)
    for c in range(8): ms(T.rs2[:, 8 * c * (c + 1):8 * c * (c + 1) + 1], 1048576.0, "rs2:%d" % c, 1)
    for b in ("lv", "df"):
        for k in (8, 9): ms(T[b][:, k, :, 0], 0.0, "%s:%d_0" % (b, k), 256)
    ts(T.pci[:, 1:2], T.pci[:, 0:1], 15, AND, "pci:0", "pci:1", 1)
    ts(T.pci[:, 2:3], T.pci[:, 0:1], 4, SHR, "pci:0", "pci:2", 1)
    ts(T.pci[:, 3:4], T.pci[:, 0:1], 4, SHR, "pci:0", "pci:3", 1, 1, AND)
    ts(T.pci[:, 4:5], T.pci[:, 0:1], 5, SHR, "pci:0", "pci:4", 1)
    cp(T.pf[:, 0:5], T.pci[:, 0:5], "pci", "pf:0", 5)
    def col(i): return T.pf[:, i:i + 1]
    cP, cR, cG, cB, cA = (col(i) for i in range(5))
    def pcol(i, src, m, a, r="pf:0"): act(col(i), src, AF.Identity, r, "pf:%d" % i, 1, scale=m, bias=a)
    pcol(5, cG, 16.0, 15.0)
    pcol(6, cB, 4096.0, 0.0)
    pcol(7, cB, -4096.0, 4096.0)
    ms(C["o16"], 2.0 ** 29, "o16", 128)
    ms(T.ff[:, 32:48], 0.0, "ff:c", 16)
    ms(T.ff[:, 32:33], -15.0 / 256, "ff:c", 1)
    ts(col(8), cR, 0.0, eq, "pf:0", "pf:8", 1, 2048.0, mul)
    pcol(26, cR, -1.0, 0.5)
    pcol(9, col(26), 1.0, col(8), "pf:8 pf:26")
    pcol(12, cB, -1.0, 1.0)
    pcol(13, cA, 16.0, cR)
    pcol(14, cA, 16.0, 15.0)
    pcol(15, cG, 4.0, 3.0)
    pcol(16, cA, 32.0, cR); pcol(17, col(16), 1.0, 16.0, "pf:16")
    pcol(18, cR, 1.0, FND - 2048.0)
    pcol(19, cR, 16.0, 0.0)
    ms(C["ones"], 1.0, "ones", 128)
    cBm = (col(12), cB)
    c128 = T.cf[:, 0:128]
    ts(C["Ex"], T.c4[:], cP, eq, "c4 pf:0", "Ex", 128)
    ts(T.t2[:], T.c15[:], cR, eq, "c15 pf:0", "t2", 512)
    act(T.diag[:], T.t2[:], AF.Identity, "t2", "diag", 512, scale=-6144.0, bias=8192.0)
    act(C["dg8"], T.t2[:, 0:128], AF.Copy, "t2", "dg8", 128, scale=8192.0)
    ts(T.hold[:], T.c15[:], 0.0, eq, "c15", "hold", 512, -1048576.0, mul)
    ts(T.idf[:], c128, cP, eq, "cf pf:0", "idf", 128)
    for n, s in (("idb", 1.0), ("nidb", -1.0), ("hidb", .5), ("nhidb", -.5), ("i8k", 8192.0), ("i83", 8320.0 * 4096), ("i4k", 4096.0), ("i2k", 2048.0), ("i18", 2.0 ** 18),
                 ("i254", 254.0), ("m1x", 4 * MAGIC), ("m7x", 512 * MAGIC), ("m12x", 16384 * MAGIC)):
        act(C[n], T.idf[:], AF.Copy, "idf", n, 128, scale=s)
    ts(T.W[:, 0], T.cf[:, 0:144], col(5), eq, "cf pf:5", "W:0", 144, BIG, mul)
    act(T.W[:, 1], T.W[:, 0], AF.Copy, "W:0", "W:1", 144, half=True, scale=-1.0)
    ts(T.W[:, 2], T.q4[:], col(15), eq, "q4 pf:15", "W:2", 144, BIG, mul)
    for i, s in enumerate((16.0, -16.0)): ts(T.B8[:, 8 * i:8 * i + 8], T.cf[:, 0:8], cG, eq, "cf pf:0", "B8:%d" % i, 8, s, mul)
    ts(C["BO"], T.c4[:], cG, eq, "c4 pf:0", "BO", 128)
    act(T.rst[:], T.hold[:, 0:128], AF.Copy, "hold", "rst", 128, scale=-16.0)
    act(C["kc"], T.c15[:, 0:128], AF.Copy, "c15", "kc", 128)
    ms(C["n20"], -2.0 ** -20, "n20", 128)
    ms(T.hit[:, 0:2], 1.0, "hit:1", 2)
    ts(T.bcl[:], T.cf[:, 0:128:16], 15.0, ad, "cf", "bcl", 8)
    pcol(22, cP, 1.0, -1.0); pcol(23, cP, -15.0, 16.0); pcol(24, cP, 84.5 * BIG, -85 * BIG)
    pcol(27, cP, -1.0, 1.0); pcol(28, cP, -18 * BIG, -102 * BIG)
    act(T.thc[:], T.c15[:], AF.Identity, "c15 pf:22 pf:23", "thc", 512, scale=col(22), bias=col(23))
    act(C["t85"], C["ones"], AF.Identity, "ones pf:24", "t85", 128, scale=col(24))
    act(C["lv2"], T.c15[:, 0:128], AF.Identity, "c15 pf:27", "lv2", 128, scale=col(27), bias=1.0)
    act(C["tq"], C["ones"], AF.Identity, "ones pf:28", "tq", 128, scale=col(28))
    ts(T.mb[:], c128, cP, ALU.is_lt, "cf pf:0", "mb", 128, -1.0, mul)
    tt(T.mb[:], T.mb[:], C["BO"], mul, "mb BO", "mb", 256)
    tt(C["UT"], T.mb[:], T.idf[:], ad, "mb idf", "UT", 256)
    act(C["nBO"], C["BO"], AF.Copy, "BO", "nBO", 128, half=True, scale=-2048.0)
    for b in range(2):
        ts(C["Pm%d" % b], T.Ks[:], col(13), eq, "Ks pf:13 pf:12 pf:0", "Pm%d" % b, 128, cBm[b], mul)
        ts(C["Pv%d" % b], T.Ks[:], col(14), eq, "Ks pf:14 pf:6 pf:7", "Pv%d" % b, 128, col(7 - b), mul)
        for q in range(2):
            ts(C["SJ%d" % (2 * b + q)], c128, col(16 + q), eq, "cf pf:16 pf:17 pf:12 pf:0", "SJ%d" % (2 * b + q), 128, cBm[b], mul)
    ts(T.wf[:, 0:1], T.wi[:, 0:1], 2048.0, ALU.is_ge, "wi:0", "wf:0", 1, -4096.0, mul)
    tt(T.sndu[:, RO, 0:1], T.wf[:, 0:1], T.wi[:, 0:1], ad, "wf:0 wi:0", "sndu:w%d_0" % RO, 1)
    send(RO, -1, "w", 0, 1)
    cp(T.wf[:, 1:2], T.landu[:, RO, 0:1], "landu:w%d_0" % RO, "wf:1", 1)
    ts(T.MU[:, 0], T.cf[:, 0:144], col(5), eq, "cf pf:5 wf:1", "MU:0", 144, T.wf[:, 1:2], mul)
    ts(T.MU[:, 1], T.MU[:, 0], -1.0, mul, "MU:0", "MU:1", 72)
    act(T.scn[:, 96:128], T.cf[:, 0:32], AF.Identity, "cf pf:18", "scn:3", 32, scale=16.0, bias=col(18))
    ts(T.prm[:], T["io"][:, 0], col(19), ad, "io:0 pf:19", "prm", 48)
    tt(T.wtm[:, 0:128], T.e1[:], T.diag[:, 0:128], sub, "e1 diag", "wtm", 256)
    scan(T.g1[:, 0:128], T.hold[:, 0:128], T.wtm[:, 0:128], ad, ALU.max, "hold wtm", "g1", 64)
    ts(T.pr2[:], T.g1[:, 15:128:16], 2048.0, ad, "g1", "pr2", 8)
    act(T.cjb[:], T["io"][:, 1, 0:32], AF.Copy, "io:1", "cjb", 32, scale=8.0)
    act(C["uf"], c128, AF.Identity, "cf", "uf", 128, scale=1.0 / 256)
    pcol(10, cR, 8.0, 24.0)
    act(col(11), col(10), AF.Identity, "pf:10 pf:0", "pf:11", 1, scale=cR, bias=15.0)
    ts(T.enl[:, 0:1], col(11), 575.0, ALU.min, "pf:11", "enl", 1)
    act(T.Dz[:], T.cf[:, 0:16], AF.Identity, "cf pf:0", "Dz", 16, scale=16.0, bias=cR)
    act(T.uwf[:], T.Dz[:], AF.Identity, "Dz", "uwf", 16, scale=1.0 / 256)
    act(T.Dz[:, 8:16], T.Dz[:, 0:8], AF.Identity, "Dz", "Dz", 8, bias=DUM + 4096.0)
    act(T.Dz[:, 0:8], T.Dz[:, 0:8], AF.Identity, "Dz", "Dz", 8, bias=DUM + 6144.0)
    ms(T.q25[:], 0.25, "q25", 512); ms(T.nq[:], -0.25, "nq", 512)
    ms(T.X[:, DUM:FND], 0.0, "X:d", 128)
    ms(T.X[:, FND:XW], 0.0, nm("X:q", 0, 2), 512)
    idb, nidb = C["idb"], C["nidb"]

    def whole(p, pn, n, x, stop):
        mm(p, C[x], T.q25[:, 0:n], False, False, x + " q25", pn, n)
        mm(p, C[x], T.nq[:, 0:n], False, stop, x + " nq", pn, n)

    VW = (0, 8, 24, 48)
    def vw(t): return T.vw[:, VW[t]:VW[t] + 8]

    def finish(terms, pn, pw, i):
        e = int(i > RO)
        off = 2048.0 * (1 + e)
        p0, p1, p2 = ps(pn, 0, 128), ps(pw, 128, 256), ps(pn, 256, 384)
        mm(p1, idb, C["dg8"], True, False, "idb dg8", pw, 128)
        for n, (l, rh, r) in enumerate(terms): mm(p1, l, rh, False, n == len(terms) - 1, r, pw, 128)
        for n, (l, rh, r) in enumerate(terms): mm(p0, l, rh, n == 0, n == len(terms) - 1, r, pn, 128)
        for n, (l, rh, r) in enumerate(terms): mm(p2, l, rh, n == 0, False, r, pn, 128)
        mm(p2, idb, C["uf"], False, False, "idb uf", pn, 128)
        mm(p2, C["i8k"], C["ones"], False, True, "i8k ones", pn, 128)
        scan(T.wsc[:, i], T.hold[:, 0:128], p1, ad, ALU.max, "hold " + pw, "wsc:%d" % i, 128)
        wv = T.wsc[:, i, 15::16]
        if not e: ts(vw(i), wv, off - 8192.0, ad, "wsc:%d" % i, "vw:%d" % i, 8)
        for c in range(8):
            n, a = 16 * c + 16, 8 * c * (c + 1)
            act(T.dab[:, e, a:a + n], ps(pn, 256, 256 + n), AF.Abs, pn + " wsc:%d" % i, "dab:%d_%d" % (e, c), n, scale=-1.0, bias=T.wsc[:, i, 16 * c + 15:16 * c + 16])
        act(T.rep[:, i], p0, AF.Identity, pn, "rep:%d" % i, 128, bias=off)
        scan(T.low[:, e], T.rs2[:], T.dab[:, e], ad, ALU.min, "rs2 " + " ".join("dab:%d_%d" % (e, c) for c in range(8)), "low:%d" % e, 288)
        tt(T.fst[:, e], T.low[:, e].indirect(T.enl[:, 0:1]), T.uwf[:], ALU.not_equal, "low:%d enl uwf" % e, "fst:%d" % e, 16, True)
        dm, dn = T.dm[:, e], "dm:%d" % e
        tt(dm, T.fst[:, e, 0:8], T.Dz[:, 8 * e:8 * e + 8], mul, "Dz fst:%d" % e, dn, 16)
        tt(dm, dm, wv, ALU.max, dn + " wsc:%d" % i, dn, 16)
        ts(T.vd[:, 8 * i:8 * i + 8], dm, off - 8192.0, ad, dn, "vd:%d" % i, 8)

    def turn(buf, k, e, t, pn):
        for b in range(2):
            for q in range(2):
                mm(T[pn][:, b:8:2, :], C["SJ%d" % (2 * b + q)], T[buf][:, k, 64 * q:64 * q + 64], q == 0, q == 1, "%s:%d SJ%d" % (buf, k, 2 * b + q), pn, 64)
        tr(T.ltr[:, e], ps(pn, 0, 128), pn, "ltr:%d" % e, 128)
        n = 2 * (t - 1) + e
        ts(T.lst[:, n], T.ltr[:, e].indirect(T.pr2[:]), 2048.0, ad, "ltr:%d pr2" % e, "lst:%d" % n, 128, G=True)

    def four(buf, k):
        name = "%s:%d" % (buf, k)
        act(T[buf][:, k, 128:256], T[buf][:, k, 0:128], AF.Copy, name, name + "x", 128, half=True)
        act(T[buf][:, k, 256:512], T[buf][:, k, 0:256], AF.Copy, name + " " + name + "x", name + "x", 256, half=True)

    ts(T.oh[0:8, :], T.vi[0:8, :], -2048.0, ad, "vi", "oh", 128)
    finish([(rows("Ex", 8), T.oh[0:8, :], "Ex oh")], "pD1", "pD2", 0)
    ts(T.A1[:, 0], T.ai[:], -2048.0, ad, "ai", "A1:0", 128)
    cp(T.jb[:], T.ji[:], "ji", "jb", 32)
    tr(T.snd[:, 0, 512:544], T.jb[:], "jb", nm("snd:j0", 0, 2), 32)
    send(0, 1, "zj")

    def ahead(t): return (T.XU[:, 0:DUM], "XU ") if t == RO and OPT["xu"] else (X1, "X:b ")

    def copy_x(t):
        dma(T.XU[:], XD, "X:b X:d", "XU", 1056)
    def step_x(t): sct(T.XU[:].indirect(T.vd[:, 8 * t:8 * t + 8]), T.xw[:, t - 1], "xw:%d vd:%d" % (t - 1, t), "XU", 128)

    def gathers(t, e, ways, win, wn):
        Gn, n = ("G1", "G2")[e], 2 * (t - 1) + e
        for c, way in enumerate(ways):
            if way in "AC": act(T[Gn][:, c], win.indirect(T.lst[:, n, 32 * c:32 * c + 32]), AF.Copy, wn + "lst:%d" % n, "%s:%d" % (Gn, c), 512, True)

    def sizes(t, e, ways, win, wn, buf, k, banks):
        ref, ref4, rn, n = T[buf][:, k, 0:128], T[buf][:, k], "%s:%d" % (buf, k), 2 * (t - 1) + e
        Gn, an = ("G1", "G2")[e], ("ab1", "ab2")[e]
        early, late = [], []
        for c, way in enumerate(ways):
            pn, o, on, a, am = banks[c % len(banks)], T[Gn][:, c], "%s:%d" % (Gn, c), T[an][:, c], "%s:%d" % (an, c)
            if way in "AC":
                if e == 0:
                    for i in range(4): mm(ps(pn, 128 * i, 128 * i + 128), nidb, ref, i == 0, False, "nidb " + rn, pn, 128)
                    mm(T[pn][:], idb, o, False, True, "idb " + on, pn, 512)
                else:
                    mm(T[pn][:], idb, o, True, False, "idb " + on, pn, 512)
                    for i in range(4): mm(ps(pn, 128 * i, 128 * i + 128), nidb, ref, False, i == 3, "nidb " + rn, pn, 128)
                if way == "A": act(a, T[pn][:], AF.Abs, pn, am, 512)
                else: act(a, T[pn][:], AF.Relu, pn, am, 512, scale=2.0)
            else:
                tt(o, win.indirect(T.lst[:, n, 32 * c:32 * c + 32]), ref4, sub, wn + "lst:%d %s %sx" % (n, rn, rn), on, 512, True)
                if way == "V": act(a, o, AF.Relu, on, am, 512, half=True, scale=2.0)
                else: act(a, o, AF.Abs, on, am, 512)
            if way in "CV": early += [(4 * c + i, 1, T[Gn][:, c, 128 * i:128 * i + 128], on) for i in range(4)]
            late += [(4 * c + i, 0, T[an][:, c, 128 * i:128 * i + 128], am) for i in range(4)]
        return early + late

    def users_a(t):
        o = t - 1
        yo, yn = T.Y[:, o, 0:128], "Y:%d" % o
        win, wn = ahead(t)
        if set(AWAY[t]) & set("VM"): four("Y", o)
        ts(T.nf[:, 0], T.NB[:].indirect(vw(o)), -2048.0, ad, "NB vw:%d" % o, "nf:0", 128, G=True)
        turn("nf", 0, 0, t, "pC0")
        gathers(t, 0, AWAY[t], win, wn)
        terms = sizes(t, 0, AWAY[t], win, wn, "Y", o, ("pC0", "pC1", "pE", "pM1") if t == 1 else ("pC1", "pC0"))
        mm(ps("pD1", 0, 128), idb, C["kc"], True, False, "idb kc", "pD1", 128)
        terms = [(k, 0, yo, yn) for k in range(16) if AWAY[t][k // 4] == "C"] + terms
        for n, (k, s, tile, tn) in enumerate(terms):
            mm(T.pD1[:, k:128:16], tile, T.B8[:, 8 * s:8 * s + 8], False, n == len(terms) - 1, "B8 " + tn, "pD1", 64)
        for i in range(2): scan(T.m1[:, i], T.rst[:], ps("pD1", 0, 128), ad, ALU.min, "rst pD1", "m1:%d" % i, 128)
        tt(T.hit[:, 2:130], T.m1[:, 0].indirect(T.bcl[:]), T.m1[:, 1], eq, "m1 bcl", "hit:0", 128, True)
        mm(ps("pD1", 384, 512), T.hold[0:1, 0:128], rows("n20", 1), True, False, "hold n20", "pD1", 128)
        mm(ps("pD1", 384, 512), T.hit[:, 2:130], idb, False, False, "hit idb", "pD1", 128)
        mm(ps("pD1", 384, 512), T.hit[:, 1:129], nidb, False, True, "hit nidb", "pD1", 128)
        tt(T.sel[:, o], ps("pD1", 384, 512), T.nf[:, 0], mul, "pD1 nf:0", "sel:%d" % o, 128)
        finish([(C["BO"], T.sel[:, o], "BO sel:%d" % o)], "pD1", "pM0" if t <= OPT["pw"] else "pD1", t)
        xn, xm = T.xn[:, o, 0:128], "xn:%d" % o
        act(xn, win.indirect(vw(t)), AF.Copy, wn + "vw:%d" % t, xm, 128, True)
        if set(FWAY[t]) & set("VM"): four("xn", o)

    def users_y(t):
        o = t - 1
        yo, yn, xn, xm = T.Y[:, o, 0:128], "Y:%d" % o, T.xn[:, o, 0:128], "xn:%d" % o
        pn = "pC0" if t > 1 else "pU"
        mm(ps(pn, 256, 384), idb, xn, True, False, xm + " idb", pn, 128)
        mm(ps(pn, 256, 384), nidb, yo, False, True, yn + " nidb", pn, 128)
        mm(ps(pn, 384, 512), C["hidb"], xn, True, False, xm + " hidb", pn, 128)
        mm(ps(pn, 384, 512), C["hidb"], yo, False, False, yn + " hidb", pn, 128)
        mm(ps(pn, 384, 512), nidb, T.q25[:, 0:128], False, False, "q25 nidb", pn, 128)
        whole(ps(pn, 384, 512), pn, 128, "m1x", True)
        act(T.xw[:, o], ps(pn, 384, 512), AF.Copy, pn, "xw:%d" % o, 128)
        act(T.Y[:, t, 0:128], ps(pn, 256, 384), AF.Abs, pn, "Y:%d" % t, 128)

    def users_g(t):
        turn("A1", t - 1, 1, t, "pC1")
        gathers(t, 1, FWAY[t], X1, "X:b ")

    def users_far(t):
        o = t - 1
        Ao, an, sn = T.A1[:, o], " A1:%d" % o, " sel:%d" % o
        terms = sizes(t, 1, FWAY[t], X1, "X:b ", "xn", o, ("pC0", "pC1", "pE", "pM1") if t == 1 else ("pC1", "pC0"))
        mm(ps("pD2", 128, 256), C["BO"], T.sel[:, o], True, False, "BO" + sn, "pD2", 128)
        mm(ps("pD2", 128, 256), nidb, Ao, False, True, "nidb" + an, "pD2", 128)
        mm(ps("pD2", 384, 512), idb, Ao, True, True, "idb" + an, "pD2", 128)
        mm(ps("pD2", 0, 128), rows("lv2", 2), rows("tq", 2), True, False, "lv2 tq", "pD2", 128)
        for c in range(4):
            if FWAY[t][c] == "C": mm(ps("pD2", 0, 128), T.W[:, 2, 12 - 4 * c:140 - 4 * c], T.xn[:, o, 0:128], False, False, "W xn:%d" % o, "pD2", 128)
        for n, (l, s, tile, tn) in enumerate(terms): mm(ps("pD2", 0, 128), shift(s, l), tile, False, n == len(terms) - 1, "W " + tn, "pD2", 128)

    def users_b(t):
        o = t - 1
        for b in range(2):
            mm(ps("pM0", 128 * b, 128 * b + 128), C["Pv%d" % b], T.sel[:, o], b == 0, False, "Pv%d sel:%d" % (b, o), "pM0", 128)
        if t == 1: ts(T.mb[:], ps("pD2", 0, 128), -120 * BIG, ALU.is_gt, "pD2", "mb", 128)
        else: ts(T.mb[:], ps("pD2", 0, 128), col(25), ad, "pD2 pf:25 pf:21", "mb", 128, col(21), ALU.is_gt)
        tt(T.fl[:], T.mb[:], ps("pD2", 128, 256), mul, "mb pD2", "fl", 128)
        tt(T.A1[:, t], T.fl[:], ps("pD2", 384, 512), ad, "fl pD2", "A1:%d" % t, 128)
        for b in range(2):
            mm(ps("pM0", 128 * b, 128 * b + 128), C["Pm%d" % b], T.A1[:, t], False, b == 1, "Pm%d A1:%d" % (b, t), "pM0", 128)
        act(T.K2[:], ps("pM0", 0, 256), AF.Identity, "pM0 pf:9", "K2", 256, scale=1.0 / 4096, bias=col(9))
        if t == RO: ts(T.fl[:], T.A1[:, t], 2048.0, ad, "A1:%d" % t, "fl", 128)
        sct(XD.indirect(T.vd[:, 8 * t:8 * t + 8]), T.xw[:, o], "xw:%d vd:%d" % (o, t), "X:b X:d", 128)
        if t == RO - 2 and OPT["xu"]: copy_x(t)
        if t > 1:
            i = 2 + t
            mm(ps("pD2", 256, 384), C["UT"], T.mb[:], True, True, "UT mb", "pD2", 128)
            ts(T.top[:], ps("pD2", 256, 384), 1.0, eq, "pD2", "top", 128)
            tt(T.oh[:], T.top[:], ps("pD2", 384, 512), mul, "top pD2", "oh", 128)
            finish([(C["nBO"], T.top[:], "nBO top oh"), (C["BO"], T.oh[:], "BO oh top")], "pD2", "pD2", i)
            sct(T.TR[:].indirect(T.vd[:, 8 * i:8 * i + 8]), T.rep[:, i], "rep:%d vd:%d" % (i, i), "TR", 128)
        sct(T.TR[:].indirect(T.vd[:, 8 * o:8 * o + 8]), T.rep[:, t], "rep:%d vd:%d" % (t, o), "TR", 128)
        n = 128 * t
        on = " ".join("vw:%d" % i for i in range(o))
        if t == 1: off, on = vw(1), "vw:1"
        else: off = T.vw[:, 0:8 * o]
        for h in range(1 if t == 1 else 0, 2):
            m = n - 128 * (h == 0)
            tt(T.wtm[:, 0:m], T.TR[:].indirect(off), T.diag[:, 0:m], sub, "TR diag " + on, "wtm", m, True)
            scan(T.g1[:, 0:m], T.hold[:, 0:m], T.wtm[:, 0:m], ad, ALU.max, "hold wtm", "g1", m // 2)
            b, a, on = (T.go, 0, "go") if h else (T.vw, VW[t] - 8 * o, "vw:g%d" % t)
            ts(b[:, a:a + m // 16], T.g1[:, 15:m:16], 2048.0, ad, "g1", on, 8 * t)
            off, on = b[:, a:a + 8 * t], on + (" vw:%d" % t) * (1 - h)
        act(T.g3[:, 0:n], T.TR[:].indirect(off), AF.Copy, "TR " + on, "g3", n, True)
        for i in range(t):
            sct(T.TR3[:].indirect(T.vd[:, 8 * i:8 * i + 8]), T.g3[:, 128 * i:128 * i + 128], "g3 vd:%d" % i, "TR3", 128)
        if t == RO:
            dma(T.yt[:], T.TR[0:128:16, 0:4096], "TR", "", 128)
            dma(T.ya[:], T.fl[:], "fl", "", 64)
            dma(T.yy[:], T.Y[:, t, 0:128], "Y:%d" % t, "", 32)
            dma(T.yv[:], T.rep[0:128:16, t], "rep:%d" % t, "", 4)

    def make_u(k, a, b):
        c, n = slice(16 * a, 16 * b), 16 * (b - a)
        p, zn, un = ps("pU", 16 * a, 16 * b), nm("snd:z%d" % k, a, b), nm("sndu:u%d" % k, a, b)
        if OPT["up"]:
            mm(p, C["i8k"], T.nq[:, 0:n], True, False, "i8k nq", "pU", n)
            mm(p, C["hidb"], T.cb[:, CB.index("ones"), 0:n], False, False, "hidb ones", "pU", n)
            for y in range(2):
                for s0 in range(16): mm(p, T.MU[:, y, 15 - s0:143 - s0], T.snd[:, k, 256 * a + s0:256 * b:16], False, False, "MU " + zn, "pU", n)
                if y == 0: whole(p, "pU", n, "m12x", False)
            mm(p, C["i8k"], T.q25[:, 0:n], False, True, "i8k q25", "pU", n)
            ts(T.sndu[:, k, c], p, -1.0, mul, "pU", un, n)
        else:
            for s0 in range(16): mm(p, T.MU[:, 0, 15 - s0:143 - s0], T.snd[:, k, 256 * a + s0:256 * b:16], s0 == 0, s0 == 15, "MU " + zn, "pU", n)
            cp(T.ku[:, c], p, "pU", nm("ku:", a, b), n)
            ts(T.pu[:, c], T.ku[:, c], 4095, AND, nm("ku:", a, b), nm("pu:", a, b), n)
            ts(T.sndu[:, k, c], T.pu[:, c], -2048.0, ad, nm("pu:", a, b), un, n)
        send(k, 1, "u", a, b)
        mm(p, C["i254"], T.nq[:, 0:n], True, False, "i254 nq", "pU", n)
        mm(p, idb, T.sndu[:, k, c], False, False, "idb " + un, "pU", n)
        whole(p, "pU", n, "m7x", False)
        mm(p, nidb, T.sndu[:, k, c], False, False, "nidb " + un, "pU", n)
        mm(p, idb, T.snd[:, k, 512 + 16 * a:512 + 16 * b], False, True, "idb " + nm("snd:j%d" % k, a, b), "pU", n)
        act(T.snd[:, k, 544 + 16 * a:544 + 16 * b], p, AF.Copy, "pU", nm("snd:c%d" % k, a, b), n, scale=-1.0)
        send(k, 1, "c", a, b)

    def seek_head(t, a, b):
        k, c, s, n = t - 1, slice(16 * a, 16 * b), slice(256 * a, 256 * b), 16 * (b - a)
        def h_(x): return nm(x, a, b)
        L, J, U = h_("land:z%d" % k), h_("land:j%d" % k), h_("landu:u%d" % k)
        mm(ps("pM1", 16 * a, 16 * b), idb, T.cjb[:, 0:n], True, False, "idb cjb", "pM1", n)
        for x in range(2):
            for q in range(2):
                mm(T.pM1[:, a:b, x::2], C["SJ%d" % (2 * x + q)], T.land[:, k, 512 + 16 * a + q:512 + 16 * b:2], False, x + q == 2, "SJ%d %s" % (2 * x + q, J), "pM1", 16)
        cp(T.jw[:, c], ps("pM1", 16 * a, 16 * b), "pM1", h_("jw:"), n)
        act(T.t2[:, s], T.K2[:].indirect(T.jw[:, c]), AF.Copy, "K2 " + h_("jw:"), h_("t2:"), 16 * n, True)
        tr(T.KT[:, s], T.t2[:, s], h_("t2:"), h_("KT:"), 16 * n)
        pu = "pM1" if SP[t] else "pE"
        for pn, x in ((pu, "i83"), ("pU", "i18")):
            mm(ps(pn, 256 * a, 256 * b), C[x], T.q25[:, 0:16 * n], True, False, x + " q25", pn, 16 * n)
        for pn, y in ((pu, "i4k"), ("pU", "i2k")):
            for i in range(15): mm(T[pn][:, 16 * a + i:16 * b:16] if SP[t] else ps(pn, 32 * i, 32 * i + 32), C[y], T.landu[:, k, c], False, i == 14, y + " " + U, pn, n)
        for h in range(a, b):
            lo, hi, m = 256 * h, 256 * h + (240 if SP[t] else 256 - 32 * h), ":%d" % h
            w = hi - lo
            if SP[t]: tt(T.hT[:, lo:hi], T.KT[:, lo:lo + 256].indirect(T.prm[:, 32:47]), T.offc[:, 512:752], sub, "KT:_%d prm offc" % h, "hT" + m, w, True)
            else: tt(T.hT[:, lo:hi], T.KT[:].indirect(T.prm[:, lo // 16:hi // 16]), T.offc[:, lo:hi], sub, "KT prm offc", "hT" + m, w, True)
            tt(T.pr[:, lo:hi], T.hT[:, lo:hi], ps(pu, lo, hi), mul, pu + " hT" + m, "pr" + m, w)
            tt(T.pt[:, lo:hi], T.pr[:, lo:hi], ps("pU", lo, hi), ad, "pU pr" + m, "pt" + m, w)
            ts(T.hi[:, lo:hi], T.pt[:, lo:hi], 5, ALU.arith_shift_right, "pt" + m, "hi" + m, w, 4095, AND)
            cp(T.hoff[:, lo:hi], T.hi[:, lo:hi], "hi" + m, "hoff" + m, w)
        ts(T.vc[:, c], T.KT[:, 256 * a:256 * b:16], -2048.5, ad, h_("KT:"), h_("vc:"), n, 2.0 ** -13, ad)
        tt(T.scn[:, c], T.scn[:, 96 + 16 * a:96 + 16 * b], T.vc[:, c], sub, "scn:3 " + h_("vc:"), h_("scn:0"), 2 * n)
        ts(T.js[:, c], T.vc[:, c], 2048.0, ad, h_("vc:"), h_("js:"), n)
        act(T.xvj[:, s], X1.indirect(T.js[:, c]), AF.Copy, "X:b " + h_("js:"), h_("xvj:"), 16 * n, True)
        mm(T.pM0[:, s], idb, T.q25[:, 0:16 * n], True, False, "idb q25", "pM0", 16 * n)
        mm(T.pM0[:, s], C["hidb"], T.land[:, k, s], False, False, "hidb " + L, "pM0", 16 * n)
        mm(T.pM0[:, s], C["nhidb"], T.xvj[:, s], False, False, "nhidb " + h_("xvj:"), "pM0", 16 * n)
        whole(T.pM0[:, s], "pM0", 16 * n, "m1x", True)
        act(T.X[:, FND + 256 * a:FND + 256 * b], T.pM0[:, s], AF.Copy, "pM0", h_("X:q"), 16 * n)

    ng = [0]
    def pair(t, gi):
        k, way, m = t - 1, WAYS[t][gi], 2 - (gi == 7)
        z, L = T.land[:, k, 0:512], nm("land:z%d" % k, 0, 2)
        if gi == 0: mm(T.pE[:], rows("t85", 2), T.thc[0:2, :], True, False, "t85 thc", "pE", 512)
        e = T.pE[:, gi + 1::16 // m]
        gd = gi - WAYS[t][:gi].count("A")
        an, dn = (" ".join("%s:%d_%d" % (b, y, i) for i in range(m)) for b, y in (("lv", gi), ("dp", gd)))
        for i in range(m):
            n = 2 * gi + i
            w, hn = X1.indirect(T.hoff[:, 32 * n:32 * n + 32]), "X:b hoff:%d " % (n // 8)
            o, on, di = T.lv[:, gi, :, i::2], "lv:%d_%d" % (gi, i), "dp:%d_%d" % (gd, i)
            if way == "A" or way == "B" and i == 0:
                s, pn = ng[0] % 4, ("pM1", "pU")[ng[0] & 1]
                ng[0] += 1
                act(T.gsl[:, s], w, AF.Copy, hn, "gsl:%d" % s, 512, True)
                mm(T[pn][:], nidb, z, True, False, "nidb " + L, pn, 512)
                mm(T[pn][:], idb, T.gsl[:, s], False, True, "idb gsl:%d" % s, pn, 512)
                act(o, T[pn][:], AF.Abs, pn, on, 512)
            else:
                tt(T.dp[:, gd, :, i], w, z, sub, hn + L, di, 512, True)
                if way != "V": act(o, T.dp[:, gd, :, i], AF.Abs, di, on, 512)
        if way == "V":
            act(T.lv[:, gi, :, 0::3 - m], T.dp[:, gd, :, 0:m], AF.Relu, dn, an, 512 * m, half=True, scale=2.0)
            for s0 in range(16): mm(e, shift(1, s0), T.dp[:, gd, s0::16, 0:m], False, False, "W " + dn, "pE", 32 * m)
        for s0 in range(16): mm(e, shift(0, s0), T.lv[:, gi, s0 // 2::8, 2 * (s0 % 2):2 * (s0 % 2) + m], False, gi == 7 and s0 == 15, "W " + an, "pE", 32 * m)

    def levels(t, h, q):
        if not SP[t]: return pair(t, 4 * h + q)
        k, gi, way, i0 = t - 1, 4 * h + q if q < 3 else 8 + h, WAYS[t][4 * h + q], int(q == 3)
        z, L = T.land[:, k, 256 * h:256 * h + 256], "land:z%d_%d" % (k, h)
        if q == 0: mm(T.pE[:, 256 * h:256 * h + 256], rows("t85", 2), T.thc[0:2, 0:256], True, False, "t85 thc", "pE", 256)
        e = T.pE[:, 256 * h + (q + 1) % 4:256 * h + 256:4]
        an, dn = (" ".join("%s:%d_%d" % (b, gi, i) for i in range(4)) for b in ("lv", "df"))
        for i in range(i0, 4, 2):
            m, n = min(2, 4 - i), 4 * q + i - i0
            hn = "X:b hoff:%d " % h
            o, on = T.lv[:, gi, :, i:i + m], " ".join("lv:%d_%d" % (gi, y) for y in range(i, i + m))
            if way == "A" or way == "B" and i == i0:
                s, pn = ng[0] % 4, ("pM1", "pU")[ng[0] & 1]
                ng[0] += 1
                out = [T[pn][:, :, y::2] for y in range(2)] if m == 2 else [ps(pn, 0, 256)]
                act(T.gsl[:, s, 0:256 * m], X1.indirect(T.hoff[:, 256 * h + 16 * n:256 * h + 16 * (n + m)]), AF.Copy, hn, "gsl:%d" % s, 256 * m, True)
                for y in range(m): mm(out[y], nidb, z, y == 0, False, "nidb " + L, pn, 256)
                for y in range(m): mm(out[y], idb, T.gsl[:, s, 256 * y:256 * y + 256], False, y == m - 1, "idb gsl:%d" % s, pn, 256)
                act(o, ps(pn, 0, 256 * m), AF.Abs, pn, on, 256 * m)
            else:
                for y in range(m):
                    tt(T.df[:, gi, :, i + y], X1.indirect(T.hoff[:, 256 * h + 16 * (n + y):256 * h + 16 * (n + y + 1)]), z, sub, hn + L, "df:%d_%d" % (gi, i + y), 256, True)
                if way != "V": act(o, T.df[:, gi, :, i:i + m], AF.Abs, on.replace("lv", "df"), on, 256 * m)
        if way == "V":
            act(T.lv[:, gi], T.df[:, gi], AF.Relu, dn, an, 1024, half=True, scale=2.0)
            for s0 in range(16): mm(e, shift(1, s0), T.df[:, gi, s0::16], False, False, "W " + dn, "pE", 64)
        for s0 in range(16): mm(e, shift(0, s0), T.lv[:, gi, s0::16], False, q == 3 and s0 == 15, "W " + an, "pE", 64)

    def choose(t, a, b):
        s = slice(256 * a, 256 * b)
        scan(T.sk[:, s], T.pE[:, s], T.KT[:, s], ALU.min, ALU.max, "pE " + nm("KT:", a, b), nm("sk:", a, b), 256 * (b - a))

    def seek_end(t, a, b):
        k, c, s, n = t - 1, slice(16 * a, 16 * b), slice(256 * a, 256 * b), 16 * (b - a)
        def h_(x): return nm(x, a, b)
        J, p3 = h_("land:j%d" % k), T.g1[:, 256 * a + 15:256 * b:16]
        ts(T.ki[:, c], T.sk[:, 256 * a + 15:256 * b:16], 4096.0, mul, h_("sk:"), h_("ki:"), n)
        ts(T.pi[:, c], T.ki[:, c], 4095, AND, h_("ki:"), h_("pi:"), n)
        cp(T.pw[:, c], T.pi[:, c], h_("pi:"), h_("pw:"), n)
        tt(T.wtm[:, s], T.TR3[:].indirect(T.pw[:, c]), T.diag[:, s], sub, "TR3 diag " + h_("pw:"), h_("wtm:"), 16 * n, True)
        scan(T.g1[:, s], T.hold[:, s], T.wtm[:, s], ad, ALU.max, "hold " + h_("wtm:"), h_("g1:"), 8 * n)
        ff, s1, s2 = T.ff[:, c], T.scn[:, 32 + 16 * a:32 + 16 * b], T.scn[:, 64 + 16 * a:64 + 16 * b]
        tt(ff, T.vc[:, c], p3, eq, h_("vc:") + " " + h_("g1:"), h_("ff:f"), 2 * n)
        tt(s1, ff, T.scn[:, c], mul, h_("ff:f") + " " + h_("scn:0"), h_("scn:1"), 2 * n)
        tt(s2, s1, p3, ad, h_("scn:1") + " " + h_("g1:"), h_("scn:2"), 2 * n)
        ts(T.pw[:, c], s2, 2048.0, ad, h_("scn:2"), h_("pw:"), n)
        xn, L = "X:b X:d %s %s " % (nm("X:q", 0, 2), h_("pw:")), h_("land:z%d" % k)
        if str(t) in OPT["xa"]:
            act(T.xf[:, s], X2.indirect(T.pw[:, c]), AF.Copy, xn, h_("xf:"), 16 * n, True)
            mm(T.pM0[:, s], nidb, T.land[:, k, s], True, False, "nidb " + L, "pM0", 16 * n)
            mm(T.pM0[:, s], idb, T.xf[:, s], False, True, "idb " + h_("xf:"), "pM0", 16 * n)
            act(T.snd[:, t, s], T.pM0[:, s], AF.Abs, "pM0", h_("snd:z%d" % t), 16 * n)
        else:
            tt(T.xf[:, s], X2.indirect(T.pw[:, c]), T.land[:, k, s], sub, xn + L, h_("xf:"), 16 * n, True)
            act(T.snd[:, t, s], T.xf[:, s], AF.Abs, h_("xf:"), h_("snd:z%d" % t), 16 * n)
        tt(T.tj[:, c], ff, T.land[:, k, 544 + 16 * a:544 + 16 * b], mul, h_("ff:f") + " " + h_("land:c%d" % k), h_("tj:"), 2 * n)
        o, on = (T.snd[:, t, 512 + 16 * a:512 + 16 * b], h_("snd:j%d" % t)) if t < RO else (T.jf[:, c], h_("jf:"))
        tt(o, T.tj[:, c], T.land[:, k, 512 + 16 * a:512 + 16 * b], ad, h_("tj:") + " " + J, on, 2 * n)

    def leave(t, a, b):
        if t < RO:
            send(t, 1, "j", a, b); send(t, 1, "z", a, b)
            make_u(t, a, b)
            return
        if b == 2:
            tr(T.sndj[:], T.jf[:], "jf", nm("sndj:f%d" % t, 0, 2), 32)
            send(t, -RO, "f")
            dma(T.yj[0::2, :], T.landj[:, 0:16], "landj", "", 8, "A")
            dma(T.yj[1::2, :], T.landj[:, 16:32], "landj", "", 8, "A")
        send(t, -RO, "z", a, b)
        dma(T.yz[:, 256 * a:256 * b], T.land[:, RO, 256 * a:256 * b], nm("land:z%d" % RO, a, b), "", 64 * (b - a))

    def finds(t):
        mm(ps("pE", 0, 48), C["o16"], T.ff[:], True, True, "o16 ff", "pE", 48)
        red(col(21), ps("pE", 0, 48), ad, "pE", "pf:21", 48)
        ts(col(25), col(21), MAGIC * 2.0 ** 33, ad, "pf:21", "pf:25", 1, -MAGIC * 2.0 ** 33, ad)

    def run(name, f, t, *a):
        label[0] = name + str(t)
        f(t, *a)
    run("f", users_g, 1)
    run("a", users_a, 1)
    run("a", users_y, 1)
    run("f", users_far, 1)
    run("a", make_u, 0, 0, 2)
    for t in range(1, RO + 1):
        run("b", users_b, t)
        run("h", seek_head, t, 0, 2 - HP[t])
        if t < RO:
            if t + 1 < RO or not OPT["xu"]:
                run("a", users_a, t + 1)
                run("a", users_y, t + 1)
            run("f", users_g, t + 1)
            run("f", users_far, t + 1)
        if t == RO - 2 and OPT["xu"]:
            run("a", step_x, t + 1)
            run("a", users_a, t + 2)
            run("a", users_y, t + 2)
        for q in range(4):
            run("r", levels, t, 0, q)
            if HP[t] and q == OPT["hq"]: run("h", seek_head, t, 1, 2)
        if SP[t]: run("e", choose, t, 0, 1)
        for q in range(4):
            run("r", levels, t, 1, q)
            if SP[t] and q == OPT["tq"]:
                run("e", seek_end, t, 0, 1)
                if HP[t + 1]: run("e", leave, t, 0, 1)
        run("e", choose, t, SP[t], 2)
        run("e", seek_end, t, SP[t], 2)
        if t < RO: run("e", finds, t)
        run("e", leave, t, SP[t] * HP[t + 1], 2)
    return ops


def depend(ops):
    acc = {}
    deps = []
    for i, (q, fn, r, w, c, kind) in enumerate(ops):
        d = {}
        for lst, wr in ((r, False), (w, True)):
            for a in lst:
                b, _, k = a.partition(":")
                for (j, k2, wr2) in acc.get(b, ()):
                    if b in BANKS: d.setdefault(j, False)
                    elif (k == k2 or not k or not k2) and (wr or wr2): d[j] = True
        for lst, wr in ((r, False), (w, True)):
            for a in lst:
                b, _, k = a.partition(":")
                old = acc.get(b, [])
                if b in BANKS: old = []
                elif wr: old = [e for e in old if k and e[1] != k]
                acc[b] = old + [(i, k, wr)]
        d.pop(i, None)
        deps.append(d)
    return deps


CASES = [(1.35, 3.0, .84, 2.5, 4500, 2200, 270, 130, 500, 0, 1.15), (1.56, 3.8, 1.0, 3.2, 5500, 3000, 220, 100, 700, 0, 1.1),
         (1.9, 5.0, 1.12, 3.0, 4500, 2500, 300, 150, 500, 0, 1.0), (1.2, 2.5, .82, 2.5, 5000, 2800, 300, 150, 800, 0, 1.25)]


def timing(ops, deps, case):
    gc, sc, f, dk, rz, rj, hop, slf, issue, two, pe = case
    n = len(ops)
    dur, alt, hold, eng = [0.0] * n, [0.0] * n, [0.0] * n, [0.0] * n
    for i, (q, fn, r, w, c, kind) in enumerate(ops):
        if kind == "c":
            by = CACHE["index"].get(i)
            if by: c = 60 + (c - 60) * (gc / GC if by == "g" else sc / SC if by == "s" else max(gc, two) / GC)
            dur[i] = alt[i] = c * f * (pe if q == "P" else 1.0)
            if i in CACHE["alt"] and not by: alt[i] = CACHE["alt"][i][1] * f
        elif kind == "d": hold[i], eng[i] = 60.0, c * dk
        else: hold[i], dur[i] = issue, rj + (rz - rj) * CACHE["size"][i]
    return dur, alt, hold, eng, hop, slf, [list(d.items()) for d in deps]


def replay(qs, case, seq, a, old):
    dur, alt, hold, eng, hop, slf, pre = case
    done, why, byq = (list(x) for x in old)
    free, last, dma = {}, {}, 0.0
    for i in seq[:a]:
        last[qs[i]] = i
        if eng[i]: dma = done[i]
    for q, i in last.items(): free[q] = byq[i] + hold[i] if hold[i] else done[i]
    for i in seq[a:]:
        q = qs[i]
        t, w = free.get(q, 0.0), -2 - last.get(q, -1)
        for j, hard in pre[i]:
            if qs[j] != q: e = done[j] + hop
            elif hard: e = done[j] + slf
            else: continue
            if e > t: t, w = e, j
        why[i], byq[i], last[q] = w, t, i
        if eng[i]:
            done[i] = dma = max(dma, t + 2000.0) + eng[i]
            free[q] = t + hold[i]
        elif hold[i]:
            done[i] = t + dur[i]
            free[q] = t + hold[i]
        else: free[q] = done[i] = t + (alt[i] if q == "V" else dur[i])
    return done, why, byq


def plan(ops, deps):
    n = len(ops)
    dur, alt, hold, eng, hop, slf, pre = timing(ops, deps, CASES[OPT["pc"]])
    qs = [o[0] for o in ops]
    cum, last = 0.0, {}
    extra = [0.0] * n
    before = [dict(d) for d in deps]
    for i, (q, fn, r, w, c, kind) in enumerate(ops):
        if kind == "c" and q == "G" or kind == "d" and not r:
            if q in last: before[i].setdefault(last[q], None)
            last[q] = i
        if kind == "d" and not r:
            cum += eng[i]
            extra[i] = 2000.0 + cum
        elif eng[i]: extra[i] = 2000.0 + eng[i]
    after = [dict() for _ in range(n)]
    for i in range(n):
        for j, e in before[i].items(): after[j][i] = e
    def held(i, q): return hold[i] or (alt[i] if q == "V" else dur[i])
    def lat(i, q): return extra[i] + (alt[i] if q == "V" else dur[i])
    def edge(j, qj, qi, hard): return held(j, qj) if hard is None or (qi == qj and not hard) else lat(j, qj) + (slf if qi == qj else hop)

    def place(seq, back):
        busy = {}
        st = [0.0] * n
        for i in seq:
            best = None
            for q in "AV" if i in CACHE["alt"] and not back else qs[i]:
                h = held(i, q)
                if back: t = max([st[s] + edge(i, q, qs[s], e) for s, e in after[i].items()] + [lat(i, q)]) - h
                else: t = max([st[j] + edge(j, qs[j], q, e) for j, e in before[i].items()] + [0.0])
                b = busy.setdefault(q, [])
                lo, hi = 0, len(b)
                while lo < hi:
                    m = (lo + hi) // 2
                    if b[m][1] <= t: lo = m + 1
                    else: hi = m
                while lo < len(b) and b[lo][0] < t + h:
                    t = max(t, b[lo][1]); lo += 1
                x = t + h + OPT["vb"] * (q == "V")
                if best is None or x < best[0]: best = (x, q, lo, t, h)
            _, qs[i], lo, t, h = best
            busy[qs[i]].insert(lo, (t, t + h))
            st[i] = t + h if back else t
        return st

    def topo_order(key, back):
        pre, post = (after, before) if back else (before, after)
        left = [len(pre[i]) for i in range(n)]
        ready = [i for i in range(n) if not left[i]]
        out = []
        while ready:
            i = min(ready, key=key.get)
            ready.remove(i); out.append(i)
            for s in post[i]:
                left[s] -= 1
                if not left[s]: ready.append(s)
        return out

    pr = [0.0] * n
    for i in range(n - 1, -1, -1): pr[i] = max([pr[s] + edge(i, qs[i], qs[s], e) for s, e in after[i].items()] + [lat(i, qs[i])])
    key = {i: (-pr[i], i) for i in range(n)}
    best, x = None, OPT["seed"]
    cases = [timing(ops, deps, c) for c in CASES]
    for it in range(OPT["passes"]):
        st = place(topo_order(key, False), False)
        seq = topo_order({i: (st[i], i) for i in range(n)}, False)
        span = sum(max(replay(qs, c, seq, 0, ([0.0] * n,) * 3)[0]) for c in cases)
        if best is None or span < best[0]: best = (span, seq, list(qs))
        bk = place(topo_order({i: (-st[i] - held(i, qs[i]), -i) for i in range(n)}, True), True)
        key = {}
        for i in range(n):
            x = (x * 1103515245 + 12345) % 2147483648
            key[i] = (-bk[i] + BIAS.get(CACHE["part"].get(i), 0.0) + OPT["noise"] * x / 2147483648.0, i)
    return best[1], best[2]


def polish(ops, deps, order, qs, steps):
    n = len(ops)
    succ = [dict() for _ in range(n)]
    for i in range(n):
        for j, hard in deps[i].items(): succ[j][i] = hard
    after = [list(d.items()) for d in succ]
    cases = [timing(ops, deps, c) for c in CASES]

    def near(rng):
        d = {}
        for k in rng:
            d.setdefault(qs[order[k]], order[k])
            if cases[0][3][order[k]]: d.setdefault("D", order[k])
            if len(d) == 6: break
        return d

    def tails(case, ts, a, b, then):
        dur, alt, hold, eng, hop, slf, pre = case
        nxt = dict(then)
        for i in reversed(order[a:b + 1]):
            q = qs[i]
            d = 2000.0 + eng[i] if eng[i] else alt[i] if q == "V" else dur[i]
            t = 0.0
            for s, hard in after[i]:
                if qs[s] != q: e = hop + ts[s]
                elif hard: e = slf + ts[s]
                else: continue
                if e > t: t = e
            if eng[i]:
                if "D" in nxt: t = max(t, ts[nxt["D"]] - 2000.0)
                nxt["D"] = i
            t += d
            if q in nxt: t = max(t, (hold[i] or d) + ts[nxt[q]])
            ts[i], nxt[q] = t, i

    def through(case, old, ts, win, q2, first, then, e):
        dur, alt, hold, eng, hop, slf, pre = case
        done, why, byq = list(old[0]), list(old[1]), list(old[2])
        free = {q: byq[i] + hold[i] if hold[i] and q != "D" else done[i] for q, i in first.items()}
        last, most, top = dict(first), 0.0, -1
        for i in win:
            q = q2[i]
            t, w = free.get(q, 0.0), -2 - last.get(q, -1)
            for j, hard in pre[i]:
                if q2[j] != q: x = done[j] + hop
                elif hard: x = done[j] + slf
                else: continue
                if x > t: t, w = x, j
            why[i], byq[i], last[q] = w, t, i
            if eng[i]:
                free[q] = t + hold[i]
                free["D"] = t = max(free.get("D", 0.0), t + 2000.0) + eng[i]
                last["D"] = i
            elif hold[i]: free[q], t = t + hold[i], t + dur[i]
            else: free[q] = t = t + (alt[i] if q == "V" else dur[i])
            done[i] = t
            if t > most: most, top = t, i
            for s, hard in after[i]:
                if pos[s] > e:
                    x = t + ts[s] + (hop if q2[s] != q else slf if hard else 0.0)
                    if x > most: most, top = x, i
        for q, i in then.items():
            x = free.get(q, 0.0) + ts[i] - 2000.0 * (q == "D")
            if x > most: most, top = x, last.get(q, -1)
        return done, why, byq, most, top

    def bound(r, lo):
        pairs = []
        for done, why, byq, most, i in r:
            while i >= 0 and pos[i] >= lo:
                j = why[i]
                if j < -1:
                    j = -2 - j
                    if qs[i] != "S" and pos[j] >= lo: pairs.append((i, j))
                i = j
        return pairs

    x = [OPT["seed"]]
    def draw(m):
        x[0] = (x[0] * 1103515245 + 12345) % 2147483648
        return (x[0] >> 8) % m
    wide, base, best = OPT["wide"], None, None
    starts = list(range(0, n - wide // 2, wide // 2))
    rounds = OPT["sweeps"] * len(starts)
    for turn in range(rounds + 1):
        pos = {y: k for k, y in enumerate(order)}
        tl = [[0.0] * n for c in cases]
        for c, ts in zip(cases, tl): tails(c, ts, 0, n, {})
        now = [through(c, ([0.0] * n,) * 3, ts, order, qs, {}, {}, n) for c, ts in zip(cases, tl)]
        base = base or [r[3] for r in now]
        cur = sum(r[3] / y for r, y in zip(now, base))
        if best is None or cur < best[0]: best = (cur, order, qs)
        if turn == rounds: return best[1], best[2]
        lo = starts[turn % len(starts)]
        hi = min(n, lo + wide) - 1
        end = near(range(hi + 1, n))
        now = [through(c, r, ts, order[lo:hi + 1], qs, near(range(lo - 1, -1, -1)), end, hi) for c, r, ts in zip(cases, now, tl)]
        pairs = bound(now, lo)
        for step in range(steps // rounds if pairs else 0):
            i, j = pairs[draw(len(pairs))]
            a, b, k, how, q2 = pos[j], pos[i], (0, 0, 1, 2, 4, 8)[draw(6)], draw(OPT["mix"]), qs
            if how >= 4:
                y = (i, j)[draw(2)]
                if y in CACHE["alt"] and how < 6:
                    q2 = list(qs)
                    q2[y] = "A" if qs[y] == "V" else "V"
                elif how == 4: continue
                a = b = pos[y]
                if how > 4:
                    b = max([pos[z] + 1 for z in deps[y]] + [a - OPT["far"], lo])
                    b += draw(min([pos[z] - 1 for z in succ[y]] + [a + OPT["far"], hi]) - b + 1)
                if b < a: a, b, win = b, a, [y] + order[b:a]
                else: win = order[a + 1:b + 1] + [y]
            elif j in deps[i]: continue
            elif how & 1:
                while k and a > lo:
                    a -= 1
                    k -= qs[order[a]] == qs[i]
                mv = [i]
                for y in reversed(order[a:b]):
                    if any(z in succ[y] for z in mv): mv.append(y)
                if j in mv: continue
                win = mv[::-1] + [y for y in order[a:b] if y not in mv]
            else:
                while k and b < hi:
                    b += 1
                    k -= qs[order[b]] == qs[i]
                mv = [j]
                for y in order[a + 1:b + 1]:
                    if any(z in deps[y] for z in mv): mv.append(y)
                if i in mv: continue
                win = [y for y in order[a + 1:b + 1] if y not in mv] + mv
            most = cur + OPT["slack"] * (1 - turn / rounds) * draw(1000) / 500
            first, then = near(range(a - 1, -1, -1)), near(range(b + 1, n))
            if cur + sum((through(c, r, ts, win, q2, first, then, b)[3] - r[3]) / y for c, r, ts, y in zip(cases, now, tl, base)) > most: continue
            r = [through(c, r, ts, win + order[b + 1:hi + 1], q2, first, end, hi) for c, r, ts in zip(cases, now, tl)]
            s = sum(y[3] / z for y, z in zip(r, base))
            if s <= most:
                cur, order, qs, now = s, order[:a] + win + order[b + 1:], q2, r
                for k, y in enumerate(win): pos[y] = a + k
                for c, ts in zip(cases, tl): tails(c, ts, lo, b, then)
                pairs = bound(r, lo) or pairs


CACHE = {}


def rank_program(g, core, T, topo):
    if T.rank_of(core) is None:
        return
    ops = build(g, core, T, topo)
    if "o" not in CACHE:
        deps = depend(ops)
        CACHE["o"] = (deps,) + polish(ops, deps, *plan(ops, deps), OPT["steps"])
    deps, order, qs = CACHE["o"]
    at = {i: n for n, i in enumerate(order)}
    Q = {"V": g.vector, "A": g.scalar, "P": g.tensor, "G": g, "S": g.sync}
    token = {}
    known = {q: {} for q in Q}
    clock = {}
    count = {}
    nd = 0
    ends = []
    for i in order:
        q, fn, r, w, c, kind = ops[i]
        if qs[i] != q: q, fn = qs[i], CACHE["alt"][i][0]
        kn = known[q]
        need = {}
        for j, hard in deps[i].items():
            if hard or qs[j] != q:
                s, v = token[j]
                if ops[j][5][0] == "r" and not any(a.startswith("land") for a in r): s = "ls" + s[2:]
                if kn.get(s, 0) < v and need.get(s, (0, 0))[0] < v: need[s] = (v, j)
        for s, (v, j) in sorted(need.items(), key=lambda e: -at[e[1][1]]):
            if kn.get(s, 0) < v:
                Q[q].wait_ge(T.sem[s], v)
                kn[s] = v
                if s[0] != "r":
                    for s2, v2 in clock[j].items():
                        if kn.get(s2, 0) < v2: kn[s2] = v2
        ins = fn()
        if kind == "c":
            s = "c" + q
            count[s] = count.get(s, 0) + 1
            ins.then_inc(T.sem[s], 1)
            token[i] = (s, count[s])
        elif kind == "d":
            s = "d%d" % nd; nd += 1
            ins.then_inc(T.sem[s], 16)
            token[i] = (s, 16); ends.append(token[i])
        else:
            token[i] = ("rs" + kind[1:], c); ends.append(token[i]); ends.append(("ls" + kind[1:], c))
        clock[i] = dict(kn)
    for s, v in list(count.items()) + ends:
        if known["G"].get(s, 0) < v: g.wait_ge(T.sem[s], v)
